import numpy as np, ml_dtypes
CORES = [16,18,20,22]
N = 4
BF = ml_dtypes.bfloat16
def gentries(a):
    return np.ascontiguousarray(a.reshape(8, 16, -1).transpose(0, 2, 1)).reshape(8, -1)
def gtable(e):
    e = np.asarray(e); return np.ascontiguousarray(e.reshape(8, -1, 16).transpose(0, 2, 1)).reshape(128, -1).astype(np.int32)
V, M, J, T, S, H = 4096, 80, 3, 3, 4, 12
L = J * M
def base(rng):
    c = np.arange(V)
    lv = rng.integers(0, 64, (N, 8, 1, V)); lv[:, 1::2] = (c * 127) // V
    x = lv + rng.integers(0, 128, (N, 8, 16, V))
    k = rng.integers(0, V, (N, 8, 16, V)); k[:, 1::2] = (c + rng.integers(-(V // 32), V // 8, (N, 4, 16, V))) & (V - 1)
    z = rng.integers(20, 200, (N, 8, 1, T, M)) + rng.integers(0, 56, (N, 8, 16, T, M))
    return x, k, z, rng.integers(0, V, (N, 8, T, J, M))
def pack(x, k, z, v):
    return {"x0": np.ascontiguousarray(x.reshape(N, 128, V)).astype(np.float32).astype(BF), "k0": np.ascontiguousarray(k.reshape(N, 128, V)).astype(np.int32),
            "z0": np.ascontiguousarray(z.reshape(N, 128, T * M)).astype(np.float32).astype(BF), "v0": np.stack([gtable(a.reshape(8, -1)) for a in v])}
def setup_inputs(rng):
    return pack(*base(rng))
def setup_inputs_spread(rng):
    x = (np.exp2(8 * rng.random((N, 8, 1, V))) * rng.random((N, 8, 16, V))).astype(np.int64)
    z = (np.exp2(8 * rng.random((N, 8, 1, T, M))) * rng.random((N, 8, 16, T, M))).astype(np.int64)
    return pack(x, (V * rng.random((N, 8, 16, V)) ** 2).astype(np.int64), z, (V * rng.random((N, 8, T, J, M)) ** 3).astype(np.int64))
def setup_inputs_ends(rng):
    def tips(hi, *shape):
        return hi * rng.integers(0, 2, shape)
    h = rng.random((N, 8, 1, V)); x = np.where(h < 0.25, 255, np.where(h < 0.5, 0, tips(255, N, 8, 16, V)))
    k = np.where(rng.random((N, 8, 16, V)) < 0.8, tips(V - 1, N, 8, 16, V), rng.integers(8, V - 1, (N, 8, 16, V)))
    h = rng.random((N, 8, 1, T, M)); z = np.where(h < 0.3, 0, np.where(h < 0.6, 255, 255 * (rng.random((N, 8, 16, T, M)) < 0.25)))
    v = np.where(rng.random((N, 8, T, J, M)) < 0.7, tips(V - 1, N, 8, T, J, M), rng.integers(8, V - 1, (N, 8, T, J, M)))
    even = ((np.arange(N)[:, None] + np.arange(8)[None, :] + N) & 1 == 0)[:, :, None]
    x[..., V - 1] = np.where(even, 255, x[..., V - 1]); x[..., 0] = np.where(even, x[..., 0], 255)
    i = np.arange(16); nl = H + 1 - (H & 1)
    z[:, :, :, 0, M - 1] = 0; z[:, :, :, 0, M - 2] = np.where(i < H, 254, 255); z[:, :, :, 0, M - 3] = np.where(i < nl, 254, 255)
    v[:, :, 0, :, M - 2:] = V - 1; k[:, :, 0, V - 1] = V - 1
    x[..., 565] = 255; k[:, :, 0, 2] = 565; k[:, :, 0, 3] = V - 1; v[:, :, 0, 0, M - 3] = 2; v[:, :, 0, 1, M - 3] = 3
    x[..., 7] = 255 - (np.argsort(rng.random((N, 8, 16)), axis=2) == 0).astype(np.int64)
    k[:, :, :15, 6] = 7; k[:, :, 15, 6] = np.where(even[:, :, 0], V - 1, 0); z[:, :, :, 0, M - 5] = 0; v[:, :, 0, :, M - 5] = 6
    z[:, :, :, 0, M - 4] = z[:, :, :, 0, M - 3]; x[..., 3673] = 255; x[..., 4093] = 255
    k[:, :, 0, 4] = 3673; k[:, :, 0, 5] = 4093; v[:, :, 0, 0, M - 4] = 4; v[:, :, 0, 1, M - 4] = 5
    return pack(x, k, z, v)
def setup_inputs_corners(rng):
    x, k, z, v = base(rng); o = rng.permutation(8); c = np.arange(V)
    x[:, o[0], 8:] = 0
    x[:, o[1]] = rng.integers(1, 101, (N, 16, V)); z[:, o[1]] = 0; h = int(rng.integers(0, N))
    x[np.array([h, (h - J) % N]), o[1]] = rng.integers(200, 256, (2, 16, V)); z[:, o[1], :, 1:] = rng.integers(100, 150, (N, 16, T - 1, M))
    k[:, o[2]] = c
    k[:, o[3]] = (c + 1) & (V - 1); x[:, o[3]] = np.where(c % (S + 1) == 0, rng.integers(200, 256, (N, 16, V)), 0); z[:, o[3]] = rng.integers(100, 151, (N, 16, T, M))
    d = rng.integers(1, S + 2, (N, T, J, M))
    d[:, 0, :, 0] = S + 1; d[:, 0, :, 1] = S; d[:, 0, 0, 2] = S; d[:, 0, 1:, 2] = S + 1; d[:, 0, :-1, 3] = S; d[:, 0, -1, 3] = 1
    v[:, o[3]] = (rng.integers(0, V // (S + 1) - 1, (N, T, J, M)) + 1) * (S + 1) - d; v[:, o[3], 0, 0, 4] = V - 1
    x[:, o[4]] = 255 * (np.argsort(rng.random((N, 16, V)), axis=1) < H - 1 + (c & 3)); k[:, o[4]] = (rng.integers(0, V, (N, 16, V)) & (V - 4)) | (c & 3); z[:, o[4]] = 100
    k[:, o[5]] = (V - 1) * rng.integers(0, 2, (N, 16, V)); v[:, o[5]] = (V - 1) * rng.integers(0, 2, (N, T, J, M))
    h = rng.integers(0, 5, (N, 16, V))
    k[:, o[6]] = np.where(h == 0, 0, np.where(h == 1, V - 1, np.where(h == 2, c, np.where(h == 3, (c + 1) & (V - 1), (c - 1) & (V - 1)))))
    v[:, o[6]] = rng.choice(np.array([0, 1, V - 2, V - 1]), (N, T, J, M))
    v[:, o[7]] = rng.integers(0, V, (T, 1, 1))
    return pack(x, k, z, v)
def setup_inputs_ties(rng):
    x, k, z, v = base(rng)
    x = rng.integers(100, 103, x.shape); z = rng.integers(100, 102, z.shape); z[..., ::8] = 102
    for q in range(N):
        for g in range(0, 8, 2):
            few = rng.permutation(V)[:64]; few[0] = V - 1; k[q, g] = few[rng.integers(0, 64, (16, V))]
    k[:, ::3, 8:] = k[:, ::3, :8]
    k[:, 7, 14:, 1::2] = V - 1; x[:, 7, :, V - 1] = 103
    return pack(x, k, z, v)
def setup_inputs_meets(rng):
    x, k, z, v = base(rng)
    for q in range(N):
        for g in range(8):
            n = 8 + 16 * g; few = rng.permutation(V)[:n]; few[0] = 0; few[1] = V - 1
            k[q, g][:, few] = few[rng.integers(0, n, (16, n))]
            for j in range(1, J + 1): v[(q - j) % N, g, :, j - 1] = few[rng.integers(0, n, (T, M))]
    return pack(x, k, z, v)
def check_inputs(d):
    bad = []
    for k, lo, hi in (("x0", 0, 255), ("k0", 0, V - 1), ("z0", 0, 255), ("v0", 0, V - 1)):
        a = np.asarray(d[k]).astype(np.float64)
        if not (np.min(a) >= lo and np.max(a) <= hi): bad.append("range of " + k)
        elif np.any(a != np.floor(a)): bad.append("whole numbers of " + k)
    return bad
def to_hosts(a):
    return np.stack([np.concatenate([a[(q - j) % N, :, j - 1] for j in range(1, J + 1)], axis=1) for q in range(N)])
def to_owners(a):
    return np.stack([np.stack([a[(r + j) % N, :, (j - 1) * M:j * M] for j in range(1, J + 1)], axis=1) for r in range(N)])
def lowest(n, on):
    a = np.flatnonzero(on)
    return a[np.unique(n[a], return_index=True)[1]]
def reference(x0, k0, z0, v0):
    X = x0.astype(np.float32).astype(np.int64).reshape(N, 8, 16, V); K = k0.astype(np.int64).reshape(N, 8, 16, V)
    Z = z0.astype(np.float32).astype(np.int64).reshape(N, 8, 16, T, M); start = np.stack([gentries(a) for a in v0]).astype(np.int64).reshape(N, 8, T, J, M)
    odd = np.zeros(N, np.int64)
    for t in range(T):
        v = to_hosts(start[:, :, t])
        z = np.stack([np.concatenate([Z[(q - j) % N, :, :, t] for j in range(1, J + 1)], axis=2) for q in range(N)])
        b = np.full((N, 8, L), S + 1, np.int64); zb = np.zeros((N, 8, 16, L), np.int64); wb = np.zeros((N, 8, L), np.int64)
        logv, logk = [], []
        for s in range(1, S + 1):
            kv = np.take_along_axis(K, v[:, :, None, :], 3)
            ix = kv.transpose(0, 1, 3, 2).reshape(N, 8, L * 16)
            xk = np.take_along_axis(X, ix[:, :, None, :], 3).reshape(N, 8, 16, L, 16)
            score = np.add.reduce(np.maximum(xk - z[..., None], 0), axis=2)
            k = np.argmax(score, axis=-1)
            w = np.take_along_axis(kv, k[:, :, None, :], 2)[:, :, 0]
            xw = np.take_along_axis(X, w[:, :, None, :], 3)
            bid = np.add.reduce((xw > z).astype(np.int64), axis=2) >= H + odd[:, None, None]
            z = (z + xw) >> 1
            now = bid & (b > S)
            b = np.where(now, s, b); wb = np.where(now, w, wb); zb = np.where(now[:, :, None, :], z, zb)
            logv.append(v); logk.append(k); v = w
        u = (wb * np.add.reduce(zb, axis=2)) & (V - 1)
        bo = to_owners(b); win = np.argmin(bo, axis=2); first = np.min(bo, axis=2)
        uo = np.take_along_axis(to_owners(u), win[:, :, None, :], 2)
        every = np.zeros((N, 8, J, M), np.int64)
        end = to_hosts(every + first[:, :, None, :]); uw = to_hosts(every + uo)
        won = to_hosts(win[:, :, None, :] == np.arange(J)[None, None, :, None]) & (end <= S); lost = ~won & (end <= S)
        for q in range(N):
            for g in range(8):
                a = lowest(wb[q, g], won[q, g]); n = wb[q, g, a]
                X[q, g][:, n] = (X[q, g][:, n] + zb[q, g][:, a]) >> 1
                for s in range(S, 0, -1):
                    a = lowest(logv[s - 1][q, g], lost[q, g] & (end[q, g] >= s))
                    n = logv[s - 1][q, g, a]; i = logk[s - 1][q, g, a]; c = K[q, g, i, n]
                    K[q, g, i, n] = (((uw[q, g, a] * c) >> 5) + c + s) & (V - 1)
        odd = np.add.reduce(won.reshape(N, -1).astype(np.int64), axis=1) & 1
    f8 = np.arange(1, 9)[None, None, :, None]
    return {"yx": np.add.reduce(X.reshape(N, 128, 8, V // 8) * f8, axis=2).astype(np.float32), "yk": np.add.reduce(K.reshape(N, 128, 8, V // 8) * f8, axis=2).astype(np.float32)}

@@ -1,0 +1,650 @@
+from concourse.bass import DstId, RemoteDMATransfer
+from concourse.mybir import AluOpType, AxisListType, ActivationFunctionType
+
+A = AluOpType
+ID = ActivationFunctionType.Identity
+RELU = ActivationFunctionType.Relu
+ABS = ActivationFunctionType.Abs
+SIGN = ActivationFunctionType.Sign
+N, M, J, RACES, S, V = 4, 80, 3, 3, 4, 4096
+L = J * M
+GROUPS = ((0, 4, True), (4, 8, True), (8, 15, False))
+BIAS = ((5400.0, 2700.0, 1700.0, 2200.0, 2200.0), (400.0, 8000.0, 1300.0, 2000.0, 1400.0), (3100.0, 2500.0, 1300.0, 4300.0, -1500.0), (1200.0, 4100.0, 1800.0, 6100.0, -2100.0))
+ND = 7
+NX = 3
+ACT_EVENTS = (1,)
+WIN = V + 256
+BIG = 2.0 ** 19
+CYC, LAT, GAMMA, SIGMA = 0.9, 160.0, 1.8, 3.5
+
+SCRATCH = {}
+for _n, _w, _d in (
+        ("xw", WIN, "bfloat16"), ("kw", WIN, "float32"), ("kin", V, "int32"), ("iw", 8192, "float32"), ("zx", ND * 256, "bfloat16"),
+        ("kvu", 256, "uint16"), ("kvf", 384, "float32"), ("sh", 384, "float16"), ("xq", 384, "bfloat16"), ("R", 384, "float32"),
+        ("eq", 384, "float32"), ("ne", 384, "float32"), ("pr", 384, "float32"), ("C", 384, "float32"), ("zT0", 128, "bfloat16"), ("zT1", 128, "bfloat16"),
+        ("E", 1024, "bfloat16"), ("xg0", 512, "bfloat16"), ("xg1", 512, "bfloat16"), ("xg2", 512, "bfloat16"), ("zg", 2400, "bfloat16"),
+        ("codeI", 64, "int32"), ("vI0", 80, "int32"), ("vI1", 80, "int32"), ("vU0", 80, "uint16"), ("vU1", 80, "uint16"),
+        ("kI", 64, "int32"), ("kU", 64, "uint16"), ("zsT", 64, "float32"), ("cntT", 64, "float32"), ("wz", 64, "int32"),
+        ("u4", 64, "int32"), ("nb", 64, "float32"), ("c1", 64, "float32"), ("m1", 32, "float32"), ("own", 48, "float32"),
+        ("d1", 64, "float32"), ("dI", 16, "int32"), ("WI", 16, "int32"), ("WU", 16, "uint16"), ("bF", 16, "float32"),
+        ("bI", 16, "int32"), ("bU", 16, "uint16"), ("rcv", 144, "float32"), ("Wm", 16, "float32"), ("x1", 16, "float32"),
+        ("x2", 16, "float32"), ("lost", 16, "float32"), ("won", 16, "float32"), ("wonb", 16, "bfloat16"), ("WmI", 16, "int32"),
+        ("bw", 16, "int32"), ("uwI", 16, "int32"), ("uwU", 16, "uint16"), ("lc", 16, "float32"), ("on", 64, "float32"),
+        ("P1", 64, "float32"), ("Wp", 16, "float32"), ("kk", 64, "float32"), ("kt1", 16, "float32"), ("key", 64, "float32"),
+        ("nkey", 64, "float32"), ("keyU", 16, "uint16"), ("vall", 960, "uint16"), ("valf", 240, "float32"), ("eqm", 7680, "bfloat16"),
+        ("fl", 960, "bfloat16"), ("Fs", 960, "bfloat16"), ("fo", 80, "float32"), ("vD", 80, "float32"), ("of", 80, "float32"),
+        ("offU", 80, "uint16"), ("urep", 240, "float32"), ("xs", 960, "float32"), ("Bs", 960, "bfloat16"), ("kp", 240, "float32"),
+        ("kt", 240, "float32"), ("kz", 240, "int32"), ("kn", 240, "int32"), ("xW", 240, "bfloat16"), ("xs2", 240, "float16"),
+        ("xt2", 240, "float16"), ("xn", 240, "bfloat16"), ("tot", 1, "float32"), ("totI", 1, "int32"), ("thr", 1, "float32"),
+        ("zs", 240, "bfloat16"), ("vs", 45, "int32"), ("zl", 720, "bfloat16"), ("vl", 135, "int32"), ("pI", 8, "int32"),
+        ("pF", 24, "float32"), ("idb", 128, "bfloat16"), ("idn", 128, "bfloat16"), ("idf", 128, "float32"), ("idS", 512, "bfloat16"),
+        ("Pm", 512, "float32"), ("U", 144, "bfloat16"), ("bo1", 128, "bfloat16"), ("BO", 128, "bfloat16"), ("BW", 128, "bfloat16"),
+        ("Wt", 1920, "bfloat16"), ("W2d", 240, "float32"), ("dg", 16, "float32"), ("Wk", 16, "bfloat16"), ("rm", 256, "float32"),
+        ("rmb", 256, "bfloat16"), ("kc", 128, "bfloat16"), ("base", 64, "float32"), ("bs", 64, "float32"), ("Dm", 64, "float32"),
+        ("ln", 16, "float32"), ("idx", 1024, "bfloat16"), ("idk", 512, "float32"), ("ox", 512, "float32"), ("ok", 512, "float32"),
+        ("ones", 128, "bfloat16")):
+    SCRATCH[_n] = ("sbuf", [128, _w], _d)
+SCRATCH["Y"] = ("sbuf", [128, 16, 256], "bfloat16")
+SCRATCH["Tt"] = ("sbuf", [128, 12, 32], "float32")
+for _n in ("ps", "pz", "pc"):
+    SCRATCH[_n] = ("psum", [128, 512], "float32")
+for _n in ("pb0", "pb1", "pb2"):
+    SCRATCH[_n] = ("psum", [128, 4, 128], "float32")
+for _n in ("pa0", "pa1"):
+    SCRATCH[_n] = ("psum", [128, 2, 256], "float32")
+SEMAPHORES = ["qV", "qS", "qT", "qG", "zin", "vin", "k0", "k1", "k2", "k3", "x0", "x1", "az", "av", "a0", "a1", "a2",
+              "lz", "lv", "l0", "l1", "l2", "oy", "ok"]
+
+
+def planner(g, T):
+    queues = {"V": g.vector, "S": g.scalar, "T": g.tensor, "G": g, "Y": g.sync}
+    ops = []
+    plan = {}
+    bias = [0.0]
+
+    def is_psum(b):
+        return b in SCRATCH and SCRATCH[b][0] == "psum"
+
+    def hazards(recs, q, R, W):
+        out = []
+        for b, lo, hi in R:
+            ps = is_psum(b)
+            for r in recs.get(b, []):
+                if r[0] < hi and lo < r[1] and r[2] or ps and r[3] != q:
+                    out.append(r)
+        for b, lo, hi in W:
+            ps = is_psum(b)
+            for r in recs.get(b, []):
+                if ps or (r[0] < hi and lo < r[1]):
+                    out.append(r)
+        return out
+
+    def note(recs, q, R, W, tag):
+        for b, lo, hi in W:
+            recs[b] = [r for r in recs.get(b, []) if not (lo <= r[0] and r[1] <= hi)] + [(lo, hi, True, q, tag)]
+        for b, lo, hi in R:
+            recs[b] = [r for r in recs.get(b, []) if not (not r[2] and r[3] == q and lo <= r[0] and r[1] <= hi and q in "VSTG")] + [(lo, hi, False, q, tag)]
+
+    def rec(q, kind, fn, R, W, dur, lat, sem=None, val=0, after=None):
+        i = len(ops)
+        rq = q if kind == "c" else kind + str(i)
+        deps = {}
+        for r in hazards(plan, rq, R, W):
+            x = 0 if (q == "T" and ops[r[4]]["q"] == "T") else ops[r[4]]["lat"]
+            deps[r[4]] = max(deps.get(r[4], 0), x)
+        if after is not None:
+            deps[after] = 0
+        note(plan, rq, R, W, i)
+        ops.append({"q": q, "kind": kind, "fn": fn, "R": R, "W": W, "dur": dur, "lat": lat, "sem": sem, "val": val, "deps": deps, "rq": rq, "bias": bias[0]})
+        return i
+
+    def emit():
+        n = len(ops)
+        succ = [[] for _ in range(n)]
+        left = [len(o["deps"]) for o in ops]
+        for i, o in enumerate(ops):
+            for d, x in o["deps"].items():
+                succ[d].append((i, x))
+        prio = [0.0] * n
+        for i in range(n - 1, -1, -1):
+            prio[i] = ops[i]["dur"] + max([x + prio[k] for k, x in succ[i]] + [0.0])
+        free = {q: 0.0 for q in queues}
+        when = [0.0] * n
+        ready = {q: [i for i in range(n) if not left[i] and ops[i]["q"] == q] for q in list(queues) + ["N"]}
+        order = []
+
+        def done(i, t):
+            for k, x in succ[i]:
+                when[k] = max(when[k], t + ops[i]["dur"] + x)
+                left[k] -= 1
+                if not left[k]:
+                    ready[ops[k]["q"]].append(k)
+        while len(order) < n:
+            while ready["N"]:
+                i = ready["N"].pop()
+                order.append((when[i], len(order), i))
+                done(i, when[i])
+            best = None
+            for q in queues:
+                if ready[q]:
+                    t = max(free[q], min(when[i] for i in ready[q]))
+                    if best is None or t < best[0]:
+                        best = (t, q)
+            if best is None:
+                continue
+            t, q = best
+            i = max((i for i in ready[q] if when[i] <= t + 1.0), key=lambda i: (prio[i] + ops[i]["bias"], -i))
+            ready[q].remove(i)
+            st = max(t, when[i])
+            free[q] = st + ops[i]["dur"]
+            order.append((st, len(order), i))
+            done(i, st)
+        order.sort()
+        cnt = {q: 0 for q in queues}
+        clk = {q: {} for q in queues}
+        snap = {}
+        live = {}
+        for _, _, i in order:
+            o = ops[i]
+            q = o["q"]
+            if o["kind"] == "n":
+                snap[(o["sem"], o["val"])] = {}
+                note(live, o["rq"], o["R"], o["W"], (o["sem"], o["val"]))
+                continue
+            need = {}
+            for r in hazards(live, o["rq"], o["R"], o["W"]):
+                if q == "T" and r[3] == "T":
+                    continue
+                sm, v = r[4]
+                if need.get(sm, 0) < v:
+                    need[sm] = v
+            c = clk[q]
+            items = [(sm, v) for sm, v in need.items() if c.get(sm, 0) < v]
+            for it in items:
+                if not any(x != it and snap.get(x, {}).get(it[0], 0) >= it[1] for x in items):
+                    queues[q].wait_ge(T.sem[it[0]], it[1])
+            for it in items:
+                for k2, v2 in list(snap.get(it, {}).items()) + [it]:
+                    if c.get(k2, 0) < v2:
+                        c[k2] = v2
+            ins = o["fn"](queues[q])
+            if o["kind"] == "c":
+                cnt[q] += 1
+                ins.then_inc(T.sem["q" + q], 1)
+                tag = ("q" + q, cnt[q])
+            else:
+                if o["kind"] == "d":
+                    ins.then_inc(T.sem[o["sem"]], 16)
+                tag = (o["sem"], o["val"])
+            snap[tag] = dict(c)
+            note(live, o["rq"], o["R"], o["W"], tag)
+        return cnt
+    return rec, emit, bias
+
+
+def rank_program(g, core, T, topo):
+    rank = T.rank_of(core)
+    if rank is None:
+        return
+    rec, emit, bias = planner(g, T)
+    peers = [T.cores[(rank + j) % N] for j in (1, 2, 3)]
+
+    def width(b):
+        return 2 if b not in SCRATCH or SCRATCH[b][2] in ("bfloat16", "float16", "uint16") else 4
+
+    def cost(W, R, two=False):
+        n = W[0][2] - W[0][1]
+        if W[0] in (("kw", 0, WIN), ("xw", 0, WIN)):
+            return 50 + SIGMA * L * CYC
+        if any(r[0] in ("kw", "xw", "Wk") or r[1:] == (0, 8192) for r in R):
+            return 50 + GAMMA * n * CYC
+        if two:
+            return max(64, n * (1 if any(SCRATCH[r[0]][0] == "psum" for r in R) else 2)) * CYC
+        return max(64, n * (0.5 if all(width(r[0]) == 2 for r in W[:1] + R[:1]) else 1)) * CYC
+
+    def op(q, fn, R, W, dur):
+        rec(q, "c", fn, R, W, dur, LAT)
+
+    def iota(name, lo, hi, pattern, base, cm):
+        if SCRATCH[name][2] != "int32":
+            fn = lambda e: e.iota(T[name][:, lo:hi], pattern, base, cm, allow_small_or_imprecise_dtypes=True)
+        else:
+            fn = lambda e: e.iota(T[name][:, lo:hi], pattern, base, cm)
+        op("G", fn, [], [(name, lo, hi)], 130 + 2 * (hi - lo) * CYC)
+
+    def ts(out, W, in0, R, s1, s2, o0, o1=None):
+        if o1 is None:
+            op("V", lambda e: e.tensor_scalar(out, in0, s1, None, o0), R, W, cost(W, R))
+        else:
+            op("V", lambda e: e.tensor_scalar(out, in0, s1, s2, o0, o1), R, W, cost(W, R))
+
+    def tt(out, W, in0, in1, R, o):
+        op("V", lambda e: e.tensor_tensor(out, in0, in1, o), R, W, cost(W, R, True))
+
+    def cp(out, W, in_, R):
+        op("V", lambda e: e.tensor_copy(out, in_), R, W, cost(W, R))
+
+    def scan(out, W, d0, d1, R, o0, o1):
+        op("V", lambda e: e.tensor_tensor_scan(out, d0, d1, 0.0, o0, o1), R, W, cost(W, R))
+
+    def act(out, W, in_, R, f=ID, bias=0.0, scale=1.0):
+        n = W[0][2] - W[0][1]
+        op("S", lambda e: e.activation(out, in_, f, bias=bias, scale=scale), R, W, max(cost(W, R), n * CYC))
+
+    def mm(out, W, lhsT, rhs, R, start, stop, n=None):
+        n = n or R[-1][2] - R[-1][1]
+        op("T", lambda e: e.matmul(out, lhsT, rhs, start, stop), R, W, max(64, n) * 0.5 * (4 if SCRATCH[R[0][0]][2] == "float32" else 1))
+
+    def ms(name, lo, hi, val):
+        op("V", lambda e: e.memset(T[name][:, lo:hi], val), [], [(name, lo, hi)], max(64, hi - lo) * CYC)
+
+    last = {}
+
+    def dma(q, sem, out, in_, R, W, lat):
+        last[q] = rec(q, "d", lambda e: e.dma_start(out, in_), R, W, 60.0, lat, sem, 16, after=last.get(q))
+
+    def send(src, dsts, R, W, rsem, lsem):
+        ids = []
+        m = None
+        for p in peers:
+            a = topo.addr(p)
+            ids.append(DstId(rid=a[0], pnc=a[1]))
+            m = topo.mask(core, p) if m is None else m & topo.mask(core, p)
+        tr = RemoteDMATransfer(dst_ids=ids, dma_engine_mask=m, remote_sem=T.sem[rsem], srcs=[src], dsts=dsts, alu_op=0)
+        n = sum(m >> e & 1 for e in range(16))
+        i = rec("G", "s", lambda e: e.remote_dma_fused([tr], local_sem=T.sem[lsem]), R, [], 900.0, 1500.0, lsem, n)
+        rec("N", "n", None, [], W, 2500.0, LAT, rsem, 3 * n, after=i)
+        return n
+
+    dma("S", "zin", T.zs[:], T.z0[:], [], [("zs", 0, 240)], 2000.0)
+    dma("S", "vin", T.vs[:], T.v0[:], [], [("vs", 0, 45)], 2000.0)
+    for i in range(4):
+        dma("YS"[i % 2], "k%d" % i, T.kin[:, 1024 * i:1024 * i + 1024], T.k0[:, 1024 * i:1024 * i + 1024], [], [("kin", 1024 * i, 1024 * i + 1024)], 8000.0 + 3000.0 * i)
+    for i in range(2):
+        dma("YS"[i], "x%d" % i, T.xw[:, 2048 * i:2048 * i + 2048], T.x0[:, 2048 * i:2048 * i + 2048], [], [("xw", 2048 * i, 2048 * i + 2048)], 20000.0)
+
+    iota("pI", 0, 1, [[0, 1]], 0, 1)
+    iota("iw", 0, 256, [[1, 256]], 0, 0)
+    ne = send(T.zs[:], [T.zl[:, 240 * j:240 * j + 240] for j in range(3)], [("zs", 0, 240)], [("zl", 0, 720)], "az", "lz")
+    send(T.vs[:], [T.vl[:, 45 * j:45 * j + 45] for j in range(3)], [("vs", 0, 45)], [("vl", 0, 135)], "av", "lv")
+    iota("kc", 0, 128, [[0, 8], [-1, 16]], 15, 0)
+    iota("rm", 0, 256, [[0, 16], [1, 16]], 0, 0)
+    iota("E", 0, 1024, [[1, 64], [0, 16]], 0, 0)
+
+    def col(i):
+        return T.pF[:, i:i + 1]
+
+    def cR(i):
+        return ("pF", i, i + 1)
+    ts(T.pI[:, 1:2], [("pI", 1, 2)], T.pI[:, 0:1], [("pI", 0, 1)], 15, None, A.bitwise_and)
+    ts(T.pI[:, 2:3], [("pI", 2, 3)], T.pI[:, 0:1], [("pI", 0, 1)], 112, None, A.bitwise_and)
+    ts(T.pI[:, 3:4], [("pI", 3, 4)], T.pI[:, 0:1], [("pI", 0, 1)], 4, 1, A.arith_shift_right, A.bitwise_and)
+    cp(T.pF[:, 0:4], [("pF", 0, 4)], T.pI[:, 0:4], [("pI", 0, 4)])
+    ts(col(4), [cR(4)], col(3), [cR(3)], -1.0, 1.0, A.mult, A.add)
+    ts(col(5), [cR(5)], col(0), [cR(0)], 16.0, None, A.add)
+    ts(col(6), [cR(6)], col(0), [cR(0)], -16.0, None, A.add)
+    ts(col(7), [cR(7)], col(2), [cR(2)], 15.0, None, A.add)
+    ts(T.idb[:], [("idb", 0, 128)], T.iw[:, 0:128], [("iw", 0, 128), cR(0)], col(0), None, A.is_equal)
+    ts(T.idf[:], [("idf", 0, 128)], T.iw[:, 0:128], [("iw", 0, 128), cR(0)], col(0), None, A.is_equal)
+    for s in range(S):
+        act(T.idS[:, 128 * s:128 * s + 128], [("idS", 128 * s, 128 * s + 128)], T.idb[:], [("idb", 0, 128)], ID, scale=1024.0 * (s + 1))
+    ts(T.idn[:], [("idn", 0, 128)], T.iw[:, 0:128], [("iw", 0, 128), cR(0)], col(0), -1.0, A.is_equal, A.mult)
+    for h in range(2):
+        for q in range(2):
+            sc = {0: 0, 1: 5, -1: 6}[q - h]
+            hc = 3 if h else 4
+            o = 128 * (2 * h + q)
+            ts(T.Pm[:, o:o + 128], [("Pm", o, o + 128)], T.iw[:, 0:128], [("iw", 0, 128), cR(sc), cR(hc)], col(sc), col(hc), A.is_equal, A.mult)
+    ts(T.U[:], [("U", 0, 144)], T.iw[:, 0:144], [("iw", 0, 144), cR(7)], col(7), 16.0, A.is_equal, A.mult)
+    ts(T.rm[:], [("rm", 0, 256)], T.rm[:], [("rm", 0, 256)], 1.0, None, A.min)
+    ts(T.E[:], [("E", 0, 1024)], T.E[:], [("E", 0, 1024), cR(0)], col(0), None, A.is_equal)
+    for name, n in (("codeI", 64), ("vI0", 80), ("vI1", 80), ("vU0", 80), ("vU1", 80), ("offU", 80)):
+        ms(name, 0, n, 0)
+    for name, n in (("zsT", 64), ("cntT", 64), ("kvf", 384), ("own", 48), ("zg", 2400), ("fo", 80)):
+        ms(name, 0, n, 0.0)
+    op("V", lambda e: e.memset(T.Y[:, 15, :], 0.0), [], [("Y", 3840, 4096)], 300.0)
+    ms("thr", 0, 1, 12.0)
+    ms("Wm", 0, 16, 2.0 ** 20)
+    ms("ones", 0, 128, 1.0)
+    iota("bs", 0, 64, [[4096, 4], [0, 16]], 4096, 0)
+    iota("Dm", 0, 64, [[0, 4], [16, 16]], 4096, 0)
+    ms("base", 0, 64, 2.0 ** 20)
+    for s in range(S):
+        iota("base", 16 * s, 16 * s + 15, [[4096, 3], [0, 5]], 16384 * (s + 1) + 4096, 0)
+    iota("iw", 256, 8192, [[1, 7936]], 256, 0)
+    cp(T.rmb[:], [("rmb", 0, 256)], T.rm[:], [("rm", 0, 256)])
+    ts(T.bo1[:], [("bo1", 0, 128)], T.iw[:, 0:128], [("iw", 0, 128), cR(2)], col(2), None, A.is_ge)
+    ts(T.BW[:], [("BW", 0, 128)], T.iw[:, 0:128], [("iw", 0, 128), cR(7)], col(7), None, A.is_le)
+    tt(T.BO[:], [("BO", 0, 128)], T.bo1[:], T.BW[:], [("bo1", 0, 128), ("BW", 0, 128)], A.mult)
+    for i in range(4):
+        ts(T.pI[:, 4 + i:5 + i], [("pI", 4 + i, 5 + i)], T.pI[:, 1:2], [("pI", 1, 2)], i, 1, A.arith_shift_right, A.bitwise_and)
+    for i in range(4):
+        ts(col(9 + i), [cR(9 + i)], T.pI[:, 4 + i:5 + i], [("pI", 4 + i, 5 + i)], 2.0 ** -(2 ** i) - 1.0, 1.0, A.mult, A.add)
+    tt(col(13), [cR(13)], col(9), col(10), [cR(9), cR(10)], A.mult)
+    tt(col(14), [cR(14)], col(11), col(12), [cR(11), cR(12)], A.mult)
+    tt(col(15), [cR(15)], col(13), col(14), [cR(13), cR(14)], A.mult)
+    ts(T.BW[:], [("BW", 0, 128)], T.BO[:], [("BO", 0, 128), cR(15)], col(15), 2.0 ** 60, A.mult, A.mult)
+    ts(T.dg[:], [("dg", 0, 16)], T.iw[:, 0:16], [("iw", 0, 16), cR(1), cR(15)], col(1), col(15), A.is_equal, A.mult)
+    for a in range(15):
+        e2 = (60 - 16 * a) // 2
+        ts(T.Wt[:, 128 * a:128 * a + 128], [("Wt", 128 * a, 128 * a + 128)], T.BW[:], [("BW", 0, 128)], 2.0 ** e2, 2.0 ** e2, A.mult, A.mult)
+        e2 = (120 - 16 * a) // 2
+        ts(T.W2d[:, 16 * a:16 * a + 16], [("W2d", 16 * a, 16 * a + 16)], T.dg[:], [("dg", 0, 16)], 2.0 ** e2, 2.5 * 2.0 ** e2, A.mult, A.mult)
+    ts(T.Wk[:], [("Wk", 0, 16)], T.iw[:, 0:16], [("iw", 0, 16), cR(1)], col(1), 1.0 / 32.0, A.is_equal, A.mult)
+    ts(T.Dm[:], [("Dm", 0, 64)], T.Dm[:], [("Dm", 0, 64), cR(1)], col(1), None, A.add)
+    ts(T.ln[:], [("ln", 0, 16)], T.Dm[:, 0:16], [("Dm", 0, 16)], -4096.0, None, A.add)
+
+    def z_start(t):
+        for j in range(3):
+            cp(T.zg[:, 80 * j:80 * j + 80], [("zg", 80 * j, 80 * j + 80)], T.zl[:, 240 * j + 80 * t:240 * j + 80 * t + 80], [("zl", 0, 720)])
+
+    def v_start(t):
+        vI, vU = "vI%d" % (t % 2), "vU%d" % (t % 2)
+        for j in range(3):
+            o = 45 * j + 15 * t + 5 * j
+            cp(T[vI][:, 5 * j:5 * j + 5], [(vI, 5 * j, 5 * j + 5)], T.vl[:, o:o + 5], [("vl", 0, 135)])
+        cp(T[vU][:, 0:15], [(vU, 0, 15)], T[vI][:, 0:15], [(vI, 0, 15)])
+
+    v_start(0)
+    z_start(0)
+    for i in range(4):
+        lo, hi = 1024 * i, 1024 * i + 1024
+        ts(T.kw[:, lo:hi], [("kw", lo, hi)], T.kin[:, lo:hi], [("kin", lo, hi)], 32.0, None, A.mult)
+
+    KW = ("kw", 0, V)
+    XW = ("xw", 0, V)
+
+    def knew(t, gr, s):
+        vU = "vU%d" % (t % 2)
+        a0, a1 = GROUPS[gr][:2]
+        lo, hi, o = 16 * a0, 16 * a1, 16 * (s - 1)
+        ts(T.kvu[:, lo:hi], [("kvu", lo, hi)], T.kw[:, 0:V].indirect(T[vU][:, o + a0:o + a1]), [KW, (vU, o + a0, o + a1)], 1.0 / 32.0, None, A.mult)
+
+    def kpick(t, gr, s):
+        vU = "vU%d" % (t % 2)
+        a0, a1 = GROUPS[gr][:2]
+        n, o, q = 16 * (a1 - a0), 16 * (s - 1), 128 * gr
+        nb = (n + 31) // 32
+        act(T.kvf[:, q:q + n], [("kvf", q, q + n)], T.kw[:, 0:V].indirect(T[vU][:, o + a0:o + a1]), [KW, (vU, o + a0, o + a1)], ID, scale=1.0 / 32.0)
+        op("V", lambda e: e.transpose(T.Tt[:, 4 * gr:4 * gr + nb, :], T.kvf[:, q:q + 32 * nb]), [("kvf", q, q + 32 * nb)], [("Tt", q, q + 32 * nb)], max(64, 32 * nb) * CYC)
+        pb = "pb%d" % gr
+        for b in range(0, nb, 2):
+            for h in range(2):
+                for w in range(2):
+                    p = 128 * (2 * h + w)
+                    mm(T[pb][:, 1:3, 16 * b + 16 * h:16 * b + 16 * h + 16], [(pb, 0, 512)], T.Pm[:, p:p + 128], T.Tt[:, 4 * gr + b:4 * gr + b + 2, 16 * w:16 * w + 16],
+                       [("Pm", p, p + 128), ("Tt", q, q + 32 * nb)], w == 0, w == 1, n=32)
+
+    def score(gr, al, ah):
+        pb = "pb%d" % gr
+        a0, a1 = GROUPS[gr][:2]
+        nb = (a1 - a0 + 1) // 2
+        if al == a0:
+            mm(T[pb][:, 0, 0:32 * nb], [(pb, 0, 512)], T.idb[:], T.kc[:, 0:32 * nb], [("idb", 0, 128), ("kc", 0, 32 * nb)], True, False)
+        end = ah + (ah - al) % 2
+        l, h = 16 * (al - a0), 16 * (end - a0)
+        for c in range(16):
+            mm(T[pb][:, 0, l:h], [(pb, 0, 512)], T.U[:, 15 - c:143 - c], T.Y[:, al:end, 16 * c:16 * c + 16],
+               [("U", 0, 144), ("Y", 256 * al, 256 * end)], False, ah == a1 and c == 15, n=16 * (end - al))
+
+    chunk = [0]
+
+    def xact(t, gr, s):
+        a0, a1 = GROUPS[gr][:2]
+        n, o = 16 * (a1 - a0), 480 * (s - 1) + 16 * a0
+        zT = "zT%d" % gr
+        mm(T.pz[0:n, 0:128], [("pz", 0, 512)], T.zg[:, o:o + n], T.idb[:], [("zg", o, o + n), ("idb", 0, 128)], True, True)
+        act(T[zT][0:n, :], [(zT, 0, 128)], T.pz[0:n, 0:128], [("pz", 0, 512)], ID, scale=-1.0)
+        for i in range((a1 - a0) // 2):
+            a = a0 + 2 * i
+            xg, pa = "xg%d" % (chunk[0] % NX), "pa%d" % (chunk[0] % 2)
+            chunk[0] += 1
+            act(T[xg][:], [(xg, 0, 512)], T.xw[:, 0:V].indirect(T.kvu[:, 16 * a:16 * a + 32]), [XW, ("kvu", 16 * a, 16 * a + 32)])
+            mm(T[pa][:, :, :], [(pa, 0, 512)], T.idb[:], T[xg][:], [("idb", 0, 128), (xg, 0, 512)], True, False)
+            mm(T[pa][:, :, :], [(pa, 0, 512)], T[zT][0:n, :], T.E[0:n, 512 * i:512 * i + 512], [(zT, 0, 128), ("E", 0, 1024)], False, True, n=512)
+            act(T.Y[:, a:a + 2, :], [("Y", 256 * a, 256 * a + 512)], T[pa][:, :, :], [(pa, 0, 512)], RELU)
+        score(gr, a0, a1)
+
+    def xvec(t, gr, s):
+        a0, a1 = GROUPS[gr][:2]
+        o = 480 * (s - 1)
+        zp, ZP = T.zg[:, o + 16 * a0:o + 16 * a1], ("zg", o + 16 * a0, o + 16 * a1)
+        for k in range(16):
+            W = [("zxv", k, k + 1)]
+            if s == 1:
+                cp(T.zx[:, k:256 * (a1 - a0):16], W, zp, [ZP])
+            else:
+                q = 128 * gr
+                ts(T.zx[:, k:256 * (a1 - a0):16], W, T.sh[:, q:q + 16 * (a1 - a0)], [("sh", q, q + 16 * (a1 - a0))], -1024.0, None, A.add)
+        for a in range(a0, a1):
+            r = 256 * (a - a0)
+            tt(T.Y[:, a, :], [("Y", 256 * a, 256 * a + 256)], T.xw[:, 0:V].indirect(T.kvu[:, 16 * a:16 * a + 16]), T.zx[:, r:r + 256],
+               [XW, ("kvu", 16 * a, 16 * a + 16), ("zxv", 0, 16)], A.max)
+        score(gr, a0, a0 + 4)
+        score(gr, a0 + 4, a1)
+
+    def count(s):
+        o, q = 480 * s, 16 * (s - 1)
+        for c in range(16):
+            mm(T.pc[:, 0:30], [("pc", 0, 512)], T.U[:, 15 - c:143 - c], T.zg[:, o + c:o + 480:16], [("U", 0, 144), ("zg", o, o + 480)], c == 0, c == 15, n=30)
+        act(T.zsT[:, q:q + 15], [("zsT", q, q + 15)], T.pc[:, 0:15], [("pc", 0, 512)], ID, scale=1.0 / 16.0)
+        act(T.cntT[:, q:q + 15], [("cntT", q, q + 15)], T.pc[:, 15:30], [("pc", 0, 512)], ID, bias=0.0 if s == S else 8.0, scale=1.0 / (16.0 if s == S else 32.0))
+
+    def pick(t, gr, s):
+        vI, vU = "vI%d" % (t % 2), "vU%d" % (t % 2)
+        a0, a1 = GROUPS[gr][:2]
+        nb = (a1 - a0 + 1) // 2
+        o, q, n, pb = 16 * s, 128 * gr, 32 * nb, "pb%d" % gr
+
+        def r(x):
+            return (x, q, q + n)
+        scan(T.R[:, q:q + n], [r("R")], T.rm[:, 0:n], T[pb][:, 0, 0:n], [("rm", 0, n), (pb, 0, 512)], A.mult, A.max)
+        tt(T.eq[:, q:q + n], [r("eq")], T.R[:, q:q + n], T[pb][:, 0, 0:n], [r("R"), (pb, 0, 512)], A.is_equal)
+        for b in range(0, nb, 2):
+            p = q + 32 * b
+            tt(T.pr[:, p:p + 64], [("pr", p, p + 64)], T.eq[:, p:p + 64], T[pb][:, 1:3, 16 * b:16 * b + 32], [("eq", p, p + 64), (pb, 0, 512)], A.mult)
+        tt(T.ne[:, q:q + n], [r("ne")], T.R[:, q:q + n], T[pb][:, 0, 0:n], [r("R"), (pb, 0, 512)], A.not_equal)
+        scan(T.C[:, q:q + n], [r("C")], T.ne[:, q:q + n], T.pr[:, q:q + n], [r("ne"), r("pr")], A.mult, A.add)
+        last_k = slice(q + 15, q + 16 * (a1 - a0), 16)
+        cp(T[vU][:, o + a0:o + a1], [(vU, o + a0, o + a1)], T.C[:, last_k], [r("C")])
+        cp(T[vI][:, o + a0:o + a1], [(vI, o + a0, o + a1)], T.C[:, last_k], [r("C")])
+        cp(T.codeI[:, o - 16 + a0:o - 16 + a1], [("codeI", o - 16 + a0, o - 16 + a1)], T.R[:, last_k], [r("R")])
+
+    def zstep(t, gr, s):
+        vU = "vU%d" % (t % 2)
+        a0, a1 = GROUPS[gr][:2]
+        lo, hi, n, o, q = 16 * a0, 16 * a1, 16 * (a1 - a0), 480 * (s - 1), 128 * gr
+        lst = T.xw[:, 0:V].indirect(T[vU][:, 16 * s + a0:16 * s + a1])
+        RD = [XW, (vU, 16 * s + a0, 16 * s + a1)]
+        zp, ZP, SH, XQ = T.zg[:, o + lo:o + hi], ("zg", o + lo, o + hi), ("sh", q, q + n), ("xq", q, q + n)
+        tt(T.sh[:, q:q + n], [SH], lst, zp, RD + [ZP], A.add)
+        ts(T.sh[:, q:q + n], [SH], T.sh[:, q:q + n], [SH], 0.5, 1023.75, A.mult, A.add)
+        ts(T.zg[:, o + 480 + lo:o + 480 + hi], [("zg", o + 480 + lo, o + 480 + hi)], T.sh[:, q:q + n], [SH], -1024.0, None, A.add)
+        if s == S:
+            tt(T.zg[:, o + 720 + lo:o + 720 + hi], [("zg", o + 720 + lo, o + 720 + hi)], lst, zp, RD + [ZP], A.is_gt)
+            return
+        act(T.xq[:, q:q + n], [XQ], lst, RD)
+        mm(T.ps[:, 0:n], [("ps", 0, 512)], T.idb[:], T.xq[:, q:q + n], [("idb", 0, 128), XQ], True, False)
+        mm(T.ps[:, 0:n], [("ps", 0, 512)], T.idn[:], zp, [("idn", 0, 128), ZP], False, True)
+        op("S", lambda e: e.activation(T.zg[:, o + 720 + lo:o + 720 + hi], T.ps[:, 0:n], SIGN, bias=-0.5), [("ps", 0, 512)], [("zg", o + 720 + lo, o + 720 + hi)], n * CYC)
+
+    def race(t):
+        for s in range(1, S + 1):
+            for gr in range(len(GROUPS)):
+                steps = (knew, kpick, xact if GROUPS[gr][2] else xvec, pick, zstep)
+                for i in range(5):
+                    bias[0] = BIAS[gr][i]
+                    steps[i](t, gr, s)
+            bias[0] = BIAS[3][0]
+            count(s)
+        bias[0] = 0.0
+        finish(t, "vI%d" % (t % 2), "vU%d" % (t % 2))
+
+    def finish(t, vI, vU):
+        f64, f16 = (0, 64), (0, 16)
+        tt(T.wz[:], [("wz",) + f64], T[vI][:, 16:80], T.zsT[:], [(vI, 16, 80), ("zsT",) + f64], A.mult)
+        ts(T.nb[:], [("nb",) + f64], T.cntT[:], [("cntT",) + f64, ("thr", 0, 1)], T.thr[:], BIG, A.is_lt, A.mult)
+        ts(T.u4[:], [("u4",) + f64], T.wz[:], [("wz",) + f64], 4095, None, A.bitwise_and)
+        tt(T.nb[:], [("nb",) + f64], T.nb[:], T.base[:], [("nb",) + f64, ("base",) + f64], A.add)
+        tt(T.c1[:], [("c1",) + f64], T.u4[:], T.nb[:], [("u4",) + f64, ("nb",) + f64], A.add)
+        tt(T.m1[:], [("m1", 0, 32)], T.c1[:, 0:32], T.c1[:, 32:64], [("c1",) + f64], A.min)
+        oo = 16 * t
+        OW = ("own", oo, oo + 16)
+        own = T.own[:, oo:oo + 16]
+        tt(own, [OW], T.m1[:, 0:16], T.m1[:, 16:32], [("m1", 0, 32)], A.min)
+        rs = 48 * t
+        send(own, [T.rcv[:, rs + 16 * j:rs + 16 * j + 16] for j in range(3)], [OW], [("rcv", rs, rs + 48)], "a%d" % t, "l%d" % t)
+        bias[0] = BIAS[3][2]
+        ts(T.nb[:], [("nb",) + f64], T.cntT[:], [("cntT",) + f64, ("thr", 0, 1)], T.thr[:], BIG, A.is_lt, A.mult)
+        tt(T.d1[:], [("d1",) + f64], T[vI][:, 16:80], T.bs[:], [(vI, 16, 80), ("bs",) + f64], A.add)
+        tt(T.d1[:], [("d1",) + f64], T.d1[:], T.nb[:], [("d1",) + f64, ("nb",) + f64], A.add)
+        tt(T.c1[:, 0:32], [("c1", 0, 32)], T.d1[:, 0:32], T.d1[:, 32:64], [("d1",) + f64], A.min)
+        tt(T.dI[:], [("dI",) + f16], T.c1[:, 0:16], T.c1[:, 16:32], [("c1", 0, 32)], A.min)
+        ts(T.WI[:], [("WI",) + f16], T.dI[:], [("dI",) + f16], 4095, None, A.bitwise_and)
+        ts(T.bI[:], [("bI",) + f16], T.dI[:], [("dI",) + f16], 12, 7, A.arith_shift_right, A.bitwise_and)
+        ts(T.kI[:], [("kI",) + f64], T.codeI[:], [("codeI",) + f64], 15, None, A.bitwise_and)
+        cp(T.WU[:], [("WU",) + f16], T.WI[:], [("WI",) + f16])
+        ts(T.bF[:], [("bF",) + f16], T.bI[:], [("bI",) + f16], 4.0, 480.0, A.min, A.mult)
+        ts(T.kU[:], [("kU",) + f64], T.kI[:], [("kI",) + f64], -1.0, 15.0, A.mult, A.add)
+        tt(T.bF[:], [("bF",) + f16], T.bF[:], T.ln[:], [("bF",) + f16, ("ln",) + f16], A.add)
+        cp(T.bU[:], [("bU",) + f16], T.bF[:], [("bF",) + f16])
+        ts(T.P1[:], [("P1",) + f64], T[vI][:, 0:64], [(vI, 0, 64)], 1.0, None, A.add)
+        ts(T.Wp[:], [("Wp",) + f16], T.WI[:], [("WI",) + f16], 4097.0, None, A.add)
+        tt(T.vD[:, 0:64], [("vD", 0, 64)], T[vI][:, 0:64], T.Dm[:], [(vI, 0, 64), ("Dm",) + f64], A.subtract)
+        tt(T.vD[:, 64:80], [("vD", 64, 80)], T.WI[:], T.Dm[:, 0:16], [("WI",) + f16, ("Dm", 0, 16)], A.subtract)
+        act(T.xW[:], [("xW", 0, 240)], T.xw[:, 0:V].indirect(T.WU[:, 0:15]), [XW, ("WU",) + f16])
+        for s in range(S, 0, -1):
+            act(T.Bs[:, 240 * s - 240:240 * s], [("Bs", 240 * s - 240, 240 * s)], T.Wk[:].indirect(T.kU[:, 16 * s - 16:16 * s - 1]), [("Wk",) + f16, ("kU",) + f64])
+        for s in [x for x in range(S, 1, -1) if x not in ACT_EVENTS]:
+            cp(T.vall[:, 240 * s - 240:240 * s], [("vall", 240 * s - 240, 240 * s)], T.iw[:].indirect(T[vU][:, 16 * s - 16:16 * s - 1]), [("iw", 0, 8192), (vU, 16 * s - 16, 16 * s)])
+        tt(T.xs2[:], [("xs2", 0, 240)], T.zg[:].indirect(T.bU[:, 0:15]), T.xW[:], [("zg", 0, 2400), ("bU",) + f16, ("xW", 0, 240)], A.add)
+        ts(T.xt2[:], [("xt2", 0, 240)], T.xs2[:], [("xs2", 0, 240)], 0.5, 1023.75, A.mult, A.add)
+        ts(T.xn[:], [("xn", 0, 240)], T.xt2[:], [("xt2", 0, 240)], -1024.0, None, A.add)
+        if t + 1 < RACES:
+            v_start(t + 1)
+            z_start(t + 1)
+
+        bias[0] = BIAS[3][1]
+        def rc(j, lo, hi):
+            o = rs + 16 * (j - 1)
+            return T.rcv[:, o + lo:o + hi]
+        RC, WM = ("rcv", rs, rs + 48), ("Wm", 0, 16)
+        tt(T.Wm[:, 0:10], [("Wm", 0, 10)], T.own[:, oo:oo + 10], rc(3, 5, 15), [OW, RC], A.min)
+        tt(T.Wm[:, 10:15], [("Wm", 10, 15)], T.own[:, oo + 10:oo + 15], rc(2, 0, 5), [OW, RC], A.min)
+        tt(T.Wm[:, 0:5], [("Wm", 0, 5)], T.Wm[:, 0:5], rc(2, 10, 15), [WM, RC], A.min)
+        tt(T.Wm[:, 5:15], [("Wm", 5, 15)], T.Wm[:, 5:15], rc(1, 0, 10), [WM, RC], A.min)
+        ts(T.x1[:], [("x1",) + f16], T.Wm[:], [WM], BIG, None, A.is_lt)
+        tt(T.x2[:], [("x2",) + f16], T.Wm[:], own, [WM, OW], A.not_equal)
+        cp(T.WmI[:], [("WmI",) + f16], T.Wm[:], [WM])
+        tt(T.lost[:], [("lost",) + f16], T.x1[:], T.x2[:], [("x1",) + f16, ("x2",) + f16], A.mult)
+        ts(T.bw[:], [("bw",) + f16], T.WmI[:], [("WmI",) + f16], 14, 7, A.arith_shift_right, A.bitwise_and)
+        ts(T.uwI[:], [("uwI",) + f16], T.WmI[:], [("WmI",) + f16], 4095, None, A.bitwise_and)
+        tt(T.lc[:], [("lc",) + f16], T.bw[:], T.lost[:], [("bw",) + f16, ("lost",) + f16], A.mult)
+        tt(T.won[:], [("won",) + f16], T.x1[:], T.lost[:], [("x1",) + f16, ("lost",) + f16], A.subtract)
+        cp(T.uwU[:], [("uwU",) + f16], T.uwI[:], [("uwI",) + f16])
+        for s in range(1, S + 1):
+            ts(T.on[:, 16 * s - 16:16 * s], [("on", 16 * s - 16, 16 * s)], T.lc[:], [("lc",) + f16], float(s), None, A.is_ge)
+        tt(T.kt1[:], [("kt1",) + f16], T.won[:], T.Wp[:], [("won",) + f16, ("Wp",) + f16], A.mult)
+        tt(T.kk[:], [("kk",) + f64], T.P1[:], T.on[:], [("P1",) + f64, ("on",) + f64], A.mult)
+        tt(T.kk[:, 0:16], [("kk", 0, 16)], T.kk[:, 0:16], T.kt1[:], [("kk", 0, 16), ("kt1",) + f16], A.add)
+        ts(T.key[:, 16:64], [("key", 16, 64)], T.kk[:, 16:64], [("kk", 16, 64)], -1.0, None, A.add)
+        ts(T.key[:, 0:16], [("key", 0, 16)], T.kk[:, 0:16], [("kk", 0, 16)], -1.0, None, A.add)
+        ts(T.nkey[:], [("nkey",) + f64], T.kk[:], [("kk",) + f64], -1.0, 1.0, A.mult, A.add)
+        cp(T.keyU[:], [("keyU",) + f16], T.key[:, 0:16], [("key", 0, 16)])
+        tt(T.fo[:, 0:64], [("fo", 0, 64)], T.on[:], T.vD[:, 0:64], [("on",) + f64, ("vD", 0, 64)], A.mult)
+        tt(T.fo[:, 64:80], [("fo", 64, 80)], T.won[:], T.vD[:, 64:80], [("won",) + f16, ("vD", 64, 80)], A.mult)
+        cp(T.wonb[:], [("wonb",) + f16], T.won[:], [("won",) + f16])
+        if 1 not in ACT_EVENTS:
+            cp(T.vall[:, 0:240], [("vall", 0, 240)], T.iw[:].indirect(T.keyU[:, 0:15]), [("iw", 0, 8192), ("keyU",) + f16])
+        mm(T.pc[:, 480:495], [("pc", 0, 512)], T.ones[:], T.wonb[:, 0:15], [("ones", 0, 128), ("wonb",) + f16], True, True)
+        if t + 1 < RACES:
+            op("V", lambda e: e.tensor_reduce(T.tot[:], T.pc[:, 480:495], AxisListType.X, A.add), [("pc", 0, 512)], [("tot", 0, 1)], 64 * CYC)
+            cp(T.totI[:], [("totI", 0, 1)], T.tot[:], [("tot", 0, 1)])
+            ts(T.totI[:], [("totI", 0, 1)], T.totI[:], [("totI", 0, 1)], 1, None, A.bitwise_and)
+            ts(T.thr[:], [("thr", 0, 1)], T.totI[:], [("totI", 0, 1)], 12.0, None, A.add)
+        bank = {4: "ps", 3: "pa1", 2: "pa0", 1: "pz"}
+
+        def flat(b, lo, hi):
+            return T[b][:, 0, lo:hi] if b[:2] == "pa" else T[b][:, lo:hi]
+
+        def event(s):
+            o, r, k0 = 1920 * (s - 1), 240 * s - 240, 16 * s - 16
+            on_act = s in ACT_EVENTS
+            if on_act:
+                lst, src = (T.keyU[:, 0:15], ("keyU",) + f16) if s == 1 else (T[vU][:, k0:k0 + 15], (vU, k0, k0 + 16))
+                act(T.valf[:], [("valf", 0, 240)], T.iw[:].indirect(lst), [("iw", 0, 8192), src])
+            for a in range(15):
+                n = 240 - 16 * a
+                if on_act:
+                    act(T.eqm[:, o:o + n], [("eqm", o, o + n)], T.valf[:, 240 - n:240], [("valf", 0, 240), ("nkey", k0, k0 + 16)], ABS, bias=T.nkey[:, k0 + a:k0 + a + 1])
+                    if a in (7, 14):
+                        e0 = 1920 * (s - 1) + (0 if a == 7 else 1472)
+                        act(T.eqm[:, e0:o + n], [("eqm", e0, o + n)], T.eqm[:, e0:o + n], [("eqm", e0, o + n)], RELU, bias=1.0, scale=-1.0)
+                else:
+                    ts(T.eqm[:, o:o + n], [("eqm", o, o + n)], T.vall[:, r + 240 - n:r + 240], [("vall", r + 240 - n, r + 240), ("key", k0, k0 + 16)],
+                       T.key[:, k0 + a:k0 + a + 1], None, A.is_equal)
+                o += n
+            o = 1920 * (s - 1)
+            for a in range(15):
+                n = 240 - 16 * a
+                mm(flat(bank[s], 16 * a, 240), [(bank[s], 0, 512)], T.Wt[:, 128 * a:128 * a + 128], T.eqm[:, o:o + n], [("Wt", 0, 1920), ("eqm", o, o + n)], a == 0, a == 14)
+                o += n
+            tt(T.fl[:, r:r + 240], [("fl", r, r + 240)], flat(bank[s], 0, 240), T.W2d[:], [(bank[s], 0, 512), ("W2d", 0, 240)], A.is_lt)
+            scan(T.Fs[:, r:r + 240], [("Fs", r, r + 240)], T.rmb[:, 0:240], T.fl[:, r:r + 240], [("rmb", 0, 240), ("fl", r, r + 240)], A.mult, A.add)
+
+            def place(k):
+                of = T.of[:, k:k + 15]
+                tt(of, [("of", k, k + 15)], T.Fs[:, r + 15:r + 240:16], T.fo[:, k:k + 15], [("Fs", r, r + 240), ("fo", k, k + 15)], A.mult)
+                tt(of, [("of", k, k + 15)], of, T.Dm[:, 0:15], [("of", k, k + 15), ("Dm", 0, 15)], A.add)
+                cp(T.offU[:, k:k + 15], [("offU", k, k + 15)], of, [("of", k, k + 15)])
+            place(k0)
+            if s == 1:
+                place(64)
+
+        cp(T.urep[:], [("urep", 0, 240)], T.iw[:].indirect(T.uwU[:, 0:15]), [("iw", 0, 8192), ("uwU",) + f16])
+        for s in range(S, 0, -1):
+            r = 240 * s - 240
+            tt(T.xs[:, r:r + 240], [("xs", r, r + 240)], T.Wk[:].indirect(T.kU[:, 16 * s - 16:16 * s - 1]), T.urep[:], [("Wk",) + f16, ("kU",) + f64, ("urep", 0, 240)], A.mult)
+            bias[0] = BIAS[3][3] if s == S else BIAS[3][4]
+            event(s)
+        bias[0] = 0.0
+        cp(T.xw[:].indirect(T.offU[:, 64:79]), [("xw", 0, WIN)], T.xn[:], [("xn", 0, 240), ("offU", 64, 80)])
+        for s in range(S, 0, -1):
+            r = 240 * s - 240
+            lst = T.kw[:, 0:V].indirect(T[vU][:, 16 * s - 16:16 * s - 1])
+            RD = [KW, (vU, 16 * s - 16, 16 * s)]
+            mm(T.pc[:, 0:240], [("pc", 0, 512)], T.idS[:, 128 * s - 128:128 * s], T.Bs[:, r:r + 240], [("idS", 0, 512), ("Bs", r, r + 240)], True, False)
+            act(T.kt[:], [("kt", 0, 240)], lst, RD, ID, bias=-131072.0)
+            mm(T.pc[:, 0:240], [("pc", 0, 512)], T.idf[:], T.kt[:], [("idf", 0, 128), ("kt", 0, 240)], False, True)
+            tt(T.kp[:], [("kp", 0, 240)], lst, T.xs[:, r:r + 240], RD + [("xs", r, r + 240)], A.mult)
+            tt(T.kz[:], [("kz", 0, 240)], T.kp[:], T.pc[:, 0:240], [("kp", 0, 240), ("pc", 0, 512)], A.add)
+            ts(T.kn[:], [("kn", 0, 240)], T.kz[:], [("kz", 0, 240)], 131040, None, A.bitwise_and)
+            cp(T.kw[:].indirect(T.offU[:, 16 * s - 16:16 * s - 1]), [("kw", 0, WIN)], T.kn[:], [("kn", 0, 240), ("offU", 16 * s - 16, 16 * s - 1)])
+
+    for t in range(RACES):
+        race(t)
+    for a in range(8):
+        act(T.idx[:, 128 * a:128 * a + 128], [("idx", 128 * a, 128 * a + 128)], T.idb[:], [("idb", 0, 128)], ID, scale=float(a + 1))
+    for a in range(4):
+        act(T.idk[:, 128 * a:128 * a + 128], [("idk", 128 * a, 128 * a + 128)], T.idb[:], [("idb", 0, 128)], ID, scale=(a + 1) / 32.0)
+    for a in range(8):
+        mm(T.ps[:], [("ps", 0, 512)], T.idx[:, 128 * a:128 * a + 128], T.xw[:, 512 * a:512 * a + 512], [("idx", 0, 1024), ("xw", 512 * a, 512 * a + 512)], a == 0, a == 7)
+    act(T.ox[:], [("ox", 0, 512)], T.ps[:], [("ps", 0, 512)])
+    dma("Y", "oy", T.yx[:], T.ox[:], [("ox", 0, 512)], [], 2000.0)
+    for a in range(4):
+        mm(T.pz[:], [("pz", 0, 512)], T.idk[:, 128 * a:128 * a + 128], T.kw[:, 512 * a:512 * a + 512], [("idk", 0, 512), ("kw", 512 * a, 512 * a + 512)], a == 0, a == 3)
+    for a in range(4, 8):
+        b = "pb%d" % (a - 4) if a < 7 else "pc"
+        act(T[b][:, :, :] if a < 7 else T[b][:], [(b, 0, 512)], T.kw[:, 512 * a:512 * a + 512], [("kw", 512 * a, 512 * a + 512)], ID, scale=(a + 1) / 32.0)
+    OK = ("ok", 0, 512)
+    cp(T.ok[:], [OK], T.pb0[:, :, :], [("pb0", 0, 512)])
+    for b in ("pb1", "pb2", "pc", "pz"):
+        tt(T.ok[:], [OK], T.ok[:], T[b][:, :, :] if b[1] == "b" else T[b][:], [OK, (b, 0, 512)], A.add)
+    dma("Y", "ok", T.yk[:], T.ok[:], [OK], [], 2000.0)
+    cnt = emit()
+    g.sync.wait_ge(T.sem.oy, 16)
+    g.sync.wait_ge(T.sem.ok, 16)
+    for q in "VSTG":
+        g.wait_ge(T.sem["q" + q], cnt[q])
+    for l in ("lz", "lv", "l0", "l1", "l2"):
+        g.wait_ge(T.sem[l], ne)

@@ -8,50 +8,38 @@ ABS = ActivationFunctionType.Abs
 SIGN = ActivationFunctionType.Sign
 N, M, J, RACES, S, V = 4, 80, 3, 3, 4, 4096
 L = J * M
-GROUPS = ((0, 4, True), (4, 8, True), (8, 15, False))
-BIAS = ((5400.0, 2700.0, 1700.0, 2200.0, 2200.0), (400.0, 8000.0, 1300.0, 2000.0, 1400.0), (3100.0, 2500.0, 1300.0, 4300.0, -1500.0), (1200.0, 4100.0, 1800.0, 6100.0, -2100.0))
-ND = 7
-NX = 3
-ACT_EVENTS = (1,)
 WIN = V + 256
 BIG = 2.0 ** 19
-CYC, LAT, GAMMA, SIGMA = 0.9, 160.0, 1.8, 3.5
+CFG = {
+    "groups": ((0, 4, "V"), (4, 10, "S"), (10, 15, "V")),
+    "xcols": 1,
+    "kbank": ("pb3", "pz", "pc"),
+    "bias": {}, "rounds": 300, "seed": 1, "span": 8000.0, "shake": 1500.0,
+    "cyc": 0.9, "lat": 160.0, "gam": 1.6, "sig": 3.8, "pe": 0.5,
+}
+PLAN = {}
 
 SCRATCH = {}
-for _n, _w, _d in (
-        ("xw", WIN, "bfloat16"), ("kw", WIN, "float32"), ("kin", V, "int32"), ("iw", 8192, "float32"), ("zx", ND * 256, "bfloat16"),
-        ("kvu", 256, "uint16"), ("kvf", 384, "float32"), ("sh", 384, "float16"), ("xq", 384, "bfloat16"), ("R", 384, "float32"),
-        ("eq", 384, "float32"), ("ne", 384, "float32"), ("pr", 384, "float32"), ("C", 384, "float32"), ("zT0", 128, "bfloat16"), ("zT1", 128, "bfloat16"),
-        ("E", 1024, "bfloat16"), ("xg0", 512, "bfloat16"), ("xg1", 512, "bfloat16"), ("xg2", 512, "bfloat16"), ("zg", 2400, "bfloat16"),
-        ("codeI", 64, "int32"), ("vI0", 80, "int32"), ("vI1", 80, "int32"), ("vU0", 80, "uint16"), ("vU1", 80, "uint16"),
-        ("kI", 64, "int32"), ("kU", 64, "uint16"), ("zsT", 64, "float32"), ("cntT", 64, "float32"), ("wz", 64, "int32"),
-        ("u4", 64, "int32"), ("nb", 64, "float32"), ("c1", 64, "float32"), ("m1", 32, "float32"), ("own", 48, "float32"),
-        ("d1", 64, "float32"), ("dI", 16, "int32"), ("WI", 16, "int32"), ("WU", 16, "uint16"), ("bF", 16, "float32"),
-        ("bI", 16, "int32"), ("bU", 16, "uint16"), ("rcv", 144, "float32"), ("Wm", 16, "float32"), ("x1", 16, "float32"),
-        ("x2", 16, "float32"), ("lost", 16, "float32"), ("won", 16, "float32"), ("wonb", 16, "bfloat16"), ("WmI", 16, "int32"),
-        ("bw", 16, "int32"), ("uwI", 16, "int32"), ("uwU", 16, "uint16"), ("lc", 16, "float32"), ("on", 64, "float32"),
-        ("P1", 64, "float32"), ("Wp", 16, "float32"), ("kk", 64, "float32"), ("kt1", 16, "float32"), ("key", 64, "float32"),
-        ("nkey", 64, "float32"), ("keyU", 16, "uint16"), ("vall", 960, "uint16"), ("valf", 240, "float32"), ("eqm", 7680, "bfloat16"),
-        ("fl", 960, "bfloat16"), ("Fs", 960, "bfloat16"), ("fo", 80, "float32"), ("vD", 80, "float32"), ("of", 80, "float32"),
-        ("offU", 80, "uint16"), ("urep", 240, "float32"), ("xs", 960, "float32"), ("Bs", 960, "bfloat16"), ("kp", 240, "float32"),
-        ("kt", 240, "float32"), ("kz", 240, "int32"), ("kn", 240, "int32"), ("xW", 240, "bfloat16"), ("xs2", 240, "float16"),
-        ("xt2", 240, "float16"), ("xn", 240, "bfloat16"), ("tot", 1, "float32"), ("totI", 1, "int32"), ("thr", 1, "float32"),
-        ("zs", 240, "bfloat16"), ("vs", 45, "int32"), ("zl", 720, "bfloat16"), ("vl", 135, "int32"), ("pI", 8, "int32"),
-        ("pF", 24, "float32"), ("idb", 128, "bfloat16"), ("idn", 128, "bfloat16"), ("idf", 128, "float32"), ("idS", 512, "bfloat16"),
-        ("Pm", 512, "float32"), ("U", 144, "bfloat16"), ("bo1", 128, "bfloat16"), ("BO", 128, "bfloat16"), ("BW", 128, "bfloat16"),
-        ("Wt", 1920, "bfloat16"), ("W2d", 240, "float32"), ("dg", 16, "float32"), ("Wk", 16, "bfloat16"), ("rm", 256, "float32"),
-        ("rmb", 256, "bfloat16"), ("kc", 128, "bfloat16"), ("base", 64, "float32"), ("bs", 64, "float32"), ("Dm", 64, "float32"),
-        ("ln", 16, "float32"), ("idx", 1024, "bfloat16"), ("idk", 512, "float32"), ("ox", 512, "float32"), ("ok", 512, "float32"),
-        ("ones", 128, "bfloat16")):
-    SCRATCH[_n] = ("sbuf", [128, _w], _d)
+for _d, _l in (
+        ("bfloat16", (("xw", WIN), ("zx", 4096), ("xq", 256), ("d0", 512), ("zT", 512), ("E", 2048), ("xg0", 512), ("xg1", 512), ("xg2", 512),
+                      ("zg", 1792), ("zs", 240), ("zl", 720), ("zc", 720), ("on", 80), ("eq1", 5760), ("eqm", 7680), ("W8", 1280), ("cs", 512),
+                      ("Bs", 960), ("xW", 240), ("zW", 240), ("xn", 240), ("idb", 128), ("idn", 128), ("idB", 128), ("idM", 128), ("idS", 512),
+                      ("U", 144), ("U1", 144), ("Us", 144), ("kc", 128), ("rm", 256), ("rz", 2048), ("cst", 256), ("cneg", 32), ("Wk", 16),
+                      ("thw", 240), ("idx", 1024), ("ones", 128))),
+        ("float16", (("kvh", 1024), ("Tt", 512), ("shp", 8192), ("shc", 512), ("z4", 512), ("Pm", 512), ("ih", 128), ("ihn", 128), ("ih32", 128), ("ihd", 128),
+                     ("Uh", 144), ("val", 960), ("v16", 80), ("v1h", 48), ("urep", 240), ("kt", 240), ("m2k", 240), ("xr", 240), ("kh", 4096), ("idk", 1024))),
+        ("float32", (("kw", WIN), ("iw", 4096), ("R", 1024), ("C", 1024), ("nb", 64), ("kcol", 64), ("k1c", 48), ("nW", 16), ("valf", 240),
+                     ("xs", 960), ("kp", 240), ("of", 80), ("Dm", 16), ("base", 64), ("bs", 64), ("ln", 16), ("bF", 16), ("ge", 16), ("xy", 16),
+                     ("d1", 64), ("w1", 64), ("tot", 1), ("thr", 1), ("pF", 24), ("ox", 512), ("ok", 512), ("t8", 8))),
+        ("int32", (("kin", V), ("vs", 45), ("vl", 135), ("vI", 48), ("wz", 64), ("u4", 64), ("c1", 64), ("m1", 16), ("m3", 16), ("own", 48),
+                   ("rcv", 144), ("x", 16), ("uI", 16), ("dI", 16), ("WI", 16), ("bI", 16), ("cI", 64), ("kI", 64), ("kz", 240), ("kn", 240),
+                   ("totI", 1), ("pI", 12))),
+        ("uint16", (("kvu", 256), ("vU", 240), ("kU", 64), ("WU", 16), ("bU", 16), ("uU", 16), ("offU", 80), ("w8l", 8)))):
+    for _n, _w in _l:
+        SCRATCH[_n] = ("sbuf", [128, _w], _d)
 SCRATCH["Y"] = ("sbuf", [128, 16, 256], "bfloat16")
-SCRATCH["Tt"] = ("sbuf", [128, 12, 32], "float32")
-for _n in ("ps", "pz", "pc"):
+for _n in ("pb0", "pb1", "pb2", "pb3", "pa0", "pa1", "pz", "pc"):
     SCRATCH[_n] = ("psum", [128, 512], "float32")
-for _n in ("pb0", "pb1", "pb2"):
-    SCRATCH[_n] = ("psum", [128, 4, 128], "float32")
-for _n in ("pa0", "pa1"):
-    SCRATCH[_n] = ("psum", [128, 2, 256], "float32")
 SEMAPHORES = ["qV", "qS", "qT", "qG", "zin", "vin", "k0", "k1", "k2", "k3", "x0", "x1", "az", "av", "a0", "a1", "a2",
               "lz", "lv", "l0", "l1", "l2", "oy", "ok"]
 
@@ -83,7 +71,7 @@ def planner(g, T):
         for b, lo, hi in W:
             recs[b] = [r for r in recs.get(b, []) if not (lo <= r[0] and r[1] <= hi)] + [(lo, hi, True, q, tag)]
         for b, lo, hi in R:
-            recs[b] = [r for r in recs.get(b, []) if not (not r[2] and r[3] == q and lo <= r[0] and r[1] <= hi and q in "VSTG")] + [(lo, hi, False, q, tag)]
+            recs[b] = recs.get(b, []) + [(lo, hi, False, q, tag)]
 
     def rec(q, kind, fn, R, W, dur, lat, sem=None, val=0, after=None):
         i = len(ops)
@@ -95,7 +83,7 @@ def planner(g, T):
         if after is not None:
             deps[after] = 0
         note(plan, rq, R, W, i)
-        ops.append({"q": q, "kind": kind, "fn": fn, "R": R, "W": W, "dur": dur, "lat": lat, "sem": sem, "val": val, "deps": deps, "rq": rq, "bias": bias[0]})
+        ops.append({"q": q, "kind": kind, "fn": fn, "dur": dur, "sem": sem, "val": val, "lat": lat, "deps": deps, "after": after, "bias": bias[0], "txt": (W[0][0] if W else kind)})
         return i
 
     def emit():
@@ -108,54 +96,70 @@ def planner(g, T):
         prio = [0.0] * n
         for i in range(n - 1, -1, -1):
             prio[i] = ops[i]["dur"] + max([x + prio[k] for k, x in succ[i]] + [0.0])
-        free = {q: 0.0 for q in queues}
-        when = [0.0] * n
-        ready = {q: [i for i in range(n) if not left[i] and ops[i]["q"] == q] for q in list(queues) + ["N"]}
-        order = []
+        pred = [list(o["deps"].items()) for o in ops]
+        dur = [o["dur"] for o in ops]
 
-        def done(i, t):
-            for k, x in succ[i]:
-                when[k] = max(when[k], t + ops[i]["dur"] + x)
-                left[k] -= 1
-                if not left[k]:
-                    ready[ops[k]["q"]].append(k)
-        while len(order) < n:
-            while ready["N"]:
-                i = ready["N"].pop()
-                order.append((when[i], len(order), i))
-                done(i, when[i])
+        def place(rank, before, back):
+            start = [0.0] * n
+            busy = {q: ([], []) for q in queues}
+            for i in rank:
+                t = max([start[d] + dur[d] + x for d, x in before[i]] + [0.0])
+                if ops[i]["q"] != "N":
+                    lo, hi = busy[ops[i]["q"]]
+                    a, b = 0, len(hi)
+                    while a < b:
+                        m = (a + b) // 2
+                        if hi[m] > t:
+                            b = m
+                        else:
+                            a = m + 1
+                    while a < len(lo) and lo[a] < t + dur[i]:
+                        t = max(t, hi[a])
+                        a += 1
+                    lo.insert(a, t)
+                    hi.insert(a, t + dur[i])
+                start[i] = t
+            return start, max(start[i] + dur[i] for i in range(n))
+        if n not in PLAN:
+            key = [-prio[i] - ops[i]["bias"] for i in range(n)]
+            for i in range(n):
+                key[i] = max([key[i]] + [key[d] + 1e-3 for d, x in pred[i]])
             best = None
-            for q in queues:
-                if ready[q]:
-                    t = max(free[q], min(when[i] for i in ready[q]))
-                    if best is None or t < best[0]:
-                        best = (t, q)
-            if best is None:
-                continue
-            t, q = best
-            i = max((i for i in ready[q] if when[i] <= t + 1.0), key=lambda i: (prio[i] + ops[i]["bias"], -i))
-            ready[q].remove(i)
-            st = max(t, when[i])
-            free[q] = st + ops[i]["dur"]
-            order.append((st, len(order), i))
-            done(i, st)
-        order.sort()
+            seed = CFG["seed"]
+            for r in range(CFG["rounds"]):
+                start, end = place(sorted(range(n), key=lambda i: (key[i], i)), pred, False)
+                if best is None or end < best[0]:
+                    best = (end, start)
+                if r % 3 == 2:
+                    seed = (seed * 1103515245 + 12345) % 2 ** 31
+                    mid, key = seed % 1000 / 1000.0 * best[0], list(best[1])
+                    for i in range(n):
+                        if abs(key[i] - mid) < CFG["span"]:
+                            seed = (seed * 1103515245 + 12345) % 2 ** 31
+                            key[i] += (seed >> 8) % 1000 / 1000.0 * CFG["shake"]
+                        key[i] = max([key[i]] + [key[d] + 1e-3 for d, x in pred[i]])
+                    continue
+                late, end = place(sorted(range(n), key=lambda i: (-start[i] - dur[i], -i)), succ, True)
+                key = [-late[i] - dur[i] for i in range(n)]
+            PLAN[n] = best
+            PLAN["ops"] = ops
+        order = sorted((PLAN[n][1][i], i, i) for i in range(n))
         cnt = {q: 0 for q in queues}
         clk = {q: {} for q in queues}
         snap = {}
-        live = {}
+        tag = {}
         for _, _, i in order:
             o = ops[i]
             q = o["q"]
             if o["kind"] == "n":
-                snap[(o["sem"], o["val"])] = {}
-                note(live, o["rq"], o["R"], o["W"], (o["sem"], o["val"]))
+                tag[i] = (o["sem"], o["val"])
+                snap[tag[i]] = {}
                 continue
             need = {}
-            for r in hazards(live, o["rq"], o["R"], o["W"]):
-                if q == "T" and r[3] == "T":
+            for d in o["deps"]:
+                if d == o["after"] or (q == "T" and ops[d]["q"] == "T"):
                     continue
-                sm, v = r[4]
+                sm, v = tag[d]
                 if need.get(sm, 0) < v:
                     need[sm] = v
             c = clk[q]
@@ -171,13 +175,12 @@ def planner(g, T):
             if o["kind"] == "c":
                 cnt[q] += 1
                 ins.then_inc(T.sem["q" + q], 1)
-                tag = ("q" + q, cnt[q])
+                tag[i] = ("q" + q, cnt[q])
             else:
                 if o["kind"] == "d":
                     ins.then_inc(T.sem[o["sem"]], 16)
-                tag = (o["sem"], o["val"])
-            snap[tag] = dict(c)
-            note(live, o["rq"], o["R"], o["W"], tag)
+                tag[i] = (o["sem"], o["val"])
+            snap[tag[i]] = dict(c)
         return cnt
     return rec, emit, bias
 
@@ -188,459 +191,500 @@ def rank_program(g, core, T, topo):
         return
     rec, emit, bias = planner(g, T)
     peers = [T.cores[(rank + j) % N] for j in (1, 2, 3)]
-
-    def width(b):
-        return 2 if b not in SCRATCH or SCRATCH[b][2] in ("bfloat16", "float16", "uint16") else 4
-
-    def cost(W, R, two=False):
-        n = W[0][2] - W[0][1]
-        if W[0] in (("kw", 0, WIN), ("xw", 0, WIN)):
-            return 50 + SIGMA * L * CYC
-        if any(r[0] in ("kw", "xw", "Wk") or r[1:] == (0, 8192) for r in R):
-            return 50 + GAMMA * n * CYC
-        if two:
-            return max(64, n * (1 if any(SCRATCH[r[0]][0] == "psum" for r in R) else 2)) * CYC
-        return max(64, n * (0.5 if all(width(r[0]) == 2 for r in W[:1] + R[:1]) else 1)) * CYC
-
-    def op(q, fn, R, W, dur):
-        rec(q, "c", fn, R, W, dur, LAT)
-
-    def iota(name, lo, hi, pattern, base, cm):
-        if SCRATCH[name][2] != "int32":
-            fn = lambda e: e.iota(T[name][:, lo:hi], pattern, base, cm, allow_small_or_imprecise_dtypes=True)
-        else:
-            fn = lambda e: e.iota(T[name][:, lo:hi], pattern, base, cm)
-        op("G", fn, [], [(name, lo, hi)], 130 + 2 * (hi - lo) * CYC)
-
-    def ts(out, W, in0, R, s1, s2, o0, o1=None):
-        if o1 is None:
-            op("V", lambda e: e.tensor_scalar(out, in0, s1, None, o0), R, W, cost(W, R))
-        else:
-            op("V", lambda e: e.tensor_scalar(out, in0, s1, s2, o0, o1), R, W, cost(W, R))
-
-    def tt(out, W, in0, in1, R, o):
-        op("V", lambda e: e.tensor_tensor(out, in0, in1, o), R, W, cost(W, R, True))
-
-    def cp(out, W, in_, R):
-        op("V", lambda e: e.tensor_copy(out, in_), R, W, cost(W, R))
-
-    def scan(out, W, d0, d1, R, o0, o1):
-        op("V", lambda e: e.tensor_tensor_scan(out, d0, d1, 0.0, o0, o1), R, W, cost(W, R))
-
-    def act(out, W, in_, R, f=ID, bias=0.0, scale=1.0):
-        n = W[0][2] - W[0][1]
-        op("S", lambda e: e.activation(out, in_, f, bias=bias, scale=scale), R, W, max(cost(W, R), n * CYC))
-
-    def mm(out, W, lhsT, rhs, R, start, stop, n=None):
-        n = n or R[-1][2] - R[-1][1]
-        op("T", lambda e: e.matmul(out, lhsT, rhs, start, stop), R, W, max(64, n) * 0.5 * (4 if SCRATCH[R[0][0]][2] == "float32" else 1))
-
-    def ms(name, lo, hi, val):
-        op("V", lambda e: e.memset(T[name][:, lo:hi], val), [], [(name, lo, hi)], max(64, hi - lo) * CYC)
+    GROUPS, CYC, LAT = CFG["groups"], CFG["cyc"], CFG["lat"]
 
     last = {}
+
+    def phase(name):
+        bias[0] = CFG["bias"].get(name, 0.0)
+
+    def B(name, lo=0, hi=None, st=1, p=128):
+        hi = SCRATCH[name][1][1] if hi is None else hi
+        n = len(range(lo, hi, st))
+        return (T[name][0:p, lo:hi:st], [(name, lo, lo + (n - 1) * st + 1)], n, 2 if "16" in SCRATCH[name][2] else 4, False, False, [])
+
+    def P(name, r0, r1, c=16, p=128):
+        return (T[name][0:p, 16 * r0:16 * r1 - 16 + c], [(name, 0, 512)], 16 * (r1 - r0 - 1) + c, 4, True, False, [])
+
+    def Yv(a0, a1, c=None):
+        if c is None:
+            return (T.Y[:, a0, :] if a1 == a0 + 1 else T.Y[:, a0:a1, :], [("Y", 256 * a0, 256 * a1)], 256 * (a1 - a0), 2, False, False, [])
+        return (T.Y[:, a0:a1, 16 * c:16 * c + 16], [("Y", 256 * a0, 256 * a1)], 16 * (a1 - a0), 2, False, False, [])
+
+    def IX(win, lst):
+        return (win[0].indirect(lst[0]), win[1], 16 * lst[2], win[3], False, True, lst[1])
+
+    def arg(x):
+        return x[0] if isinstance(x, tuple) else x
+
+    def op(q, fn, out, ins, rate=None, dur=None):
+        full = [x for x in ins if isinstance(x, tuple)]
+        R = [r for x in full for r in x[1] + x[6]] + out[6]
+        if dur is None:
+            fix = 50 if q == "V" else 65
+            if out[5]:
+                dur = fix + CFG["sig"] * out[2] * CYC
+            elif any(x[5] for x in full):
+                dur = fix + CFG["gam"] * out[2] * CYC
+            else:
+                if rate is None:
+                    rate = 0.5 if out[3] == 2 and all(x[3] == 2 for x in full if x[2] > 1) else 1
+                dur = max(64, out[2] * rate) * CYC
+        rec(q, "c", fn, R, out[1], dur, LAT)
+
+    def iota(out, pattern, base, cm):
+        if out[1][0][0] == "pI":
+            fn = lambda e: e.iota(out[0], pattern, base, cm)
+        else:
+            fn = lambda e: e.iota(out[0], pattern, base, cm, allow_small_or_imprecise_dtypes=True)
+        last["G"] = rec("G", "c", fn, [], out[1], 130 + 2 * out[2] * CYC, LAT, after=last.get("G"))
+
+    def ts(out, in0, s1, o0, s2=None, o1=None):
+        if o1 is None:
+            op("V", lambda e: e.tensor_scalar(out[0], in0[0], arg(s1), None, o0), out, [in0, s1])
+        else:
+            op("V", lambda e: e.tensor_scalar(out[0], in0[0], arg(s1), arg(s2), o0, o1), out, [in0, s1, s2])
+
+    def tt(out, in0, in1, o):
+        op("V", lambda e: e.tensor_tensor(out[0], in0[0], in1[0], o), out, [in0, in1], rate=1 if in0[4] or in1[4] else 2)
+
+    def cp(out, in_):
+        op("V", lambda e: e.tensor_copy(out[0], in_[0]), out, [in_])
+
+    def scan(out, d0, d1, o0, o1):
+        op("V", lambda e: e.tensor_tensor_scan(out[0], d0[0], d1[0], 0.0, o0, o1), out, [d0, d1])
+
+    def act(out, in_, f=ID, bias=0.0, scale=1.0):
+        op("S", lambda e: e.activation(out[0], in_[0], f, bias=arg(bias), scale=arg(scale)), out, [in_, bias, scale], rate=1)
+
+    def mm(out, lhsT, rhs, start, stop):
+        op("T", lambda e: e.matmul(out[0], lhsT[0], rhs[0], start, stop), out, [lhsT, rhs],
+           dur=max(min(64, lhsT[2]), rhs[2]) * CFG["pe"] * (4 if rhs[3] == 4 else 1))
+
+    def group(terms):
+        for i, (out, lhsT, rhs) in enumerate(terms):
+            mm(out, lhsT, rhs, i == 0, i == len(terms) - 1)
+
+    def ms(out, val):
+        op("V", lambda e: e.memset(out[0], val), out, [], rate=out[3] / 4)
 
     def dma(q, sem, out, in_, R, W, lat):
         last[q] = rec(q, "d", lambda e: e.dma_start(out, in_), R, W, 60.0, lat, sem, 16, after=last.get(q))
 
-    def send(src, dsts, R, W, rsem, lsem):
+    def send(src, dsts, W, rsem, lsem):
         ids = []
         m = None
         for p in peers:
             a = topo.addr(p)
             ids.append(DstId(rid=a[0], pnc=a[1]))
             m = topo.mask(core, p) if m is None else m & topo.mask(core, p)
-        tr = RemoteDMATransfer(dst_ids=ids, dma_engine_mask=m, remote_sem=T.sem[rsem], srcs=[src], dsts=dsts, alu_op=0)
+        tr = RemoteDMATransfer(dst_ids=ids, dma_engine_mask=m, remote_sem=T.sem[rsem], srcs=[src[0]], dsts=dsts, alu_op=0)
         n = sum(m >> e & 1 for e in range(16))
-        i = rec("G", "s", lambda e: e.remote_dma_fused([tr], local_sem=T.sem[lsem]), R, [], 900.0, 1500.0, lsem, n)
-        rec("N", "n", None, [], W, 2500.0, LAT, rsem, 3 * n, after=i)
+        i = rec("G", "s", lambda e: e.remote_dma_fused([tr], local_sem=T.sem[lsem]), src[1], [], 900.0, 1500.0, lsem, n, after=last.get("G"))
+        last["G"] = i
+        rec("N", "n", None, [], W[1], 2500.0, LAT, rsem, 3 * n, after=i)
         return n
 
-    dma("S", "zin", T.zs[:], T.z0[:], [], [("zs", 0, 240)], 2000.0)
+    phase("load")
     dma("S", "vin", T.vs[:], T.v0[:], [], [("vs", 0, 45)], 2000.0)
+    dma("S", "zin", T.zs[:], T.z0[:], [], [("zs", 0, 240)], 2000.0)
     for i in range(4):
-        dma("YS"[i % 2], "k%d" % i, T.kin[:, 1024 * i:1024 * i + 1024], T.k0[:, 1024 * i:1024 * i + 1024], [], [("kin", 1024 * i, 1024 * i + 1024)], 8000.0 + 3000.0 * i)
+        dma("YS"[i % 2], "k%d" % i, T.kin[:, 1024 * i:1024 * i + 1024], T.k0[:, 1024 * i:1024 * i + 1024], [], [("kin", 1024 * i, 1024 * i + 1024)], 4500.0 + 2300.0 * i)
     for i in range(2):
-        dma("YS"[i], "x%d" % i, T.xw[:, 2048 * i:2048 * i + 2048], T.x0[:, 2048 * i:2048 * i + 2048], [], [("xw", 2048 * i, 2048 * i + 2048)], 20000.0)
+        dma("YS"[i], "x%d" % i, T.xw[:, 2048 * i:2048 * i + 2048], T.x0[:, 2048 * i:2048 * i + 2048], [], [("xw", 2048 * i, 2048 * i + 2048)], 16000.0)
 
-    iota("pI", 0, 1, [[0, 1]], 0, 1)
-    iota("iw", 0, 256, [[1, 256]], 0, 0)
-    ne = send(T.zs[:], [T.zl[:, 240 * j:240 * j + 240] for j in range(3)], [("zs", 0, 240)], [("zl", 0, 720)], "az", "lz")
-    send(T.vs[:], [T.vl[:, 45 * j:45 * j + 45] for j in range(3)], [("vs", 0, 45)], [("vl", 0, 135)], "av", "lv")
-    iota("kc", 0, 128, [[0, 8], [-1, 16]], 15, 0)
-    iota("rm", 0, 256, [[0, 16], [1, 16]], 0, 0)
-    iota("E", 0, 1024, [[1, 64], [0, 16]], 0, 0)
+    iota(B("pI", 0, 1), [[0, 1]], 0, 1)
+    iota(B("iw", 0, 256), [[1, 256]], 0, 0)
+    iota(B("kc"), [[0, 8], [-4096, 16]], 15 * 4096, 0)
+    iota(B("rm"), [[0, 16], [1, 16]], 0, 0)
+    SW = 16 * max([a1 - a0 for a0, a1, k in GROUPS if k == "S"] + [0])
+    VW = 16 * max([a1 - a0 for a0, a1, k in GROUPS if k == "V"] + [0])
+    ne = send(B("vs"), [T.vl[:, 45 * j:45 * j + 45] for j in range(3)], B("vl"), "av", "lv")
+    send(B("zs"), [T.zl[:, 240 * j:240 * j + 240] for j in range(3)], B("zl"), "az", "lz")
+    iota(B("E", 0, 16 * SW), [[1, SW], [0, 16]], 0, 0)
+    iota(B("bs"), [[4096, 4], [0, 16]], 4096, 0)
+    iota(B("Dm"), [[16, 16]], 0, 0)
+    ms(B("base"), BIG)
+    for s in range(S):
+        iota(B("base", 16 * s, 16 * s + 15), [[4096, 3], [0, 5]], 16384 * (s + 1) + 4096, 0)
+    for i in range(4):
+        act(B("iw", 256 << i, 512 << i), B("iw", 0, 256 << i), bias=float(256 << i))
 
     def col(i):
-        return T.pF[:, i:i + 1]
+        return B("pF", i, i + 1)
 
-    def cR(i):
-        return ("pF", i, i + 1)
-    ts(T.pI[:, 1:2], [("pI", 1, 2)], T.pI[:, 0:1], [("pI", 0, 1)], 15, None, A.bitwise_and)
-    ts(T.pI[:, 2:3], [("pI", 2, 3)], T.pI[:, 0:1], [("pI", 0, 1)], 112, None, A.bitwise_and)
-    ts(T.pI[:, 3:4], [("pI", 3, 4)], T.pI[:, 0:1], [("pI", 0, 1)], 4, 1, A.arith_shift_right, A.bitwise_and)
-    cp(T.pF[:, 0:4], [("pF", 0, 4)], T.pI[:, 0:4], [("pI", 0, 4)])
-    ts(col(4), [cR(4)], col(3), [cR(3)], -1.0, 1.0, A.mult, A.add)
-    ts(col(5), [cR(5)], col(0), [cR(0)], 16.0, None, A.add)
-    ts(col(6), [cR(6)], col(0), [cR(0)], -16.0, None, A.add)
-    ts(col(7), [cR(7)], col(2), [cR(2)], 15.0, None, A.add)
-    ts(T.idb[:], [("idb", 0, 128)], T.iw[:, 0:128], [("iw", 0, 128), cR(0)], col(0), None, A.is_equal)
-    ts(T.idf[:], [("idf", 0, 128)], T.iw[:, 0:128], [("iw", 0, 128), cR(0)], col(0), None, A.is_equal)
+    def pi(i):
+        return B("pI", i, i + 1)
+    I128 = B("iw", 0, 128)
+    ts(pi(1), pi(0), 15, A.bitwise_and)
+    ts(pi(2), pi(0), 112, A.bitwise_and)
+    ts(pi(3), pi(0), 4, A.arith_shift_right, 1, A.bitwise_and)
+    ts(pi(4), pi(0), 7, A.bitwise_and)
+    ts(pi(5), pi(0), 4, A.arith_shift_right)
+    ts(pi(6), pi(0), 3, A.arith_shift_right, 1, A.bitwise_and)
+    cp(B("pF", 0, 7), B("pI", 0, 7))
+    ts(col(7), col(3), -1.0, A.mult, 1.0, A.add)
+    ts(col(8), col(0), 16.0, A.add)
+    ts(col(9), col(0), -16.0, A.add)
+    ts(col(10), col(2), 15.0, A.add)
+    ts(col(11), col(0), 16.0, A.mult, 15.0, A.add)
+    ts(B("idb"), I128, col(0), A.is_equal)
+    for name, f in (("idn", -1.0), ("idB", -8192.0), ("idM", 256.0), ("ih", 1.0), ("ihn", -1.0), ("ih32", 32.0), ("ihd", 1.0 / 32.0)):
+        act(B(name), B("idb"), scale=f)
     for s in range(S):
-        act(T.idS[:, 128 * s:128 * s + 128], [("idS", 128 * s, 128 * s + 128)], T.idb[:], [("idb", 0, 128)], ID, scale=1024.0 * (s + 1))
-    ts(T.idn[:], [("idn", 0, 128)], T.iw[:, 0:128], [("iw", 0, 128), cR(0)], col(0), -1.0, A.is_equal, A.mult)
+        act(B("idS", 128 * s, 128 * s + 128), B("idb"), scale=32.0 * (s + 1))
+    for a in range(8):
+        act(B("idx", 128 * a, 128 * a + 128), B("idb"), scale=float(a + 1))
+        act(B("idk", 128 * a, 128 * a + 128), B("idb"), scale=float(a + 1))
     for h in range(2):
-        for q in range(2):
-            sc = {0: 0, 1: 5, -1: 6}[q - h]
-            hc = 3 if h else 4
-            o = 128 * (2 * h + q)
-            ts(T.Pm[:, o:o + 128], [("Pm", o, o + 128)], T.iw[:, 0:128], [("iw", 0, 128), cR(sc), cR(hc)], col(sc), col(hc), A.is_equal, A.mult)
-    ts(T.U[:], [("U", 0, 144)], T.iw[:, 0:144], [("iw", 0, 144), cR(7)], col(7), 16.0, A.is_equal, A.mult)
-    ts(T.rm[:], [("rm", 0, 256)], T.rm[:], [("rm", 0, 256)], 1.0, None, A.min)
-    ts(T.E[:], [("E", 0, 1024)], T.E[:], [("E", 0, 1024), cR(0)], col(0), None, A.is_equal)
-    for name, n in (("codeI", 64), ("vI0", 80), ("vI1", 80), ("vU0", 80), ("vU1", 80), ("offU", 80)):
-        ms(name, 0, n, 0)
-    for name, n in (("zsT", 64), ("cntT", 64), ("kvf", 384), ("own", 48), ("zg", 2400), ("fo", 80)):
-        ms(name, 0, n, 0.0)
-    op("V", lambda e: e.memset(T.Y[:, 15, :], 0.0), [], [("Y", 3840, 4096)], 300.0)
-    ms("thr", 0, 1, 12.0)
-    ms("Wm", 0, 16, 2.0 ** 20)
-    ms("ones", 0, 128, 1.0)
-    iota("bs", 0, 64, [[4096, 4], [0, 16]], 4096, 0)
-    iota("Dm", 0, 64, [[0, 4], [16, 16]], 4096, 0)
-    ms("base", 0, 64, 2.0 ** 20)
-    for s in range(S):
-        iota("base", 16 * s, 16 * s + 15, [[4096, 3], [0, 5]], 16384 * (s + 1) + 4096, 0)
-    iota("iw", 256, 8192, [[1, 7936]], 256, 0)
-    cp(T.rmb[:], [("rmb", 0, 256)], T.rm[:], [("rm", 0, 256)])
-    ts(T.bo1[:], [("bo1", 0, 128)], T.iw[:, 0:128], [("iw", 0, 128), cR(2)], col(2), None, A.is_ge)
-    ts(T.BW[:], [("BW", 0, 128)], T.iw[:, 0:128], [("iw", 0, 128), cR(7)], col(7), None, A.is_le)
-    tt(T.BO[:], [("BO", 0, 128)], T.bo1[:], T.BW[:], [("bo1", 0, 128), ("BW", 0, 128)], A.mult)
+        for w in range(2):
+            o = 128 * (2 * h + w)
+            ts(B("Pm", o, o + 128), I128, col({0: 0, 1: 8, -1: 9}[w - h]), A.is_equal, col(3 if h else 7), A.mult)
+    ts(B("U1"), B("iw", 0, 144), col(10), A.is_equal)
+    act(B("U"), B("U1"), scale=65536.0)
+    act(B("Uh"), B("U1"))
+    ts(B("Us"), B("iw", 0, 144), col(11), A.is_equal, 2.0 ** 30, A.mult)
+    ts(B("rm"), B("rm"), 1.0, A.min)
+    ts(B("E", 0, 16 * SW), B("E", 0, 16 * SW), col(0), A.is_equal)
+    ms(B("rz", 0, 16 * VW), 2048.0)
+    ms(B("rz", 0, 16 * VW, 16), -1024.0)
+    for name in ("kvh", "on", "zg", "z4", "vI"):
+        ms(B(name), 0)
+    for a0, a1, k in GROUPS:
+        for par in range(2 * (k == "V")):
+            ms(B("shp", 4096 * par + 256 * a0, 4096 * par + 256 * a1), 0.0)
+    ms(Yv(15, 16), 0.0)
+    ms(B("thr"), 8.0)
+    ms(B("ones"), 1.0)
+    ms(B("cst"), 2048.0)
+    ms(B("cneg", 0, 16), -16384.0)
+    ms(B("cneg", 16, 32), 0.0)
     for i in range(4):
-        ts(T.pI[:, 4 + i:5 + i], [("pI", 4 + i, 5 + i)], T.pI[:, 1:2], [("pI", 1, 2)], i, 1, A.arith_shift_right, A.bitwise_and)
+        ts(pi(7 + i), pi(1), i, A.arith_shift_right, 1, A.bitwise_and)
     for i in range(4):
-        ts(col(9 + i), [cR(9 + i)], T.pI[:, 4 + i:5 + i], [("pI", 4 + i, 5 + i)], 2.0 ** -(2 ** i) - 1.0, 1.0, A.mult, A.add)
-    tt(col(13), [cR(13)], col(9), col(10), [cR(9), cR(10)], A.mult)
-    tt(col(14), [cR(14)], col(11), col(12), [cR(11), cR(12)], A.mult)
-    tt(col(15), [cR(15)], col(13), col(14), [cR(13), cR(14)], A.mult)
-    ts(T.BW[:], [("BW", 0, 128)], T.BO[:], [("BO", 0, 128), cR(15)], col(15), 2.0 ** 60, A.mult, A.mult)
-    ts(T.dg[:], [("dg", 0, 16)], T.iw[:, 0:16], [("iw", 0, 16), cR(1), cR(15)], col(1), col(15), A.is_equal, A.mult)
-    for a in range(15):
-        e2 = (60 - 16 * a) // 2
-        ts(T.Wt[:, 128 * a:128 * a + 128], [("Wt", 128 * a, 128 * a + 128)], T.BW[:], [("BW", 0, 128)], 2.0 ** e2, 2.0 ** e2, A.mult, A.mult)
-        e2 = (120 - 16 * a) // 2
-        ts(T.W2d[:, 16 * a:16 * a + 16], [("W2d", 16 * a, 16 * a + 16)], T.dg[:], [("dg", 0, 16)], 2.0 ** e2, 2.5 * 2.0 ** e2, A.mult, A.mult)
-    ts(T.Wk[:], [("Wk", 0, 16)], T.iw[:, 0:16], [("iw", 0, 16), cR(1)], col(1), 1.0 / 32.0, A.is_equal, A.mult)
-    ts(T.Dm[:], [("Dm", 0, 64)], T.Dm[:], [("Dm", 0, 64), cR(1)], col(1), None, A.add)
-    ts(T.ln[:], [("ln", 0, 16)], T.Dm[:, 0:16], [("Dm", 0, 16)], -4096.0, None, A.add)
+        ts(col(12 + i), pi(7 + i), 2.0 ** -(2 ** i) - 1.0, A.mult, 1.0, A.add)
+    tt(col(16), col(12), col(13), A.mult)
+    tt(col(17), col(14), col(15), A.mult)
+    tt(col(18), col(16), col(17), A.mult)
+    ts(B("valf"), B("rm", 0, 240), 0.5, A.mult)
+    ts(B("kp"), B("rm", 0, 240), 2.5, A.mult, -2.5, A.add)
+    scan(B("thw"), B("valf"), B("kp"), A.mult, A.add)
+    ts(B("Wk"), B("iw", 0, 16), col(1), A.is_equal)
+    ts(B("ln"), B("Dm"), col(1), A.add)
+    ts(B("Dm"), B("ln"), 4096.0 - 10240.0, A.add)
+    tt(col(19), col(4), col(5), A.is_equal)
+    ts(col(20), col(6), -15.0, A.add)
+    ts(B("t8"), B("iw", 0, 8), 2.0, A.mult, col(20), A.add)
+    ts(B("w8l"), B("t8"), col(19), A.mult, 15.0, A.add)
 
-    def z_start(t):
-        for j in range(3):
-            cp(T.zg[:, 80 * j:80 * j + 80], [("zg", 80 * j, 80 * j + 80)], T.zl[:, 240 * j + 80 * t:240 * j + 80 * t + 80], [("zl", 0, 720)])
+    KW = B("kw", 0, V)
+    XW = B("xw", 0, V)
 
-    def v_start(t):
-        vI, vU = "vI%d" % (t % 2), "vU%d" % (t % 2)
+    def vU(t, s, a0=0, a1=15):
+        return B("vU", 80 * t + 16 * s + a0, 80 * t + 16 * s + a1)
+
+    def pairs(dst, o, vals, keys):
+        for a in range(15):
+            n = 240 - 16 * a
+            ts(B(dst, o, o + n), B("val", vals + 16 * a, vals + 240), B(keys[0], keys[1] + a, keys[1] + a + 1), A.is_equal)
+            o += n
+
+    for t in range(RACES):
+        phase("start%d" % min(t, 1))
         for j in range(3):
             o = 45 * j + 15 * t + 5 * j
-            cp(T[vI][:, 5 * j:5 * j + 5], [(vI, 5 * j, 5 * j + 5)], T.vl[:, o:o + 5], [("vl", 0, 135)])
-        cp(T[vU][:, 0:15], [(vU, 0, 15)], T[vI][:, 0:15], [(vI, 0, 15)])
-
-    v_start(0)
-    z_start(0)
+            cp(B("vI", 16 * t + 5 * j, 16 * t + 5 * j + 5), B("vl", o, o + 5))
+            act(B("zc", 240 * t + 80 * j, 240 * t + 80 * j + 80), B("zl", 240 * j + 80 * t, 240 * j + 80 * t + 80))
+        cp(vU(t, 0), B("vI", 16 * t, 16 * t + 15))
+    phase("start1")
+    ts(B("k1c"), B("vI"), -2048.0, A.add)
+    ts(B("v1h"), B("vI"), -2048.0, A.add)
+    for t in range(RACES):
+        act(B("val", 240 * t, 240 * t + 240), IX(B("iw"), vU(t, 0)), bias=-2048.0)
+        pairs("eq1", 1920 * t, 240 * t, ("k1c", 16 * t))
+    phase("start0")
     for i in range(4):
-        lo, hi = 1024 * i, 1024 * i + 1024
-        ts(T.kw[:, lo:hi], [("kw", lo, hi)], T.kin[:, lo:hi], [("kin", lo, hi)], 32.0, None, A.mult)
+        ts(B("kw", 1024 * i, 1024 * i + 1024), B("kin", 1024 * i, 1024 * i + 1024), 32.0, A.mult)
 
-    KW = ("kw", 0, V)
-    XW = ("xw", 0, V)
+    def sh(gr, s, st=1):
+        a0, a1, k = GROUPS[gr]
+        if s == S:
+            return B("z4", 16 * a0, 16 * a1)
+        if k == "V":
+            return B("shp", 4096 * (s % 2) + 256 * a0, 4096 * (s % 2) + 256 * a1, 16 * st)
+        return B("shc", 256 * (s % 2) + 16 * a0, 256 * (s % 2) + 16 * a1)
+
+    def zform(gr, s):
+        a0, a1, k = GROUPS[gr]
+        n = 16 * (a1 - a0)
+        if k == "V":
+            o = 4096 * (s % 2) + 256 * a0
+            scan(B("zx", 256 * a0, 256 * a1), B("rz", 0, 16 * n), B("shp", o, o + 16 * n), A.min, A.add)
+        else:
+            group([(P("pb%d" % gr, 0, 8, p=n), sh(gr, s), B("ih"))])
+            act(B("zT", 128 * gr, 128 * gr + 128, p=n), P("pb%d" % gr, 0, 8, p=n), bias=1024.0, scale=-1.0)
+
+    def zinit(t):
+        for gr, (a0, a1, k) in enumerate(GROUPS):
+            act(sh(gr, 0), B("zc", 240 * t + 16 * a0, 240 * t + 16 * a1), bias=1024.0)
+            zform(gr, 0)
 
     def knew(t, gr, s):
-        vU = "vU%d" % (t % 2)
-        a0, a1 = GROUPS[gr][:2]
-        lo, hi, o = 16 * a0, 16 * a1, 16 * (s - 1)
-        ts(T.kvu[:, lo:hi], [("kvu", lo, hi)], T.kw[:, 0:V].indirect(T[vU][:, o + a0:o + a1]), [KW, (vU, o + a0, o + a1)], 1.0 / 32.0, None, A.mult)
-
-    def kpick(t, gr, s):
-        vU = "vU%d" % (t % 2)
-        a0, a1 = GROUPS[gr][:2]
-        n, o, q = 16 * (a1 - a0), 16 * (s - 1), 128 * gr
-        nb = (n + 31) // 32
-        act(T.kvf[:, q:q + n], [("kvf", q, q + n)], T.kw[:, 0:V].indirect(T[vU][:, o + a0:o + a1]), [KW, (vU, o + a0, o + a1)], ID, scale=1.0 / 32.0)
-        op("V", lambda e: e.transpose(T.Tt[:, 4 * gr:4 * gr + nb, :], T.kvf[:, q:q + 32 * nb]), [("kvf", q, q + 32 * nb)], [("Tt", q, q + 32 * nb)], max(64, 32 * nb) * CYC)
-        pb = "pb%d" % gr
-        for b in range(0, nb, 2):
-            for h in range(2):
-                for w in range(2):
-                    p = 128 * (2 * h + w)
-                    mm(T[pb][:, 1:3, 16 * b + 16 * h:16 * b + 16 * h + 16], [(pb, 0, 512)], T.Pm[:, p:p + 128], T.Tt[:, 4 * gr + b:4 * gr + b + 2, 16 * w:16 * w + 16],
-                       [("Pm", p, p + 128), ("Tt", q, q + 32 * nb)], w == 0, w == 1, n=32)
+        a0, a1, k = GROUPS[gr]
+        nb, o = (a1 - a0 + 1) // 2, 256 * (s - 1) + 16 * a0
+        act(B("kvh", o, o + 16 * (a1 - a0)), IX(KW, vU(t, s - 1, a0, a1)), bias=-2048.0, scale=1.0 / 32.0)
+        ts(B("kvu", 16 * a0, 16 * a1), B("kvh", o, o + 16 * (a1 - a0)), 2048.0, A.add)
+        tb, src = B("Tt", 128 * gr, 128 * gr + 32 * nb), B("kvh", o, o + 32 * nb)
+        op("V", lambda e: e.transpose(tb[0], src[0]), tb, [src])
 
     def score(gr, al, ah):
-        pb = "pb%d" % gr
-        a0, a1 = GROUPS[gr][:2]
-        nb = (a1 - a0 + 1) // 2
+        a0, a1, k = GROUPS[gr]
+        pb, w = "pb%d" % gr, 2 * ((a1 - a0 + 1) // 2)
         if al == a0:
-            mm(T[pb][:, 0, 0:32 * nb], [(pb, 0, 512)], T.idb[:], T.kc[:, 0:32 * nb], [("idb", 0, 128), ("kc", 0, 32 * nb)], True, False)
-        end = ah + (ah - al) % 2
-        l, h = 16 * (al - a0), 16 * (end - a0)
+            mm(P(pb, 0, w), B("idb"), B("kc", 0, 16 * w), True, False)
+        end = a0 + w if ah == a1 else ah
         for c in range(16):
-            mm(T[pb][:, 0, l:h], [(pb, 0, 512)], T.U[:, 15 - c:143 - c], T.Y[:, al:end, 16 * c:16 * c + 16],
-               [("U", 0, 144), ("Y", 256 * al, 256 * end)], False, ah == a1 and c == 15, n=16 * (end - al))
+            mm(P(pb, al - a0, end - a0), B("U", 15 - c, 143 - c), Yv(al, end, c), False, ah == a1 and c == 15)
 
     chunk = [0]
 
-    def xact(t, gr, s):
-        a0, a1 = GROUPS[gr][:2]
-        n, o = 16 * (a1 - a0), 480 * (s - 1) + 16 * a0
-        zT = "zT%d" % gr
-        mm(T.pz[0:n, 0:128], [("pz", 0, 512)], T.zg[:, o:o + n], T.idb[:], [("zg", o, o + n), ("idb", 0, 128)], True, True)
-        act(T[zT][0:n, :], [(zT, 0, 128)], T.pz[0:n, 0:128], [("pz", 0, 512)], ID, scale=-1.0)
-        for i in range((a1 - a0) // 2):
-            a = a0 + 2 * i
-            xg, pa = "xg%d" % (chunk[0] % NX), "pa%d" % (chunk[0] % 2)
+    def xact(gr):
+        a0, a1, k = GROUPS[gr]
+        n = 16 * (a1 - a0)
+        for a in range(a0, a1, 2):
+            e = min(a + 2, a1)
+            xg, pa, o = B("xg%d" % (chunk[0] % 3), 0, 256 * (e - a)), P("pa%d" % (chunk[0] % 2), 0, 16 * (e - a)), 256 * (a - a0)
             chunk[0] += 1
-            act(T[xg][:], [(xg, 0, 512)], T.xw[:, 0:V].indirect(T.kvu[:, 16 * a:16 * a + 32]), [XW, ("kvu", 16 * a, 16 * a + 32)])
-            mm(T[pa][:, :, :], [(pa, 0, 512)], T.idb[:], T[xg][:], [("idb", 0, 128), (xg, 0, 512)], True, False)
-            mm(T[pa][:, :, :], [(pa, 0, 512)], T[zT][0:n, :], T.E[0:n, 512 * i:512 * i + 512], [(zT, 0, 128), ("E", 0, 1024)], False, True, n=512)
-            act(T.Y[:, a:a + 2, :], [("Y", 256 * a, 256 * a + 512)], T[pa][:, :, :], [(pa, 0, 512)], RELU)
+            act(xg, IX(XW, B("kvu", 16 * a, 16 * e)))
+            group([(pa, B("idb"), xg), (pa, B("zT", 128 * gr, 128 * gr + 128, p=n), B("E", o, o + 256 * (e - a), p=n))])
+            act(Yv(a, e), pa, RELU)
         score(gr, a0, a1)
 
-    def xvec(t, gr, s):
-        a0, a1 = GROUPS[gr][:2]
-        o = 480 * (s - 1)
-        zp, ZP = T.zg[:, o + 16 * a0:o + 16 * a1], ("zg", o + 16 * a0, o + 16 * a1)
-        for k in range(16):
-            W = [("zxv", k, k + 1)]
-            if s == 1:
-                cp(T.zx[:, k:256 * (a1 - a0):16], W, zp, [ZP])
-            else:
-                q = 128 * gr
-                ts(T.zx[:, k:256 * (a1 - a0):16], W, T.sh[:, q:q + 16 * (a1 - a0)], [("sh", q, q + 16 * (a1 - a0))], -1024.0, None, A.add)
-        for a in range(a0, a1):
-            r = 256 * (a - a0)
-            tt(T.Y[:, a, :], [("Y", 256 * a, 256 * a + 256)], T.xw[:, 0:V].indirect(T.kvu[:, 16 * a:16 * a + 16]), T.zx[:, r:r + 256],
-               [XW, ("kvu", 16 * a, 16 * a + 16), ("zxv", 0, 16)], A.max)
-        score(gr, a0, a0 + 4)
-        score(gr, a0 + 4, a1)
-
-    def count(s):
-        o, q = 480 * s, 16 * (s - 1)
-        for c in range(16):
-            mm(T.pc[:, 0:30], [("pc", 0, 512)], T.U[:, 15 - c:143 - c], T.zg[:, o + c:o + 480:16], [("U", 0, 144), ("zg", o, o + 480)], c == 0, c == 15, n=30)
-        act(T.zsT[:, q:q + 15], [("zsT", q, q + 15)], T.pc[:, 0:15], [("pc", 0, 512)], ID, scale=1.0 / 16.0)
-        act(T.cntT[:, q:q + 15], [("cntT", q, q + 15)], T.pc[:, 15:30], [("pc", 0, 512)], ID, bias=0.0 if s == S else 8.0, scale=1.0 / (16.0 if s == S else 32.0))
+    def xvec(gr):
+        a0, a1, k = GROUPS[gr]
+        for a in range(a0, a1, CFG["xcols"]):
+            e = min(a + CFG["xcols"], a1)
+            tt(Yv(a, e), IX(XW, B("kvu", 16 * a, 16 * e)), B("zx", 256 * a, 256 * e), A.max)
+        if a1 - a0 >= 7:
+            score(gr, a0, a0 + 4)
+            score(gr, a0 + 4, a1)
+        else:
+            score(gr, a0, a1)
 
     def pick(t, gr, s):
-        vI, vU = "vI%d" % (t % 2), "vU%d" % (t % 2)
-        a0, a1 = GROUPS[gr][:2]
+        a0, a1, k = GROUPS[gr]
         nb = (a1 - a0 + 1) // 2
-        o, q, n, pb = 16 * s, 128 * gr, 32 * nb, "pb%d" % gr
+        n, o, pb = 32 * nb, 256 * (s - 1) + 16 * a0, "pb%d" % gr
+        key, R, D, C = P(pb, 0, 2 * nb), B("R", o, o + n), B("d0", 128 * gr, 128 * gr + n), B("C", o, o + n)
+        scan(R, B("rm", 0, n), key, A.mult, A.max)
+        tt(D, R, key, A.subtract)
+        pk = CFG["kbank"][gr]
+        terms = [(P(pk, 16, 16 + 2 * nb), B("idb"), B("cst", 0, n))]
+        for b in range(nb):
+            for h in range(2):
+                for w in range(2):
+                    q = 128 * gr + 32 * b + 16 * w
+                    terms.append((P(pk, 16 + 2 * b + h, 17 + 2 * b + h), B("Pm", 128 * (2 * h + w), 128 * (2 * h + w) + 128), B("Tt", q, q + 16)))
+        group(terms + [(P(pk, 16, 16 + 2 * nb), B("idn"), D)])
+        scan(C, D, P(pk, 16, 16 + 2 * nb), A.min, A.max)
+        cp(vU(t, s, a0, a1), B("C", o + 15, o + 16 * (a1 - a0), 16))
 
-        def r(x):
-            return (x, q, q + n)
-        scan(T.R[:, q:q + n], [r("R")], T.rm[:, 0:n], T[pb][:, 0, 0:n], [("rm", 0, n), (pb, 0, 512)], A.mult, A.max)
-        tt(T.eq[:, q:q + n], [r("eq")], T.R[:, q:q + n], T[pb][:, 0, 0:n], [r("R"), (pb, 0, 512)], A.is_equal)
-        for b in range(0, nb, 2):
-            p = q + 32 * b
-            tt(T.pr[:, p:p + 64], [("pr", p, p + 64)], T.eq[:, p:p + 64], T[pb][:, 1:3, 16 * b:16 * b + 32], [("eq", p, p + 64), (pb, 0, 512)], A.mult)
-        tt(T.ne[:, q:q + n], [r("ne")], T.R[:, q:q + n], T[pb][:, 0, 0:n], [r("R"), (pb, 0, 512)], A.not_equal)
-        scan(T.C[:, q:q + n], [r("C")], T.ne[:, q:q + n], T.pr[:, q:q + n], [r("ne"), r("pr")], A.mult, A.add)
-        last_k = slice(q + 15, q + 16 * (a1 - a0), 16)
-        cp(T[vU][:, o + a0:o + a1], [(vU, o + a0, o + a1)], T.C[:, last_k], [r("C")])
-        cp(T[vI][:, o + a0:o + a1], [(vI, o + a0, o + a1)], T.C[:, last_k], [r("C")])
-        cp(T.codeI[:, o - 16 + a0:o - 16 + a1], [("codeI", o - 16 + a0, o - 16 + a1)], T.R[:, last_k], [r("R")])
+    zb = [0]
 
     def zstep(t, gr, s):
-        vU = "vU%d" % (t % 2)
-        a0, a1 = GROUPS[gr][:2]
-        lo, hi, n, o, q = 16 * a0, 16 * a1, 16 * (a1 - a0), 480 * (s - 1), 128 * gr
-        lst = T.xw[:, 0:V].indirect(T[vU][:, 16 * s + a0:16 * s + a1])
-        RD = [XW, (vU, 16 * s + a0, 16 * s + a1)]
-        zp, ZP, SH, XQ = T.zg[:, o + lo:o + hi], ("zg", o + lo, o + hi), ("sh", q, q + n), ("xq", q, q + n)
-        tt(T.sh[:, q:q + n], [SH], lst, zp, RD + [ZP], A.add)
-        ts(T.sh[:, q:q + n], [SH], T.sh[:, q:q + n], [SH], 0.5, 1023.75, A.mult, A.add)
-        ts(T.zg[:, o + 480 + lo:o + 480 + hi], [("zg", o + 480 + lo, o + 480 + hi)], T.sh[:, q:q + n], [SH], -1024.0, None, A.add)
-        if s == S:
-            tt(T.zg[:, o + 720 + lo:o + 720 + hi], [("zg", o + 720 + lo, o + 720 + hi)], lst, zp, RD + [ZP], A.is_gt)
-            return
-        act(T.xq[:, q:q + n], [XQ], lst, RD)
-        mm(T.ps[:, 0:n], [("ps", 0, 512)], T.idb[:], T.xq[:, q:q + n], [("idb", 0, 128), XQ], True, False)
-        mm(T.ps[:, 0:n], [("ps", 0, 512)], T.idn[:], zp, [("idn", 0, 128), ZP], False, True)
-        op("S", lambda e: e.activation(T.zg[:, o + 720 + lo:o + 720 + hi], T.ps[:, 0:n], SIGN, bias=-0.5), [("ps", 0, 512)], [("zg", o + 720 + lo, o + 720 + hi)], n * CYC)
+        a0, a1, k = GROUPS[gr]
+        w, pz = a1 - a0, "pb%d" % gr
+        xq, old, new = B("xq", 16 * a0, 16 * a1), sh(gr, s - 1), sh(gr, s)
+        act(xq, IX(XW, vU(t, s, a0, a1)))
+        group([(P(pz, 8, 8 + w), B("idb"), xq), (P(pz, 8, 8 + w), B("ih"), old)])
+        group([(P(pz, 24, 24 + w), B("idb"), xq), (P(pz, 24, 24 + w), B("ihn"), old)])
+        act(new, P(pz, 8, 8 + w), bias=511.75, scale=0.5)
+        o = 256 * (s - 1) + 16 * a0
+        act(B("z4", 256 + 16 * a0, 256 + 16 * a1) if s == S else B("zg", o + 1024, o + 1024 + 16 * w), P(pz, 24, 24 + w), SIGN, bias=1023.5)
+        if s < S:
+            zform(gr, s)
+        phase("zc")
+        act(B("zg", o, o + 16 * w), new, bias=-1024.0)
 
     def race(t):
         for s in range(1, S + 1):
             for gr in range(len(GROUPS)):
-                steps = (knew, kpick, xact if GROUPS[gr][2] else xvec, pick, zstep)
-                for i in range(5):
-                    bias[0] = BIAS[gr][i]
-                    steps[i](t, gr, s)
-            bias[0] = BIAS[3][0]
-            count(s)
-        bias[0] = 0.0
-        finish(t, "vI%d" % (t % 2), "vU%d" % (t % 2))
+                phase("k%d" % gr)
+                knew(t, gr, s)
+                phase("x%d" % gr)
+                (xvec if GROUPS[gr][2] == "V" else xact)(gr)
+                phase("p%d" % gr)
+                pick(t, gr, s)
+                phase("z%d" % gr)
+                zstep(t, gr, s)
+            if s == S - 1:
+                early(t)
+        finish(t)
 
-    def finish(t, vI, vU):
-        f64, f16 = (0, 64), (0, 16)
-        tt(T.wz[:], [("wz",) + f64], T[vI][:, 16:80], T.zsT[:], [(vI, 16, 80), ("zsT",) + f64], A.mult)
-        ts(T.nb[:], [("nb",) + f64], T.cntT[:], [("cntT",) + f64, ("thr", 0, 1)], T.thr[:], BIG, A.is_lt, A.mult)
-        ts(T.u4[:], [("u4",) + f64], T.wz[:], [("wz",) + f64], 4095, None, A.bitwise_and)
-        tt(T.nb[:], [("nb",) + f64], T.nb[:], T.base[:], [("nb",) + f64, ("base",) + f64], A.add)
-        tt(T.c1[:], [("c1",) + f64], T.u4[:], T.nb[:], [("u4",) + f64, ("nb",) + f64], A.add)
-        tt(T.m1[:], [("m1", 0, 32)], T.c1[:, 0:32], T.c1[:, 32:64], [("c1",) + f64], A.min)
-        oo = 16 * t
-        OW = ("own", oo, oo + 16)
-        own = T.own[:, oo:oo + 16]
-        tt(own, [OW], T.m1[:, 0:16], T.m1[:, 16:32], [("m1", 0, 32)], A.min)
+    def early(t):
+        phase("early")
+        group([(P("pc", 0, 7), B("U1", 15 - c, 143 - c), B("zg", c, 1792, 16)) for c in range(16)])
+        tt(B("wz", 0, 48), B("C", 15, 768, 16), P("pc", 0, 3), A.mult)
+        ts(B("nb", 0, 48), P("pc", 4, 7), B("thr"), A.is_lt, BIG, A.mult)
+        ts(B("u4", 0, 48), B("wz", 0, 48), 4095, A.bitwise_and)
+        tt(B("d1", 0, 48), B("nb", 0, 48), B("base", 0, 48), A.add)
+        tt(B("c1", 0, 48), B("u4", 0, 48), B("d1", 0, 48), A.add)
+        tt(B("m1"), B("c1", 0, 16), B("c1", 16, 32), A.min)
+        ts(B("c1", 0, 16), B("c1", 32, 48), BIG, A.min)
+        tt(B("m3"), B("m1"), B("c1", 0, 16), A.min)
+        phase("pairs")
+        ts(B("kcol", 16, 64), B("C", 15, 768, 16), -2048.0, A.add)
+        act(B("v16", 16, 64), B("C", 15, 768, 16), bias=-2048.0)
+        for s in (4, 3, 2):
+            act(B("val", 240 * s - 240, 240 * s), IX(B("iw"), vU(t, s - 1)), bias=-2048.0)
+            pairs("eqm", 1920 * (s - 1), 240 * s - 240, ("kcol", 16 * s - 16))
+
+    def finish(t):
+        phase("own")
+        own = B("own", 16 * t, 16 * t + 16)
+        group([(P("pc", 8, 10), B("idb"), B("cneg"))] + [(P("pc", 8, 10), B("Uh", 15 - c, 143 - c), B("z4", c, 512, 16)) for c in range(16)])
+        tt(B("wz", 48, 64), B("C", 768 + 15, 1024, 16), P("pc", 8, 9), A.mult)
+        ts(B("nb", 48, 64), P("pc", 9, 10), B("thr"), A.is_lt, BIG, A.mult)
+        ts(B("u4", 48, 64), B("wz", 48, 64), 4095, A.bitwise_and)
+        tt(B("d1", 48, 64), B("nb", 48, 64), B("base", 48, 64), A.add)
+        tt(B("c1", 48, 64), B("u4", 48, 64), B("d1", 48, 64), A.add)
+        tt(own, B("c1", 48, 64), B("m3"), A.min)
         rs = 48 * t
-        send(own, [T.rcv[:, rs + 16 * j:rs + 16 * j + 16] for j in range(3)], [OW], [("rcv", rs, rs + 48)], "a%d" % t, "l%d" % t)
-        bias[0] = BIAS[3][2]
-        ts(T.nb[:], [("nb",) + f64], T.cntT[:], [("cntT",) + f64, ("thr", 0, 1)], T.thr[:], BIG, A.is_lt, A.mult)
-        tt(T.d1[:], [("d1",) + f64], T[vI][:, 16:80], T.bs[:], [(vI, 16, 80), ("bs",) + f64], A.add)
-        tt(T.d1[:], [("d1",) + f64], T.d1[:], T.nb[:], [("d1",) + f64, ("nb",) + f64], A.add)
-        tt(T.c1[:, 0:32], [("c1", 0, 32)], T.d1[:, 0:32], T.d1[:, 32:64], [("d1",) + f64], A.min)
-        tt(T.dI[:], [("dI",) + f16], T.c1[:, 0:16], T.c1[:, 16:32], [("c1", 0, 32)], A.min)
-        ts(T.WI[:], [("WI",) + f16], T.dI[:], [("dI",) + f16], 4095, None, A.bitwise_and)
-        ts(T.bI[:], [("bI",) + f16], T.dI[:], [("dI",) + f16], 12, 7, A.arith_shift_right, A.bitwise_and)
-        ts(T.kI[:], [("kI",) + f64], T.codeI[:], [("codeI",) + f64], 15, None, A.bitwise_and)
-        cp(T.WU[:], [("WU",) + f16], T.WI[:], [("WI",) + f16])
-        ts(T.bF[:], [("bF",) + f16], T.bI[:], [("bI",) + f16], 4.0, 480.0, A.min, A.mult)
-        ts(T.kU[:], [("kU",) + f64], T.kI[:], [("kI",) + f64], -1.0, 15.0, A.mult, A.add)
-        tt(T.bF[:], [("bF",) + f16], T.bF[:], T.ln[:], [("bF",) + f16, ("ln",) + f16], A.add)
-        cp(T.bU[:], [("bU",) + f16], T.bF[:], [("bF",) + f16])
-        ts(T.P1[:], [("P1",) + f64], T[vI][:, 0:64], [(vI, 0, 64)], 1.0, None, A.add)
-        ts(T.Wp[:], [("Wp",) + f16], T.WI[:], [("WI",) + f16], 4097.0, None, A.add)
-        tt(T.vD[:, 0:64], [("vD", 0, 64)], T[vI][:, 0:64], T.Dm[:], [(vI, 0, 64), ("Dm",) + f64], A.subtract)
-        tt(T.vD[:, 64:80], [("vD", 64, 80)], T.WI[:], T.Dm[:, 0:16], [("WI",) + f16, ("Dm", 0, 16)], A.subtract)
-        act(T.xW[:], [("xW", 0, 240)], T.xw[:, 0:V].indirect(T.WU[:, 0:15]), [XW, ("WU",) + f16])
+        send(own, [T.rcv[:, rs + 16 * j:rs + 16 * j + 16] for j in range(3)], B("rcv", rs, rs + 48), "a%d" % t, "l%d" % t)
+        phase("logs")
+        tt(B("w1"), B("C", 15, 1024, 16), B("bs"), A.add)
+        tt(B("w1"), B("w1"), B("nb"), A.add)
+        tt(B("d1", 0, 32), B("w1", 0, 32), B("w1", 32, 64), A.min)
+        tt(B("dI"), B("d1", 0, 16), B("d1", 16, 32), A.min)
+        ts(B("WI"), B("dI"), 4095, A.bitwise_and)
+        ts(B("bI"), B("dI"), 12, A.arith_shift_right, 7, A.bitwise_and)
+        cp(B("WU"), B("WI"))
+        ts(B("nW"), B("WI"), -1.0, A.mult)
+        ts(B("v16", 0, 16), B("WI"), -2048.0, A.add)
+        ts(B("bF"), B("bI"), 256.0, A.mult, -256.0, A.add)
+        tt(B("bF"), B("bF"), B("ln"), A.add)
+        cp(B("bU"), B("bF"))
+        cp(B("cI"), B("R", 15, 1024, 16))
+        ts(B("kI"), B("cI"), 12, A.arith_shift_right, 15, A.bitwise_and)
+        ts(B("kU"), B("kI"), -1.0, A.mult, 15.0, A.add)
+        phase("masks")
         for s in range(S, 0, -1):
-            act(T.Bs[:, 240 * s - 240:240 * s], [("Bs", 240 * s - 240, 240 * s)], T.Wk[:].indirect(T.kU[:, 16 * s - 16:16 * s - 1]), [("Wk",) + f16, ("kU",) + f64])
-        for s in [x for x in range(S, 1, -1) if x not in ACT_EVENTS]:
-            cp(T.vall[:, 240 * s - 240:240 * s], [("vall", 240 * s - 240, 240 * s)], T.iw[:].indirect(T[vU][:, 16 * s - 16:16 * s - 1]), [("iw", 0, 8192), (vU, 16 * s - 16, 16 * s)])
-        tt(T.xs2[:], [("xs2", 0, 240)], T.zg[:].indirect(T.bU[:, 0:15]), T.xW[:], [("zg", 0, 2400), ("bU",) + f16, ("xW", 0, 240)], A.add)
-        ts(T.xt2[:], [("xt2", 0, 240)], T.xs2[:], [("xs2", 0, 240)], 0.5, 1023.75, A.mult, A.add)
-        ts(T.xn[:], [("xn", 0, 240)], T.xt2[:], [("xt2", 0, 240)], -1024.0, None, A.add)
+            act(B("Bs", 240 * s - 240, 240 * s), IX(B("Wk"), B("kU", 16 * s - 16, 16 * s - 1)))
+        phase("wpairs")
+        act(B("valf"), IX(B("iw"), B("WU", 0, 15)))
+        o = e0 = 0
+        for a in range(15):
+            n = 240 - 16 * a
+            act(B("eqm", o, o + n), B("valf", 16 * a, 240), ABS, bias=B("nW", a, a + 1))
+            o += n
+            if a in (2, 6, 14):
+                act(B("eqm", e0, o), B("eqm", e0, o), RELU, bias=1.0, scale=-1.0)
+                e0 = o
+        phase("xnew")
+        act(B("xW"), IX(XW, B("WU", 0, 15)))
+        act(B("zW"), IX(B("zg", 0, 1024), B("bU", 0, 15)))
+        group([(P("pc", 16, 31), B("idb"), B("xW")), (P("pc", 16, 31), B("idb"), B("zW"))])
+        act(B("xr"), P("pc", 16, 31), bias=1023.75, scale=0.5)
+        act(B("xn"), B("xr"), bias=-1024.0)
         if t + 1 < RACES:
-            v_start(t + 1)
-            z_start(t + 1)
+            phase("zinit")
+            zinit(t + 1)
 
-        bias[0] = BIAS[3][1]
-        def rc(j, lo, hi):
-            o = rs + 16 * (j - 1)
-            return T.rcv[:, o + lo:o + hi]
-        RC, WM = ("rcv", rs, rs + 48), ("Wm", 0, 16)
-        tt(T.Wm[:, 0:10], [("Wm", 0, 10)], T.own[:, oo:oo + 10], rc(3, 5, 15), [OW, RC], A.min)
-        tt(T.Wm[:, 10:15], [("Wm", 10, 15)], T.own[:, oo + 10:oo + 15], rc(2, 0, 5), [OW, RC], A.min)
-        tt(T.Wm[:, 0:5], [("Wm", 0, 5)], T.Wm[:, 0:5], rc(2, 10, 15), [WM, RC], A.min)
-        tt(T.Wm[:, 5:15], [("Wm", 5, 15)], T.Wm[:, 5:15], rc(1, 0, 10), [WM, RC], A.min)
-        ts(T.x1[:], [("x1",) + f16], T.Wm[:], [WM], BIG, None, A.is_lt)
-        tt(T.x2[:], [("x2",) + f16], T.Wm[:], own, [WM, OW], A.not_equal)
-        cp(T.WmI[:], [("WmI",) + f16], T.Wm[:], [WM])
-        tt(T.lost[:], [("lost",) + f16], T.x1[:], T.x2[:], [("x1",) + f16, ("x2",) + f16], A.mult)
-        ts(T.bw[:], [("bw",) + f16], T.WmI[:], [("WmI",) + f16], 14, 7, A.arith_shift_right, A.bitwise_and)
-        ts(T.uwI[:], [("uwI",) + f16], T.WmI[:], [("WmI",) + f16], 4095, None, A.bitwise_and)
-        tt(T.lc[:], [("lc",) + f16], T.bw[:], T.lost[:], [("bw",) + f16, ("lost",) + f16], A.mult)
-        tt(T.won[:], [("won",) + f16], T.x1[:], T.lost[:], [("x1",) + f16, ("lost",) + f16], A.subtract)
-        cp(T.uwU[:], [("uwU",) + f16], T.uwI[:], [("uwI",) + f16])
-        for s in range(1, S + 1):
-            ts(T.on[:, 16 * s - 16:16 * s], [("on", 16 * s - 16, 16 * s)], T.lc[:], [("lc",) + f16], float(s), None, A.is_ge)
-        tt(T.kt1[:], [("kt1",) + f16], T.won[:], T.Wp[:], [("won",) + f16, ("Wp",) + f16], A.mult)
-        tt(T.kk[:], [("kk",) + f64], T.P1[:], T.on[:], [("P1",) + f64, ("on",) + f64], A.mult)
-        tt(T.kk[:, 0:16], [("kk", 0, 16)], T.kk[:, 0:16], T.kt1[:], [("kk", 0, 16), ("kt1",) + f16], A.add)
-        ts(T.key[:, 16:64], [("key", 16, 64)], T.kk[:, 16:64], [("kk", 16, 64)], -1.0, None, A.add)
-        ts(T.key[:, 0:16], [("key", 0, 16)], T.kk[:, 0:16], [("kk", 0, 16)], -1.0, None, A.add)
-        ts(T.nkey[:], [("nkey",) + f64], T.kk[:], [("kk",) + f64], -1.0, 1.0, A.mult, A.add)
-        cp(T.keyU[:], [("keyU",) + f16], T.key[:, 0:16], [("key", 0, 16)])
-        tt(T.fo[:, 0:64], [("fo", 0, 64)], T.on[:], T.vD[:, 0:64], [("on",) + f64, ("vD", 0, 64)], A.mult)
-        tt(T.fo[:, 64:80], [("fo", 64, 80)], T.won[:], T.vD[:, 64:80], [("won",) + f16, ("vD", 64, 80)], A.mult)
-        cp(T.wonb[:], [("wonb",) + f16], T.won[:], [("won",) + f16])
-        if 1 not in ACT_EVENTS:
-            cp(T.vall[:, 0:240], [("vall", 0, 240)], T.iw[:].indirect(T.keyU[:, 0:15]), [("iw", 0, 8192), ("keyU",) + f16])
-        mm(T.pc[:, 480:495], [("pc", 0, 512)], T.ones[:], T.wonb[:, 0:15], [("ones", 0, 128), ("wonb",) + f16], True, True)
-        if t + 1 < RACES:
-            op("V", lambda e: e.tensor_reduce(T.tot[:], T.pc[:, 480:495], AxisListType.X, A.add), [("pc", 0, 512)], [("tot", 0, 1)], 64 * CYC)
-            cp(T.totI[:], [("totI", 0, 1)], T.tot[:], [("tot", 0, 1)])
-            ts(T.totI[:], [("totI", 0, 1)], T.totI[:], [("totI", 0, 1)], 1, None, A.bitwise_and)
-            ts(T.thr[:], [("thr", 0, 1)], T.totI[:], [("totI", 0, 1)], 12.0, None, A.add)
-        bank = {4: "ps", 3: "pa1", 2: "pa0", 1: "pz"}
+        phase("win")
 
-        def flat(b, lo, hi):
-            return T[b][:, 0, lo:hi] if b[:2] == "pa" else T[b][:, lo:hi]
+        def rc(j, b):
+            o = rs + 16 * (j - 1) + 5 * b
+            return B("rcv", o, o + 5)
+        for b, (j1, b1, j2, b2) in enumerate(((3, 1, 2, 2), (3, 2, 1, 0), (2, 0, 1, 1))):
+            tt(B("x", 5 * b, 5 * b + 5), rc(j1, b1), rc(j2, b2), A.min)
+        x, ow = B("x", 0, 15), B("own", 16 * t, 16 * t + 15)
 
-        def event(s):
-            o, r, k0 = 1920 * (s - 1), 240 * s - 240, 16 * s - 16
-            on_act = s in ACT_EVENTS
-            if on_act:
-                lst, src = (T.keyU[:, 0:15], ("keyU",) + f16) if s == 1 else (T[vU][:, k0:k0 + 15], (vU, k0, k0 + 16))
-                act(T.valf[:], [("valf", 0, 240)], T.iw[:].indirect(lst), [("iw", 0, 8192), src])
+        def on(e):
+            return B("on", 16 * e, 16 * e + 15)
+        tt(on(0), x, ow, A.is_lt)
+        ts(B("ge", 0, 15), x, 16384.0 * S, A.is_ge)
+        tt(on(3), on(0), B("ge", 0, 15), A.mult)
+        ts(B("uI", 0, 15), x, 4095, A.bitwise_and)
+        cp(B("uU", 0, 15), B("uI", 0, 15))
+        phase("win2")
+        tt(B("xy", 0, 15), x, on(0), A.mult)
+        for s in (3, 2):
+            ts(on(s - 1), B("xy", 0, 15), 16384.0 * s, A.is_ge)
+        tt(on(4), ow, x, A.is_lt)
+        phase("xs")
+        act(B("urep"), IX(B("iw"), B("uU", 0, 15)), bias=-2048.0)
+        for pa, s in (("pa0", 3), ("pa1", 1)):
+            group([(P(pa, 0, 30), B("idM"), B("Bs", 240 * s - 240, 240 * s + 240)), (P(pa, 15, 30), B("ihd"), B("urep")), (P(pa, 0, 15), B("ihd"), B("urep"))])
+            act(B("xs", 240 * s, 240 * s + 240), P(pa, 15, 30), RELU, bias=64.0 - 256.0)
+            act(B("xs", 240 * s - 240, 240 * s), P(pa, 0, 15), RELU, bias=64.0 - 256.0)
+
+        def event(e):
+            phase("ev%d" % e)
+            p1, o = "pb%d" % (e % 2), 256 * e
+            src, r = ("eq1", 1920 * t) if e == 0 else ("eqm", 1920 * (e % 4))
+            lst = IX(B("on", 16 * e, 16 * e + 16), B("w8l"))
+            act(B("W8", o, o + 128), lst, scale=col(18))
+            act(B("W8", o + 128, o + 256), lst, scale=2.0)
+            terms = [(P(p1, 0, 15, p=8), B("idb", 0, 8), B("thw"))]
             for a in range(15):
                 n = 240 - 16 * a
-                if on_act:
-                    act(T.eqm[:, o:o + n], [("eqm", o, o + n)], T.valf[:, 240 - n:240], [("valf", 0, 240), ("nkey", k0, k0 + 16)], ABS, bias=T.nkey[:, k0 + a:k0 + a + 1])
-                    if a in (7, 14):
-                        e0 = 1920 * (s - 1) + (0 if a == 7 else 1472)
-                        act(T.eqm[:, e0:o + n], [("eqm", e0, o + n)], T.eqm[:, e0:o + n], [("eqm", e0, o + n)], RELU, bias=1.0, scale=-1.0)
-                else:
-                    ts(T.eqm[:, o:o + n], [("eqm", o, o + n)], T.vall[:, r + 240 - n:r + 240], [("vall", r + 240 - n, r + 240), ("key", k0, k0 + 16)],
-                       T.key[:, k0 + a:k0 + a + 1], None, A.is_equal)
-                o += n
-            o = 1920 * (s - 1)
-            for a in range(15):
-                n = 240 - 16 * a
-                mm(flat(bank[s], 16 * a, 240), [(bank[s], 0, 512)], T.Wt[:, 128 * a:128 * a + 128], T.eqm[:, o:o + n], [("Wt", 0, 1920), ("eqm", o, o + n)], a == 0, a == 14)
-                o += n
-            tt(T.fl[:, r:r + 240], [("fl", r, r + 240)], flat(bank[s], 0, 240), T.W2d[:], [(bank[s], 0, 512), ("W2d", 0, 240)], A.is_lt)
-            scan(T.Fs[:, r:r + 240], [("Fs", r, r + 240)], T.rmb[:, 0:240], T.fl[:, r:r + 240], [("rmb", 0, 240), ("fl", r, r + 240)], A.mult, A.add)
+                terms.append((P(p1, a, a + 1, p=8), B("W8", o + 8 * a, o + 8 * a + 8), B(src, r, r + 16)))
+                if a < 14:
+                    terms.append((P(p1, a + 1, 15, p=8), B("W8", o + 128 + 8 * a, o + 128 + 8 * a + 8), B(src, r + 16, r + n)))
+                r += n
+            group(terms)
+            q = 256 * (e % 2)
+            act(B("cs", q, q + 240, p=8), P(p1, 0, 15, p=8), RELU)
+            out = P("pb2", 0, 1, c=15)
+            vh = B("v1h", 16 * t, 16 * t + 15) if e == 0 else B("v16", 16 * (e % 4), 16 * (e % 4) + 15)
+            group([(out, B("ih"), vh), (out, B("idB"), on(e))] + [(out, B("Us", 15 - c, 143 - c, p=8), B("cs", q + c, q + 240, 16, p=8)) for c in range(16)])
+            tt(B("of", 16 * e, 16 * e + 15), out, B("Dm", 0, 15), A.min)
+            ts(B("offU", 16 * e, 16 * e + 15), B("of", 16 * e, 16 * e + 15), 10240.0, A.add)
 
-            def place(k):
-                of = T.of[:, k:k + 15]
-                tt(of, [("of", k, k + 15)], T.Fs[:, r + 15:r + 240:16], T.fo[:, k:k + 15], [("Fs", r, r + 240), ("fo", k, k + 15)], A.mult)
-                tt(of, [("of", k, k + 15)], of, T.Dm[:, 0:15], [("of", k, k + 15), ("Dm", 0, 15)], A.add)
-                cp(T.offU[:, k:k + 15], [("offU", k, k + 15)], of, [("of", k, k + 15)])
-            place(k0)
-            if s == 1:
-                place(64)
-
-        cp(T.urep[:], [("urep", 0, 240)], T.iw[:].indirect(T.uwU[:, 0:15]), [("iw", 0, 8192), ("uwU",) + f16])
         for s in range(S, 0, -1):
-            r = 240 * s - 240
-            tt(T.xs[:, r:r + 240], [("xs", r, r + 240)], T.Wk[:].indirect(T.kU[:, 16 * s - 16:16 * s - 1]), T.urep[:], [("Wk",) + f16, ("kU",) + f64, ("urep", 0, 240)], A.mult)
-            bias[0] = BIAS[3][3] if s == S else BIAS[3][4]
-            event(s)
-        bias[0] = 0.0
-        cp(T.xw[:].indirect(T.offU[:, 64:79]), [("xw", 0, WIN)], T.xn[:], [("xn", 0, 240), ("offU", 64, 80)])
-        for s in range(S, 0, -1):
-            r = 240 * s - 240
-            lst = T.kw[:, 0:V].indirect(T[vU][:, 16 * s - 16:16 * s - 1])
-            RD = [KW, (vU, 16 * s - 16, 16 * s)]
-            mm(T.pc[:, 0:240], [("pc", 0, 512)], T.idS[:, 128 * s - 128:128 * s], T.Bs[:, r:r + 240], [("idS", 0, 512), ("Bs", r, r + 240)], True, False)
-            act(T.kt[:], [("kt", 0, 240)], lst, RD, ID, bias=-131072.0)
-            mm(T.pc[:, 0:240], [("pc", 0, 512)], T.idf[:], T.kt[:], [("idf", 0, 128), ("kt", 0, 240)], False, True)
-            tt(T.kp[:], [("kp", 0, 240)], lst, T.xs[:, r:r + 240], RD + [("xs", r, r + 240)], A.mult)
-            tt(T.kz[:], [("kz", 0, 240)], T.kp[:], T.pc[:, 0:240], [("kp", 0, 240), ("pc", 0, 512)], A.add)
-            ts(T.kn[:], [("kn", 0, 240)], T.kz[:], [("kz", 0, 240)], 131040, None, A.bitwise_and)
-            cp(T.kw[:].indirect(T.offU[:, 16 * s - 16:16 * s - 1]), [("kw", 0, WIN)], T.kn[:], [("kn", 0, 240), ("offU", 16 * s - 16, 16 * s - 1)])
+            event(s - 1)
+            phase("st%d" % s)
+            r, pz = 240 * s - 240, P("pb3" if s % 2 else "pz", 0, 15)
+            lst = IX(KW, vU(t, s - 1))
+            kt = B("kvh", 768, 1008) if s == S else B("kt")
+            mm(pz, B("ih32"), B("m2k"), True, False)
+            mm(pz, B("idS", 128 * s - 128, 128 * s), B("Bs", r, r + 240), False, False)
+            if s < S:
+                act(kt, lst, bias=-2048.0, scale=1.0 / 32.0)
+            mm(pz, B("ih32"), kt, False, True)
+            tt(B("kp"), lst, B("xs", r, r + 240), A.mult)
+            tt(B("kz"), B("kp"), pz, A.add)
+            ts(B("kn"), B("kz"), 131040, A.bitwise_and)
+            cp(IX(B("kw"), B("offU", 16 * s - 16, 16 * s - 1)), B("kn"))
+        event(4)
+        cp(IX(B("xw"), B("offU", 64, 79)), B("xn"))
+        if t + 1 < RACES:
+            phase("thr")
+            group([(P("pc", 12, 13, c=15), B("ones"), on(4))])
+            op("V", lambda e: e.tensor_reduce(T.tot[:], T.pc[:, 192:207], AxisListType.X, A.add), B("tot"), [P("pc", 12, 13, c=15)])
+            cp(B("totI"), B("tot"))
+            ts(B("totI"), B("totI"), 1, A.bitwise_and)
+            ts(B("thr"), B("totI"), 2.0, A.mult, 8.0, A.add)
 
+    phase("start1")
+    ms(B("m2k"), -2048.0)
+    phase("start0")
+    zinit(0)
     for t in range(RACES):
         race(t)
-    for a in range(8):
-        act(T.idx[:, 128 * a:128 * a + 128], [("idx", 128 * a, 128 * a + 128)], T.idb[:], [("idb", 0, 128)], ID, scale=float(a + 1))
-    for a in range(4):
-        act(T.idk[:, 128 * a:128 * a + 128], [("idk", 128 * a, 128 * a + 128)], T.idb[:], [("idb", 0, 128)], ID, scale=(a + 1) / 32.0)
-    for a in range(8):
-        mm(T.ps[:], [("ps", 0, 512)], T.idx[:, 128 * a:128 * a + 128], T.xw[:, 512 * a:512 * a + 512], [("idx", 0, 1024), ("xw", 512 * a, 512 * a + 512)], a == 0, a == 7)
-    act(T.ox[:], [("ox", 0, 512)], T.ps[:], [("ps", 0, 512)])
+    phase("out")
+    group([(P("pa0", 0, 32), B("idx", 128 * a, 128 * a + 128), B("xw", 512 * a, 512 * a + 512)) for a in range(8)])
+    act(B("ox"), P("pa0", 0, 32))
     dma("Y", "oy", T.yx[:], T.ox[:], [("ox", 0, 512)], [], 2000.0)
-    for a in range(4):
-        mm(T.pz[:], [("pz", 0, 512)], T.idk[:, 128 * a:128 * a + 128], T.kw[:, 512 * a:512 * a + 512], [("idk", 0, 512), ("kw", 512 * a, 512 * a + 512)], a == 0, a == 3)
-    for a in range(4, 8):
-        b = "pb%d" % (a - 4) if a < 7 else "pc"
-        act(T[b][:, :, :] if a < 7 else T[b][:], [(b, 0, 512)], T.kw[:, 512 * a:512 * a + 512], [("kw", 512 * a, 512 * a + 512)], ID, scale=(a + 1) / 32.0)
-    OK = ("ok", 0, 512)
-    cp(T.ok[:], [OK], T.pb0[:, :, :], [("pb0", 0, 512)])
-    for b in ("pb1", "pb2", "pc", "pz"):
-        tt(T.ok[:], [OK], T.ok[:], T[b][:, :, :] if b[1] == "b" else T[b][:], [OK, (b, 0, 512)], A.add)
-    dma("Y", "ok", T.yk[:], T.ok[:], [OK], [], 2000.0)
+    for a in range(8):
+        kb, kh = B("kw", 512 * a, 512 * a + 512), B("kh", 512 * a, 512 * a + 512)
+        if a % 2:
+            act(kh, kb, bias=-2048.0, scale=1.0 / 32.0)
+        else:
+            ts(kh, kb, 1.0 / 32.0, A.mult, -2048.0, A.add)
+    group([(P("pa1", 0, 32), B("idk", 128 * a, 128 * a + 128), B("kh", 512 * a, 512 * a + 512)) for a in range(8)])
+    ts(B("ok"), P("pa1", 0, 32), 36.0 * 2048.0, A.add)
+    dma("Y", "ok", T.yk[:], T.ok[:], [("ok", 0, 512)], [], 2000.0)
     cnt = emit()
     g.sync.wait_ge(T.sem.oy, 16)
     g.sync.wait_ge(T.sem.ok, 16)

@@ -11,11 +11,12 @@ L = J * M
 WIN = V + 256
 BIG = 2.0 ** 19
 CFG = {
-    "groups": ((0, 4, "V"), (4, 10, "S"), (10, 15, "V")),
+    "groups": ((0, 4, "V"), (4, 8, "S"), (8, 12, "V"), (12, 15, "S")),
     "xcols": 1,
-    "kbank": ("pb3", "pz", "pc"),
-    "bias": {}, "rounds": 300, "seed": 1, "span": 8000.0, "shake": 1500.0,
-    "cyc": 0.9, "lat": 160.0, "gam": 1.6, "sig": 3.8, "pe": 0.5,
+    "kbank": ("pz", "pb1", "pc", "pb3"),
+    "zv": (4,), "kv": ((1, 0),), "gz": True, "w8v": (3,), "halves": True, "wpos": 2, "run": 240.0, "zfirst": 1,
+    "bias": {}, "rounds": 1800, "lead": 8000.0, "seed": 1, "span": 6000.0, "shake": 2000.0,
+    "cyc": 0.85, "lat": 220.0, "gam": 1.6, "sig": 3.8, "pe": 0.45,
 }
 PLAN = {}
 
@@ -27,10 +28,10 @@ for _d, _l in (
                       ("U", 144), ("U1", 144), ("Us", 144), ("kc", 128), ("rm", 256), ("rz", 2048), ("cst", 256), ("cneg", 32), ("Wk", 16),
                       ("thw", 240), ("idx", 1024), ("ones", 128))),
         ("float16", (("kvh", 1024), ("Tt", 512), ("shp", 8192), ("shc", 512), ("z4", 512), ("Pm", 512), ("ih", 128), ("ihn", 128), ("ih32", 128), ("ihd", 128),
-                     ("Uh", 144), ("val", 960), ("v16", 80), ("v1h", 48), ("urep", 240), ("kt", 240), ("m2k", 240), ("xr", 240), ("kh", 4096), ("idk", 1024))),
+                     ("Uh", 144), ("val", 960), ("v16", 80), ("v1h", 48), ("urep", 240), ("kt", 240), ("m2k", 240), ("zt", 256), ("xr", 240), ("kh", 4096), ("idk", 1024))),
         ("float32", (("kw", WIN), ("iw", 4096), ("R", 1024), ("C", 1024), ("nb", 64), ("kcol", 64), ("k1c", 48), ("nW", 16), ("valf", 240),
                      ("xs", 960), ("kp", 240), ("of", 80), ("Dm", 16), ("base", 64), ("bs", 64), ("ln", 16), ("bF", 16), ("ge", 16), ("xy", 16),
-                     ("d1", 64), ("w1", 64), ("tot", 1), ("thr", 1), ("pF", 24), ("ox", 512), ("ok", 512), ("t8", 8))),
+                     ("d1", 64), ("w1", 64), ("tot", 1), ("thr", 2), ("wt", 32), ("cm", 240), ("pF", 24), ("ox", 512), ("ok", 512), ("t8", 8))),
         ("int32", (("kin", V), ("vs", 45), ("vl", 135), ("vI", 48), ("wz", 64), ("u4", 64), ("c1", 64), ("m1", 16), ("m3", 16), ("own", 48),
                    ("rcv", 144), ("x", 16), ("uI", 16), ("dI", 16), ("WI", 16), ("bI", 16), ("cI", 64), ("kI", 64), ("kz", 240), ("kn", 240),
                    ("totI", 1), ("pI", 12))),
@@ -48,7 +49,7 @@ def planner(g, T):
     queues = {"V": g.vector, "S": g.scalar, "T": g.tensor, "G": g, "Y": g.sync}
     ops = []
     plan = {}
-    bias = [0.0]
+    bias = [0.0, (-1, ""), 0]
 
     def is_psum(b):
         return b in SCRATCH and SCRATCH[b][0] == "psum"
@@ -83,7 +84,8 @@ def planner(g, T):
         if after is not None:
             deps[after] = 0
         note(plan, rq, R, W, i)
-        ops.append({"q": q, "kind": kind, "fn": fn, "dur": dur, "sem": sem, "val": val, "lat": lat, "deps": deps, "after": after, "bias": bias[0], "txt": (W[0][0] if W else kind)})
+        bias[2] += 1
+        ops.append({"id": (bias[1][0], bias[1][1], bias[2]), "q": q, "kind": kind, "fn": fn, "dur": dur, "sem": sem, "val": val, "lat": lat, "deps": deps, "after": after, "bias": bias[0], "txt": (W[0][0] if W else kind)})
         return i
 
     def emit():
@@ -98,28 +100,32 @@ def planner(g, T):
             prio[i] = ops[i]["dur"] + max([x + prio[k] for k, x in succ[i]] + [0.0])
         pred = [list(o["deps"].items()) for o in ops]
         dur = [o["dur"] for o in ops]
+        queue = [o["q"] for o in ops]
+        twin = {o["id"]: i for i, o in enumerate(ops)}
 
         def place(rank, before, back):
             start = [0.0] * n
             busy = {q: ([], []) for q in queues}
+            end = [0.0] * n
             for i in rank:
-                t = max([start[d] + dur[d] + x for d, x in before[i]] + [0.0])
-                if ops[i]["q"] != "N":
-                    lo, hi = busy[ops[i]["q"]]
-                    a, b = 0, len(hi)
-                    while a < b:
-                        m = (a + b) // 2
-                        if hi[m] > t:
-                            b = m
-                        else:
-                            a = m + 1
-                    while a < len(lo) and lo[a] < t + dur[i]:
-                        t = max(t, hi[a])
+                t, w = 0.0, dur[i]
+                for d, x in before[i]:
+                    if end[d] + x > t:
+                        t = end[d] + x
+                if queue[i] != "N":
+                    lo, hi = busy[queue[i]]
+                    a = b = len(hi)
+                    while a and hi[a - 1] > t:
+                        a -= 1
+                    while a < b and lo[a] < t + w:
+                        if hi[a] > t:
+                            t = hi[a]
                         a += 1
                     lo.insert(a, t)
-                    hi.insert(a, t + dur[i])
+                    hi.insert(a, t + w)
                 start[i] = t
-            return start, max(start[i] + dur[i] for i in range(n))
+                end[i] = t + w
+            return start, max(end)
         if n not in PLAN:
             key = [-prio[i] - ops[i]["bias"] for i in range(n)]
             for i in range(n):
@@ -132,12 +138,21 @@ def planner(g, T):
                     best = (end, start)
                 if r % 3 == 2:
                     seed = (seed * 1103515245 + 12345) % 2 ** 31
-                    mid, key = seed % 1000 / 1000.0 * best[0], list(best[1])
+                    mid, key = (seed >> 8) % 1000 / 1000.0 * best[0], list(best[1])
                     for i in range(n):
                         if abs(key[i] - mid) < CFG["span"]:
                             seed = (seed * 1103515245 + 12345) % 2 ** 31
                             key[i] += (seed >> 8) % 1000 / 1000.0 * CFG["shake"]
-                        key[i] = max([key[i]] + [key[d] + 1e-3 for d, x in pred[i]])
+                    if r % 6 == 2:
+                        at = [best[1][i] for i in range(n) if ops[i]["kind"] == "s"][-RACES:]
+                        m = min(range(RACES), key=lambda t: abs(at[t] - CFG["lead"] - mid))
+                        for i in range(n):
+                            if (m,) + ops[i]["id"][1:] in twin and ops[i]["id"][0] >= 0:
+                                key[i] = key[twin[(m,) + ops[i]["id"][1:]]] - at[m] + at[ops[i]["id"][0]]
+                    for i in range(n):
+                        for d, x in pred[i]:
+                            if key[i] <= key[d]:
+                                key[i] = key[d] + 1e-3
                     continue
                 late, end = place(sorted(range(n), key=lambda i: (-start[i] - dur[i], -i)), succ, True)
                 key = [-late[i] - dur[i] for i in range(n)]
@@ -194,9 +209,11 @@ def rank_program(g, core, T, topo):
     GROUPS, CYC, LAT = CFG["groups"], CFG["cyc"], CFG["lat"]
 
     last = {}
+    now = [-1, 0]
 
     def phase(name):
         bias[0] = CFG["bias"].get(name, 0.0)
+        bias[1], bias[2] = (now[0], (now[1], name)), 0
 
     def B(name, lo=0, hi=None, st=1, p=128):
         hi = SCRATCH[name][1][1] if hi is None else hi
@@ -257,13 +274,14 @@ def rank_program(g, core, T, topo):
     def act(out, in_, f=ID, bias=0.0, scale=1.0):
         op("S", lambda e: e.activation(out[0], in_[0], f, bias=arg(bias), scale=arg(scale)), out, [in_, bias, scale], rate=1)
 
-    def mm(out, lhsT, rhs, start, stop):
-        op("T", lambda e: e.matmul(out[0], lhsT[0], rhs[0], start, stop), out, [lhsT, rhs],
-           dur=max(min(64, lhsT[2]), rhs[2]) * CFG["pe"] * (4 if rhs[3] == 4 else 1))
-
-    def group(terms):
+    def group(terms, cuts=(), start=True, stop=True):
+        run, dur = [], 0.0
         for i, (out, lhsT, rhs) in enumerate(terms):
-            mm(out, lhsT, rhs, i == 0, i == len(terms) - 1)
+            run.append((out[0], lhsT[0], rhs[0], start and i == 0, stop and i == len(terms) - 1))
+            dur += max(min(64, lhsT[2]), rhs[2]) * CFG["pe"] * (4 if rhs[3] == 4 else 1)
+            if dur >= CFG["run"] or i + 1 in cuts or i + 1 - len(terms) in cuts or i + 1 == len(terms):
+                op("T", lambda e, run=run: [e.matmul(*m) for m in run][-1], out, [x for u in terms[i + 1 - len(run):i + 1] for x in u[1:]], dur=dur)
+                run, dur = [], 0.0
 
     def ms(out, val):
         op("V", lambda e: e.memset(out[0], val), out, [], rate=out[3] / 4)
@@ -329,10 +347,10 @@ def rank_program(g, core, T, topo):
     ts(col(10), col(2), 15.0, A.add)
     ts(col(11), col(0), 16.0, A.mult, 15.0, A.add)
     ts(B("idb"), I128, col(0), A.is_equal)
-    for name, f in (("idn", -1.0), ("idB", -8192.0), ("idM", 256.0), ("ih", 1.0), ("ihn", -1.0), ("ih32", 32.0), ("ihd", 1.0 / 32.0)):
+    for name, f in (("idn", -1.0), ("idB", -16384.0), ("idM", 8192.0), ("ih", 1.0), ("ihn", -1.0), ("ih32", 32.0), ("ihd", 1.0 / 32.0)):
         act(B(name), B("idb"), scale=f)
     for s in range(S):
-        act(B("idS", 128 * s, 128 * s + 128), B("idb"), scale=32.0 * (s + 1))
+        act(B("idS", 128 * s, 128 * s + 128), B("idb"), scale=1024.0 * (s + 1))
     for a in range(8):
         act(B("idx", 128 * a, 128 * a + 128), B("idb"), scale=float(a + 1))
         act(B("idk", 128 * a, 128 * a + 128), B("idb"), scale=float(a + 1))
@@ -343,7 +361,7 @@ def rank_program(g, core, T, topo):
     ts(B("U1"), B("iw", 0, 144), col(10), A.is_equal)
     act(B("U"), B("U1"), scale=65536.0)
     act(B("Uh"), B("U1"))
-    ts(B("Us"), B("iw", 0, 144), col(11), A.is_equal, 2.0 ** 30, A.mult)
+    ts(B("Us"), B("iw", 0, 144), col(11), A.is_equal, 8192.0, A.mult)
     ts(B("rm"), B("rm"), 1.0, A.min)
     ts(B("E", 0, 16 * SW), B("E", 0, 16 * SW), col(0), A.is_equal)
     ms(B("rz", 0, 16 * VW), 2048.0)
@@ -354,7 +372,8 @@ def rank_program(g, core, T, topo):
         for par in range(2 * (k == "V")):
             ms(B("shp", 4096 * par + 256 * a0, 4096 * par + 256 * a1), 0.0)
     ms(Yv(15, 16), 0.0)
-    ms(B("thr"), 8.0)
+    ms(B("thr", 0, 1), 8.0)
+    ms(B("thr", 1, 2), 12.0)
     ms(B("ones"), 1.0)
     ms(B("cst"), 2048.0)
     ms(B("cneg", 0, 16), -16384.0)
@@ -366,12 +385,18 @@ def rank_program(g, core, T, topo):
     tt(col(16), col(12), col(13), A.mult)
     tt(col(17), col(14), col(15), A.mult)
     tt(col(18), col(16), col(17), A.mult)
-    ts(B("valf"), B("rm", 0, 240), 0.5, A.mult)
-    ts(B("kp"), B("rm", 0, 240), 2.5, A.mult, -2.5, A.add)
+    ms(B("valf"), 0.5)
+    ms(B("kp"), 0.0)
+    ts(B("kp", 0, 1), B("valf", 0, 1), -5.0 * 2.0 ** 55, A.mult, 2.0 ** 60, A.mult)
     scan(B("thw"), B("valf"), B("kp"), A.mult, A.add)
-    ts(B("Wk"), B("iw", 0, 16), col(1), A.is_equal)
+    ms(B("ge"), 2.0 ** -16)
+    ms(B("xy"), 0.0)
+    ts(B("xy", 0, 1), col(18), 2.0 ** 55, A.mult, 2.0 ** 60, A.mult)
+    scan(B("wt", 0, 15), B("ge", 0, 15), B("xy", 0, 15), A.mult, A.add)
+    ts(B("wt", 16, 31), B("wt", 0, 15), -1.0, A.mult)
+    ts(B("Wk"), B("iw", 0, 16), col(1), A.is_equal, 1.0 / 32.0, A.mult)
     ts(B("ln"), B("Dm"), col(1), A.add)
-    ts(B("Dm"), B("ln"), 4096.0 - 10240.0, A.add)
+    ts(B("Dm"), B("ln"), 4096.0 - 26624.0, A.add)
     tt(col(19), col(4), col(5), A.is_equal)
     ts(col(20), col(6), -15.0, A.add)
     ts(B("t8"), B("iw", 0, 8), 2.0, A.mult, col(20), A.add)
@@ -386,7 +411,7 @@ def rank_program(g, core, T, topo):
     def pairs(dst, o, vals, keys):
         for a in range(15):
             n = 240 - 16 * a
-            ts(B(dst, o, o + n), B("val", vals + 16 * a, vals + 240), B(keys[0], keys[1] + a, keys[1] + a + 1), A.is_equal)
+            ts(B(dst, o, o + n), B("val", vals + 16 * a, vals + 240), B(keys[0], keys[1] + a, keys[1] + a + 1), A.is_equal, B("wt", a, a + 1), A.mult)
             o += n
 
     for t in range(RACES):
@@ -433,7 +458,10 @@ def rank_program(g, core, T, topo):
         a0, a1, k = GROUPS[gr]
         nb, o = (a1 - a0 + 1) // 2, 256 * (s - 1) + 16 * a0
         act(B("kvh", o, o + 16 * (a1 - a0)), IX(KW, vU(t, s - 1, a0, a1)), bias=-2048.0, scale=1.0 / 32.0)
-        ts(B("kvu", 16 * a0, 16 * a1), B("kvh", o, o + 16 * (a1 - a0)), 2048.0, A.add)
+        if (s, gr) in CFG["kv"]:
+            ts(B("kvu", 16 * a0, 16 * a1), IX(KW, vU(t, s - 1, a0, a1)), 1.0 / 32.0, A.mult)
+        else:
+            ts(B("kvu", 16 * a0, 16 * a1), B("kvh", o, o + 16 * (a1 - a0)), 2048.0, A.add)
         tb, src = B("Tt", 128 * gr, 128 * gr + 32 * nb), B("kvh", o, o + 32 * nb)
         op("V", lambda e: e.transpose(tb[0], src[0]), tb, [src])
 
@@ -441,10 +469,9 @@ def rank_program(g, core, T, topo):
         a0, a1, k = GROUPS[gr]
         pb, w = "pb%d" % gr, 2 * ((a1 - a0 + 1) // 2)
         if al == a0:
-            mm(P(pb, 0, w), B("idb"), B("kc", 0, 16 * w), True, False)
+            group([(P(pb, 0, w), B("idb"), B("kc", 0, 16 * w))], stop=False)
         end = a0 + w if ah == a1 else ah
-        for c in range(16):
-            mm(P(pb, al - a0, end - a0), B("U", 15 - c, 143 - c), Yv(al, end, c), False, ah == a1 and c == 15)
+        group([(P(pb, al - a0, end - a0), B("U", 15 - c, 143 - c), Yv(al, end, c)) for c in range(16)], start=False, stop=ah == a1)
 
     chunk = [0]
 
@@ -456,7 +483,7 @@ def rank_program(g, core, T, topo):
             xg, pa, o = B("xg%d" % (chunk[0] % 3), 0, 256 * (e - a)), P("pa%d" % (chunk[0] % 2), 0, 16 * (e - a)), 256 * (a - a0)
             chunk[0] += 1
             act(xg, IX(XW, B("kvu", 16 * a, 16 * e)))
-            group([(pa, B("idb"), xg), (pa, B("zT", 128 * gr, 128 * gr + 128, p=n), B("E", o, o + 256 * (e - a), p=n))])
+            group([(pa, B("zT", 128 * gr, 128 * gr + 128, p=n), B("E", o, o + 256 * (e - a), p=n)), (pa, B("idb"), xg)][::CFG["zfirst"]], (1,))
             act(Yv(a, e), pa, RELU)
         score(gr, a0, a1)
 
@@ -485,29 +512,43 @@ def rank_program(g, core, T, topo):
                 for w in range(2):
                     q = 128 * gr + 32 * b + 16 * w
                     terms.append((P(pk, 16 + 2 * b + h, 17 + 2 * b + h), B("Pm", 128 * (2 * h + w), 128 * (2 * h + w) + 128), B("Tt", q, q + 16)))
-        group(terms + [(P(pk, 16, 16 + 2 * nb), B("idn"), D)])
+        group(terms + [(P(pk, 16, 16 + 2 * nb), B("idn"), D)], (-1,))
         scan(C, D, P(pk, 16, 16 + 2 * nb), A.min, A.max)
         cp(vU(t, s, a0, a1), B("C", o + 15, o + 16 * (a1 - a0), 16))
 
-    zb = [0]
+    nev = [0]
 
     def zstep(t, gr, s):
         a0, a1, k = GROUPS[gr]
-        w, pz = a1 - a0, "pb%d" % gr
-        xq, old, new = B("xq", 16 * a0, 16 * a1), sh(gr, s - 1), sh(gr, s)
-        act(xq, IX(XW, vU(t, s, a0, a1)))
-        group([(P(pz, 8, 8 + w), B("idb"), xq), (P(pz, 8, 8 + w), B("ih"), old)])
-        group([(P(pz, 24, 24 + w), B("idb"), xq), (P(pz, 24, 24 + w), B("ihn"), old)])
-        act(new, P(pz, 8, 8 + w), bias=511.75, scale=0.5)
-        o = 256 * (s - 1) + 16 * a0
-        act(B("z4", 256 + 16 * a0, 256 + 16 * a1) if s == S else B("zg", o + 1024, o + 1024 + 16 * w), P(pz, 24, 24 + w), SIGN, bias=1023.5)
+        w, pz, o = a1 - a0, "pb%d" % gr, 256 * (s - 1) + 16 * a0
+        xq, old, new, lst = B("xq", 16 * a0, 16 * a1), sh(gr, s - 1), sh(gr, s), IX(XW, vU(t, s, a0, a1))
+        onv = s in CFG["zv"] and (k == "V" or s == S)
+        if onv:
+            zp = B("zx", 256 * a0, 256 * a1, 16) if k == "V" else B("zg", o - 256, o - 256 + 16 * w)
+            tt(B("zt", 16 * a0, 16 * a1), lst, zp, A.add)
+            ts(new, B("zt", 16 * a0, 16 * a1), 0.5, A.mult, 1023.75, A.add)
+        if onv and s == S:
+            tt(B("z4", 256 + 16 * a0, 256 + 16 * a1), lst, zp, A.is_gt)
+        else:
+            act(xq, lst)
+            if not onv:
+                group([(P(pz, 8, 8 + w), B("idb"), xq), (P(pz, 8, 8 + w), B("ih"), old)])
+            group([(P(pz, 24, 24 + w), B("idb"), xq), (P(pz, 24, 24 + w), B("ihn"), old)])
+            if not onv:
+                act(new, P(pz, 8, 8 + w), bias=511.75, scale=0.5)
+            act(B("z4", 256 + 16 * a0, 256 + 16 * a1) if s == S else B("zg", o + 1024, o + 1024 + 16 * w), P(pz, 24, 24 + w), SIGN, bias=1023.5)
         if s < S:
             zform(gr, s)
-        phase("zc")
-        act(B("zg", o, o + 16 * w), new, bias=-1024.0)
+        zc = B("zg", o, o + 16 * w)
+        if CFG["gz"] and k == "V" and s < S:
+            src = B("zx", 256 * a0, 256 * a1, 16)
+            op("G", lambda e: e.affine_select(zc[0], src[0], [[0, 16 * w]], A.is_gt, 0.0, 1, 0), zc, [src], dur=170 + 32 * w * CYC)
+        else:
+            act(zc, new, bias=-1024.0)
 
     def race(t):
         for s in range(1, S + 1):
+            now[0], now[1] = t, s
             for gr in range(len(GROUPS)):
                 phase("k%d" % gr)
                 knew(t, gr, s)
@@ -525,7 +566,7 @@ def rank_program(g, core, T, topo):
         phase("early")
         group([(P("pc", 0, 7), B("U1", 15 - c, 143 - c), B("zg", c, 1792, 16)) for c in range(16)])
         tt(B("wz", 0, 48), B("C", 15, 768, 16), P("pc", 0, 3), A.mult)
-        ts(B("nb", 0, 48), P("pc", 4, 7), B("thr"), A.is_lt, BIG, A.mult)
+        ts(B("nb", 0, 48), P("pc", 4, 7), B("thr", 0, 1), A.is_lt, BIG, A.mult)
         ts(B("u4", 0, 48), B("wz", 0, 48), 4095, A.bitwise_and)
         tt(B("d1", 0, 48), B("nb", 0, 48), B("base", 0, 48), A.add)
         tt(B("c1", 0, 48), B("u4", 0, 48), B("d1", 0, 48), A.add)
@@ -542,9 +583,9 @@ def rank_program(g, core, T, topo):
     def finish(t):
         phase("own")
         own = B("own", 16 * t, 16 * t + 16)
-        group([(P("pc", 8, 10), B("idb"), B("cneg"))] + [(P("pc", 8, 10), B("Uh", 15 - c, 143 - c), B("z4", c, 512, 16)) for c in range(16)])
+        group([(P("pc", 8, 10), B("idb"), B("cneg"))] + [(P("pc", 8, 10), B("Uh", 15 - c, 143 - c), B("z4", c, 512, 16)) for c in range(16)], (1,))
         tt(B("wz", 48, 64), B("C", 768 + 15, 1024, 16), P("pc", 8, 9), A.mult)
-        ts(B("nb", 48, 64), P("pc", 9, 10), B("thr"), A.is_lt, BIG, A.mult)
+        ts(B("nb", 48, 64), P("pc", 9, 10), B("thr", 1, 2) if S in CFG["zv"] else B("thr", 0, 1), A.is_lt, BIG, A.mult)
         ts(B("u4", 48, 64), B("wz", 48, 64), 4095, A.bitwise_and)
         tt(B("d1", 48, 64), B("nb", 48, 64), B("base", 48, 64), A.add)
         tt(B("c1", 48, 64), B("u4", 48, 64), B("d1", 48, 64), A.add)
@@ -572,14 +613,14 @@ def rank_program(g, core, T, topo):
             act(B("Bs", 240 * s - 240, 240 * s), IX(B("Wk"), B("kU", 16 * s - 16, 16 * s - 1)))
         phase("wpairs")
         act(B("valf"), IX(B("iw"), B("WU", 0, 15)))
-        o = e0 = 0
+        o = 0
         for a in range(15):
             n = 240 - 16 * a
             act(B("eqm", o, o + n), B("valf", 16 * a, 240), ABS, bias=B("nW", a, a + 1))
+            act(B("eqm", o, o + n), B("eqm", o, o + n), RELU, bias=B("wt", a, a + 1), scale=B("wt", 16 + a, 17 + a))
             o += n
-            if a in (2, 6, 14):
-                act(B("eqm", e0, o), B("eqm", e0, o), RELU, bias=1.0, scale=-1.0)
-                e0 = o
+        phase("cm")
+        tt(B("cm"), IX(KW, vU(t, S - 1)), B("Bs", 720, 960), A.mult)
         phase("xnew")
         act(B("xW"), IX(XW, B("WU", 0, 15)))
         act(B("zW"), IX(B("zg", 0, 1024), B("bU", 0, 15)))
@@ -613,58 +654,65 @@ def rank_program(g, core, T, topo):
         tt(on(4), ow, x, A.is_lt)
         phase("xs")
         act(B("urep"), IX(B("iw"), B("uU", 0, 15)), bias=-2048.0)
-        for pa, s in (("pa0", 3), ("pa1", 1)):
-            group([(P(pa, 0, 30), B("idM"), B("Bs", 240 * s - 240, 240 * s + 240)), (P(pa, 15, 30), B("ihd"), B("urep")), (P(pa, 0, 15), B("ihd"), B("urep"))])
-            act(B("xs", 240 * s, 240 * s + 240), P(pa, 15, 30), RELU, bias=64.0 - 256.0)
-            act(B("xs", 240 * s - 240, 240 * s), P(pa, 0, 15), RELU, bias=64.0 - 256.0)
+        for s in (3, 2, 1):
+            pa = P("pa%d" % (s % 2), 0, 15)
+            group([(pa, B("idM"), B("Bs", 240 * s - 240, 240 * s)), (pa, B("ihd"), B("urep"))], (1,))
+            act(B("xs", 240 * s - 240, 240 * s), pa, RELU, bias=64.0 - 256.0)
 
         def event(e):
             phase("ev%d" % e)
-            p1, o = "pb%d" % (e % 2), 256 * e
+            nev[0] += 1
+            p1, o = "pb%d" % (nev[0] % 2), 128 * e
             src, r = ("eq1", 1920 * t) if e == 0 else ("eqm", 1920 * (e % 4))
             lst = IX(B("on", 16 * e, 16 * e + 16), B("w8l"))
-            act(B("W8", o, o + 128), lst, scale=col(18))
-            act(B("W8", o + 128, o + 256), lst, scale=2.0)
+            if e in CFG["w8v"]:
+                cp(B("W8", o, o + 128), lst)
+            else:
+                act(B("W8", o, o + 128), lst)
             terms = [(P(p1, 0, 15, p=8), B("idb", 0, 8), B("thw"))]
             for a in range(15):
                 n = 240 - 16 * a
-                terms.append((P(p1, a, a + 1, p=8), B("W8", o + 8 * a, o + 8 * a + 8), B(src, r, r + 16)))
-                if a < 14:
-                    terms.append((P(p1, a + 1, 15, p=8), B("W8", o + 128 + 8 * a, o + 128 + 8 * a + 8), B(src, r + 16, r + n)))
+                terms.append((P(p1, a, 15, p=8), B("W8", o + 8 * a, o + 8 * a + 8), B(src, r, r + n)))
                 r += n
-            group(terms)
-            q = 256 * (e % 2)
-            act(B("cs", q, q + 240, p=8), P(p1, 0, 15, p=8), RELU)
+            group(terms, (1,))
+            q = 256 * (nev[0] % 2)
+            act(B("cs", q, q + 240, p=8), P(p1, 0, 15, p=8), SIGN)
             out = P("pb2", 0, 1, c=15)
             vh = B("v1h", 16 * t, 16 * t + 15) if e == 0 else B("v16", 16 * (e % 4), 16 * (e % 4) + 15)
-            group([(out, B("ih"), vh), (out, B("idB"), on(e))] + [(out, B("Us", 15 - c, 143 - c, p=8), B("cs", q + c, q + 240, 16, p=8)) for c in range(16)])
+            group([(out, B("ih"), vh), (out, B("idB"), on(e))] + [(out, B("Us", 15 - c, 143 - c, p=8), B("cs", q + c, q + 240, 16, p=8)) for c in range(16)], (2,))
             tt(B("of", 16 * e, 16 * e + 15), out, B("Dm", 0, 15), A.min)
-            ts(B("offU", 16 * e, 16 * e + 15), B("of", 16 * e, 16 * e + 15), 10240.0, A.add)
+            ts(B("offU", 16 * e, 16 * e + 15), B("of", 16 * e, 16 * e + 15), 26624.0, A.add)
 
         for s in range(S, 0, -1):
             event(s - 1)
             phase("st%d" % s)
-            r, pz = 240 * s - 240, P("pb3" if s % 2 else "pz", 0, 15)
-            lst = IX(KW, vU(t, s - 1))
-            kt = B("kvh", 768, 1008) if s == S else B("kt")
-            mm(pz, B("ih32"), B("m2k"), True, False)
-            mm(pz, B("idS", 128 * s - 128, 128 * s), B("Bs", r, r + 240), False, False)
-            if s < S:
-                act(kt, lst, bias=-2048.0, scale=1.0 / 32.0)
-            mm(pz, B("ih32"), kt, False, True)
-            tt(B("kp"), lst, B("xs", r, r + 240), A.mult)
-            tt(B("kz"), B("kp"), pz, A.add)
-            ts(B("kn"), B("kz"), 131040, A.bitwise_and)
+            r = 240 * s - 240
+            parts = ((0, 8, "pz"), (8, 15, "pb3")) if CFG["halves"] and s < S else ((0, 15, "pb3" if s % 2 else "pz"),)
+            for a0, a1, bank in parts:
+                lo, hi, pz = 16 * a0, 16 * a1, P(bank, a0, a1)
+                lst = IX(KW, vU(t, s - 1, a0, a1))
+                kt = B("kvh", 768, 1008) if s == S else B("kt", lo, hi)
+                group([(pz, B("ih32"), B("m2k", lo, hi)), (pz, B("idS", 128 * s - 128, 128 * s), B("Bs", r + lo, r + hi))], stop=False)
+                if s < S:
+                    act(kt, lst, bias=-2048.0, scale=1.0 / 32.0)
+                    tt(B("kp", lo, hi), lst, B("xs", r + lo, r + hi), A.mult)
+                else:
+                    tt(B("kp"), IX(B("iw"), B("uU", 0, 15)), B("cm"), A.mult)
+                group([(pz, B("ih32"), kt)], start=False)
+                tt(B("kz", lo, hi), B("kp", lo, hi), pz, A.add)
+                ts(B("kn", lo, hi), B("kz", lo, hi), 131040, A.bitwise_and)
             cp(IX(B("kw"), B("offU", 16 * s - 16, 16 * s - 1)), B("kn"))
-        event(4)
-        cp(IX(B("xw"), B("offU", 64, 79)), B("xn"))
+            if s == CFG["wpos"]:
+                event(4)
+                cp(IX(B("xw"), B("offU", 64, 79)), B("xn"))
         if t + 1 < RACES:
             phase("thr")
             group([(P("pc", 12, 13, c=15), B("ones"), on(4))])
             op("V", lambda e: e.tensor_reduce(T.tot[:], T.pc[:, 192:207], AxisListType.X, A.add), B("tot"), [P("pc", 12, 13, c=15)])
             cp(B("totI"), B("tot"))
             ts(B("totI"), B("totI"), 1, A.bitwise_and)
-            ts(B("thr"), B("totI"), 2.0, A.mult, 8.0, A.add)
+            ts(B("thr", 0, 1), B("totI"), 2.0, A.mult, 8.0, A.add)
+            ts(B("thr", 1, 2), B("totI"), 12.0, A.add)
 
     phase("start1")
     ms(B("m2k"), -2048.0)
@@ -672,6 +720,7 @@ def rank_program(g, core, T, topo):
     zinit(0)
     for t in range(RACES):
         race(t)
+    now[0] = -1
     phase("out")
     group([(P("pa0", 0, 32), B("idx", 128 * a, 128 * a + 128), B("xw", 512 * a, 512 * a + 512)) for a in range(8)])
     act(B("ox"), P("pa0", 0, 32))

@@ -13,36 +13,42 @@ BIG = 2.0 ** 19
 CFG = {
     "groups": ((0, 4, "V"), (4, 8, "S"), (8, 12, "V"), (12, 15, "S")),
     "xcols": 1,
-    "kbank": ("pz", "pb1", "pc", "pb3"),
-    "zv": (4,), "kv": ((1, 0),), "gz": True, "w8v": (3,), "halves": True, "wpos": 2, "run": 240.0, "zfirst": 1,
-    "bias": {}, "rounds": 1800, "lead": 8000.0, "seed": 1, "span": 6000.0, "shake": 2000.0,
-    "cyc": 0.85, "lat": 220.0, "gam": 1.6, "sig": 3.8, "pe": 0.45,
+    "kbank": ("pb0", "pz", "pb2", "pc"), "gate": True, "cbank": "pz", "signs": {1: (1,), 2: (2,), 3: (3,)}, "early": True, "xparts": ((0, 8), (8, 15)),
+    "zv": (), "kv": ((1, 0),) + tuple((s, g) for s in (1, 2, 3, 4) for g in (1, 3)), "w8v": (3,), "halves": True, "wpos": 3, "run": 512.0, "zfirst": -1,
+    "bias": {}, "rounds": 8000, "rounds2": 90, "lead": 13000.0, "heat": 0.0, "fb": 3, "parts": 0.3, "scols": 2, "seed": 2, "span": 4000.0, "shake": 1500.0,
+    "cyc": 1.0, "lat": 240.0, "gam": 1.75, "sig": 4.3, "pe": 0.52,
+    "others": ({"weight": 1.2, "cyc": 0.85, "lat": 210.0, "gam": 1.5, "sig": 3.5, "pe": 0.45}, {"weight": 0.8, "cyc": 1.22, "lat": 280.0, "gam": 1.9, "sig": 5.0, "pe": 0.62}),
 }
 PLAN = {}
 
 SCRATCH = {}
+PIECE = {}
 for _d, _l in (
-        ("bfloat16", (("xw", WIN), ("zx", 4096), ("xq", 256), ("d0", 512), ("zT", 512), ("E", 2048), ("xg0", 512), ("xg1", 512), ("xg2", 512),
-                      ("zg", 1792), ("zs", 240), ("zl", 720), ("zc", 720), ("on", 80), ("eq1", 5760), ("eqm", 7680), ("W8", 1280), ("cs", 512),
+        ("bfloat16", (("xw", WIN), ("zx", 4096), ("xq", 768), ("d0", 512), ("zT", 512), ("E", 2048), ("xg0", 512), ("xg1", 512), ("xg2", 512),
+                      ("zg", 1024), ("zs", 240), ("zl", 720), ("zc", 720), ("on", 80), ("eq1", 5760), ("eqm", 7680), ("W8", 1280), ("cs", 512),
                       ("Bs", 960), ("xW", 240), ("zW", 240), ("xn", 240), ("idb", 128), ("idn", 128), ("idB", 128), ("idM", 128), ("idS", 512),
-                      ("U", 144), ("U1", 144), ("Us", 144), ("kc", 128), ("rm", 256), ("rz", 2048), ("cst", 256), ("cneg", 32), ("Wk", 16),
+                      ("U", 144), ("U1", 144), ("Us", 144), ("kc", 128), ("rm", 256), ("rz", 2048), ("cst", 256), ("cneg", 96), ("cls", 32), ("z3", 256), ("Wk", 16),
                       ("thw", 240), ("idx", 1024), ("ones", 128))),
-        ("float16", (("kvh", 1024), ("Tt", 512), ("shp", 8192), ("shc", 512), ("z4", 512), ("Pm", 512), ("ih", 128), ("ihn", 128), ("ih32", 128), ("ihd", 128),
-                     ("Uh", 144), ("val", 960), ("v16", 80), ("v1h", 48), ("urep", 240), ("kt", 240), ("m2k", 240), ("zt", 256), ("xr", 240), ("kh", 4096), ("idk", 1024))),
+        ("float16", (("kvh", 1024), ("Tt", 512), ("shp", 8192), ("zh", 2304), ("ih2", 128), ("Pm", 512), ("ih", 128), ("ihn", 128), ("ih32", 128), ("ihd", 128),
+                     ("Uh", 144), ("val", 960), ("v16", 80), ("v1h", 48), ("urep", 240), ("kt", 240), ("m2k", 240), ("zt", 1024), ("xr", 240), ("kh", 4096), ("idk", 1024))),
         ("float32", (("kw", WIN), ("iw", 4096), ("R", 1024), ("C", 1024), ("nb", 64), ("kcol", 64), ("k1c", 48), ("nW", 16), ("valf", 240),
                      ("xs", 960), ("kp", 240), ("of", 80), ("Dm", 16), ("base", 64), ("bs", 64), ("ln", 16), ("bF", 16), ("ge", 16), ("xy", 16),
-                     ("d1", 64), ("w1", 64), ("tot", 1), ("thr", 2), ("wt", 32), ("cm", 240), ("pF", 24), ("ox", 512), ("ok", 512), ("t8", 8))),
-        ("int32", (("kin", V), ("vs", 45), ("vl", 135), ("vI", 48), ("wz", 64), ("u4", 64), ("c1", 64), ("m1", 16), ("m3", 16), ("own", 48),
-                   ("rcv", 144), ("x", 16), ("uI", 16), ("dI", 16), ("WI", 16), ("bI", 16), ("cI", 64), ("kI", 64), ("kz", 240), ("kn", 240),
+                     ("d1", 64), ("w1", 64), ("tot", 1), ("thr", 2), ("wt", 32), ("cm", 240), ("x3", 16), ("op", 16), ("g0", 16), ("wf", 16), ("ow1", 16), ("ow2", 16), ("ow4", 16), ("owE", 128), ("pF", 24), ("ox", 512), ("ok", 512), ("t8", 8))),
+        ("int32", (("kin", V), ("vs", 45), ("vl", 135), ("vI", 48), ("wz", 64), ("u4", 64), ("c1", 64), ("m1", 16), ("m3", 48), ("own", 48),
+                   ("rcv", 288), ("x", 16), ("uI", 16), ("dI", 16), ("WI", 16), ("bI", 16), ("cI", 64), ("kI", 64), ("kz", 240), ("kn", 240),
                    ("totI", 1), ("pI", 12))),
         ("uint16", (("kvu", 256), ("vU", 240), ("kU", 64), ("WU", 16), ("bU", 16), ("uU", 16), ("offU", 80), ("w8l", 8)))):
     for _n, _w in _l:
-        SCRATCH[_n] = ("sbuf", [128, _w], _d)
+        if _d == "float32" and _w <= 64:
+            PIECE[_n] = ("small", 64 * len(PIECE), _w)
+        else:
+            SCRATCH[_n] = ("sbuf", [128, _w], _d)
+SCRATCH["small"] = ("sbuf", [128, 64 * len(PIECE)], "float32")
 SCRATCH["Y"] = ("sbuf", [128, 16, 256], "bfloat16")
 for _n in ("pb0", "pb1", "pb2", "pb3", "pa0", "pa1", "pz", "pc"):
     SCRATCH[_n] = ("psum", [128, 512], "float32")
-SEMAPHORES = ["qV", "qS", "qT", "qG", "zin", "vin", "k0", "k1", "k2", "k3", "x0", "x1", "az", "av", "a0", "a1", "a2",
-              "lz", "lv", "l0", "l1", "l2", "oy", "ok"]
+SEMAPHORES = ["qV", "qS", "qT", "qG", "zin", "vin", "ld0", "ld1", "ld2", "ld3", "ld4", "ld5", "az", "av", "a0", "a1", "a2",
+              "lz", "lv", "l0", "l1", "l2", "oy", "ok0", "ok1", "e0", "e1", "e2", "f0", "f1", "f2"]
 
 
 def planner(g, T):
@@ -50,6 +56,9 @@ def planner(g, T):
     ops = []
     plan = {}
     bias = [0.0, (-1, ""), 0]
+
+    def cost(p, m):
+        return p[0] + m["cyc"] * (p[1] + m["gam"] * p[2] + m["sig"] * p[3]) + m["pe"] * p[4]
 
     def is_psum(b):
         return b in SCRATCH and SCRATCH[b][0] == "psum"
@@ -76,6 +85,8 @@ def planner(g, T):
 
     def rec(q, kind, fn, R, W, dur, lat, sem=None, val=0, after=None):
         i = len(ops)
+        parts = dur if isinstance(dur, tuple) else (dur, 0, 0, 0, 0)
+        dur = cost(parts, CFG)
         rq = q if kind == "c" else kind + str(i)
         deps = {}
         for r in hazards(plan, rq, R, W):
@@ -85,7 +96,7 @@ def planner(g, T):
             deps[after] = 0
         note(plan, rq, R, W, i)
         bias[2] += 1
-        ops.append({"id": (bias[1][0], bias[1][1], bias[2]), "q": q, "kind": kind, "fn": fn, "dur": dur, "sem": sem, "val": val, "lat": lat, "deps": deps, "after": after, "bias": bias[0], "txt": (W[0][0] if W else kind)})
+        ops.append({"id": (bias[1][0], bias[1][1], bias[2]), "q": q, "kind": kind, "fn": fn, "dur": dur, "parts": parts, "sem": sem, "val": val, "lat": lat, "deps": deps, "after": after, "bias": bias[0], "txt": (W[0][0] if W else kind)})
         return i
 
     def emit():
@@ -100,13 +111,14 @@ def planner(g, T):
             prio[i] = ops[i]["dur"] + max([x + prio[k] for k, x in succ[i]] + [0.0])
         pred = [list(o["deps"].items()) for o in ops]
         dur = [o["dur"] for o in ops]
+        others = [(m["weight"], m["lat"], [cost(o["parts"], m) for o in ops]) for m in CFG["others"]]
         queue = [o["q"] for o in ops]
         twin = {o["id"]: i for i, o in enumerate(ops)}
 
-        def place(rank, before, back):
-            start = [0.0] * n
+        def place(rank, before):
+            start = {}
             busy = {q: ([], []) for q in queues}
-            end = [0.0] * n
+            end = [-1e9] * n
             for i in rank:
                 t, w = 0.0, dur[i]
                 for d, x in before[i]:
@@ -126,38 +138,58 @@ def planner(g, T):
                 start[i] = t
                 end[i] = t + w
             return start, max(end)
-        if n not in PLAN:
-            key = [-prio[i] - ops[i]["bias"] for i in range(n)]
-            for i in range(n):
-                key[i] = max([key[i]] + [key[d] + 1e-3 for d, x in pred[i]])
-            best = None
-            seed = CFG["seed"]
-            for r in range(CFG["rounds"]):
-                start, end = place(sorted(range(n), key=lambda i: (key[i], i)), pred, False)
-                if best is None or end < best[0]:
-                    best = (end, start)
-                if r % 3 == 2:
-                    seed = (seed * 1103515245 + 12345) % 2 ** 31
-                    mid, key = (seed >> 8) % 1000 / 1000.0 * best[0], list(best[1])
-                    for i in range(n):
-                        if abs(key[i] - mid) < CFG["span"]:
-                            seed = (seed * 1103515245 + 12345) % 2 ** 31
-                            key[i] += (seed >> 8) % 1000 / 1000.0 * CFG["shake"]
-                    if r % 6 == 2:
-                        at = [best[1][i] for i in range(n) if ops[i]["kind"] == "s"][-RACES:]
-                        m = min(range(RACES), key=lambda t: abs(at[t] - CFG["lead"] - mid))
-                        for i in range(n):
-                            if (m,) + ops[i]["id"][1:] in twin and ops[i]["id"][0] >= 0:
-                                key[i] = key[twin[(m,) + ops[i]["id"][1:]]] - at[m] + at[ops[i]["id"][0]]
-                    for i in range(n):
-                        for d, x in pred[i]:
+        seed = [CFG["seed"]]
+
+        def draw():
+            seed[0] = (seed[0] * 1103515245 + 12345) % 2 ** 31
+            return (seed[0] >> 8) % 4096 / 4096.0
+
+        def improve(part, key, rounds):
+            inside = set(part)
+            fore = {i: [e for e in pred[i] if e[0] in inside] for i in part}
+            back = {i: [e for e in succ[i] if e[0] in inside] for i in part}
+            best = top = None
+            for r in range(rounds):
+                if r % CFG["fb"] == 0:
+                    for i in part:
+                        for d, x in fore[i]:
                             if key[i] <= key[d]:
                                 key[i] = key[d] + 1e-3
-                    continue
-                late, end = place(sorted(range(n), key=lambda i: (-start[i] - dur[i], -i)), succ, True)
-                key = [-late[i] - dur[i] for i in range(n)]
-            PLAN[n] = best
-            PLAN["ops"] = ops
+                start, end = place(sorted(part, key=lambda i: (key[i], i)), fore)
+                if best is None or end < 1.01 * best[0]:
+                    rank, score = sorted(part, key=lambda i: (start[i], i)), end
+                    for w, lat, other in others:
+                        fin, free = {}, {q: 0.0 for q in "VSTGYN"}
+                        for i in rank:
+                            t = free[queue[i]] if queue[i] != "N" else 0.0
+                            for d, x in fore[i]:
+                                if fin[d] + (lat if x == CFG["lat"] else x) > t:
+                                    t = fin[d] + (lat if x == CFG["lat"] else x)
+                            fin[i] = free[queue[i]] = t + other[i]
+                        score += w * max(fin.values())
+                    if best is None or score < best[2]:
+                        best = top = (end, start, score)
+                if r % CFG["fb"] == CFG["fb"] - 1:
+                    mid, key = draw() * best[0], dict(best[1])
+                    if draw() < CFG["parts"]:
+                        j, by = part[int(draw() * len(part))], (draw() - 0.5) * 2 * CFG["shake"]
+                        for i in part:
+                            if ops[i]["id"][:2] == ops[j]["id"][:2]:
+                                key[i] += by
+                    else:
+                        for i in part:
+                            if abs(key[i] - mid) < CFG["span"]:
+                                key[i] += draw() * CFG["shake"]
+                else:
+                    late, end = place(sorted(part, key=lambda i: (-start[i] - dur[i], -i)), back)
+                    key = {i: -late[i] - dur[i] for i in part}
+            return top
+        if n not in PLAN:
+            span, one, _ = improve([i for i in range(n) if ops[i]["id"][0] == 1], {i: -prio[i] for i in range(n)}, CFG["rounds"])
+            key = {i: (prio[0] - prio[i] if ops[i]["id"][0] < 0 else CFG["lead"] + span * ops[i]["id"][0] + one[twin[(1,) + ops[i]["id"][1:]]]) for i in range(n)}
+            PLAN["one"] = span
+            PLAN[n] = improve(list(range(n)), key, CFG["rounds2"])
+        PLAN["ops"] = ops
         order = sorted((PLAN[n][1][i], i, i) for i in range(n))
         cnt = {q: 0 for q in queues}
         clk = {q: {} for q in queues}
@@ -216,6 +248,9 @@ def rank_program(g, core, T, topo):
         bias[1], bias[2] = (now[0], (now[1], name)), 0
 
     def B(name, lo=0, hi=None, st=1, p=128):
+        if name in PIECE:
+            name, o, w = PIECE[name]
+            lo, hi = o + lo, o + (w if hi is None else hi)
         hi = SCRATCH[name][1][1] if hi is None else hi
         n = len(range(lo, hi, st))
         return (T[name][0:p, lo:hi:st], [(name, lo, lo + (n - 1) * st + 1)], n, 2 if "16" in SCRATCH[name][2] else 4, False, False, [])
@@ -240,13 +275,13 @@ def rank_program(g, core, T, topo):
         if dur is None:
             fix = 50 if q == "V" else 65
             if out[5]:
-                dur = fix + CFG["sig"] * out[2] * CYC
+                dur = (fix, 0, 0, out[2], 0)
             elif any(x[5] for x in full):
-                dur = fix + CFG["gam"] * out[2] * CYC
+                dur = (fix, 0, out[2], 0, 0)
             else:
                 if rate is None:
                     rate = 0.5 if out[3] == 2 and all(x[3] == 2 for x in full if x[2] > 1) else 1
-                dur = max(64, out[2] * rate) * CYC
+                dur = (0, max(64, out[2] * rate), 0, 0, 0)
         rec(q, "c", fn, R, out[1], dur, LAT)
 
     def iota(out, pattern, base, cm):
@@ -254,7 +289,7 @@ def rank_program(g, core, T, topo):
             fn = lambda e: e.iota(out[0], pattern, base, cm)
         else:
             fn = lambda e: e.iota(out[0], pattern, base, cm, allow_small_or_imprecise_dtypes=True)
-        last["G"] = rec("G", "c", fn, [], out[1], 130 + 2 * out[2] * CYC, LAT, after=last.get("G"))
+        last["G"] = rec("G", "c", fn, [], out[1], (130, 2 * out[2], 0, 0, 0), LAT, after=last.get("G"))
 
     def ts(out, in0, s1, o0, s2=None, o1=None):
         if o1 is None:
@@ -278,9 +313,9 @@ def rank_program(g, core, T, topo):
         run, dur = [], 0.0
         for i, (out, lhsT, rhs) in enumerate(terms):
             run.append((out[0], lhsT[0], rhs[0], start and i == 0, stop and i == len(terms) - 1))
-            dur += max(min(64, lhsT[2]), rhs[2]) * CFG["pe"] * (4 if rhs[3] == 4 else 1)
+            dur += max(min(64, lhsT[2]), rhs[2]) * (4 if rhs[3] == 4 else 1)
             if dur >= CFG["run"] or i + 1 in cuts or i + 1 - len(terms) in cuts or i + 1 == len(terms):
-                op("T", lambda e, run=run: [e.matmul(*m) for m in run][-1], out, [x for u in terms[i + 1 - len(run):i + 1] for x in u[1:]], dur=dur)
+                op("T", lambda e, run=run: [e.matmul(*m) for m in run][-1], out, [x for u in terms[i + 1 - len(run):i + 1] for x in u[1:]], dur=(0, 0, 0, 0, dur))
                 run, dur = [], 0.0
 
     def ms(out, val):
@@ -306,10 +341,10 @@ def rank_program(g, core, T, topo):
     phase("load")
     dma("S", "vin", T.vs[:], T.v0[:], [], [("vs", 0, 45)], 2000.0)
     dma("S", "zin", T.zs[:], T.z0[:], [], [("zs", 0, 240)], 2000.0)
-    for i in range(4):
-        dma("YS"[i % 2], "k%d" % i, T.kin[:, 1024 * i:1024 * i + 1024], T.k0[:, 1024 * i:1024 * i + 1024], [], [("kin", 1024 * i, 1024 * i + 1024)], 4500.0 + 2300.0 * i)
-    for i in range(2):
-        dma("YS"[i], "x%d" % i, T.xw[:, 2048 * i:2048 * i + 2048], T.x0[:, 2048 * i:2048 * i + 2048], [], [("xw", 2048 * i, 2048 * i + 2048)], 16000.0)
+    loads = [("kin", T.k0, 1024 * i, 1024 * i + 1024) for i in range(4)] + [("xw", T.x0, 2048 * i, 2048 * i + 2048) for i in range(2)]
+    for i, (name, src, lo, hi) in enumerate(loads):
+        gate = [(loads[i - 2][0], loads[i - 2][2], loads[i - 2][2] + 1)] if i >= 2 and CFG["gate"] else []
+        dma("Y", "ld%d" % i, T[name][:, lo:hi], src[:, lo:hi], gate, [(name, lo, hi)], 4500.0 + 2300.0 * (i == 1) if CFG["gate"] else 4500.0 + 2300.0 * i)
 
     iota(B("pI", 0, 1), [[0, 1]], 0, 1)
     iota(B("iw", 0, 256), [[1, 256]], 0, 0)
@@ -347,7 +382,7 @@ def rank_program(g, core, T, topo):
     ts(col(10), col(2), 15.0, A.add)
     ts(col(11), col(0), 16.0, A.mult, 15.0, A.add)
     ts(B("idb"), I128, col(0), A.is_equal)
-    for name, f in (("idn", -1.0), ("idB", -16384.0), ("idM", 8192.0), ("ih", 1.0), ("ihn", -1.0), ("ih32", 32.0), ("ihd", 1.0 / 32.0)):
+    for name, f in (("idn", -1.0), ("idB", -16384.0), ("idM", 8192.0), ("ih", 1.0), ("ihn", -1.0), ("ih2", -2.0), ("ih32", 32.0), ("ihd", 1.0 / 32.0)):
         act(B(name), B("idb"), scale=f)
     for s in range(S):
         act(B("idS", 128 * s, 128 * s + 128), B("idb"), scale=1024.0 * (s + 1))
@@ -366,8 +401,12 @@ def rank_program(g, core, T, topo):
     ts(B("E", 0, 16 * SW), B("E", 0, 16 * SW), col(0), A.is_equal)
     ms(B("rz", 0, 16 * VW), 2048.0)
     ms(B("rz", 0, 16 * VW, 16), -1024.0)
-    for name in ("kvh", "on", "zg", "z4", "vI"):
+    for name in ("on", "vI", "x", "ow4"):
         ms(B(name), 0)
+    for o in range(240, 2304, 256):
+        ms(B("zh", o, o + 16), 1024.0)
+    for o in range(240, 1024, 256):
+        ms(B("kvh", o, o + 16), 0.0)
     for a0, a1, k in GROUPS:
         for par in range(2 * (k == "V")):
             ms(B("shp", 4096 * par + 256 * a0, 4096 * par + 256 * a1), 0.0)
@@ -376,8 +415,9 @@ def rank_program(g, core, T, topo):
     ms(B("thr", 1, 2), 12.0)
     ms(B("ones"), 1.0)
     ms(B("cst"), 2048.0)
-    ms(B("cneg", 0, 16), -16384.0)
-    ms(B("cneg", 16, 32), 0.0)
+    ms(B("cneg", 0, 48), -16384.0)
+    ms(B("cneg", 48, 96), 0.0)
+    ms(B("cls", 0, 16), -16384.0)
     for i in range(4):
         ts(pi(7 + i), pi(1), i, A.arith_shift_right, 1, A.bitwise_and)
     for i in range(4):
@@ -431,13 +471,15 @@ def rank_program(g, core, T, topo):
     for i in range(4):
         ts(B("kw", 1024 * i, 1024 * i + 1024), B("kin", 1024 * i, 1024 * i + 1024), 32.0, A.mult)
 
-    def sh(gr, s, st=1):
+    def zh(s, a0=0, a1=15):
+        o = (0, 768, 1024, 1280, 256)[s]
+        return B("zh", o + 16 * a0, o + 16 * a1)
+
+    def sh(gr, s):
         a0, a1, k = GROUPS[gr]
-        if s == S:
-            return B("z4", 16 * a0, 16 * a1)
-        if k == "V":
-            return B("shp", 4096 * (s % 2) + 256 * a0, 4096 * (s % 2) + 256 * a1, 16 * st)
-        return B("shc", 256 * (s % 2) + 16 * a0, 256 * (s % 2) + 16 * a1)
+        if k == "V" and s < S:
+            return B("shp", 4096 * (s % 2) + 256 * a0, 4096 * (s % 2) + 256 * a1, 16)
+        return zh(s, a0, a1)
 
     def zform(gr, s):
         a0, a1, k = GROUPS[gr]
@@ -450,8 +492,10 @@ def rank_program(g, core, T, topo):
             act(B("zT", 128 * gr, 128 * gr + 128, p=n), P("pb%d" % gr, 0, 8, p=n), bias=1024.0, scale=-1.0)
 
     def zinit(t):
+        act(zh(0), B("zc", 240 * t, 240 * t + 240), bias=1024.0)
         for gr, (a0, a1, k) in enumerate(GROUPS):
-            act(sh(gr, 0), B("zc", 240 * t + 16 * a0, 240 * t + 16 * a1), bias=1024.0)
+            if k == "V":
+                act(sh(gr, 0), B("zc", 240 * t + 16 * a0, 240 * t + 16 * a1), bias=1024.0)
             zform(gr, 0)
 
     def knew(t, gr, s):
@@ -478,8 +522,8 @@ def rank_program(g, core, T, topo):
     def xact(gr):
         a0, a1, k = GROUPS[gr]
         n = 16 * (a1 - a0)
-        for a in range(a0, a1, 2):
-            e = min(a + 2, a1)
+        for a in range(a0, a1, CFG["scols"]):
+            e = min(a + CFG["scols"], a1)
             xg, pa, o = B("xg%d" % (chunk[0] % 3), 0, 256 * (e - a)), P("pa%d" % (chunk[0] % 2), 0, 16 * (e - a)), 256 * (a - a0)
             chunk[0] += 1
             act(xg, IX(XW, B("kvu", 16 * a, 16 * e)))
@@ -521,30 +565,30 @@ def rank_program(g, core, T, topo):
     def zstep(t, gr, s):
         a0, a1, k = GROUPS[gr]
         w, pz, o = a1 - a0, "pb%d" % gr, 256 * (s - 1) + 16 * a0
-        xq, old, new, lst = B("xq", 16 * a0, 16 * a1), sh(gr, s - 1), sh(gr, s), IX(XW, vU(t, s, a0, a1))
-        onv = s in CFG["zv"] and (k == "V" or s == S)
-        if onv:
-            zp = B("zx", 256 * a0, 256 * a1, 16) if k == "V" else B("zg", o - 256, o - 256 + 16 * w)
-            tt(B("zt", 16 * a0, 16 * a1), lst, zp, A.add)
-            ts(new, B("zt", 16 * a0, 16 * a1), 0.5, A.mult, 1023.75, A.add)
-        if onv and s == S:
-            tt(B("z4", 256 + 16 * a0, 256 + 16 * a1), lst, zp, A.is_gt)
+        old, new, lst = sh(gr, s - 1), sh(gr, s), IX(XW, vU(t, s, a0, a1))
+        if s == S or gr in CFG["zv"]:
+            tt(B("zt", o, o + 16 * w), lst, old, A.add)
+            ts(new, B("zt", o, o + 16 * w), 0.5, A.mult, 511.75, A.add)
         else:
-            act(xq, lst)
-            if not onv:
-                group([(P(pz, 8, 8 + w), B("idb"), xq), (P(pz, 8, 8 + w), B("ih"), old)])
-            group([(P(pz, 24, 24 + w), B("idb"), xq), (P(pz, 24, 24 + w), B("ihn"), old)])
-            if not onv:
-                act(new, P(pz, 8, 8 + w), bias=511.75, scale=0.5)
-            act(B("z4", 256 + 16 * a0, 256 + 16 * a1) if s == S else B("zg", o + 1024, o + 1024 + 16 * w), P(pz, 24, 24 + w), SIGN, bias=1023.5)
-        if s < S:
-            zform(gr, s)
-        zc = B("zg", o, o + 16 * w)
-        if CFG["gz"] and k == "V" and s < S:
-            src = B("zx", 256 * a0, 256 * a1, 16)
-            op("G", lambda e: e.affine_select(zc[0], src[0], [[0, 16 * w]], A.is_gt, 0.0, 1, 0), zc, [src], dur=170 + 32 * w * CYC)
-        else:
-            act(zc, new, bias=-1024.0)
+            act(B("xq", o, o + 16 * w), lst)
+            group([(P(pz, 8, 8 + w), B("ih"), old), (P(pz, 8, 8 + w), B("idb"), B("xq", o, o + 16 * w))])
+            act(new, P(pz, 8, 8 + w), bias=511.75, scale=0.5)
+        if s == S:
+            tt(B("zh", 512 + 16 * a0, 512 + 16 * a1), lst, B("zx", 256 * a0, 256 * a1, 16) if k == "V" else B("z3", 16 * a0, 16 * a1), A.is_gt)
+            return
+        zform(gr, s)
+        if k == "V":
+            zc = zh(s, a0, a1)
+            op("G", lambda e: e.affine_select(zc[0], new[0], [[0, 16 * w]], A.is_gt, 0.0, 1, 0), zc, [new], dur=(170, 32 * w, 0, 0, 0))
+        elif s == S - 1:
+            act(B("z3", 16 * a0, 16 * a1), new, bias=-1024.0)
+        for r in CFG["signs"].get(s, ()):
+            o, pa = 256 * (r - 1) + 16 * a0, P(pz, 24, 24 + w)
+            if gr in CFG["zv"]:
+                group([(pa, B("ih"), B("zt", o, o + 16 * w)), (pa, B("ih2"), zh(r - 1, a0, a1))])
+            else:
+                group([(pa, B("idb"), B("xq", o, o + 16 * w)), (pa, B("ihn"), zh(r - 1, a0, a1))])
+            act(B("zh", 1536 + o, 1536 + o + 16 * w), pa, SIGN, bias=1023.5)
 
     def race(t):
         for s in range(1, S + 1):
@@ -562,17 +606,31 @@ def rank_program(g, core, T, topo):
                 early(t)
         finish(t)
 
+    def least(name, rs):
+        for b, (j1, b1, j2, b2) in enumerate(((3, 1, 2, 2), (3, 2, 1, 0), (2, 0, 1, 1))):
+            o1, o2 = rs + 16 * (j1 - 1) + 5 * b1, rs + 16 * (j2 - 1) + 5 * b2
+            tt(B(name, 5 * b, 5 * b + 5), B("rcv", o1, o1 + 5), B("rcv", o2, o2 + 5), A.min)
+
     def early(t):
         phase("early")
-        group([(P("pc", 0, 7), B("U1", 15 - c, 143 - c), B("zg", c, 1792, 16)) for c in range(16)])
-        tt(B("wz", 0, 48), B("C", 15, 768, 16), P("pc", 0, 3), A.mult)
-        ts(B("nb", 0, 48), P("pc", 4, 7), B("thr", 0, 1), A.is_lt, BIG, A.mult)
+        pc = CFG["cbank"]
+        group([(P(pc, 0, 6), B("idb"), B("cneg"))] + [(P(pc, 0, 6), B("Uh", 15 - c, 143 - c), B("zh", 768 + c, 2304, 16)) for c in range(16)], (1,))
+        tt(B("wz", 0, 48), B("C", 15, 768, 16), P(pc, 0, 3), A.mult)
+        ts(B("nb", 0, 48), P(pc, 3, 6), B("thr", 0, 1), A.is_lt, BIG, A.mult)
         ts(B("u4", 0, 48), B("wz", 0, 48), 4095, A.bitwise_and)
         tt(B("d1", 0, 48), B("nb", 0, 48), B("base", 0, 48), A.add)
         tt(B("c1", 0, 48), B("u4", 0, 48), B("d1", 0, 48), A.add)
         tt(B("m1"), B("c1", 0, 16), B("c1", 16, 32), A.min)
-        ts(B("c1", 0, 16), B("c1", 32, 48), BIG, A.min)
-        tt(B("m3"), B("m1"), B("c1", 0, 16), A.min)
+        m3 = B("m3", 16 * t, 16 * t + 16)
+        tt(m3, B("m1"), B("c1", 32, 48), A.min)
+        if CFG["early"]:
+            rs = 144 + 48 * t
+            send(m3, [T.rcv[:, rs + 16 * j:rs + 16 * j + 16] for j in range(3)], B("rcv", rs, rs + 48), "e%d" % t, "f%d" % t)
+            least("x3", rs)
+            ts(B("x3", 0, 15), B("x3", 0, 15), BIG, A.is_ge)
+        ts(B("op"), m3, BIG, A.is_ge)
+        ts(B("cls", 16, 32), m3, BIG, A.is_lt, 32.0, A.mult)
+        tt(B("g0"), m3, B("base", 48, 64), A.min)
         phase("pairs")
         ts(B("kcol", 16, 64), B("C", 15, 768, 16), -2048.0, A.add)
         act(B("v16", 16, 64), B("C", 15, 768, 16), bias=-2048.0)
@@ -583,13 +641,13 @@ def rank_program(g, core, T, topo):
     def finish(t):
         phase("own")
         own = B("own", 16 * t, 16 * t + 16)
-        group([(P("pc", 8, 10), B("idb"), B("cneg"))] + [(P("pc", 8, 10), B("Uh", 15 - c, 143 - c), B("z4", c, 512, 16)) for c in range(16)], (1,))
-        tt(B("wz", 48, 64), B("C", 768 + 15, 1024, 16), P("pc", 8, 9), A.mult)
-        ts(B("nb", 48, 64), P("pc", 9, 10), B("thr", 1, 2) if S in CFG["zv"] else B("thr", 0, 1), A.is_lt, BIG, A.mult)
+        tt(B("wf"), B("C", 768 + 15, 1024, 16), B("op"), A.mult)
+        group([(P("pc", 8, 10), B("idb"), B("cls"))] + [(P("pc", 8, 10), B("Uh", 15 - c, 143 - c), B("zh", 256 + c, 768, 16)) for c in range(16)], (1,))
+        tt(B("wz", 48, 64), B("wf"), P("pc", 8, 9), A.mult)
+        ts(B("nb", 48, 64), P("pc", 9, 10), B("thr", 1, 2), A.is_lt, BIG, A.mult)
         ts(B("u4", 48, 64), B("wz", 48, 64), 4095, A.bitwise_and)
-        tt(B("d1", 48, 64), B("nb", 48, 64), B("base", 48, 64), A.add)
-        tt(B("c1", 48, 64), B("u4", 48, 64), B("d1", 48, 64), A.add)
-        tt(own, B("c1", 48, 64), B("m3"), A.min)
+        tt(B("d1", 48, 64), B("nb", 48, 64), B("g0"), A.add)
+        tt(own, B("u4", 48, 64), B("d1", 48, 64), A.add)
         rs = 48 * t
         send(own, [T.rcv[:, rs + 16 * j:rs + 16 * j + 16] for j in range(3)], B("rcv", rs, rs + 48), "a%d" % t, "l%d" % t)
         phase("logs")
@@ -623,7 +681,9 @@ def rank_program(g, core, T, topo):
         tt(B("cm"), IX(KW, vU(t, S - 1)), B("Bs", 720, 960), A.mult)
         phase("xnew")
         act(B("xW"), IX(XW, B("WU", 0, 15)))
-        act(B("zW"), IX(B("zg", 0, 1024), B("bU", 0, 15)))
+        act(B("zg", 0, 768), B("zh", 768, 1536), bias=-1024.0)
+        act(B("zg", 768, 1024), B("zh", 256, 512), bias=-1024.0)
+        act(B("zW"), IX(B("zg"), B("bU", 0, 15)))
         group([(P("pc", 16, 31), B("idb"), B("xW")), (P("pc", 16, 31), B("idb"), B("zW"))])
         act(B("xr"), P("pc", 16, 31), bias=1023.75, scale=0.5)
         act(B("xn"), B("xr"), bias=-1024.0)
@@ -631,27 +691,31 @@ def rank_program(g, core, T, topo):
             phase("zinit")
             zinit(t + 1)
 
+        phase("own4")
+        x, ow, ow2 = B("x", 0, 15), B("ow1", 0, 15), B("ow2", 0, 15)
+        ts(ow, B("own", 16 * t, 16 * t + 15), BIG, A.min)
+        tt(ow2, B("own", 16 * t, 16 * t + 15), B("nb", 48, 63), A.add)
+        if CFG["early"]:
+            tt(B("ow4", 0, 15), ow, B("x3", 0, 15), A.mult)
+            act(B("owE"), IX(B("ow4"), B("w8l")))
         phase("win")
-
-        def rc(j, b):
-            o = rs + 16 * (j - 1) + 5 * b
-            return B("rcv", o, o + 5)
-        for b, (j1, b1, j2, b2) in enumerate(((3, 1, 2, 2), (3, 2, 1, 0), (2, 0, 1, 1))):
-            tt(B("x", 5 * b, 5 * b + 5), rc(j1, b1), rc(j2, b2), A.min)
-        x, ow = B("x", 0, 15), B("own", 16 * t, 16 * t + 15)
+        least("x", rs)
 
         def on(e):
             return B("on", 16 * e, 16 * e + 15)
         tt(on(0), x, ow, A.is_lt)
-        ts(B("ge", 0, 15), x, 16384.0 * S, A.is_ge)
-        tt(on(3), on(0), B("ge", 0, 15), A.mult)
+        if CFG["early"]:
+            tt(on(3), x, B("ow4", 0, 15), A.is_lt)
+        else:
+            ts(B("ge", 0, 15), x, 16384.0 * S, A.is_ge)
+            tt(on(3), on(0), B("ge", 0, 15), A.mult)
         ts(B("uI", 0, 15), x, 4095, A.bitwise_and)
         cp(B("uU", 0, 15), B("uI", 0, 15))
         phase("win2")
         tt(B("xy", 0, 15), x, on(0), A.mult)
         for s in (3, 2):
             ts(on(s - 1), B("xy", 0, 15), 16384.0 * s, A.is_ge)
-        tt(on(4), ow, x, A.is_lt)
+        tt(on(4), ow2, x, A.is_lt)
         phase("xs")
         act(B("urep"), IX(B("iw"), B("uU", 0, 15)), bias=-2048.0)
         for s in (3, 2, 1):
@@ -665,7 +729,9 @@ def rank_program(g, core, T, topo):
             p1, o = "pb%d" % (nev[0] % 2), 128 * e
             src, r = ("eq1", 1920 * t) if e == 0 else ("eqm", 1920 * (e % 4))
             lst = IX(B("on", 16 * e, 16 * e + 16), B("w8l"))
-            if e in CFG["w8v"]:
+            if e == S - 1 and CFG["early"]:
+                tt(B("W8", o, o + 128), IX(B("x"), B("w8l")), B("owE"), A.is_lt)
+            elif e in CFG["w8v"]:
                 cp(B("W8", o, o + 128), lst)
             else:
                 act(B("W8", o, o + 128), lst)
@@ -704,11 +770,12 @@ def rank_program(g, core, T, topo):
             cp(IX(B("kw"), B("offU", 16 * s - 16, 16 * s - 1)), B("kn"))
             if s == CFG["wpos"]:
                 event(4)
-                cp(IX(B("xw"), B("offU", 64, 79)), B("xn"))
+                for a0, a1 in CFG["xparts"]:
+                    cp(IX(B("xw"), B("offU", 64 + a0, 64 + a1)), B("xn", 16 * a0, 16 * a1))
         if t + 1 < RACES:
             phase("thr")
             group([(P("pc", 12, 13, c=15), B("ones"), on(4))])
-            op("V", lambda e: e.tensor_reduce(T.tot[:], T.pc[:, 192:207], AxisListType.X, A.add), B("tot"), [P("pc", 12, 13, c=15)])
+            op("V", lambda e: e.tensor_reduce(B("tot")[0], T.pc[:, 192:207], AxisListType.X, A.add), B("tot"), [P("pc", 12, 13, c=15)])
             cp(B("totI"), B("tot"))
             ts(B("totI"), B("totI"), 1, A.bitwise_and)
             ts(B("thr", 0, 1), B("totI"), 2.0, A.mult, 8.0, A.add)
@@ -725,19 +792,24 @@ def rank_program(g, core, T, topo):
     group([(P("pa0", 0, 32), B("idx", 128 * a, 128 * a + 128), B("xw", 512 * a, 512 * a + 512)) for a in range(8)])
     act(B("ox"), P("pa0", 0, 32))
     dma("Y", "oy", T.yx[:], T.ox[:], [("ox", 0, 512)], [], 2000.0)
-    for a in range(8):
-        kb, kh = B("kw", 512 * a, 512 * a + 512), B("kh", 512 * a, 512 * a + 512)
-        if a % 2:
-            act(kh, kb, bias=-2048.0, scale=1.0 / 32.0)
+    for h in range(2):
+        for a in range(8):
+            o = 512 * a + 256 * h
+            if a % 2:
+                act(B("kh", o, o + 256), B("kw", o, o + 256), bias=-2048.0, scale=1.0 / 32.0)
+            else:
+                ts(B("kh", o, o + 256), B("kw", o, o + 256), 1.0 / 32.0, A.mult, -2048.0, A.add)
+        pb = P("pb%d" % h, 0, 16)
+        group([(pb, B("idk", 128 * a, 128 * a + 128), B("kh", 512 * a + 256 * h, 512 * a + 256 * h + 256)) for a in range(8)], (2, 4, 6))
+        if h:
+            ts(B("ok", 256, 512), pb, 36.0 * 2048.0, A.add)
         else:
-            ts(kh, kb, 1.0 / 32.0, A.mult, -2048.0, A.add)
-    group([(P("pa1", 0, 32), B("idk", 128 * a, 128 * a + 128), B("kh", 512 * a, 512 * a + 512)) for a in range(8)])
-    ts(B("ok"), P("pa1", 0, 32), 36.0 * 2048.0, A.add)
-    dma("Y", "ok", T.yk[:], T.ok[:], [("ok", 0, 512)], [], 2000.0)
+            act(B("ok", 0, 256), pb, bias=36.0 * 2048.0)
+        dma("YS"[h], "ok%d" % h, T.yk[:, 256 * h:256 * h + 256], T.ok[:, 256 * h:256 * h + 256], [("ok", 256 * h, 256 * h + 256)], [], 2000.0)
     cnt = emit()
-    g.sync.wait_ge(T.sem.oy, 16)
-    g.sync.wait_ge(T.sem.ok, 16)
+    for sem in ("oy", "ok0", "ok1"):
+        g.sync.wait_ge(T.sem[sem], 16)
     for q in "VSTG":
         g.wait_ge(T.sem["q" + q], cnt[q])
-    for l in ("lz", "lv", "l0", "l1", "l2"):
+    for l in ("lz", "lv", "l0", "l1", "l2") + ("f0", "f1", "f2") * CFG["early"]:
         g.wait_ge(T.sem[l], ne)

@@ -13,29 +13,29 @@ BIG = 2.0 ** 19
 CFG = {
     "groups": ((0, 4, "V"), (4, 8, "S"), (8, 12, "V"), (12, 15, "S")),
     "xcols": 1,
-    "kbank": ("pb0", "pz", "pb2", "pc"), "gate": True, "cbank": "pz", "signs": {1: (1,), 2: (2,), 3: (3,)}, "early": True, "xparts": ((0, 8), (8, 15)),
-    "zv": (), "kv": ((1, 0),) + tuple((s, g) for s in (1, 2, 3, 4) for g in (1, 3)), "w8v": (3,), "halves": True, "wpos": 3, "run": 512.0, "zfirst": -1,
-    "bias": {}, "rounds": 8000, "rounds2": 90, "lead": 13000.0, "heat": 0.0, "fb": 3, "parts": 0.3, "scols": 2, "seed": 2, "span": 4000.0, "shake": 1500.0,
-    "cyc": 1.0, "lat": 240.0, "gam": 1.75, "sig": 4.3, "pe": 0.52,
-    "others": ({"weight": 1.2, "cyc": 0.85, "lat": 210.0, "gam": 1.5, "sig": 3.5, "pe": 0.45}, {"weight": 0.8, "cyc": 1.22, "lat": 280.0, "gam": 1.9, "sig": 5.0, "pe": 0.62}),
+    "kbank": ("pb3", "pz", "pc"), "inorder": False, "d1v": (), "flight": 2, "first": 7000.0, "piece": 2300.0, "ktv": (1, 2, 3), "abank": ("pa0", "pa1"), "batches": ((3,), (2,), (1, 4), (0,)), "spairs": {}, "gzx": True, "teams": ((0, 1), (2,), (3,)), "zv4": (0, 1, 2, 3), "cbank": "pz", "early": True, "xparts": ((0, 8), (8, 15)),
+    "zv": (0, 2), "kv": ((1, 0), (1, 1)), "w8v": (3,), "wpos": 3, "run": 512.0, "zfirst": -1,
+    "bias": {}, "rounds": 5000, "rounds2": 60, "lead": 13000.0, "heat": 150.0, "swap": 0.5, "tries": 1, "rounds0": 0, "fb": 2, "parts": 0.3, "scols": 2, "seed": 3, "span": 4000.0, "shake": 1500.0,
+    "cyc": 1.0, "lat": 240.0, "gam": 1.75, "sig": 4.3, "pe": 0.52, "rem": 0.9,
+    "others": ({"weight": 1.2, "cyc": 0.85, "lat": 210.0, "gam": 1.5, "sig": 3.5, "pe": 0.45, "rem": 1.2}, {"weight": 0.8, "cyc": 1.22, "lat": 280.0, "gam": 1.9, "sig": 5.0, "pe": 0.62, "rem": 0.7}),
 }
 PLAN = {}
 
 SCRATCH = {}
 PIECE = {}
 for _d, _l in (
-        ("bfloat16", (("xw", WIN), ("zx", 4096), ("xq", 768), ("d0", 512), ("zT", 512), ("E", 2048), ("xg0", 512), ("xg1", 512), ("xg2", 512),
-                      ("zg", 1024), ("zs", 240), ("zl", 720), ("zc", 720), ("on", 80), ("eq1", 5760), ("eqm", 7680), ("W8", 1280), ("cs", 512),
+        ("bfloat16", (("xw", WIN), ("zx", 4096), ("xq", 1024), ("d0", 512), ("zT", 512), ("E", 1536), ("xg0", 512), ("xg1", 512), ("xg2", 512),
+                      ("zg", 1024), ("zs", 240), ("zl", 720), ("zc", 720), ("on", 80), ("eq1", 5760), ("eqm", 7680), ("W8", 640), ("cs", 1280),
                       ("Bs", 960), ("xW", 240), ("zW", 240), ("xn", 240), ("idb", 128), ("idn", 128), ("idB", 128), ("idM", 128), ("idS", 512),
-                      ("U", 144), ("U1", 144), ("Us", 144), ("kc", 128), ("rm", 256), ("rz", 2048), ("cst", 256), ("cneg", 96), ("cls", 32), ("z3", 256), ("Wk", 16),
+                      ("U", 144), ("U1", 144), ("Us", 144), ("kc", 128), ("rm", 256), ("rz", 1280), ("cst", 256), ("cneg", 96), ("cls", 16), ("gt4", 256), ("Un", 144), ("z3", 256), ("Wk", 16),
                       ("thw", 240), ("idx", 1024), ("ones", 128))),
         ("float16", (("kvh", 1024), ("Tt", 512), ("shp", 8192), ("zh", 2304), ("ih2", 128), ("Pm", 512), ("ih", 128), ("ihn", 128), ("ih32", 128), ("ihd", 128),
-                     ("Uh", 144), ("val", 960), ("v16", 80), ("v1h", 48), ("urep", 240), ("kt", 240), ("m2k", 240), ("zt", 1024), ("xr", 240), ("kh", 4096), ("idk", 1024))),
-        ("float32", (("kw", WIN), ("iw", 4096), ("R", 1024), ("C", 1024), ("nb", 64), ("kcol", 64), ("k1c", 48), ("nW", 16), ("valf", 240),
-                     ("xs", 960), ("kp", 240), ("of", 80), ("Dm", 16), ("base", 64), ("bs", 64), ("ln", 16), ("bF", 16), ("ge", 16), ("xy", 16),
-                     ("d1", 64), ("w1", 64), ("tot", 1), ("thr", 2), ("wt", 32), ("cm", 240), ("x3", 16), ("op", 16), ("g0", 16), ("wf", 16), ("ow1", 16), ("ow2", 16), ("ow4", 16), ("owE", 128), ("pF", 24), ("ox", 512), ("ok", 512), ("t8", 8))),
+                     ("Uh", 144), ("val", 960), ("v16", 80), ("v1h", 48), ("urep", 240), ("kt", 240), ("m2k", 240), ("zt", 1024), ("xr", 240), ("idk", 1024))),
+        ("float32", (("kw", WIN), ("iw", V), ("R", 1024), ("C", 1024), ("nb", 64), ("kcol", 64), ("nk", 64), ("k1c", 48), ("nW", 16), ("valf", 240),
+                     ("xs", 960), ("kp", 240), ("of", 80), ("Dm", 64), ("base", 64), ("bs", 64), ("ln", 16), ("bF", 16), ("ge", 16), ("xy", 16),
+                     ("d1", 64), ("w1", 64), ("tot", 1), ("thr", 2), ("wt", 32), ("cm", 240), ("x3", 16), ("op", 16), ("g0", 16), ("wf", 16), ("ow1", 16), ("ow2", 16), ("ow4", 16), ("owE", 128), ("dd", 512), ("pF", 24), ("ox", 512), ("ok", 512), ("t8", 8))),
         ("int32", (("kin", V), ("vs", 45), ("vl", 135), ("vI", 48), ("wz", 64), ("u4", 64), ("c1", 64), ("m1", 16), ("m3", 48), ("own", 48),
-                   ("rcv", 288), ("x", 16), ("uI", 16), ("dI", 16), ("WI", 16), ("bI", 16), ("cI", 64), ("kI", 64), ("kz", 240), ("kn", 240),
+                   ("rcv", 432), ("rk", 48), ("xu", 16), ("x", 16), ("uI", 16), ("dI", 16), ("WI", 16), ("bI", 16), ("cI", 64), ("kI", 64), ("kz", 240), ("kn", 240),
                    ("totI", 1), ("pI", 12))),
         ("uint16", (("kvu", 256), ("vU", 240), ("kU", 64), ("WU", 16), ("bU", 16), ("uU", 16), ("offU", 80), ("w8l", 8)))):
     for _n, _w in _l:
@@ -48,7 +48,7 @@ SCRATCH["Y"] = ("sbuf", [128, 16, 256], "bfloat16")
 for _n in ("pb0", "pb1", "pb2", "pb3", "pa0", "pa1", "pz", "pc"):
     SCRATCH[_n] = ("psum", [128, 512], "float32")
 SEMAPHORES = ["qV", "qS", "qT", "qG", "zin", "vin", "ld0", "ld1", "ld2", "ld3", "ld4", "ld5", "az", "av", "a0", "a1", "a2",
-              "lz", "lv", "l0", "l1", "l2", "oy", "ok0", "ok1", "e0", "e1", "e2", "f0", "f1", "f2"]
+              "lz", "lv", "l0", "l1", "l2", "oy", "ok0", "ok1", "e0", "e1", "e2", "f0", "f1", "f2", "u0", "u1", "u2", "w0", "w1", "w2"]
 
 
 def planner(g, T):
@@ -58,7 +58,7 @@ def planner(g, T):
     bias = [0.0, (-1, ""), 0]
 
     def cost(p, m):
-        return p[0] + m["cyc"] * (p[1] + m["gam"] * p[2] + m["sig"] * p[3]) + m["pe"] * p[4]
+        return p[0] + m["cyc"] * (p[1] + m["gam"] * p[2] + m["sig"] * p[3]) + m["pe"] * p[4] + m["rem"] * sum(p[5:])
 
     def is_psum(b):
         return b in SCRATCH and SCRATCH[b][0] == "psum"
@@ -89,9 +89,10 @@ def planner(g, T):
         dur = cost(parts, CFG)
         rq = q if kind == "c" else kind + str(i)
         deps = {}
-        for r in hazards(plan, rq, R, W):
-            x = 0 if (q == "T" and ops[r[4]]["q"] == "T") else ops[r[4]]["lat"]
-            deps[r[4]] = max(deps.get(r[4], 0), x)
+        for reads, found in ((True, hazards(plan, rq, R, [])), (False, hazards(plan, rq, [], W))):
+            for r in found:
+                x = 0 if r[3] == rq and (q == "T" or not reads and CFG["inorder"]) else ops[r[4]]["lat"]
+                deps[r[4]] = max(deps.get(r[4], 0), x)
         if after is not None:
             deps[after] = 0
         note(plan, rq, R, W, i)
@@ -167,11 +168,28 @@ def planner(g, T):
                                     t = fin[d] + (lat if x == CFG["lat"] else x)
                             fin[i] = free[queue[i]] = t + other[i]
                         score += w * max(fin.values())
-                    if best is None or score < best[2]:
-                        best = top = (end, start, score)
+                    if best is None or score < best[2] + CFG["heat"] * (1.0 - r / rounds) * draw():
+                        best = (end, start, score)
+                        top = best if top is None or score < top[2] else top
+                        ahead, tight, i = {}, [], rank[-1]
+                        free = {}
+                        for j in rank:
+                            ahead[j], free[queue[j]] = free.get(queue[j]), j
+                            if start[j] + dur[j] > start[i] + dur[i]:
+                                i = j
+                        while i is not None:
+                            j = [d for d, x in fore[i] if start[d] + dur[d] + x > start[i] - 1e-3]
+                            if not j and ahead[i] is not None and start[ahead[i]] + dur[ahead[i]] > start[i] - 1e-3:
+                                tight.append((ahead[i], i))
+                                j = [ahead[i]]
+                            i = j[0] if j else None
                 if r % CFG["fb"] == CFG["fb"] - 1:
                     mid, key = draw() * best[0], dict(best[1])
-                    if draw() < CFG["parts"]:
+                    if tight and draw() < CFG["swap"]:
+                        for _ in range(1 + int(draw() * 2)):
+                            j, i = tight[int(draw() * len(tight))]
+                            key[j] = key[i] + 1.0 + draw() * draw() * CFG["shake"]
+                    elif draw() < CFG["parts"]:
                         j, by = part[int(draw() * len(part))], (draw() - 0.5) * 2 * CFG["shake"]
                         for i in part:
                             if ops[i]["id"][:2] == ops[j]["id"][:2]:
@@ -185,7 +203,17 @@ def planner(g, T):
                     key = {i: -late[i] - dur[i] for i in part}
             return top
         if n not in PLAN:
-            span, one, _ = improve([i for i in range(n) if ops[i]["id"][0] == 1], {i: -prio[i] for i in range(n)}, CFG["rounds"])
+            part = [i for i in range(n) if ops[i]["id"][0] == 1]
+            key = {i: -prio[i] for i in range(n)}
+            if CFG["rounds0"]:
+                need = {max(i for i in part if ops[i]["kind"] == "s")}
+                for i in reversed(part):
+                    if i in need:
+                        need.update(d for d, x in pred[i] if ops[d]["id"][0] == 1)
+                span, one, _ = min((improve(sorted(need), dict(key), CFG["rounds0"]) for _ in range(CFG["tries"])), key=lambda b: b[2])
+                PLAN["pre"] = span
+                key = {i: one[i] if i in need else span + prio[max(need)] - prio[i] + 1e5 for i in part}
+            span, one, _ = improve(part, key, CFG["rounds"])
             key = {i: (prio[0] - prio[i] if ops[i]["id"][0] < 0 else CFG["lead"] + span * ops[i]["id"][0] + one[twin[(1,) + ops[i]["id"][1:]]]) for i in range(n)}
             PLAN["one"] = span
             PLAN[n] = improve(list(range(n)), key, CFG["rounds2"])
@@ -204,7 +232,7 @@ def planner(g, T):
                 continue
             need = {}
             for d in o["deps"]:
-                if d == o["after"] or (q == "T" and ops[d]["q"] == "T"):
+                if not o["deps"][d]:
                     continue
                 sm, v = tag[d]
                 if need.get(sm, 0) < v:
@@ -318,24 +346,26 @@ def rank_program(g, core, T, topo):
                 op("T", lambda e, run=run: [e.matmul(*m) for m in run][-1], out, [x for u in terms[i + 1 - len(run):i + 1] for x in u[1:]], dur=(0, 0, 0, 0, dur))
                 run, dur = [], 0.0
 
+    def gcp(out, in_, after=None, pieces=None):
+        rec("G", "c", lambda e: e.affine_select(out[0], in_[0], [[0, out[2]]], A.is_gt, 0.0, 1, 0), in_[1], pieces or out[1], (170, 2 * out[2], 0, 0, 0), LAT, after=after)
+
     def ms(out, val):
         op("V", lambda e: e.memset(out[0], val), out, [], rate=out[3] / 4)
 
     def dma(q, sem, out, in_, R, W, lat):
         last[q] = rec(q, "d", lambda e: e.dma_start(out, in_), R, W, 60.0, lat, sem, 16, after=last.get(q))
 
-    def send(src, dsts, W, rsem, lsem):
-        ids = []
-        m = None
-        for p in peers:
-            a = topo.addr(p)
-            ids.append(DstId(rid=a[0], pnc=a[1]))
-            m = topo.mask(core, p) if m is None else m & topo.mask(core, p)
-        tr = RemoteDMATransfer(dst_ids=ids, dma_engine_mask=m, remote_sem=T.sem[rsem], srcs=[src[0]], dsts=dsts, alu_op=0)
-        n = sum(m >> e & 1 for e in range(16))
-        i = rec("G", "s", lambda e: e.remote_dma_fused([tr], local_sem=T.sem[lsem]), src[1], [], 900.0, 1500.0, lsem, n, after=last.get("G"))
+    def send(src, dsts, W, rsem, lsem, more=()):
+        ids = [DstId(rid=topo.addr(p)[0], pnc=topo.addr(p)[1]) for p in peers]
+        eng = [e for e in topo.engines(core, peers[0]) if all(e in topo.engines(core, p) for p in peers)]
+        pieces = [(src, dsts, W)] + list(more)
+        n = len(eng) // len(pieces)
+        trs = [RemoteDMATransfer(dst_ids=ids, dma_engine_mask=sum(1 << e for e in eng[n * k:n * k + n]), remote_sem=T.sem[rsem], srcs=[u[0][0]], dsts=u[1], alu_op=0)
+               for k, u in enumerate(pieces)]
+        n *= len(pieces)
+        i = rec("G", "s", lambda e: e.remote_dma_fused(trs, local_sem=T.sem[lsem]), [r for u in pieces for r in u[0][1]], [], (0, 0, 0, 0, 0, 900.0), 1500.0, lsem, n, after=last.get("G"))
         last["G"] = i
-        rec("N", "n", None, [], W[1], 2500.0, LAT, rsem, 3 * n, after=i)
+        rec("N", "n", None, [], [r for u in pieces for r in u[2][1]], (0, 0, 0, 0, 0, 2500.0) if now[0] >= 0 else CFG["first"], LAT, rsem, 3 * n, after=i)
         return n
 
     phase("load")
@@ -343,8 +373,9 @@ def rank_program(g, core, T, topo):
     dma("S", "zin", T.zs[:], T.z0[:], [], [("zs", 0, 240)], 2000.0)
     loads = [("kin", T.k0, 1024 * i, 1024 * i + 1024) for i in range(4)] + [("xw", T.x0, 2048 * i, 2048 * i + 2048) for i in range(2)]
     for i, (name, src, lo, hi) in enumerate(loads):
-        gate = [(loads[i - 2][0], loads[i - 2][2], loads[i - 2][2] + 1)] if i >= 2 and CFG["gate"] else []
-        dma("Y", "ld%d" % i, T[name][:, lo:hi], src[:, lo:hi], gate, [(name, lo, hi)], 4500.0 + 2300.0 * (i == 1) if CFG["gate"] else 4500.0 + 2300.0 * i)
+        w = CFG["flight"]
+        gate = [(loads[i - w][0], loads[i - w][2], loads[i - w][2] + 1)] if i >= w else []
+        dma("Y", "ld%d" % i, T[name][:, lo:hi], src[:, lo:hi], gate, [(name, lo, hi)], 2200.0 + CFG["piece"] * (i + 1) if i < w else CFG["piece"] * w)
 
     iota(B("pI", 0, 1), [[0, 1]], 0, 1)
     iota(B("iw", 0, 256), [[1, 256]], 0, 0)
@@ -356,7 +387,7 @@ def rank_program(g, core, T, topo):
     send(B("zs"), [T.zl[:, 240 * j:240 * j + 240] for j in range(3)], B("zl"), "az", "lz")
     iota(B("E", 0, 16 * SW), [[1, SW], [0, 16]], 0, 0)
     iota(B("bs"), [[4096, 4], [0, 16]], 4096, 0)
-    iota(B("Dm"), [[16, 16]], 0, 0)
+    iota(B("Dm"), [[0, 4], [16, 16]], 0, 0)
     ms(B("base"), BIG)
     for s in range(S):
         iota(B("base", 16 * s, 16 * s + 15), [[4096, 3], [0, 5]], 16384 * (s + 1) + 4096, 0)
@@ -412,12 +443,13 @@ def rank_program(g, core, T, topo):
             ms(B("shp", 4096 * par + 256 * a0, 4096 * par + 256 * a1), 0.0)
     ms(Yv(15, 16), 0.0)
     ms(B("thr", 0, 1), 8.0)
-    ms(B("thr", 1, 2), 12.0)
+    ms(B("thr", 1, 2), 12.0 * BIG)
+    ms(B("gt4", 240, 256), 0.0)
+    act(B("Un"), B("U1"), scale=-BIG)
     ms(B("ones"), 1.0)
     ms(B("cst"), 2048.0)
     ms(B("cneg", 0, 48), -16384.0)
     ms(B("cneg", 48, 96), 0.0)
-    ms(B("cls", 0, 16), -16384.0)
     for i in range(4):
         ts(pi(7 + i), pi(1), i, A.arith_shift_right, 1, A.bitwise_and)
     for i in range(4):
@@ -435,12 +467,14 @@ def rank_program(g, core, T, topo):
     scan(B("wt", 0, 15), B("ge", 0, 15), B("xy", 0, 15), A.mult, A.add)
     ts(B("wt", 16, 31), B("wt", 0, 15), -1.0, A.mult)
     ts(B("Wk"), B("iw", 0, 16), col(1), A.is_equal, 1.0 / 32.0, A.mult)
-    ts(B("ln"), B("Dm"), col(1), A.add)
-    ts(B("Dm"), B("ln"), 4096.0 - 26624.0, A.add)
+    ts(B("ln"), B("Dm", 0, 16), col(1), A.add)
+    ts(B("Dm"), B("Dm"), col(1), A.add, 4096.0 - 26624.0, A.add)
     tt(col(19), col(4), col(5), A.is_equal)
     ts(col(20), col(6), -15.0, A.add)
     ts(B("t8"), B("iw", 0, 8), 2.0, A.mult, col(20), A.add)
     ts(B("w8l"), B("t8"), col(19), A.mult, 15.0, A.add)
+
+    ms(B("cs"), 0.0)
 
     KW = B("kw", 0, V)
     XW = B("xw", 0, V)
@@ -448,10 +482,18 @@ def rank_program(g, core, T, topo):
     def vU(t, s, a0=0, a1=15):
         return B("vU", 80 * t + 16 * s + a0, 80 * t + 16 * s + a1)
 
-    def pairs(dst, o, vals, keys):
+    def spairs(o, vals, keys, upto):
+        for a in range(upto):
+            n = 240 - 16 * a
+            act(B("eqm", o, o + n), B(vals[0], vals[1] + 16 * a, vals[1] + 240), ABS, bias=B(keys[0], keys[1] + a, keys[1] + a + 1))
+            act(B("eqm", o, o + n), B("eqm", o, o + n), RELU, bias=B("wt", a, a + 1), scale=B("wt", 16 + a, 17 + a))
+            o += n
+
+    def pairs(dst, o, vals, keys, since=0):
         for a in range(15):
             n = 240 - 16 * a
-            ts(B(dst, o, o + n), B("val", vals + 16 * a, vals + 240), B(keys[0], keys[1] + a, keys[1] + a + 1), A.is_equal, B("wt", a, a + 1), A.mult)
+            if a >= since:
+                ts(B(dst, o, o + n), B("val", vals + 16 * a, vals + 240), B(keys[0], keys[1] + a, keys[1] + a + 1), A.is_equal, B("wt", a, a + 1), A.mult)
             o += n
 
     for t in range(RACES):
@@ -465,11 +507,16 @@ def rank_program(g, core, T, topo):
     ts(B("k1c"), B("vI"), -2048.0, A.add)
     ts(B("v1h"), B("vI"), -2048.0, A.add)
     for t in range(RACES):
-        act(B("val", 240 * t, 240 * t + 240), IX(B("iw"), vU(t, 0)), bias=-2048.0)
+        act(B("val", 240 * t, 240 * t + 240), IX(B("iw", 0, V), vU(t, 0)), bias=-2048.0)
         pairs("eq1", 1920 * t, 240 * t, ("k1c", 16 * t))
     phase("start0")
     for i in range(4):
         ts(B("kw", 1024 * i, 1024 * i + 1024), B("kin", 1024 * i, 1024 * i + 1024), 32.0, A.mult)
+
+    TEAMS = CFG["teams"]
+
+    def span(tm):
+        return min(GROUPS[gr][0] for gr in TEAMS[tm]), max(GROUPS[gr][1] for gr in TEAMS[tm])
 
     def zh(s, a0=0, a1=15):
         o = (0, 768, 1024, 1280, 256)[s]
@@ -488,18 +535,24 @@ def rank_program(g, core, T, topo):
             o = 4096 * (s % 2) + 256 * a0
             scan(B("zx", 256 * a0, 256 * a1), B("rz", 0, 16 * n), B("shp", o, o + 16 * n), A.min, A.add)
         else:
-            group([(P("pb%d" % gr, 0, 8, p=n), sh(gr, s), B("ih"))])
-            act(B("zT", 128 * gr, 128 * gr + 128, p=n), P("pb%d" % gr, 0, 8, p=n), bias=1024.0, scale=-1.0)
+            pb = P("pb%d" % [tm for tm, team in enumerate(TEAMS) if gr in team][0], 0, 8, p=n)
+            group([(pb, sh(gr, s), B("ih"))])
+            act(B("zT", 128 * gr, 128 * gr + 128, p=n), pb, bias=1024.0, scale=-1.0)
 
     def zinit(t):
         act(zh(0), B("zc", 240 * t, 240 * t + 240), bias=1024.0)
         for gr, (a0, a1, k) in enumerate(GROUPS):
             if k == "V":
                 act(sh(gr, 0), B("zc", 240 * t + 16 * a0, 240 * t + 16 * a1), bias=1024.0)
-            zform(gr, 0)
+            if k == "V" and t and CFG["gzx"]:
+                for c in range(16):
+                    gcp(B("zx", 256 * a0 + c, 256 * a1, 16), B("zc", 240 * t + 16 * a0, 240 * t + 16 * a1), last["G"],
+                        [("zx", 256 * a + c, 256 * a + c + 1) for a in range(a0, a1)])
+            else:
+                zform(gr, 0)
 
     def knew(t, gr, s):
-        a0, a1, k = GROUPS[gr]
+        a0, a1 = span(gr)
         nb, o = (a1 - a0 + 1) // 2, 256 * (s - 1) + 16 * a0
         act(B("kvh", o, o + 16 * (a1 - a0)), IX(KW, vU(t, s - 1, a0, a1)), bias=-2048.0, scale=1.0 / 32.0)
         if (s, gr) in CFG["kv"]:
@@ -509,13 +562,14 @@ def rank_program(g, core, T, topo):
         tb, src = B("Tt", 128 * gr, 128 * gr + 32 * nb), B("kvh", o, o + 32 * nb)
         op("V", lambda e: e.transpose(tb[0], src[0]), tb, [src])
 
-    def score(gr, al, ah):
-        a0, a1, k = GROUPS[gr]
-        pb, w = "pb%d" % gr, 2 * ((a1 - a0 + 1) // 2)
-        if al == a0:
-            group([(P(pb, 0, w), B("idb"), B("kc", 0, 16 * w))], stop=False)
-        end = a0 + w if ah == a1 else ah
-        group([(P(pb, al - a0, end - a0), B("U", 15 - c, 143 - c), Yv(al, end, c)) for c in range(16)], start=False, stop=ah == a1)
+    def score(tm):
+        a0, a1 = span(tm)
+        pb, w = "pb%d" % tm, 2 * ((a1 - a0 + 1) // 2)
+        group([(P(pb, 0, w), B("idb"), B("kc", 0, 16 * w))], stop=False)
+        for gr in TEAMS[tm]:
+            al, ah = GROUPS[gr][:2]
+            end = a0 + w if ah == a1 else ah
+            group([(P(pb, al - a0, end - a0), B("U", 15 - c, 143 - c), Yv(al, end, c)) for c in range(16)], start=False, stop=gr == TEAMS[tm][-1])
 
     chunk = [0]
 
@@ -524,31 +578,25 @@ def rank_program(g, core, T, topo):
         n = 16 * (a1 - a0)
         for a in range(a0, a1, CFG["scols"]):
             e = min(a + CFG["scols"], a1)
-            xg, pa, o = B("xg%d" % (chunk[0] % 3), 0, 256 * (e - a)), P("pa%d" % (chunk[0] % 2), 0, 16 * (e - a)), 256 * (a - a0)
+            xg, pa, o = B("xg%d" % (chunk[0] % 3), 0, 256 * (e - a)), P(CFG["abank"][chunk[0] % len(CFG["abank"])], 0, 16 * (e - a)), 256 * (a - a0)
             chunk[0] += 1
             act(xg, IX(XW, B("kvu", 16 * a, 16 * e)))
             group([(pa, B("zT", 128 * gr, 128 * gr + 128, p=n), B("E", o, o + 256 * (e - a), p=n)), (pa, B("idb"), xg)][::CFG["zfirst"]], (1,))
             act(Yv(a, e), pa, RELU)
-        score(gr, a0, a1)
 
     def xvec(gr):
         a0, a1, k = GROUPS[gr]
         for a in range(a0, a1, CFG["xcols"]):
             e = min(a + CFG["xcols"], a1)
             tt(Yv(a, e), IX(XW, B("kvu", 16 * a, 16 * e)), B("zx", 256 * a, 256 * e), A.max)
-        if a1 - a0 >= 7:
-            score(gr, a0, a0 + 4)
-            score(gr, a0 + 4, a1)
-        else:
-            score(gr, a0, a1)
 
     def pick(t, gr, s):
-        a0, a1, k = GROUPS[gr]
+        a0, a1 = span(gr)
         nb = (a1 - a0 + 1) // 2
         n, o, pb = 32 * nb, 256 * (s - 1) + 16 * a0, "pb%d" % gr
         key, R, D, C = P(pb, 0, 2 * nb), B("R", o, o + n), B("d0", 128 * gr, 128 * gr + n), B("C", o, o + n)
-        scan(R, B("rm", 0, n), key, A.mult, A.max)
-        tt(D, R, key, A.subtract)
+        if gr not in CFG["d1v"]:
+            score(gr)
         pk = CFG["kbank"][gr]
         terms = [(P(pk, 16, 16 + 2 * nb), B("idb"), B("cst", 0, n))]
         for b in range(nb):
@@ -556,60 +604,82 @@ def rank_program(g, core, T, topo):
                 for w in range(2):
                     q = 128 * gr + 32 * b + 16 * w
                     terms.append((P(pk, 16 + 2 * b + h, 17 + 2 * b + h), B("Pm", 128 * (2 * h + w), 128 * (2 * h + w) + 128), B("Tt", q, q + 16)))
-        group(terms + [(P(pk, 16, 16 + 2 * nb), B("idn"), D)], (-1,))
-        scan(C, D, P(pk, 16, 16 + 2 * nb), A.min, A.max)
+        if gr in CFG["d1v"]:
+            group(terms)
+            score(gr)
+        scan(R, B("rm", 0, n), key, A.mult, A.max)
+        tt(D, R, key, A.subtract)
+        if gr in CFG["d1v"]:
+            d1 = B("dd", 128 * gr, 128 * gr + n)
+            tt(d1, P(pk, 16, 16 + 2 * nb), D, A.subtract)
+        else:
+            d1 = P(pk, 16, 16 + 2 * nb)
+            group(terms + [(d1, B("idn"), D)], (-1,))
+        scan(C, D, d1, A.min, A.max)
         cp(vU(t, s, a0, a1), B("C", o + 15, o + 16 * (a1 - a0), 16))
 
     nev = [0]
 
-    def zstep(t, gr, s):
-        a0, a1, k = GROUPS[gr]
-        w, pz, o = a1 - a0, "pb%d" % gr, 256 * (s - 1) + 16 * a0
-        old, new, lst = sh(gr, s - 1), sh(gr, s), IX(XW, vU(t, s, a0, a1))
-        if s == S or gr in CFG["zv"]:
-            tt(B("zt", o, o + 16 * w), lst, old, A.add)
-            ts(new, B("zt", o, o + 16 * w), 0.5, A.mult, 511.75, A.add)
-        else:
-            act(B("xq", o, o + 16 * w), lst)
-            group([(P(pz, 8, 8 + w), B("ih"), old), (P(pz, 8, 8 + w), B("idb"), B("xq", o, o + 16 * w))])
-            act(new, P(pz, 8, 8 + w), bias=511.75, scale=0.5)
+    def zstep(t, tm, s):
+        t0, pz, o = span(tm)[0], "pb%d" % tm, 256 * (s - 1)
+        onv = [gr for gr in TEAMS[tm] if gr in CFG["zv4" if s == S else "zv"]]
+        ons = [gr for gr in TEAMS[tm] if gr not in onv]
+        for gr in onv:
+            a0, a1, k = GROUPS[gr]
+            lst, zt = IX(XW, vU(t, s, a0, a1)), B("zt", o + 16 * a0, o + 16 * a1)
+            tt(zt, lst, sh(gr, s - 1), A.add)
+            ts(sh(gr, s), zt, 0.5, A.mult, 511.75, A.add)
+            if s == S:
+                tt(B("gt4", 16 * a0, 16 * a1), lst, B("zx", 256 * a0, 256 * a1, 16) if k == "V" else B("z3", 16 * a0, 16 * a1), A.is_gt)
+        if ons:
+            b0, b1 = GROUPS[ons[0]][0], GROUPS[ons[-1]][1]
+            xq = B("xq", o + 16 * b0, o + 16 * b1)
+            act(xq, IX(XW, vU(t, s, b0, b1)))
+            group([(P(pz, 8 + b0 - t0, 8 + b1 - t0), B("idb"), xq)] + [(P(pz, 8 + GROUPS[gr][0] - t0, 8 + GROUPS[gr][1] - t0), B("ih"), sh(gr, s - 1)) for gr in ons])
+            if s == S:
+                group([(P(pz, 24 + b0 - t0, 24 + b1 - t0), B("idb"), xq)] + [(P(pz, 24 + GROUPS[gr][0] - t0, 24 + GROUPS[gr][1] - t0), B("ihn"), sh(gr, s - 1)) for gr in ons])
+                act(zh(s, b0, b1), P(pz, 8 + b0 - t0, 8 + b1 - t0), bias=511.75, scale=0.5)
+                act(B("zh", 512 + 16 * b0, 512 + 16 * b1), P(pz, 24 + b0 - t0, 24 + b1 - t0), SIGN, bias=1023.5)
+            for gr in ons * (s < S):
+                act(sh(gr, s), P(pz, 8 + GROUPS[gr][0] - t0, 8 + GROUPS[gr][1] - t0), bias=511.75, scale=0.5)
         if s == S:
-            tt(B("zh", 512 + 16 * a0, 512 + 16 * a1), lst, B("zx", 256 * a0, 256 * a1, 16) if k == "V" else B("z3", 16 * a0, 16 * a1), A.is_gt)
             return
-        zform(gr, s)
-        if k == "V":
-            zc = zh(s, a0, a1)
-            op("G", lambda e: e.affine_select(zc[0], new[0], [[0, 16 * w]], A.is_gt, 0.0, 1, 0), zc, [new], dur=(170, 32 * w, 0, 0, 0))
-        elif s == S - 1:
-            act(B("z3", 16 * a0, 16 * a1), new, bias=-1024.0)
-        for r in CFG["signs"].get(s, ()):
-            o, pa = 256 * (r - 1) + 16 * a0, P(pz, 24, 24 + w)
-            if gr in CFG["zv"]:
-                group([(pa, B("ih"), B("zt", o, o + 16 * w)), (pa, B("ih2"), zh(r - 1, a0, a1))])
-            else:
-                group([(pa, B("idb"), B("xq", o, o + 16 * w)), (pa, B("ihn"), zh(r - 1, a0, a1))])
-            act(B("zh", 1536 + o, 1536 + o + 16 * w), pa, SIGN, bias=1023.5)
+        for gr in TEAMS[tm]:
+            a0, a1, k = GROUPS[gr]
+            zform(gr, s)
+            if k == "V":
+                gcp(zh(s, a0, a1), sh(gr, s))
+            elif s == S - 1 and gr in CFG["zv4"]:
+                act(B("z3", 16 * a0, 16 * a1), sh(gr, s), bias=-1024.0)
+        for gr in onv:
+            a0, a1, k = GROUPS[gr]
+            pa = P(pz, 24 + a0 - t0, 24 + a1 - t0)
+            group([(pa, B("ih"), B("zt", o + 16 * a0, o + 16 * a1)), (pa, B("ih2"), zh(s - 1, a0, a1))])
+        if ons:
+            pa = P(pz, 24 + b0 - t0, 24 + b1 - t0)
+            group([(pa, B("idb"), xq), (pa, B("ihn"), zh(s - 1, b0, b1))])
+        a0, a1 = span(tm)
+        act(B("zh", 1536 + o + 16 * a0, 1536 + o + 16 * a1), P(pz, 24, 24 + a1 - a0), SIGN, bias=1023.5)
 
     def race(t):
         for s in range(1, S + 1):
             now[0], now[1] = t, s
-            for gr in range(len(GROUPS)):
-                phase("k%d" % gr)
-                knew(t, gr, s)
-                phase("x%d" % gr)
-                (xvec if GROUPS[gr][2] == "V" else xact)(gr)
-                phase("p%d" % gr)
-                pick(t, gr, s)
-                phase("z%d" % gr)
-                zstep(t, gr, s)
+            for tm in range(len(TEAMS)):
+                phase("k%d" % tm)
+                knew(t, tm, s)
+                for gr in TEAMS[tm]:
+                    phase("x%d" % gr)
+                    (xvec if GROUPS[gr][2] == "V" else xact)(gr)
+                phase("p%d" % tm)
+                pick(t, tm, s)
+                phase("z%d" % tm)
+                zstep(t, tm, s)
             if s == S - 1:
                 early(t)
         finish(t)
 
     def least(name, rs):
-        for b, (j1, b1, j2, b2) in enumerate(((3, 1, 2, 2), (3, 2, 1, 0), (2, 0, 1, 1))):
-            o1, o2 = rs + 16 * (j1 - 1) + 5 * b1, rs + 16 * (j2 - 1) + 5 * b2
-            tt(B(name, 5 * b, 5 * b + 5), B("rcv", o1, o1 + 5), B("rcv", o2, o2 + 5), A.min)
+        tt(B(name, 0, 15), B("rcv", rs + 5, rs + 20), B("rcv", rs + 25, rs + 40), A.min)
 
     def early(t):
         phase("early")
@@ -625,31 +695,40 @@ def rank_program(g, core, T, topo):
         tt(m3, B("m1"), B("c1", 32, 48), A.min)
         if CFG["early"]:
             rs = 144 + 48 * t
-            send(m3, [T.rcv[:, rs + 16 * j:rs + 16 * j + 16] for j in range(3)], B("rcv", rs, rs + 48), "e%d" % t, "f%d" % t)
+            send(B("m3", 16 * t, 16 * t + 15), [T.rcv[:, rs + 30 - 15 * j:rs + 45 - 15 * j] for j in range(3)], B("rcv", rs, rs + 48), "e%d" % t, "f%d" % t)
             least("x3", rs)
             ts(B("x3", 0, 15), B("x3", 0, 15), BIG, A.is_ge)
         ts(B("op"), m3, BIG, A.is_ge)
-        ts(B("cls", 16, 32), m3, BIG, A.is_lt, 32.0, A.mult)
+        ts(B("cls"), B("op"), B("thr", 1, 2), A.mult)
         tt(B("g0"), m3, B("base", 48, 64), A.min)
         phase("pairs")
         ts(B("kcol", 16, 64), B("C", 15, 768, 16), -2048.0, A.add)
         act(B("v16", 16, 64), B("C", 15, 768, 16), bias=-2048.0)
         for s in (4, 3, 2):
-            act(B("val", 240 * s - 240, 240 * s), IX(B("iw"), vU(t, s - 1)), bias=-2048.0)
-            pairs("eqm", 1920 * (s - 1), 240 * s - 240, ("kcol", 16 * s - 16))
+            act(B("val", 240 * s - 240, 240 * s), IX(B("iw", 0, V), vU(t, s - 1)), bias=-2048.0)
+            n = CFG["spairs"].get(s, 0)
+            if n:
+                act(B("nk", 16 * s - 16, 16 * s), B("C", 256 * s - 512 + 15, 256 * s - 256, 16), bias=2048.0, scale=-1.0)
+            spairs(1920 * (s - 1), ("val", 240 * s - 240), ("nk", 16 * s - 16), n)
+            pairs("eqm", 1920 * (s - 1), 240 * s - 240, ("kcol", 16 * s - 16), n)
 
     def finish(t):
         phase("own")
         own = B("own", 16 * t, 16 * t + 16)
         tt(B("wf"), B("C", 768 + 15, 1024, 16), B("op"), A.mult)
-        group([(P("pc", 8, 10), B("idb"), B("cls"))] + [(P("pc", 8, 10), B("Uh", 15 - c, 143 - c), B("zh", 256 + c, 768, 16)) for c in range(16)], (1,))
-        tt(B("wz", 48, 64), B("wf"), P("pc", 8, 9), A.mult)
-        ts(B("nb", 48, 64), P("pc", 9, 10), B("thr", 1, 2), A.is_lt, BIG, A.mult)
-        ts(B("u4", 48, 64), B("wz", 48, 64), 4095, A.bitwise_and)
-        tt(B("d1", 48, 64), B("nb", 48, 64), B("g0"), A.add)
-        tt(own, B("u4", 48, 64), B("d1", 48, 64), A.add)
+        rk, short = B("rk", 16 * t, 16 * t + 16), P("pc", 9, 10)
+        group([(short, B("idb"), B("cls"))] + [(short, B("Un", 15 - c, 143 - c), B("gt4", c, 256, 16)) for c in range(16)], (1,))
+        tt(rk, short, B("g0"), A.max)
         rs = 48 * t
-        send(own, [T.rcv[:, rs + 16 * j:rs + 16 * j + 16] for j in range(3)], B("rcv", rs, rs + 48), "a%d" % t, "l%d" % t)
+        send(B("rk", 16 * t, 16 * t + 15), [T.rcv[:, rs + 30 - 15 * j:rs + 45 - 15 * j] for j in range(3)], B("rcv", rs, rs + 48), "a%d" % t, "l%d" % t)
+        phase("ownu")
+        ts(B("nb", 48, 64), short, 0.0, A.is_gt, 16 * BIG, A.mult)
+        group([(P("pz", 8, 9), B("idb"), B("cneg", 0, 16))] + [(P("pz", 8, 9), B("Uh", 15 - c, 143 - c), B("zh", 256 + c, 512, 16)) for c in range(16)], (1,))
+        tt(B("wz", 48, 64), B("wf"), P("pz", 8, 9), A.mult)
+        ts(B("u4", 48, 64), B("wz", 48, 64), 4095, A.bitwise_and)
+        tt(own, B("u4", 48, 64), rk, A.add)
+        ru = 288 + 48 * t
+        send(B("own", 16 * t, 16 * t + 15), [T.rcv[:, ru + 30 - 15 * j:ru + 45 - 15 * j] for j in range(3)], B("rcv", ru, ru + 48), "u%d" % t, "w%d" % t)
         phase("logs")
         tt(B("w1"), B("C", 15, 1024, 16), B("bs"), A.add)
         tt(B("w1"), B("w1"), B("nb"), A.add)
@@ -670,13 +749,8 @@ def rank_program(g, core, T, topo):
         for s in range(S, 0, -1):
             act(B("Bs", 240 * s - 240, 240 * s), IX(B("Wk"), B("kU", 16 * s - 16, 16 * s - 1)))
         phase("wpairs")
-        act(B("valf"), IX(B("iw"), B("WU", 0, 15)))
-        o = 0
-        for a in range(15):
-            n = 240 - 16 * a
-            act(B("eqm", o, o + n), B("valf", 16 * a, 240), ABS, bias=B("nW", a, a + 1))
-            act(B("eqm", o, o + n), B("eqm", o, o + n), RELU, bias=B("wt", a, a + 1), scale=B("wt", 16 + a, 17 + a))
-            o += n
+        act(B("valf"), IX(B("iw", 0, V), B("WU", 0, 15)))
+        spairs(0, ("valf", 0), ("nW", 0), 15)
         phase("cm")
         tt(B("cm"), IX(KW, vU(t, S - 1)), B("Bs", 720, 960), A.mult)
         phase("xnew")
@@ -693,8 +767,8 @@ def rank_program(g, core, T, topo):
 
         phase("own4")
         x, ow, ow2 = B("x", 0, 15), B("ow1", 0, 15), B("ow2", 0, 15)
-        ts(ow, B("own", 16 * t, 16 * t + 15), BIG, A.min)
-        tt(ow2, B("own", 16 * t, 16 * t + 15), B("nb", 48, 63), A.add)
+        ts(ow, B("rk", 16 * t, 16 * t + 15), BIG, A.min)
+        tt(ow2, B("rk", 16 * t, 16 * t + 15), B("nb", 48, 63), A.add)
         if CFG["early"]:
             tt(B("ow4", 0, 15), ow, B("x3", 0, 15), A.mult)
             act(B("owE"), IX(B("ow4"), B("w8l")))
@@ -709,7 +783,9 @@ def rank_program(g, core, T, topo):
         else:
             ts(B("ge", 0, 15), x, 16384.0 * S, A.is_ge)
             tt(on(3), on(0), B("ge", 0, 15), A.mult)
-        ts(B("uI", 0, 15), x, 4095, A.bitwise_and)
+        phase("winu")
+        least("xu", ru)
+        ts(B("uI", 0, 15), B("xu", 0, 15), 4095, A.bitwise_and)
         cp(B("uU", 0, 15), B("uI", 0, 15))
         phase("win2")
         tt(B("xy", 0, 15), x, on(0), A.mult)
@@ -717,7 +793,7 @@ def rank_program(g, core, T, topo):
             ts(on(s - 1), B("xy", 0, 15), 16384.0 * s, A.is_ge)
         tt(on(4), ow2, x, A.is_lt)
         phase("xs")
-        act(B("urep"), IX(B("iw"), B("uU", 0, 15)), bias=-2048.0)
+        act(B("urep"), IX(B("iw", 0, V), B("uU", 0, 15)), bias=-2048.0)
         for s in (3, 2, 1):
             pa = P("pa%d" % (s % 2), 0, 15)
             group([(pa, B("idM"), B("Bs", 240 * s - 240, 240 * s)), (pa, B("ihd"), B("urep"))], (1,))
@@ -741,37 +817,48 @@ def rank_program(g, core, T, topo):
                 terms.append((P(p1, a, 15, p=8), B("W8", o + 8 * a, o + 8 * a + 8), B(src, r, r + n)))
                 r += n
             group(terms, (1,))
-            q = 256 * (nev[0] % 2)
-            act(B("cs", q, q + 240, p=8), P(p1, 0, 15, p=8), SIGN)
-            out = P("pb2", 0, 1, c=15)
-            vh = B("v1h", 16 * t, 16 * t + 15) if e == 0 else B("v16", 16 * (e % 4), 16 * (e % 4) + 15)
-            group([(out, B("ih"), vh), (out, B("idB"), on(e))] + [(out, B("Us", 15 - c, 143 - c, p=8), B("cs", q + c, q + 240, 16, p=8)) for c in range(16)], (2,))
-            tt(B("of", 16 * e, 16 * e + 15), out, B("Dm", 0, 15), A.min)
-            ts(B("offU", 16 * e, 16 * e + 15), B("of", 16 * e, 16 * e + 15), 26624.0, A.add)
+            act(B("cs", 256 * slot[e], 256 * slot[e] + 240, p=8), P(p1, 0, 15, p=8), SIGN)
+
+        slot = {e: i for i, e in enumerate(e for batch in CFG["batches"] for e in batch)}
+        for batch in CFG["batches"]:
+            for e in batch:
+                event(e)
+            phase("of%d" % batch[0])
+            n, q = len(batch), slot[batch[0]]
+            out = P("pb2", 0, n, c=15)
+            terms = [(out, B("idb"), B("cneg", 48, 47 + 16 * n))] * (n > 1)
+            for i, e in enumerate(batch):
+                vh = B("v1h", 16 * t, 16 * t + 15) if e == 0 else B("v16", 16 * (e % 4), 16 * (e % 4) + 15)
+                terms += [(P("pb2", i, i + 1, c=15), B("ih"), vh), (P("pb2", i, i + 1, c=15), B("idB"), on(e))]
+            group(terms + [(out, B("Us", 15 - c, 143 - c, p=8), B("cs", 256 * q + c, 256 * (q + n) - 16, 16, p=8)) for c in range(16)], (len(terms),))
+            tt(B("of", 16 * q, 16 * (q + n) - 1), out, B("Dm", 0, 16 * n - 1), A.min)
+            ts(B("offU", 16 * q, 16 * (q + n) - 1), B("of", 16 * q, 16 * (q + n) - 1), 26624.0, A.add)
+
+        def write(win, src, e):
+            for a0, a1 in CFG["xparts"] if e == 4 else ((0, 15),):
+                cp(IX(B(win), B("offU", 16 * slot[e] + a0, 16 * slot[e] + a1)), B(src, 16 * a0, 16 * a1))
 
         for s in range(S, 0, -1):
-            event(s - 1)
             phase("st%d" % s)
             r = 240 * s - 240
-            parts = ((0, 8, "pz"), (8, 15, "pb3")) if CFG["halves"] and s < S else ((0, 15, "pb3" if s % 2 else "pz"),)
-            for a0, a1, bank in parts:
+            for a0, a1, bank in ((8, 15, "pb3"), (0, 8, "pz")):
                 lo, hi, pz = 16 * a0, 16 * a1, P(bank, a0, a1)
                 lst = IX(KW, vU(t, s - 1, a0, a1))
-                kt = B("kvh", 768, 1008) if s == S else B("kt", lo, hi)
+                kt = B("kvh", 768 + lo, 768 + hi) if s == S else B("kt", lo, hi)
                 group([(pz, B("ih32"), B("m2k", lo, hi)), (pz, B("idS", 128 * s - 128, 128 * s), B("Bs", r + lo, r + hi))], stop=False)
                 if s < S:
-                    act(kt, lst, bias=-2048.0, scale=1.0 / 32.0)
+                    if a0 == 0 and s in CFG["ktv"]:
+                        ts(kt, lst, 1.0 / 32.0, A.mult, -2048.0, A.add)
+                    else:
+                        act(kt, lst, bias=-2048.0, scale=1.0 / 32.0)
                     tt(B("kp", lo, hi), lst, B("xs", r + lo, r + hi), A.mult)
                 else:
-                    tt(B("kp"), IX(B("iw"), B("uU", 0, 15)), B("cm"), A.mult)
+                    tt(B("kp", lo, hi), IX(B("iw"), B("uU", a0, a1)), B("cm", lo, hi), A.mult)
                 group([(pz, B("ih32"), kt)], start=False)
                 tt(B("kz", lo, hi), B("kp", lo, hi), pz, A.add)
                 ts(B("kn", lo, hi), B("kz", lo, hi), 131040, A.bitwise_and)
-            cp(IX(B("kw"), B("offU", 16 * s - 16, 16 * s - 1)), B("kn"))
-            if s == CFG["wpos"]:
-                event(4)
-                for a0, a1 in CFG["xparts"]:
-                    cp(IX(B("xw"), B("offU", 64 + a0, 64 + a1)), B("xn", 16 * a0, 16 * a1))
+            write("kw", "kn", s - 1)
+        write("xw", "xn", 4)
         if t + 1 < RACES:
             phase("thr")
             group([(P("pc", 12, 13, c=15), B("ones"), on(4))])
@@ -779,7 +866,7 @@ def rank_program(g, core, T, topo):
             cp(B("totI"), B("tot"))
             ts(B("totI"), B("totI"), 1, A.bitwise_and)
             ts(B("thr", 0, 1), B("totI"), 2.0, A.mult, 8.0, A.add)
-            ts(B("thr", 1, 2), B("totI"), 12.0, A.add)
+            ts(B("thr", 1, 2), B("totI"), 12.0, A.add, BIG, A.mult)
 
     phase("start1")
     ms(B("m2k"), -2048.0)
@@ -796,11 +883,11 @@ def rank_program(g, core, T, topo):
         for a in range(8):
             o = 512 * a + 256 * h
             if a % 2:
-                act(B("kh", o, o + 256), B("kw", o, o + 256), bias=-2048.0, scale=1.0 / 32.0)
+                act(B("shp", o, o + 256), B("kw", o, o + 256), bias=-2048.0, scale=1.0 / 32.0)
             else:
-                ts(B("kh", o, o + 256), B("kw", o, o + 256), 1.0 / 32.0, A.mult, -2048.0, A.add)
+                ts(B("shp", o, o + 256), B("kw", o, o + 256), 1.0 / 32.0, A.mult, -2048.0, A.add)
         pb = P("pb%d" % h, 0, 16)
-        group([(pb, B("idk", 128 * a, 128 * a + 128), B("kh", 512 * a + 256 * h, 512 * a + 256 * h + 256)) for a in range(8)], (2, 4, 6))
+        group([(pb, B("idk", 128 * a, 128 * a + 128), B("shp", 512 * a + 256 * h, 512 * a + 256 * h + 256)) for a in range(8)], (2, 4, 6))
         if h:
             ts(B("ok", 256, 512), pb, 36.0 * 2048.0, A.add)
         else:
@@ -811,5 +898,5 @@ def rank_program(g, core, T, topo):
         g.sync.wait_ge(T.sem[sem], 16)
     for q in "VSTG":
         g.wait_ge(T.sem["q" + q], cnt[q])
-    for l in ("lz", "lv", "l0", "l1", "l2") + ("f0", "f1", "f2") * CFG["early"]:
+    for l in ("lz", "lv", "l0", "l1", "l2", "w0", "w1", "w2") + ("f0", "f1", "f2") * CFG["early"]:
         g.wait_ge(T.sem[l], ne)

@@ -9,35 +9,40 @@ SIGN = ActivationFunctionType.Sign
 N, M, J, RACES, S, V = 4, 80, 3, 3, 4, 4096
 L = J * M
 WIN = V + 256
+X0, K0 = 128, 128 + V
 BIG = 2.0 ** 19
 CFG = {
     "groups": ((0, 4, "V"), (4, 8, "S"), (8, 12, "V"), (12, 15, "S")),
-    "xcols": 1,
-    "kbank": ("pb3", "pz", "pc"), "inorder": False, "d1v": (), "flight": 2, "first": 7000.0, "piece": 2300.0, "ktv": (1, 2, 3), "abank": ("pa0", "pa1"), "batches": ((3,), (2,), (1, 4), (0,)), "spairs": {}, "gzx": True, "teams": ((0, 1), (2,), (3,)), "zv4": (0, 1, 2, 3), "cbank": "pz", "early": True, "xparts": ((0, 8), (8, 15)),
-    "zv": (0, 2), "kv": ((1, 0), (1, 1)), "w8v": (3,), "wpos": 3, "run": 512.0, "zfirst": -1,
-    "bias": {}, "rounds": 5000, "rounds2": 60, "lead": 13000.0, "heat": 150.0, "swap": 0.5, "tries": 1, "rounds0": 0, "fb": 2, "parts": 0.3, "scols": 2, "seed": 3, "span": 4000.0, "shake": 1500.0,
-    "cyc": 1.0, "lat": 240.0, "gam": 1.75, "sig": 4.3, "pe": 0.52, "rem": 0.9,
-    "others": ({"weight": 1.2, "cyc": 0.85, "lat": 210.0, "gam": 1.5, "sig": 3.5, "pe": 0.45, "rem": 1.2}, {"weight": 0.8, "cyc": 1.22, "lat": 280.0, "gam": 1.9, "sig": 5.0, "pe": 0.62, "rem": 0.7}),
+    "polish": (6000, 12000, 20000, 8000, 18000, 38000, 8000), "period": 7400.0, "heatc": 1500.0, "alap": 1200.0, "spare": 1, "binds": 12, "heat5": 500.0, "tries": (10, 1), "heat0": 1200.0, "heat4": 1000.0, "since": 0.0, "heat1": 150.0, "turns": 10, "heat2": 500.0, "heat3": 400.0, "any": 0.05, "far": 12, "hope": 30.0,
+    "zbank": ("pb3", "pb3", "pb3"), "tbank": ("pc", "pc", "pc"), "sbank": ("pb3", "pb3", "pb3"),
+    "eqs": 0, "vparts": {}, "onS": ("kU4", "WU", "v16", "nW", "kcol", "uU", "cI4"), "quad": True, "khs": (), "ksc": (3,), "kload": ((0, 1024), (1024, 2560), (2560, 4096)), "xload": ((0, 2048), (2048, 4096)), "jbatches": ((3,), (2,), (1,), (0, 4)), "wV": 5, "apart": (), "kparts": ((10, 15, 0), (4, 10, 0), (0, 4, 1)), "half": (), "w0": 0, "kvv": (), "ke": 3, "xh": (), "gsp": 0, "wS": 6, "z4s": (0,),
+    "kbank": ("pb0", "pz", "pb2"), "inorder": False, "d1v": (), "flight": 2, "first": 7000.0, "piece": 2300.0, "ktv": (1, 2, 3), "abank": ("pa0", "pa1"), "batches": ((3,), (2,), (1, 4), (0,)), "spairs": {2: 11}, "gzx": True, "teams": ((0, 1), (2,), (3,)), "zv4": (0, 1, 2, 3), "cbank": "pc", "cbank2": "pc", "push": 2500.0, "early": True, "xparts": ((0, 4), (4, 8), (8, 12), (12, 15)),
+    "zv": (0, 2), "kv": ((1, 1), (2, 1), (3, 1)), "w8v": (3,), "wpos": 3, "run": 512.0, "zfirst": (1, 1), "dif": (0, 1, 2),
+    "bias": {}, "rounds": 60, "rounds2": 5, "lead": 13000.0, "heat": 150.0, "swap": 0.5, "rounds0": 0, "fb": 2, "parts": 0.3, "scols": 2, "seed": 52, "span": 4000.0, "shake": 1500.0,
+    "cyc": 1.05, "lat": 220.0, "gam": 1.85, "sig": 4.3, "pe": 0.52, "rem": 0.9,
+    "others": ({"weight": 1.1, "cyc": 0.85, "lat": 200.0, "gam": 1.5, "sig": 3.5, "pe": 0.45, "rem": 1.2},
+               {"weight": 0.6, "cyc": 1.22, "lat": 270.0, "gam": 1.7, "sig": 5.4, "pe": 0.62, "rem": 0.8},
+               {"weight": 1.1, "cyc": 1.24, "lat": 190.0, "gam": 2.05, "sig": 4.0, "pe": 0.58, "rem": 1.5}),
 }
 PLAN = {}
 
 SCRATCH = {}
 PIECE = {}
 for _d, _l in (
-        ("bfloat16", (("xw", WIN), ("zx", 4096), ("xq", 1024), ("d0", 512), ("zT", 512), ("E", 1536), ("xg0", 512), ("xg1", 512), ("xg2", 512),
-                      ("zg", 1024), ("zs", 240), ("zl", 720), ("zc", 720), ("on", 80), ("eq1", 5760), ("eqm", 7680), ("W8", 640), ("cs", 1280),
-                      ("Bs", 960), ("xW", 240), ("zW", 240), ("xn", 240), ("idb", 128), ("idn", 128), ("idB", 128), ("idM", 128), ("idS", 512),
-                      ("U", 144), ("U1", 144), ("Us", 144), ("kc", 128), ("rm", 256), ("rz", 1280), ("cst", 256), ("cneg", 96), ("cls", 16), ("gt4", 256), ("Un", 144), ("z3", 256), ("Wk", 16),
+        ("bfloat16", (("xw", WIN), ("zx", 4096), ("xq", 1024), ("d0", 512), ("E", 2048), ("csu", 128), ("xg0", 512), ("xg1", 512), ("xg2", 512),
+                      ("zs", 240), ("zl", 720), ("zc", 720), ("on", 80), ("eq1", 5760), ("eqm", 7680), ("W8", 640), ("cs", 1280),
+                      ("Bs", 960), ("xW", 240), ("xn", 240), ("idb", 128), ("idn", 128), ("idB", 128), ("idM", 128), ("idX", 128), ("idS", 512),
+                      ("U", 144), ("U1", 144), ("Us", 144), ("kc", 128), ("rm", 256), ("rz", 256), ("cst", 128), ("cneg", 128), ("cls", 64), ("gt4", 256), ("Un", 144), ("z3", 256), ("Wk", 32),
                       ("thw", 240), ("idx", 1024), ("ones", 128))),
-        ("float16", (("kvh", 1024), ("Tt", 512), ("shp", 8192), ("zh", 2304), ("ih2", 128), ("Pm", 512), ("ih", 128), ("ihn", 128), ("ih32", 128), ("ihd", 128),
-                     ("Uh", 144), ("val", 960), ("v16", 80), ("v1h", 48), ("urep", 240), ("kt", 240), ("m2k", 240), ("zt", 1024), ("xr", 240), ("idk", 1024))),
-        ("float32", (("kw", WIN), ("iw", V), ("R", 1024), ("C", 1024), ("nb", 64), ("kcol", 64), ("nk", 64), ("k1c", 48), ("nW", 16), ("valf", 240),
+        ("float16", (("shp", 4096), ("zh", 2304), ("ih2", 128), ("Dif", 16), ("ih", 128), ("ihn", 128), ("ih32", 128), ("ihd", 128),
+                     ("Uh", 144), ("zT", 768), ("En", 2048), ("zW", 240), ("toth", 1), ("val", 1680), ("v16", 80), ("v1h", 48), ("urep", 240), ("kt", 240), ("m2k", 480), ("zt", 1024), ("xr", 240), ("idk", 1024))),
+        ("float32", (("kw", K0 + WIN), ("iw", V), ("R", 1024), ("C", 1024), ("nb", 64), ("kcol", 64), ("nk", 64), ("k1c", 48), ("nW", 16), ("valf", 240),
                      ("xs", 960), ("kp", 240), ("of", 80), ("Dm", 64), ("base", 64), ("bs", 64), ("ln", 16), ("bF", 16), ("ge", 16), ("xy", 16),
-                     ("d1", 64), ("w1", 64), ("tot", 1), ("thr", 2), ("wt", 32), ("cm", 240), ("x3", 16), ("op", 16), ("g0", 16), ("wf", 16), ("ow1", 16), ("ow2", 16), ("ow4", 16), ("owE", 128), ("dd", 512), ("pF", 24), ("ox", 512), ("ok", 512), ("t8", 8))),
-        ("int32", (("kin", V), ("vs", 45), ("vl", 135), ("vI", 48), ("wz", 64), ("u4", 64), ("c1", 64), ("m1", 16), ("m3", 48), ("own", 48),
+                     ("d1", 64), ("w1", 64), ("tot", 16), ("zg", 1040), ("DJ", 16), ("v1K", 48), ("WF", 16), ("kF", 16), ("nw", 16), ("b4", 16), ("p4", 16), ("thr", 2), ("wt", 32), ("cm", 240), ("x3", 16), ("op", 16), ("op2", 16), ("g0", 16), ("wf", 16), ("ow1", 16), ("ow2", 16), ("ow4", 16), ("owE", 128), ("pF", 24), ("ox", 512), ("ok", 512), ("t8", 8))),
+        ("int32", (("kin", V), ("vs", 45), ("vl", 135), ("vI", 48), ("wz", 64), ("u4", 64), ("m1", 32), ("m3", 96), ("fl", 48), ("own", 48),
                    ("rcv", 432), ("rk", 48), ("xu", 16), ("x", 16), ("uI", 16), ("dI", 16), ("WI", 16), ("bI", 16), ("cI", 64), ("kI", 64), ("kz", 240), ("kn", 240),
-                   ("totI", 1), ("pI", 12))),
-        ("uint16", (("kvu", 256), ("vU", 240), ("kU", 64), ("WU", 16), ("bU", 16), ("uU", 16), ("offU", 80), ("w8l", 8)))):
+                   ("nI", 32), ("pI", 12))),
+        ("uint16", (("kvu", 256), ("vU", 240), ("kU", 64), ("WU", 16), ("bU", 16), ("uU", 16), ("nU", 16), ("XU", 16), ("GU", 16), ("offU", 80), ("w8l", 8)))):
     for _n, _w in _l:
         if _d == "float32" and _w <= 64:
             PIECE[_n] = ("small", 64 * len(PIECE), _w)
@@ -45,13 +50,18 @@ for _d, _l in (
             SCRATCH[_n] = ("sbuf", [128, _w], _d)
 SCRATCH["small"] = ("sbuf", [128, 64 * len(PIECE)], "float32")
 SCRATCH["Y"] = ("sbuf", [128, 16, 256], "bfloat16")
-for _n in ("pb0", "pb1", "pb2", "pb3", "pa0", "pa1", "pz", "pc"):
+BANKS = ["ps%d" % _n for _n in range(8)]
+for _n in BANKS:
     SCRATCH[_n] = ("psum", [128, 512], "float32")
+SCRATCH["zy"] = ("sbuf", [128, 256, 16], "bfloat16")
+SCRATCH["cw"] = ("sbuf", [128, 3, 32], "float32")
+SCRATCH["Ys"] = ("sbuf", [128, 256, 16], "bfloat16")
+SCRATCH["kE"] = ("sbuf", [128, 16, 32], "float16")
 SEMAPHORES = ["qV", "qS", "qT", "qG", "zin", "vin", "ld0", "ld1", "ld2", "ld3", "ld4", "ld5", "az", "av", "a0", "a1", "a2",
               "lz", "lv", "l0", "l1", "l2", "oy", "ok0", "ok1", "e0", "e1", "e2", "f0", "f1", "f2", "u0", "u1", "u2", "w0", "w1", "w2"]
 
 
-def planner(g, T):
+def planner(g, T, late_bound):
     queues = {"V": g.vector, "S": g.scalar, "T": g.tensor, "G": g, "Y": g.sync}
     ops = []
     plan = {}
@@ -61,7 +71,7 @@ def planner(g, T):
         return p[0] + m["cyc"] * (p[1] + m["gam"] * p[2] + m["sig"] * p[3]) + m["pe"] * p[4] + m["rem"] * sum(p[5:])
 
     def is_psum(b):
-        return b in SCRATCH and SCRATCH[b][0] == "psum"
+        return b[0] == "@"
 
     def hazards(recs, q, R, W):
         out = []
@@ -97,7 +107,7 @@ def planner(g, T):
             deps[after] = 0
         note(plan, rq, R, W, i)
         bias[2] += 1
-        ops.append({"id": (bias[1][0], bias[1][1], bias[2]), "q": q, "kind": kind, "fn": fn, "dur": dur, "parts": parts, "sem": sem, "val": val, "lat": lat, "deps": deps, "after": after, "bias": bias[0], "txt": (W[0][0] if W else kind)})
+        ops.append({"id": (bias[1][0], bias[1][1], bias[2]), "q": q, "kind": kind, "fn": fn, "dur": dur, "parts": parts, "sem": sem, "val": val, "lat": lat, "deps": deps, "uses": {b for b, lo, hi in list(R) + list(W) if is_psum(b)}, "txt": (W[0][0] if W else kind)})
         return i
 
     def emit():
@@ -110,6 +120,10 @@ def planner(g, T):
         prio = [0.0] * n
         for i in range(n - 1, -1, -1):
             prio[i] = ops[i]["dur"] + max([x + prio[k] for k, x in succ[i]] + [0.0])
+        push = [CFG["push"] if o["txt"] == "xw" and o["id"][0] >= 0 else 0.0 for o in ops]
+        near = [0.0] * n
+        for i in range(n - 1, -1, -1):
+            near[i] = ops[i]["dur"] + max([x + near[k] for k, x in succ[i] if ops[k]["id"][0] == ops[i]["id"][0]] + [push[i]])
         pred = [list(o["deps"].items()) for o in ops]
         dur = [o["dur"] for o in ops]
         others = [(m["weight"], m["lat"], [cost(o["parts"], m) for o in ops]) for m in CFG["others"]]
@@ -202,6 +216,463 @@ def planner(g, T):
                     late, end = place(sorted(part, key=lambda i: (-start[i] - dur[i], -i)), back)
                     key = {i: -late[i] - dur[i] for i in part}
             return top
+        models = [(CFG["w0"], CFG["lat"], dur)] * (CFG["w0"] > 0) + others
+
+        def polish(seq, rounds, heat, after=None, since=0.0, until=1.0):
+            loc = {i: k for k, i in enumerate(seq)}
+            m, nm = len(seq), len(models)
+            above, ps = [0] * m, []
+            for k, i in enumerate(seq):
+                d0 = [(loc[d], x) for d, x in pred[i] if d in loc]
+                ps.append([(d, x) for d, x in d0 if x not in (0, CFG["lat"]) or not any(above[e] >> d & 1 for e, y in d0)])
+                for d, x in d0:
+                    above[k] |= above[d] | 1 << d
+            ss = [[] for _ in seq]
+            for k in range(m):
+                for d, x in ps[k]:
+                    ss[d].append((k, x))
+            du = [[o[i] for i in seq] for w, lat, o in models]
+            pm = [[[(d, du[j][d] + (models[j][1] if x == CFG["lat"] else x)) for d, x in ps[k]] for k in range(m)] for j in range(nm)]
+            sm = [[[(d, models[j][1] if x == CFG["lat"] else x) for d, x in ss[k]] for k in range(m)] for j in range(nm)]
+            pd, sd = [[d for d, x in e] for e in ps], [[d for d, x in e] for e in ss]
+            qu = [queue[i] for i in seq]
+            ex = [[after(j, i) if after else 0.0 for i in seq] for j in range(nm)]
+            wt = [w for w, lat, o in models]
+            order, pos = list(range(m)), list(range(m))
+            mp, mn, free = [-1] * m, [-1] * m, {}
+            for k in order:
+                if qu[k] != "N":
+                    if qu[k] in free:
+                        mp[k], mn[free[qu[k]]] = free[qu[k]], k
+                    free[qu[k]] = k
+            hd, tl = [[0.0] * m for _ in models], [[0.0] * m for _ in models]
+
+            def heads(run, j, h):
+                d, p = du[j], pm[j]
+                for k in run:
+                    e = mp[k]
+                    t = h[e] + d[e] if e >= 0 else 0.0
+                    for e, x in p[k]:
+                        if h[e] + x > t:
+                            t = h[e] + x
+                    h[k] = t
+
+            def tails(run, j, h):
+                d, p, q = du[j], sm[j], ex[j]
+                for k in run:
+                    e = mn[k]
+                    t = q[k]
+                    if e >= 0 and h[e] > t:
+                        t = h[e]
+                    for e, x in p[k]:
+                        if h[e] + x > t:
+                            t = h[e] + x
+                    h[k] = t + d[k]
+
+            def link(run):
+                for x, y in zip(run, run[1:]):
+                    if x >= 0:
+                        mn[x] = y
+                    if y >= 0:
+                        mp[y] = x
+
+            def tight(j):
+                h, g, top = hd[j], tl[j], cur[j] - 1e-3
+                return [k for k in range(m) if h[k] + g[k] > top and since * top <= h[k] <= until * top and mp[k] >= 0 and h[mp[k]] + du[j][mp[k]] > h[k] - 1e-3 and h[mp[k]] + g[mp[k]] > top]
+            for j in range(nm):
+                heads(order, j, hd[j])
+                tails(order[::-1], j, tl[j])
+            cur = [max(a + b for a, b in zip(hd[j], tl[j])) for j in range(nm)]
+            crit = [tight(j) for j in range(nm)]
+            best = (sum(w * c for w, c in zip(wt, cur)), list(order), list(cur))
+            for r in range(rounds):
+                j = int(draw() * nm)
+                c = crit[j] = crit[j] or tight(j)
+                if not c or draw() < CFG["any"]:
+                    v = order[int((since + draw() * (until - since)) * m)]
+                    if mp[v] < 0:
+                        continue
+                else:
+                    v = c[int(draw() * len(c))]
+                u, far = mp[v], int(draw() ** 3 * CFG["far"])
+                if draw() < 0.5:
+                    while far and mp[u] >= 0:
+                        u, far = mp[u], far - 1
+                    win, mark, q = order[pos[u]:pos[v] + 1], {v}, qu[v]
+                    for k in win[-2::-1]:
+                        if (mn[k] in mark and qu[k] != q) or not mark.isdisjoint(sd[k]):
+                            mark.add(k)
+                    if u in mark:
+                        continue
+                    new = [k for k in win if k in mark] + [k for k in win if k not in mark]
+                else:
+                    while far and mn[v] >= 0:
+                        v, far = mn[v], far - 1
+                    win, mark, q = order[pos[u]:pos[v] + 1], {u}, qu[v]
+                    for k in win[1:]:
+                        if (mp[k] in mark and qu[k] != q) or not mark.isdisjoint(pd[k]):
+                            mark.add(k)
+                    if v in mark:
+                        continue
+                    new = [k for k in win if k not in mark] + [k for k in win if k in mark]
+                a, b = mp[u], mn[v]
+                link([a] + [k for k in new if qu[k] == q] + [b])
+                keep, gain, room = [], 0.0, heat * (1.0 - r / rounds) * draw() ** 2
+                for j in range(nm):
+                    h, g = hd[j], tl[j]
+                    keep.append(([h[k] for k in new], [g[k] for k in new]))
+                    heads(new, j, h)
+                    tails(new[::-1], j, g)
+                    e = max(h[k] + g[k] for k in new) - cur[j]
+                    gain += wt[j] * (e if e > 0 else max(e, -CFG["hope"]) * 0.5)
+                if gain > room:
+                    for j in range(nm):
+                        for k, x, y in zip(new, *keep[j]):
+                            hd[j][k], tl[j][k] = x, y
+                    link([a] + [k for k in win if qu[k] == q] + [b])
+                    continue
+                p0 = pos[win[0]]
+                order[p0:p0 + len(new)] = new
+                for k, i in enumerate(new):
+                    pos[i] = p0 + k
+                hi = max([pos[e] for k in new for e in sd[k]] + [pos[mn[k]] for k in new if mn[k] >= 0] + [0])
+                lo = min([pos[e] for k in new for e in pd[k]] + [pos[mp[k]] for k in new if mp[k] >= 0] + [m])
+                for j in range(nm):
+                    h, d, p, far, i = hd[j], du[j], pm[j], hi, p0 + len(new)
+                    while i <= far:
+                        k = order[i]
+                        i += 1
+                        e = mp[k]
+                        t = h[e] + d[e] if e >= 0 else 0.0
+                        for e, x in p[k]:
+                            if h[e] + x > t:
+                                t = h[e] + x
+                        if t != h[k]:
+                            h[k] = t
+                            e = mn[k]
+                            if e >= 0 and pos[e] > far:
+                                far = pos[e]
+                            for e in sd[k]:
+                                if pos[e] > far:
+                                    far = pos[e]
+                    h, p, q, far, i = tl[j], sm[j], ex[j], lo, p0 - 1
+                    while i >= far:
+                        k = order[i]
+                        i -= 1
+                        e = mn[k]
+                        t = q[k]
+                        if e >= 0 and h[e] > t:
+                            t = h[e]
+                        for e, x in p[k]:
+                            if h[e] + x > t:
+                                t = h[e] + x
+                        t += d[k]
+                        if t != h[k]:
+                            h[k] = t
+                            e = mp[k]
+                            if e >= 0 and pos[e] < far:
+                                far = pos[e]
+                            for e in pd[k]:
+                                if pos[e] < far:
+                                    far = pos[e]
+                    cur[j] = max(h)
+                crit = [None] * nm
+                e = sum(w * c for w, c in zip(wt, cur))
+                if e < best[0]:
+                    best = (e, list(order), list(cur))
+            return [seq[k] for k in best[1]], best[2]
+
+        def times(seq, j):
+            w, lat, o = models[j] if j >= 0 else (1.0, CFG["lat"], dur)
+            start, free = {}, {}
+            for i in seq:
+                t = free.get(queue[i], 0.0) if queue[i] != "N" else 0.0
+                for d, x in pred[i]:
+                    if d in start:
+                        t = max(t, start[d] + o[d] + (lat if x == CFG["lat"] else x))
+                start[i] = t
+                free[queue[i]] = t + o[i]
+            return start, max(start[i] + o[i] for i in seq)
+
+        def cyclic(seq, rounds, heat, after=None):
+            loc = {i: k for k, i in enumerate(seq)}
+            m, nm = len(seq), len(models)
+            start = times(seq, -1)[0]
+            step = [ops[i]["id"][1][0] for i in seq]
+            names = [(ops[i]["id"][1][1], ops[i]["id"][2], ops[i]["id"][1][1][0] == "z" and s == S) for i, s in zip(seq, step)]
+            kinds = {x: k for k, x in enumerate(sorted(set(names)))}
+            kind, per = [kinds[x] for x in names], CFG["period"]
+            ph = [0.0] * len(kinds)
+            for s in (4, 1, 3, 2):
+                for k, i in enumerate(seq):
+                    if step[k] == s:
+                        ph[kind[k]] = start[i] - per * s + 1e-3 * k
+            ps = [[(loc[d], x) for d, x in pred[i] if d in loc] for i in seq]
+            du = [[o[i] for i in seq] for w, lat, o in models]
+            pm = [[[(d, du[j][d] + (models[j][1] if x == CFG["lat"] else x)) for d, x in ps[k]] for k in range(m)] for j in range(nm)]
+            ex = [[du[j][k] + (after(j, i) if after else 0.0) for k, i in enumerate(seq)] for j in range(nm)]
+            arcs = sorted({(kind[d], kind[k], per * (step[k] - step[d])) for k in range(m) for d, x in ps[k]})
+            up, down = [[] for _ in kinds], [[] for _ in kinds]
+            for a, b, c in arcs:
+                up[b].append((a, c))
+                down[a].append((b, c))
+            qu = [queue[i] for i in seq]
+
+            def mend(ph, todo, sign):
+                for _ in range(400):
+                    if not todo:
+                        return True
+                    b = todo.pop()
+                    for a, c in (up if sign < 0 else down)[b]:
+                        if sign < 0 and ph[a] >= ph[b] + c or sign > 0 and ph[a] + c <= ph[b]:
+                            ph[a] = ph[b] - sign * c + sign * 0.01
+                            todo.append(a)
+                return False
+
+            def rate(ph):
+                order = sorted(range(m), key=lambda k: ph[kind[k]] + per * step[k])
+                mp, free, hs = [-1] * m, {}, []
+                for k in order:
+                    if qu[k] != "N":
+                        mp[k] = free.get(qu[k], -1)
+                        free[qu[k]] = k
+                for j in range(nm):
+                    h, d, p = [0.0] * m, du[j], pm[j]
+                    for k in order:
+                        e = mp[k]
+                        t = h[e] + d[e] if e >= 0 else 0.0
+                        for e, x in p[k]:
+                            if h[e] + x > t:
+                                t = h[e] + x
+                        h[k] = t
+                    hs.append(h)
+                ends = [max(map(sum, zip(hs[j], ex[j]))) for j in range(nm)]
+                return sum(w[0] * e for w, e in zip(models, ends)), order, mp, hs, ends
+
+            def tight(state, j):
+                h, mp, out = state[3][j], state[2], []
+                k = max(range(m), key=lambda k: h[k] + ex[j][k])
+                while k >= 0:
+                    e = [d for d, x in pm[j][k] if h[d] + x > h[k] - 1e-3]
+                    if not e and mp[k] >= 0:
+                        out.append(k)
+                        e = [mp[k]]
+                    k = e[0] if e else -1
+                return out
+            while not mend(ph, list(range(len(kinds))), 1):
+                pass
+            cur = best = rate(ph)
+            crit = [None] * nm
+            for r in range(rounds):
+                j = int(draw() * nm)
+                c = crit[j] = crit[j] or tight(cur, j)
+                v = c[int(draw() * len(c))] if c and draw() > CFG["any"] else int(draw() * m)
+                u, far, mp = cur[2][v], int(draw() ** 3 * CFG["far"]), cur[2]
+                if u < 0 or kind[u] == kind[v]:
+                    continue
+                new = list(ph)
+                if draw() < 0.5:
+                    while far and mp[u] >= 0:
+                        u, far = mp[u], far - 1
+                    new[kind[v]] = ph[kind[u]] + per * (step[u] - step[v]) - 0.5 - draw()
+                    ok = mend(new, [kind[v]], -1) and new[kind[u]] == ph[kind[u]]
+                else:
+                    new[kind[u]] = ph[kind[v]] + per * (step[v] - step[u]) + 0.5 + draw() + far * draw() * 150.0
+                    ok = mend(new, [kind[u]], 1) and new[kind[v]] == ph[kind[v]]
+                if ok:
+                    e = rate(new)
+                    if e[0] < cur[0] + heat * (1.0 - r / rounds) * draw() ** 2:
+                        ph, cur, crit = new, e, [None] * nm
+                        if e[0] < best[0]:
+                            best = e
+                        if r % 16 == 0:
+                            t = [0.0] * len(kinds)
+                            for k in cur[1]:
+                                t[kind[k]] = ph[kind[k]]
+            return [seq[k] for k in best[1]], best[4]
+
+        def better(seq, rounds, heat, after=None, turns=CFG["turns"]):
+            inside = set(seq)
+            fore = {i: [e for e in pred[i] if e[0] in inside] for i in seq}
+            back = {i: [e for e in succ[i] if e[0] in inside] for i in seq}
+            best = None
+            for r in range(turns):
+                seq, e = polish(seq, rounds // turns, heat * (1.0 - r / turns), after)
+                e0 = sum(w[0] * x for w, x in zip(models, e))
+                if best is None or e0 < best[0]:
+                    best = (e0, seq, e)
+                start = times(seq, -1)[0]
+                late = place(sorted(seq, key=lambda i: (-start[i] - dur[i], -i)), back)[0]
+                start = place(sorted(seq, key=lambda i: (-late[i] - dur[i], i)), fore)[0]
+                seq = sorted(seq, key=lambda i: (start[i], i))
+            return best[1:]
+
+        members, extra = {}, []
+        for i in range(n):
+            for u in ops[i]["uses"]:
+                members.setdefault(u, []).append(i)
+
+        def bind(lists):
+            for d, i, x in extra:
+                pred[i].remove((d, x))
+                succ[d].remove((i, x))
+            extra[:] = [(d, members[w][0], 0 if queue[d] == "T" else CFG["lat"]) for e in lists.values() for u, w in zip(e, e[1:]) for d in members[u]]
+            for d, i, x in extra:
+                pred[i].append((d, x))
+                succ[d].append((i, x))
+
+        def topo(part, key):
+            inside = set(part)
+            left = {i: sum(d in inside for d, x in pred[i]) for i in part}
+            ready, out = [i for i in part if not left[i]], []
+            while ready:
+                i = min(ready, key=lambda i: (key[i], i))
+                ready.remove(i)
+                out.append(i)
+                for k, x in succ[i]:
+                    if k in inside:
+                        left[k] -= 1
+                        if not left[k]:
+                            ready.append(k)
+            return out
+
+        def banks(seq, alap, spare):
+            start = times(seq, -1)[0]
+            bind({})
+            mem = {u: e for u, e in members.items() if e[0] in start}
+            bit, above, key = {u: 1 << k for k, u in enumerate(mem)}, {}, dict(start)
+            for i in seq:
+                above[i] = 0
+                for d, x in pred[i]:
+                    if d in start:
+                        above[i] |= above[d] | sum(bit[u] for u in ops[d]["uses"])
+            opens = {e[0]: u for u, e in mem.items()}
+            for k0, i in reversed(list(enumerate(seq))):
+                if alap is None:
+                    key[i] = k0
+                elif queue[i] == "T":
+                    key[i] = max(start[i], min(key[k] - dur[i] - (alap if x else alap / 4) for k, x in succ[i] if k in start))
+            need = {u: 0 for u in mem}
+            for u, e in mem.items():
+                for i in e:
+                    need[u] |= above[i]
+                need[u] &= ~bit[u]
+            lists, where, todo, done, got = {b: [] for b in BANKS}, {}, {u: len(e) for u, e in mem.items()}, {b: -1.0 for b in BANKS}, 0
+            left = {i: sum(d in start for d, x in pred[i]) for i in seq}
+            ready, out = [i for i in seq if not left[i]], []
+            while ready:
+                idle = [b for b in BANKS if not lists[b] or not todo[lists[b][-1]]]
+                i = min([i for i in ready if i not in opens or len(idle) > (spare if need[opens[i]] & ~got else 0)], key=lambda i: (key[i], i))
+                if i in opens:
+                    where[opens[i]] = min(idle, key=lambda b: (done[b], b))
+                    lists[where[opens[i]]].append(opens[i])
+                    got |= bit[opens[i]]
+                for u in ops[i]["uses"]:
+                    todo[u] -= 1
+                    done[where[u]] = max(done[where[u]], start[i] + dur[i])
+                ready.remove(i)
+                out.append(i)
+                for k, x in succ[i]:
+                    if k in start:
+                        left[k] -= 1
+                        if not left[k]:
+                            ready.append(k)
+            bind(lists)
+            return out, lists
+
+        def follow(part, nxt):
+            rest, first = [], []
+            for w, lat, o in models:
+                g, free = {}, {}
+                for i in reversed(nxt):
+                    t = max([g[k] + (lat if x == CFG["lat"] else x) for k, x in succ[i] if k in g] + [free.get(queue[i], 0.0)])
+                    g[i] = t + o[i]
+                    if queue[i] != "N":
+                        free[queue[i]] = g[i]
+                top = max(g.values())
+                rest.append({i: max([g[k] + (lat if x == CFG["lat"] else x) - top for k, x in succ[i] if k in g] + [free.get(queue[i], 0.0) - top]) for i in part})
+            return lambda j, i: rest[j][i]
+        if n not in PLAN and CFG["polish"]:
+            race = [[i for i in range(n) if ops[i]["id"][0] == t] for t in range(RACES)]
+            if CFG.get("probe"):
+                part = [i for i in race[1] if CFG["probe"](ops[i])]
+                span, one, _ = improve(part, {i: -prio[i] for i in range(n)}, CFG["rounds"])
+                mid, e = better(sorted(part, key=lambda i: (one[i], i)), CFG["polish"][1], CFG["heat2"])
+                if CFG["polish"][2] > 1:
+                    mid, e = cyclic(mid, CFG["polish"][2], CFG["heatc"])
+                    PLAN["cyc"] = e
+                mid, e = better(mid, CFG["polish"][0], CFG["heat1"])
+                PLAN.update(ops=ops, seq=mid, e=e, st=times(mid, 0)[0])
+                raise ValueError("probe")
+            need = {i for i in race[1] if ops[i]["kind"] == "s"}
+            for i in reversed(race[1]):
+                if i in need:
+                    need.update(d for d, x in pred[i] if ops[d]["id"][0] == 1)
+            inside, rest = set(race[1]), []
+            for w, lat, o in models:
+                g = {}
+                for i in reversed(race[1]):
+                    g[i] = max([g[k] + o[k] + (lat if x == CFG["lat"] else x) for k, x in succ[i] if k in inside and k not in need] + [0.0])
+                rest.append(g)
+            score = lambda e: sum(w[0] * x for w, x in zip(models, e[1]))
+            tried = []
+            for _ in range(CFG["tries"][0]):
+                one = improve(sorted(need), {i: -prio[i] for i in range(n)}, CFG["rounds"])[1]
+                tried.append(better(sorted(need, key=lambda i: (one[i], i)), CFG["polish"][3], CFG["heat0"], lambda j, i: rest[j][i]))
+            PLAN["tried"] = [round(score(e)) for e in tried]
+            first, PLAN["first"] = better(min(tried, key=score)[0], CFG["polish"][3], CFG["heat2"], lambda j, i: rest[j][i])
+            one = place(first + sorted(inside - need, key=lambda i: (-near[i], i)), {i: [e for e in pred[i] if e[0] in inside] for i in race[1]})[0]
+            mid = sorted(race[1], key=lambda i: (one[i], i))
+
+            def like(t):
+                rank = {ops[i]["id"][1:]: k for k, i in enumerate(mid)}
+                key = {}
+                for i in race[t]:
+                    key[i] = max([rank.get(ops[i]["id"][1:], 0)] + [key[d] + 1e-3 for d, x in pred[i] if d in key])
+                return sorted(race[t], key=lambda i: (key[i], i))
+            after = follow(mid, like(2))
+            tried = [polish(mid, CFG["polish"][4], CFG["heat4"], lambda j, i: after(j, i) + push[i], CFG["since"]) for _ in range(CFG["tries"][1])]
+            PLAN["second"] = [round(score(e)) for e in tried]
+            mid = min(tried, key=score)[0]
+            mid, PLAN["free"] = better(mid, CFG["polish"][0], CFG["heat1"], after)
+            mid, lists = banks(mid, CFG["alap"], CFG["spare"])
+            best, PLAN["log"] = None, []
+            for r in range(CFG["binds"]):
+                e = better(mid, CFG["polish"][5] // CFG["binds"], CFG["heat5"] * (1.0 - r / CFG["binds"]), after, 2)
+                PLAN["log"].append(round(score(e)))
+                if best is None or score(e) < score(best[0]):
+                    best = (e, lists)
+                mid, lists = banks(e[0], None, 0)
+            (mid, PLAN["one"]), lists = best
+            begin = [i for i in range(n) if ops[i]["id"][0] < 0 and i < race[0][0]]
+            close = [i for i in range(n) if ops[i]["id"][0] < 0 and i > race[2][0]]
+            bind(lists)
+            one = times(mid, -1)[0]
+            bind({})
+            tail, last = banks(like(2) + close, None, 1)
+            best = None
+            for r in range(CFG["binds"] // 2):
+                e = better(tail, CFG["polish"][2] // (CFG["binds"] // 2), CFG["heat5"] * (1.0 - 2 * r / CFG["binds"]), lambda j, i: push[i] * (r < 2), 2)
+                if best is None or score(e) < score(best[0]):
+                    best = (e, last)
+                tail, last = banks(e[0], None, 0)
+            (tail, PLAN["tail"]), last = best
+            ident = {ops[e[0]]["id"]: u for u, e in members.items()}
+            whole = {b: [ident[(0,) + ops[members[u][0]]["id"][1:]] for u in e] + e + last[b] for b, e in lists.items()}
+            for b, u in zip(BANKS, [u for u, e in members.items() if e[0] in begin]):
+                whole[b].insert(0, u)
+            bind(whole)
+            PLAN["bank"], PLAN["extra"] = {u: b for b, e in whole.items() for u in e}, list(extra)
+            key = {i: (prio[0] - prio[i] if ops[i]["id"][0] < 0 else CFG["lead"] + one[twin[(1,) + ops[i]["id"][1:]]]) for i in begin + race[0]}
+            head = begin + race[0]
+            inside = set(head)
+            st = place(topo(head, key), {i: [e for e in pred[i] if e[0] in inside] for i in head})[0]
+            head, PLAN["head"] = better(sorted(head, key=lambda i: (st[i], i)), CFG["polish"][1], CFG["heat3"], follow(head, mid))
+            head, PLAN["head"] = polish(head, CFG["polish"][6], CFG["heat3"], follow(head, mid), 0.0, 0.45)
+            seq = head + mid + tail
+            PLAN["all"] = [times(seq, j)[1] for j in range(len(models))]
+            PLAN["seq"] = seq
+            PLAN[n] = (PLAN["all"][0], times(seq, 0)[0], sum(w[0] * e for w, e in zip(models, PLAN["all"])))
         if n not in PLAN:
             part = [i for i in range(n) if ops[i]["id"][0] == 1]
             key = {i: -prio[i] for i in range(n)}
@@ -218,7 +689,12 @@ def planner(g, T):
             PLAN["one"] = span
             PLAN[n] = improve(list(range(n)), key, CFG["rounds2"])
         PLAN["ops"] = ops
-        order = sorted((PLAN[n][1][i], i, i) for i in range(n))
+        for d, i, x in PLAN["extra"]:
+            ops[i]["deps"][d] = max(x, ops[i]["deps"].get(d, 0))
+        for e in late_bound:
+            u, p0, p, lo, hi = e[7]
+            e[0] = T[PLAN["bank"][u]][p0:p0 + p, lo:hi]
+        order = [(0, 0, i) for i in PLAN["seq"]] if "seq" in PLAN else sorted((PLAN[n][1][i], i, i) for i in range(n))
         cnt = {q: 0 for q in queues}
         clk = {q: {} for q in queues}
         snap = {}
@@ -264,7 +740,8 @@ def rank_program(g, core, T, topo):
     rank = T.rank_of(core)
     if rank is None:
         return
-    rec, emit, bias = planner(g, T)
+    late, uses = [], [0]
+    rec, emit, bias = planner(g, T, late)
     peers = [T.cores[(rank + j) % N] for j in (1, 2, 3)]
     GROUPS, CYC, LAT = CFG["groups"], CFG["cyc"], CFG["lat"]
 
@@ -283,8 +760,20 @@ def rank_program(g, core, T, topo):
         n = len(range(lo, hi, st))
         return (T[name][0:p, lo:hi:st], [(name, lo, lo + (n - 1) * st + 1)], n, 2 if "16" in SCRATCH[name][2] else 4, False, False, [])
 
-    def P(name, r0, r1, c=16, p=128):
-        return (T[name][0:p, 16 * r0:16 * r1 - 16 + c], [(name, 0, 512)], 16 * (r1 - r0 - 1) + c, 4, True, False, [])
+    def P(name, r0, r1, c=16, p=128, p0=0):
+        late.append([None, [(name, 0, 512)], 16 * (r1 - r0 - 1) + c, 4, True, False, [], (name, p0, p, 16 * r0, 16 * r1 - 16 + c)])
+        return late[-1]
+
+    def new():
+        uses[0] += 1
+        return "@%d" % uses[0]
+
+    def Ke(a0, a1, w):
+        return (T.kE[:, a0:a1, 16 * w:16 * w + 16], [("kE", 32 * a + 16 * w, 32 * a + 16 * w + 16) for a in range(a0, a1)], 16 * (a1 - a0), 2, False, False, [])
+
+    def Tv(r0, r1, st=1, c=0):
+        n = len(range(r0, r1, st))
+        return (T.Tt[:, r0, c:16] if n == 1 else T.Tt[:, r0:r1:st, c:16], [("Tt", 16 * r0, 16 * r1)], n * (16 - c), 2, False, False, [])
 
     def Yv(a0, a1, c=None):
         if c is None:
@@ -295,10 +784,10 @@ def rank_program(g, core, T, topo):
         return (win[0].indirect(lst[0]), win[1], 16 * lst[2], win[3], False, True, lst[1])
 
     def arg(x):
-        return x[0] if isinstance(x, tuple) else x
+        return x[0] if isinstance(x, (tuple, list)) else x
 
     def op(q, fn, out, ins, rate=None, dur=None):
-        full = [x for x in ins if isinstance(x, tuple)]
+        full = [x for x in ins if isinstance(x, (tuple, list))]
         R = [r for x in full for r in x[1] + x[6]] + out[6]
         if dur is None:
             fix = 50 if q == "V" else 65
@@ -337,13 +826,19 @@ def rank_program(g, core, T, topo):
     def act(out, in_, f=ID, bias=0.0, scale=1.0):
         op("S", lambda e: e.activation(out[0], in_[0], f, bias=arg(bias), scale=arg(scale)), out, [in_, bias, scale], rate=1)
 
+    def lin(name, out, in_, scale=1.0, add=0.0):
+        if name in CFG["onS"]:
+            act(out, in_, bias=add, scale=scale)
+        else:
+            ts(out, in_, scale, A.mult, add, A.add)
+
     def group(terms, cuts=(), start=True, stop=True):
         run, dur = [], 0.0
-        for i, (out, lhsT, rhs) in enumerate(terms):
-            run.append((out[0], lhsT[0], rhs[0], start and i == 0, stop and i == len(terms) - 1))
+        for i, (out, lhsT, rhs, *ends) in enumerate(terms):
+            run.append((out, lhsT[0], rhs[0], start and i == 0, stop and (i == len(terms) - 1 or any(ends))))
             dur += max(min(64, lhsT[2]), rhs[2]) * (4 if rhs[3] == 4 else 1)
             if dur >= CFG["run"] or i + 1 in cuts or i + 1 - len(terms) in cuts or i + 1 == len(terms):
-                op("T", lambda e, run=run: [e.matmul(*m) for m in run][-1], out, [x for u in terms[i + 1 - len(run):i + 1] for x in u[1:]], dur=(0, 0, 0, 0, dur))
+                op("T", lambda e, run=run: [e.matmul(m[0][0], *m[1:]) for m in run][-1], out, [x for u in terms[i + 1 - len(run):i + 1] for x in u[1:3]], dur=(0, 0, 0, 0, dur))
                 run, dur = [], 0.0
 
     def gcp(out, in_, after=None, pieces=None):
@@ -371,11 +866,12 @@ def rank_program(g, core, T, topo):
     phase("load")
     dma("S", "vin", T.vs[:], T.v0[:], [], [("vs", 0, 45)], 2000.0)
     dma("S", "zin", T.zs[:], T.z0[:], [], [("zs", 0, 240)], 2000.0)
-    loads = [("kin", T.k0, 1024 * i, 1024 * i + 1024) for i in range(4)] + [("xw", T.x0, 2048 * i, 2048 * i + 2048) for i in range(2)]
+    loads = [("xw", T.x0, lo, hi) for lo, hi in CFG["xload"]] + [("kin", T.k0, lo, hi) for lo, hi in CFG["kload"]]
+    size = [CFG["piece"] * (hi - lo) / (1024 if name == "kin" else 2048) for name, src, lo, hi in loads]
     for i, (name, src, lo, hi) in enumerate(loads):
         w = CFG["flight"]
         gate = [(loads[i - w][0], loads[i - w][2], loads[i - w][2] + 1)] if i >= w else []
-        dma("Y", "ld%d" % i, T[name][:, lo:hi], src[:, lo:hi], gate, [(name, lo, hi)], 2200.0 + CFG["piece"] * (i + 1) if i < w else CFG["piece"] * w)
+        dma("Y", "ld%d" % i, T[name][:, lo:hi], src[:, lo:hi], gate, [(name, lo, hi)], 2200.0 + sum(size[:i + 1]) if i < w else sum(size[i + 1 - w:i + 1]))
 
     iota(B("pI", 0, 1), [[0, 1]], 0, 1)
     iota(B("iw", 0, 256), [[1, 256]], 0, 0)
@@ -386,13 +882,16 @@ def rank_program(g, core, T, topo):
     ne = send(B("vs"), [T.vl[:, 45 * j:45 * j + 45] for j in range(3)], B("vl"), "av", "lv")
     send(B("zs"), [T.zl[:, 240 * j:240 * j + 240] for j in range(3)], B("zl"), "az", "lz")
     iota(B("E", 0, 16 * SW), [[1, SW], [0, 16]], 0, 0)
-    iota(B("bs"), [[4096, 4], [0, 16]], 4096, 0)
+    for h in range(2 * bool(CFG["half"])):
+        iota(B("E", 1024 + 512 * h, 1536 + 512 * h), [[16, 4], [2, 8], [0, 16]], h, 0)
     iota(B("Dm"), [[0, 4], [16, 16]], 0, 0)
     ms(B("base"), BIG)
     for s in range(S):
         iota(B("base", 16 * s, 16 * s + 15), [[4096, 3], [0, 5]], 16384 * (s + 1) + 4096, 0)
-    for i in range(4):
+    for i in range(3):
         act(B("iw", 256 << i, 512 << i), B("iw", 0, 256 << i), bias=float(256 << i))
+    act(B("iw", 2048, 3072), B("iw", 0, 1024), bias=2048.0)
+    iota(B("iw", 3072, V), [[1, 1024]], 3072, 0)
 
     def col(i):
         return B("pF", i, i + 1)
@@ -413,14 +912,11 @@ def rank_program(g, core, T, topo):
     ts(col(10), col(2), 15.0, A.add)
     ts(col(11), col(0), 16.0, A.mult, 15.0, A.add)
     ts(B("idb"), I128, col(0), A.is_equal)
-    for name, f in (("idn", -1.0), ("idB", -16384.0), ("idM", 8192.0), ("ih", 1.0), ("ihn", -1.0), ("ih2", -2.0), ("ih32", 32.0), ("ihd", 1.0 / 32.0)):
+    for name, f in (("idn", -1.0), ("idB", -16384.0), ("idM", 8192.0), ("ih", 1.0), ("ihn", -1.0), ("ih2", -2.0), ("ih32", 32.0), ("ihd", 16.0), ("idX", -16.0)):
         act(B(name), B("idb"), scale=f)
     for s in range(S):
-        act(B("idS", 128 * s, 128 * s + 128), B("idb"), scale=1024.0 * (s + 1))
-    for a in range(8):
-        act(B("idx", 128 * a, 128 * a + 128), B("idb"), scale=float(a + 1))
-        act(B("idk", 128 * a, 128 * a + 128), B("idb"), scale=float(a + 1))
-    for h in range(2):
+        act(B("idS", 128 * s, 128 * s + 128), B("idb"), scale=32.0 * (s + 1))
+    for h in range(2 * (not CFG["quad"])):
         for w in range(2):
             o = 128 * (2 * h + w)
             ts(B("Pm", o, o + 128), I128, col({0: 0, 1: 8, -1: 9}[w - h]), A.is_equal, col(3 if h else 7), A.mult)
@@ -429,27 +925,42 @@ def rank_program(g, core, T, topo):
     act(B("Uh"), B("U1"))
     ts(B("Us"), B("iw", 0, 144), col(11), A.is_equal, 8192.0, A.mult)
     ts(B("rm"), B("rm"), 1.0, A.min)
-    ts(B("E", 0, 16 * SW), B("E", 0, 16 * SW), col(0), A.is_equal)
-    ms(B("rz", 0, 16 * VW), 2048.0)
-    ms(B("rz", 0, 16 * VW, 16), -1024.0)
+    ts(B("En", 0, 16 * SW), B("E", 0, 16 * SW), col(0), A.is_equal, -1.0, A.mult)
+    ms(B("rz"), 2048.0)
+    ms(B("rz", 0, 256, 16), -1024.0)
     for name in ("on", "vI", "x", "ow4"):
         ms(B(name), 0)
-    for o in range(240, 2304, 256):
-        ms(B("zh", o, o + 16), 1024.0)
-    for o in range(240, 1024, 256):
-        ms(B("kvh", o, o + 16), 0.0)
+    ms(B("ones"), 1.0)
+    for o in [496] + list(range(1008, 2304, 256)):
+        act(B("zh", o, o + 16), B("ones", 0, 16), scale=1024.0)
+    for o in range(240, 1024, 256) if not CFG["quad"] else ():
+        act(B("kvh", o, o + 16), B("ones", 0, 16))
     for a0, a1, k in GROUPS:
-        for par in range(2 * (k == "V")):
-            ms(B("shp", 4096 * par + 256 * a0, 4096 * par + 256 * a1), 0.0)
-    ms(Yv(15, 16), 0.0)
+        if k == "V":
+            ms(B("shp", 256 * a0, 256 * a1), 0.0)
+    ms((T.Ys[:, 240:256, :], [("Ys", 3840, 4096)], 256, 2, False, False, []), 0.0)
+    for h in range(2 * bool(CFG["half"])):
+        o = 1024 + 512 * h
+        ts(B("En", o, o + 512), B("E", o, o + 512), col(0), A.is_equal, -1.0, A.mult)
     ms(B("thr", 0, 1), 8.0)
-    ms(B("thr", 1, 2), 12.0 * BIG)
+    ms(B("cls", 48, 64), 12.0 * BIG)
     ms(B("gt4", 240, 256), 0.0)
     act(B("Un"), B("U1"), scale=-BIG)
-    ms(B("ones"), 1.0)
-    ms(B("cst"), 2048.0)
+    ms(B("csu"), 2048.0)
+    ms(B("cst"), 0.0)
+    ms(B("cst", 15, 128, 16), 2048.0)
+    if CFG["quad"]:
+        ts(B("ge"), B("iw", 0, 16), col(1), A.is_equal)
+        ts(B("xy"), B("iw", 0, 16), 1.0, A.add, col(1), A.is_equal)
+        tt(B("Dif"), B("ge"), B("xy"), A.subtract)
+        act(col(21), col(7), scale=-2048.0)
+        act(col(22), col(3), scale=-2048.0)
+    else:
+        act(B("Pn"), B("Pm"), scale=-1.0)
     ms(B("cneg", 0, 48), -16384.0)
-    ms(B("cneg", 48, 96), 0.0)
+    ms(B("cneg", 48, 96), 26624.0)
+    ms(B("cneg", 96, 112), 26624.0 + K0)
+    ms(B("cneg", 112, 128), 26624.0 + X0)
     for i in range(4):
         ts(pi(7 + i), pi(1), i, A.arith_shift_right, 1, A.bitwise_and)
     for i in range(4):
@@ -466,33 +977,38 @@ def rank_program(g, core, T, topo):
     ts(B("xy", 0, 1), col(18), 2.0 ** 55, A.mult, 2.0 ** 60, A.mult)
     scan(B("wt", 0, 15), B("ge", 0, 15), B("xy", 0, 15), A.mult, A.add)
     ts(B("wt", 16, 31), B("wt", 0, 15), -1.0, A.mult)
-    ts(B("Wk"), B("iw", 0, 16), col(1), A.is_equal, 1.0 / 32.0, A.mult)
-    ts(B("ln"), B("Dm", 0, 16), col(1), A.add)
-    ts(B("Dm"), B("Dm"), col(1), A.add, 4096.0 - 26624.0, A.add)
+    ts(B("Wk"), B("iw", 0, 32), -1.0, A.add, col(1), A.is_equal)
+    ts(B("ln"), B("Dm", 0, 16), col(1), A.add, -240.0, A.add)
+    ts(B("DJ"), B("Dm", 0, 16), col(1), A.add, K0 + 4096.0, A.add)
+    ms(B("zg", 0, 16), 1024.0)
+    ms(B("kw", 0, X0), 0.0)
+    ts(B("Dm"), B("Dm"), col(1), A.add, 4096.0, A.add)
     tt(col(19), col(4), col(5), A.is_equal)
     ts(col(20), col(6), -15.0, A.add)
     ts(B("t8"), B("iw", 0, 8), 2.0, A.mult, col(20), A.add)
     ts(B("w8l"), B("t8"), col(19), A.mult, 15.0, A.add)
 
-    ms(B("cs"), 0.0)
+    for o in range(240, 1280, 256):
+        act(B("cs", o, o + 16), B("ones", 0, 16))
 
-    KW = B("kw", 0, V)
-    XW = B("xw", 0, V)
+    KW = B("kw", K0, K0 + V)
+    XW = B("kw", X0, X0 + V)
 
     def vU(t, s, a0=0, a1=15):
         return B("vU", 80 * t + 16 * s + a0, 80 * t + 16 * s + a1)
 
-    def spairs(o, vals, keys, upto):
-        for a in range(upto):
-            n = 240 - 16 * a
-            act(B("eqm", o, o + n), B(vals[0], vals[1] + 16 * a, vals[1] + 240), ABS, bias=B(keys[0], keys[1] + a, keys[1] + a + 1))
-            act(B("eqm", o, o + n), B("eqm", o, o + n), RELU, bias=B("wt", a, a + 1), scale=B("wt", 16 + a, 17 + a))
-            o += n
-
-    def pairs(dst, o, vals, keys, since=0):
+    def spairs(o, vals, keys, since):
         for a in range(15):
             n = 240 - 16 * a
             if a >= since:
+                act(B("eqm", o, o + n), B(vals[0], vals[1] + 16 * a, vals[1] + 240), ABS, bias=B(keys[0], keys[1] + a, keys[1] + a + 1))
+                act(B("eqm", o, o + n), B("eqm", o, o + n), RELU, bias=B("wt", a, a + 1), scale=B("wt", 16 + a, 17 + a))
+            o += n
+
+    def pairs(dst, o, vals, keys, upto=15):
+        for a in range(15):
+            n = 240 - 16 * a
+            if a < upto:
                 ts(B(dst, o, o + n), B("val", vals + 16 * a, vals + 240), B(keys[0], keys[1] + a, keys[1] + a + 1), A.is_equal, B("wt", a, a + 1), A.mult)
             o += n
 
@@ -500,18 +1016,24 @@ def rank_program(g, core, T, topo):
         phase("start%d" % min(t, 1))
         for j in range(3):
             o = 45 * j + 15 * t + 5 * j
-            cp(B("vI", 16 * t + 5 * j, 16 * t + 5 * j + 5), B("vl", o, o + 5))
+            (act if t else cp)(B("vI", 16 * t + 5 * j, 16 * t + 5 * j + 5), B("vl", o, o + 5))
             act(B("zc", 240 * t + 80 * j, 240 * t + 80 * j + 80), B("zl", 240 * j + 80 * t, 240 * j + 80 * t + 80))
         cp(vU(t, 0), B("vI", 16 * t, 16 * t + 15))
     phase("start1")
     ts(B("k1c"), B("vI"), -2048.0, A.add)
     ts(B("v1h"), B("vI"), -2048.0, A.add)
+    act(B("v1K"), B("vI"), bias=float(K0))
     for t in range(RACES):
-        act(B("val", 240 * t, 240 * t + 240), IX(B("iw", 0, V), vU(t, 0)), bias=-2048.0)
-        pairs("eq1", 1920 * t, 240 * t, ("k1c", 16 * t))
+        act(B("val", 960 + 240 * t, 1200 + 240 * t), IX(B("iw", 0, V), vU(t, 0)), bias=-2048.0)
+        if t < CFG["eqs"]:
+            pairs("eq1", 1920 * t, 960 + 240 * t, ("k1c", 16 * t))
     phase("start0")
-    for i in range(4):
-        ts(B("kw", 1024 * i, 1024 * i + 1024), B("kin", 1024 * i, 1024 * i + 1024), 32.0, A.mult)
+    for o in range(0, V, 256):
+        (act if o // 256 % 4 else cp)(B("kw", K0 + o, K0 + o + 256), B("kin", o, o + 256))
+    for lo, hi in CFG["xload"]:
+        mid = lo + (hi - lo) // 4
+        cp(B("kw", X0 + lo, X0 + mid), B("xw", lo, mid))
+        act(B("kw", X0 + mid, X0 + hi), B("xw", mid, hi))
 
     TEAMS = CFG["teams"]
 
@@ -525,132 +1047,191 @@ def rank_program(g, core, T, topo):
     def sh(gr, s):
         a0, a1, k = GROUPS[gr]
         if k == "V" and s < S:
-            return B("shp", 4096 * (s % 2) + 256 * a0, 4096 * (s % 2) + 256 * a1, 16)
+            return B("shp", 256 * a0, 256 * a1, 16)
         return zh(s, a0, a1)
+
+    def Zy(a0, a1, c0=0, c1=16):
+        ap = T.zy[:, 16 * a0:16 * a1, c0] if c1 == c0 + 1 else T.zy[:, 16 * a0:16 * a1, c0:c1]
+        return (ap, [("zy", 256 * a0, 256 * a1)], 16 * (a1 - a0) * (c1 - c0), 2, False, False, [])
+
+    def double(a0, a1, after=None):
+        for c in (1, 2, 4, 8):
+            gcp(Zy(a0, a1, c, 2 * c), Zy(a0, a1, 0, c), after)
 
     def zform(gr, s):
         a0, a1, k = GROUPS[gr]
         n = 16 * (a1 - a0)
         if k == "V":
-            o = 4096 * (s % 2) + 256 * a0
-            scan(B("zx", 256 * a0, 256 * a1), B("rz", 0, 16 * n), B("shp", o, o + 16 * n), A.min, A.add)
+            am = a1 - CFG["gsp"]
+            for a in range(a0, am):
+                o = 256 * a
+                scan(B("zx", 256 * a, 256 * a + 256), B("rz", 0, 256), B("shp", o, o + 256), A.min, A.add)
+            if am < a1:
+                o = 0
+                lin("zy", Zy(am, a1, 0, 1), B("shp", o + 256 * am, o + 256 * a1, 16), 1.0, -1024.0)
+                double(am, a1)
         else:
-            pb = P("pb%d" % [tm for tm, team in enumerate(TEAMS) if gr in team][0], 0, 8, p=n)
-            group([(pb, sh(gr, s), B("ih"))])
-            act(B("zT", 128 * gr, 128 * gr + 128, p=n), pb, bias=1024.0, scale=-1.0)
+            pb, zT = P(new(), 0, 8, p=n), B("zT", 128 * gr, 128 * gr + 128, p=n)
+            if s == 0:
+                group([(pb, sh(gr, s), B("ih"))])
+                act(zT, pb)
+            else:
+                o = 256 * (s - 1)
+                group([(pb, B("ih", 0, n, p=n), zT), (pb, B("xq", o + 16 * a0, o + 16 * a1), B("idb"))], (1,))
+                act(zT, pb, bias=511.75, scale=0.5)
 
     def zinit(t):
         act(zh(0), B("zc", 240 * t, 240 * t + 240), bias=1024.0)
         for gr, (a0, a1, k) in enumerate(GROUPS):
-            if k == "V":
+            if k == "V" and not (t and CFG["gzx"]):
                 act(sh(gr, 0), B("zc", 240 * t + 16 * a0, 240 * t + 16 * a1), bias=1024.0)
             if k == "V" and t and CFG["gzx"]:
-                for c in range(16):
-                    gcp(B("zx", 256 * a0 + c, 256 * a1, 16), B("zc", 240 * t + 16 * a0, 240 * t + 16 * a1), last["G"],
-                        [("zx", 256 * a + c, 256 * a + c + 1) for a in range(a0, a1)])
+                am = a1 - CFG["gsp"]
+                for c in range(16 * (am > a0)):
+                    gcp(B("zx", 256 * a0 + c, 256 * am, 16), B("zc", 240 * t + 16 * a0, 240 * t + 16 * am), last["G"],
+                        [("zx", 256 * a + c, 256 * a + c + 1) for a in range(a0, am)])
+                if am < a1:
+                    gcp(Zy(am, a1, 0, 1), B("zc", 240 * t + 16 * am, 240 * t + 16 * a1), last["G"])
+                    double(am, a1, last["G"])
             else:
                 zform(gr, 0)
+
+    def halved(gr, s):
+        return gr in CFG["half"] and (s, [tm for tm, team in enumerate(TEAMS) if gr in team][0]) not in CFG["kv"]
+
+    def Ys(l0, l1, st=1):
+        return (T.Ys[:, l0:l1:st, :], [("Ys", 16 * l, 16 * l + 16) for l in range(l0, l1, st)] if st > 1 else [("Ys", 16 * l0, 16 * l1)], 16 * len(range(l0, l1, st)), 2, False, False, [])
 
     def knew(t, gr, s):
         a0, a1 = span(gr)
         nb, o = (a1 - a0 + 1) // 2, 256 * (s - 1) + 16 * a0
-        act(B("kvh", o, o + 16 * (a1 - a0)), IX(KW, vU(t, s - 1, a0, a1)), bias=-2048.0, scale=1.0 / 32.0)
         if (s, gr) in CFG["kv"]:
-            ts(B("kvu", 16 * a0, 16 * a1), IX(KW, vU(t, s - 1, a0, a1)), 1.0 / 32.0, A.mult)
+            cp(B("kvu", 16 * a0, 16 * a1), IX(KW if t else B("kin"), vU(t, s - 1, a0, a1)))
         else:
-            ts(B("kvu", 16 * a0, 16 * a1), B("kvh", o, o + 16 * (a1 - a0)), 2048.0, A.add)
-        tb, src = B("Tt", 128 * gr, 128 * gr + 32 * nb), B("kvh", o, o + 32 * nb)
+            act(B("kvu", 16 * a0, 16 * a1), IX(KW if t else B("kin"), vU(t, s - 1, a0, a1)))
+        if CFG["quad"]:
+            for w in range(2):
+                if (gr, w) in CFG["khs"]:
+                    act(Ke(a0, a1, w), B("kvu", 16 * a0, 16 * a1), bias=col(21 + w), scale=col(3 if w else 7))
+                else:
+                    ts(Ke(a0, a1, w), B("kvu", 16 * a0, 16 * a1), -2048.0, A.add, col(3 if w else 7), A.mult)
+            return
+        if gr in CFG["khs"]:
+            act(B("kvh", o, o + 16 * (a1 - a0)), B("kvu", 16 * a0, 16 * a1), bias=-2048.0)
+        else:
+            ts(B("kvh", o, o + 16 * (a1 - a0)), B("kvu", 16 * a0, 16 * a1), -2048.0, A.add)
+        tb, src = Tv(a0, a0 + 2 * nb), B("kvh", o, o + 32 * nb)
         op("V", lambda e: e.transpose(tb[0], src[0]), tb, [src])
 
-    def score(tm):
+    def score(tm, pb):
         a0, a1 = span(tm)
-        pb, w = "pb%d" % tm, 2 * ((a1 - a0 + 1) // 2)
+        w = 2 * ((a1 - a0 + 1) // 2)
         group([(P(pb, 0, w), B("idb"), B("kc", 0, 16 * w))], stop=False)
         for gr in TEAMS[tm]:
             al, ah = GROUPS[gr][:2]
             end = a0 + w if ah == a1 else ah
-            group([(P(pb, al - a0, end - a0), B("U", 15 - c, 143 - c), Yv(al, end, c)) for c in range(16)], start=False, stop=gr == TEAMS[tm][-1])
+            cs = list(range(0, 16, 2)) + list(range(1, 16, 2))
+            group([(P(pb, al - a0, end - a0), B("U", 15 - c, 143 - c), Yv(al, end, c) if GROUPS[gr][2] == "V" else Ys(16 * al + c, 16 * end, 16)) for c in cs],
+                  start=False, stop=gr == TEAMS[tm][-1])
 
     chunk = [0]
 
     def xact(gr):
         a0, a1, k = GROUPS[gr]
         n = 16 * (a1 - a0)
-        for a in range(a0, a1, CFG["scols"]):
+        for h in range(2 * halved(gr, now[1])):
+            xg, pa = B("xg%d" % (chunk[0] % 3), 0, 8 * n), P(new(), 0, n // 2)
+            chunk[0] += 1
+            act(xg, IX(XW, B("kvu", 16 * a0 + h * n // 2, 16 * a0 + (h + 1) * n // 2)))
+            group([(pa, B("zT", 128 * gr, 128 * gr + 128, p=n), B("En", 1024 + 512 * h, 1024 + 512 * h + 8 * n, p=n)), (pa, B("idb"), xg)][::CFG["zfirst"][h]], (1,))
+            act(Ys(16 * a0 + h, 16 * a1, 2), pa, RELU, bias=1024.0)
+        for a in range(a0, a1, CFG["scols"]) if not halved(gr, now[1]) else ():
             e = min(a + CFG["scols"], a1)
-            xg, pa, o = B("xg%d" % (chunk[0] % 3), 0, 256 * (e - a)), P(CFG["abank"][chunk[0] % len(CFG["abank"])], 0, 16 * (e - a)), 256 * (a - a0)
+            xg, pa, o = B("xg%d" % (chunk[0] % 3), 0, 256 * (e - a)), P(new(), 0, 16 * (e - a)), 256 * (a - a0)
             chunk[0] += 1
             act(xg, IX(XW, B("kvu", 16 * a, 16 * e)))
-            group([(pa, B("zT", 128 * gr, 128 * gr + 128, p=n), B("E", o, o + 256 * (e - a), p=n)), (pa, B("idb"), xg)][::CFG["zfirst"]], (1,))
-            act(Yv(a, e), pa, RELU)
+            group([(pa, B("zT", 128 * gr, 128 * gr + 128, p=n), B("En", o, o + 256 * (e - a), p=n)), (pa, B("idb"), xg)][::CFG["zfirst"][a > a0]], (1,))
+            act(Ys(16 * a, 16 * e), pa, RELU, bias=1024.0)
 
     def xvec(gr):
         a0, a1, k = GROUPS[gr]
-        for a in range(a0, a1, CFG["xcols"]):
-            e = min(a + CFG["xcols"], a1)
-            tt(Yv(a, e), IX(XW, B("kvu", 16 * a, 16 * e)), B("zx", 256 * a, 256 * e), A.max)
+        for a in range(a0, a1):
+            n = 8 if a - a0 in CFG["xh"] else 16
+            for l in range(16 * a, 16 * a + 16, n):
+                y = (T.Y[:, a, 16 * (l - 16 * a):16 * (l + n - 16 * a)], [("Y", 16 * l, 16 * (l + n))], 16 * n, 2, False, False, [])
+                z = (T.zy[:, l:l + n, :], [("zy", 16 * l, 16 * (l + n))], 16 * n, 2, False, False, [])
+                tt(y, IX(XW, B("kvu", l, l + n)), B("zx", 16 * l, 16 * (l + n)) if a < a1 - CFG["gsp"] else z, A.max)
 
     def pick(t, gr, s):
         a0, a1 = span(gr)
         nb = (a1 - a0 + 1) // 2
-        n, o, pb = 32 * nb, 256 * (s - 1) + 16 * a0, "pb%d" % gr
-        key, R, D, C = P(pb, 0, 2 * nb), B("R", o, o + n), B("d0", 128 * gr, 128 * gr + n), B("C", o, o + n)
-        if gr not in CFG["d1v"]:
-            score(gr)
-        pk = CFG["kbank"][gr]
-        terms = [(P(pk, 16, 16 + 2 * nb), B("idb"), B("cst", 0, n))]
-        for b in range(nb):
-            for h in range(2):
-                for w in range(2):
-                    q = 128 * gr + 32 * b + 16 * w
-                    terms.append((P(pk, 16 + 2 * b + h, 17 + 2 * b + h), B("Pm", 128 * (2 * h + w), 128 * (2 * h + w) + 128), B("Tt", q, q + 16)))
-        if gr in CFG["d1v"]:
+        n, o, pb = 32 * nb, 256 * (s - 1) + 16 * a0, new()
+        key, R, D, C = P(pb, 0, 2 * nb), B("R", o, o + n), B("d0", 16 * a0, 16 * a0 + n), B("C", o, o + n)
+        pk = pb if gr in CFG["dif"] and gr not in CFG["apart"] else new()
+        d1 = P(pk, 16, 16 + 2 * nb)
+        dif = gr in CFG["dif"]
+        terms = [(d1, B("idb"), B("cst" if dif else "csu", 0, n))]
+        for a in range(a1 - a0):
+            for q in range(0, 128, 32) if CFG["quad"] else ():
+                terms.append((P(pk, 16 + a, 17 + a, p=32, p0=q), (T.kE[q:q + 32, a0 + a, :], [("kE", 32 * (a0 + a), 32 * (a0 + a) + 32)], 32, 2, False, False, []),
+                              (T.Dif[q:q + 32, :], [("Dif", 0, 16)], 16, 2, False, False, []), a == a1 - a0 - 1))
+            for w in range(2 * (not CFG["quad"])):
+                q, b = 128 * (2 * (a % 2) + w), a0 + a - a % 2 + w
+                terms.append((P(pk, 16 + a, 17 + a), B("Pm", q, q + 128), Tv(b, b + 1)))
+                if dif:
+                    terms.append((P(pk, 16 + a, 17 + a, c=15), B("Pn", q, q + 128), Tv(b, b + 1, 1, 1)))
+        if dif:
             group(terms)
-            score(gr)
+        score(gr, pb)
         scan(R, B("rm", 0, n), key, A.mult, A.max)
-        tt(D, R, key, A.subtract)
-        if gr in CFG["d1v"]:
-            d1 = B("dd", 128 * gr, 128 * gr + n)
-            tt(d1, P(pk, 16, 16 + 2 * nb), D, A.subtract)
+        if dif:
+            tt(D, R, key, A.is_gt)
+            scan(C, D, d1, A.mult, A.add)
         else:
-            d1 = P(pk, 16, 16 + 2 * nb)
+            tt(D, R, key, A.subtract)
             group(terms + [(d1, B("idn"), D)], (-1,))
-        scan(C, D, d1, A.min, A.max)
+            scan(C, D, d1, A.min, A.max)
         cp(vU(t, s, a0, a1), B("C", o + 15, o + 16 * (a1 - a0), 16))
 
     nev = [0]
 
     def zstep(t, tm, s):
-        t0, pz, o = span(tm)[0], "pb%d" % tm, 256 * (s - 1)
-        onv = [gr for gr in TEAMS[tm] if gr in CFG["zv4" if s == S else "zv"]]
+        t0, pz, o = span(tm)[0], new(), 256 * (s - 1)
+        if s == S:
+            a0, a1 = span(tm)
+            lst, zt = IX(XW, vU(t, s, a0, a1)), B("zt", o + 16 * a0, o + 16 * a1)
+            tt(B("gt4", 16 * a0, 16 * a1), lst, B("z3", 16 * a0, 16 * a1), A.is_gt)
+            if tm in CFG["z4s"]:
+                xq, pa = B("xq", o + 16 * a0, o + 16 * a1), P(pz, 8, 8 + a1 - a0)
+                act(xq, lst)
+                group([(pa, B("ih"), zh(s - 1, a0, a1)), (pa, B("idb"), xq)], (1,))
+                act(zh(s, a0, a1), pa, bias=511.75, scale=0.5)
+            else:
+                tt(zt, lst, zh(s - 1, a0, a1), A.add)
+                ts(zh(s, a0, a1), zt, 0.5, A.mult, 511.75, A.add)
+            return
+        onv = [gr for gr in TEAMS[tm] if gr in CFG["zv"]]
         ons = [gr for gr in TEAMS[tm] if gr not in onv]
         for gr in onv:
             a0, a1, k = GROUPS[gr]
             lst, zt = IX(XW, vU(t, s, a0, a1)), B("zt", o + 16 * a0, o + 16 * a1)
-            tt(zt, lst, sh(gr, s - 1), A.add)
+            tt(zt, lst, zh(s - 1, a0, a1), A.add)
             ts(sh(gr, s), zt, 0.5, A.mult, 511.75, A.add)
-            if s == S:
-                tt(B("gt4", 16 * a0, 16 * a1), lst, B("zx", 256 * a0, 256 * a1, 16) if k == "V" else B("z3", 16 * a0, 16 * a1), A.is_gt)
         if ons:
             b0, b1 = GROUPS[ons[0]][0], GROUPS[ons[-1]][1]
             xq = B("xq", o + 16 * b0, o + 16 * b1)
             act(xq, IX(XW, vU(t, s, b0, b1)))
-            group([(P(pz, 8 + b0 - t0, 8 + b1 - t0), B("idb"), xq)] + [(P(pz, 8 + GROUPS[gr][0] - t0, 8 + GROUPS[gr][1] - t0), B("ih"), sh(gr, s - 1)) for gr in ons])
-            if s == S:
-                group([(P(pz, 24 + b0 - t0, 24 + b1 - t0), B("idb"), xq)] + [(P(pz, 24 + GROUPS[gr][0] - t0, 24 + GROUPS[gr][1] - t0), B("ihn"), sh(gr, s - 1)) for gr in ons])
-                act(zh(s, b0, b1), P(pz, 8 + b0 - t0, 8 + b1 - t0), bias=511.75, scale=0.5)
-                act(B("zh", 512 + 16 * b0, 512 + 16 * b1), P(pz, 24 + b0 - t0, 24 + b1 - t0), SIGN, bias=1023.5)
-            for gr in ons * (s < S):
+            group([(P(pz, 8 + b0 - t0, 8 + b1 - t0), B("idb"), xq)] + [(P(pz, 8 + GROUPS[gr][0] - t0, 8 + GROUPS[gr][1] - t0), B("ih"), zh(s - 1, *GROUPS[gr][:2])) for gr in ons])
+            for gr in ons:
                 act(sh(gr, s), P(pz, 8 + GROUPS[gr][0] - t0, 8 + GROUPS[gr][1] - t0), bias=511.75, scale=0.5)
-        if s == S:
-            return
         for gr in TEAMS[tm]:
             a0, a1, k = GROUPS[gr]
             zform(gr, s)
             if k == "V":
                 gcp(zh(s, a0, a1), sh(gr, s))
-            elif s == S - 1 and gr in CFG["zv4"]:
-                act(B("z3", 16 * a0, 16 * a1), sh(gr, s), bias=-1024.0)
+        if s == S - 1:
+            act(B("z3", 16 * span(tm)[0], 16 * span(tm)[1]), zh(s, *span(tm)), bias=-1024.0)
+        pz = new()
         for gr in onv:
             a0, a1, k = GROUPS[gr]
             pa = P(pz, 24 + a0 - t0, 24 + a1 - t0)
@@ -662,6 +1243,11 @@ def rank_program(g, core, T, topo):
         act(B("zh", 1536 + o + 16 * a0, 1536 + o + 16 * a1), P(pz, 24, 24 + a1 - a0), SIGN, bias=1023.5)
 
     def race(t):
+        chunk[0] = nev[0] = 0
+        now[0], now[1] = t, 1
+        phase("eqn")
+        if CFG["eqs"] == 0:
+            pairs("eq1", 1920 * t, 960 + 240 * t, ("k1c", 16 * t))
         for s in range(1, S + 1):
             now[0], now[1] = t, s
             for tm in range(len(TEAMS)):
@@ -674,6 +1260,10 @@ def rank_program(g, core, T, topo):
                 pick(t, tm, s)
                 phase("z%d" % tm)
                 zstep(t, tm, s)
+            phase("zg")
+            gcp(B("zg", 256 * s - 240, 256 * s + 16), zh(s, 0, 16))
+            for o in range(1024 * s - 1024, 1024 * s, 512) if t == RACES - 1 else ():
+                gcp(B("xw", o, o + 512), B("kw", X0 + o, X0 + o + 512))
             if s == S - 1:
                 early(t)
         finish(t)
@@ -681,33 +1271,54 @@ def rank_program(g, core, T, topo):
     def least(name, rs):
         tt(B(name, 0, 15), B("rcv", rs + 5, rs + 20), B("rcv", rs + 25, rs + 40), A.min)
 
+    def rows(s0, s1):
+        if s1 > s0:
+            lin("cI%d" % s1, B("cI", 16 * s0, 16 * s1), B("R", 256 * s0 + 15, 256 * s1, 16))
+            ts(B("kI", 16 * s0, 16 * s1), B("cI", 16 * s0, 16 * s1), 12, A.arith_shift_right, 15, A.bitwise_and)
+            lin("kU%d" % s1, B("kU", 16 * s0, 16 * s1), B("kI", 16 * s0, 16 * s1), -1.0, 16.0)
+        for s in range(s1, s0, -1):
+            if s == 1 and now[0] < RACES - 1:
+                act(B("kF"), B("kI", 0, 16), bias=16.0, scale=-1.0)
+            else:
+                act(B("Bs", 240 * s - 240, 240 * s), IX(B("Wk"), B("kU", 16 * s - 16, 16 * s - 1)))
+
     def early(t):
         phase("early")
-        pc = CFG["cbank"]
-        group([(P(pc, 0, 6), B("idb"), B("cneg"))] + [(P(pc, 0, 6), B("Uh", 15 - c, 143 - c), B("zh", 768 + c, 2304, 16)) for c in range(16)], (1,))
-        tt(B("wz", 0, 48), B("C", 15, 768, 16), P(pc, 0, 3), A.mult)
+        pc = new()
+        group([(P(pc, 3, 6), B("Uh", 15 - c, 143 - c), B("zh", 1536 + c, 2304, 16)) for c in range(16)])
+        ts(B("cls", 0, 48), P(pc, 3, 6), B("thr", 0, 1), A.is_ge, -16.0 * BIG, A.mult)
         ts(B("nb", 0, 48), P(pc, 3, 6), B("thr", 0, 1), A.is_lt, BIG, A.mult)
+        tt(B("op2"), B("cls", 0, 16), B("cls", 16, 32), A.min)
+        tt(B("fl", 16 * t, 16 * t + 16), B("op2"), B("cls", 32, 48), A.min)
+        rs = 144 + 48 * t
+        send(B("fl", 16 * t, 16 * t + 15), [T.rcv[:, rs + 30 - 15 * j:rs + 45 - 15 * j] for j in range(3)], B("rcv", rs, rs + 48), "e%d" % t, "f%d" % t)
+        least("x3", rs)
+        phase("early2")
+        pc = new()
+        group([(P(pc, 0, 3), B("idb"), B("cneg", 0, 48))] + [(P(pc, 0, 3), B("Uh", 15 - c, 143 - c), B("zh", 768 + c, 1536, 16)) for c in range(16)], (1,))
+        tt(B("wz", 0, 48), B("C", 15, 768, 16), P(pc, 0, 3), A.mult)
         ts(B("u4", 0, 48), B("wz", 0, 48), 4095, A.bitwise_and)
         tt(B("d1", 0, 48), B("nb", 0, 48), B("base", 0, 48), A.add)
-        tt(B("c1", 0, 48), B("u4", 0, 48), B("d1", 0, 48), A.add)
-        tt(B("m1"), B("c1", 0, 16), B("c1", 16, 32), A.min)
-        m3 = B("m3", 16 * t, 16 * t + 16)
-        tt(m3, B("m1"), B("c1", 32, 48), A.min)
-        if CFG["early"]:
-            rs = 144 + 48 * t
-            send(B("m3", 16 * t, 16 * t + 15), [T.rcv[:, rs + 30 - 15 * j:rs + 45 - 15 * j] for j in range(3)], B("rcv", rs, rs + 48), "e%d" % t, "f%d" % t)
-            least("x3", rs)
-            ts(B("x3", 0, 15), B("x3", 0, 15), BIG, A.is_ge)
-        ts(B("op"), m3, BIG, A.is_ge)
-        ts(B("cls"), B("op"), B("thr", 1, 2), A.mult)
+        def cw(s0, s1, c0, c1):
+            return (T.cw[:, s0, c0:c1] if s1 == s0 + 1 else T.cw[:, s0:s1, c0:c1], [("cw", 32 * s + c0, 32 * s + c1) for s in range(s0, s1)], (s1 - s0) * (c1 - c0), 4, False, False, [])
+        tt(cw(0, 3, 0, 16), B("u4", 0, 48), B("d1", 0, 48), A.add)
+        tt(cw(0, 3, 16, 32), B("C", 15, 768, 16), B("d1", 0, 48), A.add)
+        tt(B("m1"), cw(0, 1, 0, 32), cw(1, 2, 0, 32), A.min)
+        m3 = B("m3", 32 * t, 32 * t + 16)
+        tt(B("m3", 32 * t, 32 * t + 32), B("m1"), cw(2, 3, 0, 32), A.min)
+        ts(B("op"), B("fl", 16 * t, 16 * t + 16), 0.0, A.is_ge)
         tt(B("g0"), m3, B("base", 48, 64), A.min)
+        phase("masks")
+        rows(0, CFG["ke"])
         phase("pairs")
-        ts(B("kcol", 16, 64), B("C", 15, 768, 16), -2048.0, A.add)
         act(B("v16", 16, 64), B("C", 15, 768, 16), bias=-2048.0)
         for s in (4, 3, 2):
-            act(B("val", 240 * s - 240, 240 * s), IX(B("iw", 0, V), vU(t, s - 1)), bias=-2048.0)
-            n = CFG["spairs"].get(s, 0)
-            if n:
+            phase("pairs%d" % s)
+            lin("kc%d" % s, B("kcol", 16 * s - 16, 16 * s), B("C", 256 * s - 512 + 15, 256 * s - 256, 16), 1.0, -2048.0)
+            for a0, a1 in CFG["vparts"].get(s, ((0, 15),)):
+                act(B("val", 240 * s - 240 + 16 * a0, 240 * s - 240 + 16 * a1), IX(B("iw", 0, V), vU(t, s - 1, a0, a1)), bias=-2048.0)
+            n = CFG["spairs"].get(s, 15)
+            if n < 15:
                 act(B("nk", 16 * s - 16, 16 * s), B("C", 256 * s - 512 + 15, 256 * s - 256, 16), bias=2048.0, scale=-1.0)
             spairs(1920 * (s - 1), ("val", 240 * s - 240), ("nk", 16 * s - 16), n)
             pairs("eqm", 1920 * (s - 1), 240 * s - 240, ("kcol", 16 * s - 16), n)
@@ -716,51 +1327,56 @@ def rank_program(g, core, T, topo):
         phase("own")
         own = B("own", 16 * t, 16 * t + 16)
         tt(B("wf"), B("C", 768 + 15, 1024, 16), B("op"), A.mult)
-        rk, short = B("rk", 16 * t, 16 * t + 16), P("pc", 9, 10)
-        group([(short, B("idb"), B("cls"))] + [(short, B("Un", 15 - c, 143 - c), B("gt4", c, 256, 16)) for c in range(16)], (1,))
+        rk, short = B("rk", 16 * t, 16 * t + 16), P(new(), 0, 1)
+        group([(short, B("idb"), B("cls", 16 * s, 16 * s + 16)) for s in (3, 0, 1, 2)] + [(short, B("Un", 15 - c, 143 - c), B("gt4", c, 256, 16)) for c in range(16)], (4,))
         tt(rk, short, B("g0"), A.max)
         rs = 48 * t
         send(B("rk", 16 * t, 16 * t + 15), [T.rcv[:, rs + 30 - 15 * j:rs + 45 - 15 * j] for j in range(3)], B("rcv", rs, rs + 48), "a%d" % t, "l%d" % t)
         phase("ownu")
         ts(B("nb", 48, 64), short, 0.0, A.is_gt, 16 * BIG, A.mult)
-        group([(P("pz", 8, 9), B("idb"), B("cneg", 0, 16))] + [(P("pz", 8, 9), B("Uh", 15 - c, 143 - c), B("zh", 256 + c, 512, 16)) for c in range(16)], (1,))
-        tt(B("wz", 48, 64), B("wf"), P("pz", 8, 9), A.mult)
+        pa = P(new(), 0, 1)
+        group([(pa, B("idb"), B("cneg", 0, 16))] + [(pa, B("Uh", 15 - c, 143 - c), B("zh", 256 + c, 512, 16)) for c in range(16)], (1,))
+        tt(B("wz", 48, 64), B("wf"), pa, A.mult)
         ts(B("u4", 48, 64), B("wz", 48, 64), 4095, A.bitwise_and)
         tt(own, B("u4", 48, 64), rk, A.add)
         ru = 288 + 48 * t
         send(B("own", 16 * t, 16 * t + 15), [T.rcv[:, ru + 30 - 15 * j:ru + 45 - 15 * j] for j in range(3)], B("rcv", ru, ru + 48), "u%d" % t, "w%d" % t)
         phase("logs")
-        tt(B("w1"), B("C", 15, 1024, 16), B("bs"), A.add)
-        tt(B("w1"), B("w1"), B("nb"), A.add)
-        tt(B("d1", 0, 32), B("w1", 0, 32), B("w1", 32, 64), A.min)
-        tt(B("dI"), B("d1", 0, 16), B("d1", 16, 32), A.min)
+        act(B("w1", 0, 16), B("C", 768 + 15, 1024, 16), bias=16384.0 * S)
+        tt(B("dI"), B("m3", 32 * t + 16, 32 * t + 32), B("w1", 0, 16), A.min)
         ts(B("WI"), B("dI"), 4095, A.bitwise_and)
-        ts(B("bI"), B("dI"), 12, A.arith_shift_right, 7, A.bitwise_and)
-        cp(B("WU"), B("WI"))
-        ts(B("nW"), B("WI"), -1.0, A.mult)
-        ts(B("v16", 0, 16), B("WI"), -2048.0, A.add)
-        ts(B("bF"), B("bI"), 256.0, A.mult, -256.0, A.add)
-        tt(B("bF"), B("bF"), B("ln"), A.add)
-        cp(B("bU"), B("bF"))
-        cp(B("cI"), B("R", 15, 1024, 16))
-        ts(B("kI"), B("cI"), 12, A.arith_shift_right, 15, A.bitwise_and)
-        ts(B("kU"), B("kI"), -1.0, A.mult, 15.0, A.add)
-        phase("masks")
-        for s in range(S, 0, -1):
-            act(B("Bs", 240 * s - 240, 240 * s), IX(B("Wk"), B("kU", 16 * s - 16, 16 * s - 1)))
+        ts(B("bI"), B("dI"), 6, A.arith_shift_right, 1792, A.bitwise_and)
+        lin("WU", B("WU"), B("WI"))
+        lin("v16", B("v16", 0, 16), B("WI"), 1.0, -2048.0)
+        lin("nW", B("nW"), B("WI"), -1.0, 2048.0)
+        if CFG["wV"]:
+            lin("kcol", B("kcol", 0, 16), B("WI"), 1.0, -2048.0)
+        joint = t < RACES - 1
+        tt(B("bF" if joint else "bU"), B("bI"), B("ln"), A.add)
+        if joint:
+            act(B("WF"), B("WI"), bias=float(X0))
+        phase("masks4")
+        rows(CFG["ke"], S)
         phase("wpairs")
-        act(B("valf"), IX(B("iw", 0, V), B("WU", 0, 15)))
-        spairs(0, ("valf", 0), ("nW", 0), 15)
+        act(B("val", 0, 240), IX(B("iw", 0, V), B("WU", 0, 15)), bias=-2048.0)
+        spairs(0, ("val", 0), ("nW", 0), CFG["wV"])
+        pairs("eqm", 0, 0, ("kcol", 0), CFG["wV"])
         phase("cm")
-        tt(B("cm"), IX(KW, vU(t, S - 1)), B("Bs", 720, 960), A.mult)
+        pa = P(new(), 0, 15)
+        if CFG["quad"]:
+            group([(pa, B("ih"), Ke(0, 15, 0)), (pa, B("ih"), Ke(0, 15, 1)), (pa, B("idB"), B("Bs", 720, 960))], (2,))
+        else:
+            group([(pa, B("ih32"), B("kvh", 768, 1008)), (pa, B("idB"), B("Bs", 720, 960))], (1,))
+        act(B("cm"), pa, RELU, bias=2048.0)
+        act(B("b4"), B("C", 768 + 15, 1024, 16), bias=32.0 * S - 131072.0, scale=32.0)
         phase("xnew")
-        act(B("xW"), IX(XW, B("WU", 0, 15)))
-        act(B("zg", 0, 768), B("zh", 768, 1536), bias=-1024.0)
-        act(B("zg", 768, 1024), B("zh", 256, 512), bias=-1024.0)
-        act(B("zW"), IX(B("zg"), B("bU", 0, 15)))
-        group([(P("pc", 16, 31), B("idb"), B("xW")), (P("pc", 16, 31), B("idb"), B("zW"))])
-        act(B("xr"), P("pc", 16, 31), bias=1023.75, scale=0.5)
-        act(B("xn"), B("xr"), bias=-1024.0)
+        if not joint:
+            act(B("xW"), IX(XW, B("WU", 0, 15)))
+            act(B("zW"), IX(B("zg"), B("bU", 0, 15)))
+            pa = P(new(), 0, 15)
+            group([(pa, B("idb"), B("xW")), (pa, B("ih"), B("zW"))])
+            act(B("xr"), pa, bias=511.75, scale=0.5)
+            act(B("xn"), B("xr"), bias=-1024.0)
         if t + 1 < RACES:
             phase("zinit")
             zinit(t + 1)
@@ -770,7 +1386,7 @@ def rank_program(g, core, T, topo):
         ts(ow, B("rk", 16 * t, 16 * t + 15), BIG, A.min)
         tt(ow2, B("rk", 16 * t, 16 * t + 15), B("nb", 48, 63), A.add)
         if CFG["early"]:
-            tt(B("ow4", 0, 15), ow, B("x3", 0, 15), A.mult)
+            tt(B("ow4", 0, 15), ow, B("x3", 0, 15), A.add)
             act(B("owE"), IX(B("ow4"), B("w8l")))
         phase("win")
         least("x", rs)
@@ -786,23 +1402,34 @@ def rank_program(g, core, T, topo):
         phase("winu")
         least("xu", ru)
         ts(B("uI", 0, 15), B("xu", 0, 15), 4095, A.bitwise_and)
-        cp(B("uU", 0, 15), B("uI", 0, 15))
+        lin("uU", B("uU", 0, 15), B("uI", 0, 15))
         phase("win2")
         tt(B("xy", 0, 15), x, on(0), A.mult)
         for s in (3, 2):
             ts(on(s - 1), B("xy", 0, 15), 16384.0 * s, A.is_ge)
         tt(on(4), ow2, x, A.is_lt)
+        if joint:
+            phase("joint")
+            tt(B("nw", 0, 15), ow2, x, A.is_ge)
+            tt(B("kU", 0, 15), B("kF", 0, 15), B("nw", 0, 15), A.mult)
+            act(B("Bs", 0, 240), IX(B("Wk"), B("kU", 0, 15)))
+            tt(B("bU", 0, 15), B("bF", 0, 15), on(4), A.mult)
+            act(B("zW"), IX(B("zg"), B("bU", 0, 15)))
+            tt(B("XU", 0, 15), B("WF", 0, 15), on(4), A.mult)
+            act(B("xW"), IX(B("kw", 0, K0), B("XU", 0, 15)))
+            tt(B("bF", 0, 15), B("v1K", 16 * t, 16 * t + 15), B("nw", 0, 15), A.mult)
+            tt(B("GU", 0, 15), B("bF", 0, 15), B("XU", 0, 15), A.add)
         phase("xs")
         act(B("urep"), IX(B("iw", 0, V), B("uU", 0, 15)), bias=-2048.0)
         for s in (3, 2, 1):
-            pa = P("pa%d" % (s % 2), 0, 15)
-            group([(pa, B("idM"), B("Bs", 240 * s - 240, 240 * s)), (pa, B("ihd"), B("urep"))], (1,))
-            act(B("xs", 240 * s - 240, 240 * s), pa, RELU, bias=64.0 - 256.0)
+            pa = P(new(), 0, 15)
+            group([(pa, B("idM"), B("Bs", 240 * s - 240, 240 * s)), (pa, B("ih"), B("urep"))], (1,))
+            act(B("xs", 240 * s - 240, 240 * s), pa, RELU, bias=2048.0 - 8192.0)
 
         def event(e):
             phase("ev%d" % e)
             nev[0] += 1
-            p1, o = "pb%d" % (nev[0] % 2), 128 * e
+            p1, o = new(), 128 * e
             src, r = ("eq1", 1920 * t) if e == 0 else ("eqm", 1920 * (e % 4))
             lst = IX(B("on", 16 * e, 16 * e + 16), B("w8l"))
             if e == S - 1 and CFG["early"]:
@@ -819,74 +1446,97 @@ def rank_program(g, core, T, topo):
             group(terms, (1,))
             act(B("cs", 256 * slot[e], 256 * slot[e] + 240, p=8), P(p1, 0, 15, p=8), SIGN)
 
-        slot = {e: i for i, e in enumerate(e for batch in CFG["batches"] for e in batch)}
-        for batch in CFG["batches"]:
+        batches = CFG["jbatches" if joint else "batches"]
+        slot = {e: i for i, e in enumerate(e for batch in batches for e in batch)}
+        for batch in batches:
             for e in batch:
                 event(e)
             phase("of%d" % batch[0])
             n, q = len(batch), slot[batch[0]]
-            out = P("pb2", 0, n, c=15)
-            terms = [(out, B("idb"), B("cneg", 48, 47 + 16 * n))] * (n > 1)
+            c0 = 15 if n == 1 else 16
+            pb = new()
+            out = P(pb, 0, n, c=c0)
+            both = joint and batch == (0, 4)
+            terms = [(out, B("idb"), B("cneg", 96, 128) if both else B("cneg", 48, 32 + 16 * n + c0))]
             for i, e in enumerate(batch):
                 vh = B("v1h", 16 * t, 16 * t + 15) if e == 0 else B("v16", 16 * (e % 4), 16 * (e % 4) + 15)
-                terms += [(P("pb2", i, i + 1, c=15), B("ih"), vh), (P("pb2", i, i + 1, c=15), B("idB"), on(e))]
-            group(terms + [(out, B("Us", 15 - c, 143 - c, p=8), B("cs", 256 * q + c, 256 * (q + n) - 16, 16, p=8)) for c in range(16)], (len(terms),))
-            tt(B("of", 16 * q, 16 * (q + n) - 1), out, B("Dm", 0, 16 * n - 1), A.min)
-            ts(B("offU", 16 * q, 16 * (q + n) - 1), B("of", 16 * q, 16 * (q + n) - 1), 26624.0, A.add)
+                terms += [(P(pb, i, i + 1, c=15), B("ih"), vh), (P(pb, i, i + 1, c=15), B("idB"), on(e))]
+            group(terms + [(out, B("Us", 15 - c, 143 - c, p=8), B("cs", 256 * q + c, 256 * (q + n) - 256 + 16 * c0, 16, p=8)) for c in range(16)], (len(terms),))
+            e = 16 * (q + n) - 16 + c0
+            if both:
+                tt(B("of", 0, 15), P(pb, 0, 1, c=15), B("DJ", 0, 15), A.min)
+                tt(B("offU", 16 * q, 16 * q + 15), P(pb, 1, 2, c=15), B("of", 0, 15), A.min)
+            else:
+                tt(B("offU", 16 * q, e), out, B("Dm", 0, e - 16 * q), A.min)
 
         def write(win, src, e):
             for a0, a1 in CFG["xparts"] if e == 4 else ((0, 15),):
-                cp(IX(B(win), B("offU", 16 * slot[e] + a0, 16 * slot[e] + a1)), B(src, 16 * a0, 16 * a1))
+                cp(IX(win, B("offU", 16 * slot[e] + a0, 16 * slot[e] + a1)), B(src, 16 * a0, 16 * a1))
 
-        for s in range(S, 0, -1):
+        phase("st4")
+        tt(B("p4", 0, 15), B("C", 768 + 15, 1008, 16), B("uI", 0, 15), A.mult)
+        tt(B("nI", 0, 15), B("p4", 0, 15), B("b4", 0, 15), A.add)
+        ts(B("nI", 16, 31), B("nI", 0, 15), 5, A.arith_shift_right, 4095, A.bitwise_and)
+        lin("nU", B("nU", 0, 15), B("nI", 16, 31))
+        tt(B("kp"), IX(B("iw"), B("nU", 0, 15)), B("Bs", 720, 960), A.mult)
+        tt(IX(B("kw", K0), B("offU", 16 * slot[S - 1], 16 * slot[S - 1] + 15)), B("kp"), B("cm"), A.add)
+        for s in range(S - 1, 0, -1):
             phase("st%d" % s)
             r = 240 * s - 240
-            for a0, a1, bank in ((8, 15, "pb3"), (0, 8, "pz")):
-                lo, hi, pz = 16 * a0, 16 * a1, P(bank, a0, a1)
-                lst = IX(KW, vU(t, s - 1, a0, a1))
-                kt = B("kvh", 768 + lo, 768 + hi) if s == S else B("kt", lo, hi)
-                group([(pz, B("ih32"), B("m2k", lo, hi)), (pz, B("idS", 128 * s - 128, 128 * s), B("Bs", r + lo, r + hi))], stop=False)
-                if s < S:
-                    if a0 == 0 and s in CFG["ktv"]:
-                        ts(kt, lst, 1.0 / 32.0, A.mult, -2048.0, A.add)
-                    else:
-                        act(kt, lst, bias=-2048.0, scale=1.0 / 32.0)
-                    tt(B("kp", lo, hi), lst, B("xs", r + lo, r + hi), A.mult)
+            for a0, a1, onv in CFG["kparts"]:
+                lo, hi, pz = 16 * a0, 16 * a1, P(new(), a0, a1)
+                both = joint and s == 1
+                lst = IX(B("kw", 0, K0 + V), B("GU", a0, a1)) if both else IX(KW, vU(t, s - 1, a0, a1))
+                kt = B("kt", lo, hi)
+                group([(pz, B("ih32"), B("m2k", 240 * both + lo, 240 * both + hi)), (pz, B("idS", 128 * s - 128, 128 * s), B("Bs", r + lo, r + hi))]
+                      + [(pz, B("ihd"), B("zW", lo, hi)), (pz, B("idX"), B("xW", lo, hi))] * both, stop=False)
+                if onv:
+                    ts(kt, lst, -2048.0, A.add)
                 else:
-                    tt(B("kp", lo, hi), IX(B("iw"), B("uU", a0, a1)), B("cm", lo, hi), A.mult)
+                    act(kt, lst, bias=-2048.0)
+                tt(B("kp", lo, hi), lst, B("xs", r + lo, r + hi), A.mult)
                 group([(pz, B("ih32"), kt)], start=False)
                 tt(B("kz", lo, hi), B("kp", lo, hi), pz, A.add)
-                ts(B("kn", lo, hi), B("kz", lo, hi), 131040, A.bitwise_and)
-            write("kw", "kn", s - 1)
-        write("xw", "xn", 4)
+                ts(B("kn", lo, hi), B("kz", lo, hi), 5, A.arith_shift_right, 4095, A.bitwise_and)
+            write(B("kw") if joint and s == 1 else B("kw", K0), "kn", s - 1)
+        if not joint:
+            phase("xout")
+            write(B("xw"), "xn", 4)
         if t + 1 < RACES:
             phase("thr")
-            group([(P("pc", 12, 13, c=15), B("ones"), on(4))])
-            op("V", lambda e: e.tensor_reduce(B("tot")[0], T.pc[:, 192:207], AxisListType.X, A.add), B("tot"), [P("pc", 12, 13, c=15)])
-            cp(B("totI"), B("tot"))
-            ts(B("totI"), B("totI"), 1, A.bitwise_and)
-            ts(B("thr", 0, 1), B("totI"), 2.0, A.mult, 8.0, A.add)
-            ts(B("thr", 1, 2), B("totI"), 12.0, A.add, BIG, A.mult)
+            pa = P(new(), 0, 1, c=15)
+            group([(pa, B("ones"), on(4))])
+            op("S", lambda e: e.activation(B("tot", 1, 16)[0], pa[0], ID, accum_out=B("tot", 0, 1)[0]), B("tot"), [pa], dur=(20, 64, 0, 0, 0))
+            act(B("toth"), B("tot", 0, 1), bias=1023.75, scale=0.5)
+            act(B("tot", 1, 2), B("tot", 0, 1), bias=4104.0, scale=2.0)
+            act(B("thr", 0, 1), B("toth"), bias=B("tot", 1, 2), scale=-4.0)
+            act(B("thr", 1, 2), B("thr", 0, 1), bias=8.0 * BIG, scale=BIG / 2)
+            act(B("cls", 48, 64), B("ones", 0, 16), scale=B("thr", 1, 2))
 
     phase("start1")
-    ms(B("m2k"), -2048.0)
+    ms(B("m2k", 0, 240), -2048.0)
+    ms(B("m2k", 240, 480), -2560.0)
     phase("start0")
     zinit(0)
     for t in range(RACES):
         race(t)
     now[0] = -1
     phase("out")
-    group([(P("pa0", 0, 32), B("idx", 128 * a, 128 * a + 128), B("xw", 512 * a, 512 * a + 512)) for a in range(8)])
-    act(B("ox"), P("pa0", 0, 32))
+    for a in range(8):
+        act(B("idx", 128 * a, 128 * a + 128), B("idb"), scale=float(a + 1))
+        act(B("idk", 128 * a, 128 * a + 128), B("idb"), scale=float(a + 1))
+    pa = P(new(), 0, 32)
+    group([(pa, B("idx", 128 * a, 128 * a + 128), B("xw", 512 * a, 512 * a + 512)) for a in range(8)])
+    act(B("ox"), pa)
     dma("Y", "oy", T.yx[:], T.ox[:], [("ox", 0, 512)], [], 2000.0)
     for h in range(2):
         for a in range(8):
             o = 512 * a + 256 * h
             if a % 2:
-                act(B("shp", o, o + 256), B("kw", o, o + 256), bias=-2048.0, scale=1.0 / 32.0)
+                act(B("shp", o, o + 256), B("kw", K0 + o, K0 + o + 256), bias=-2048.0)
             else:
-                ts(B("shp", o, o + 256), B("kw", o, o + 256), 1.0 / 32.0, A.mult, -2048.0, A.add)
-        pb = P("pb%d" % h, 0, 16)
+                ts(B("shp", o, o + 256), B("kw", K0 + o, K0 + o + 256), -2048.0, A.add)
+        pb = P(new(), 0, 16)
         group([(pb, B("idk", 128 * a, 128 * a + 128), B("shp", 512 * a + 256 * h, 512 * a + 256 * h + 256)) for a in range(8)], (2, 4, 6))
         if h:
             ts(B("ok", 256, 512), pb, 36.0 * 2048.0, A.add)

@@ -11,38 +11,41 @@ L = J * M
 WIN = V + 256
 X0, K0 = 128, 128 + V
 BIG = 2.0 ** 19
+LAST = 2 ** 18 + 3 * 4096
 CFG = {
     "groups": ((0, 4, "V"), (4, 8, "S"), (8, 12, "V"), (12, 15, "S")),
-    "polish": (6000, 12000, 20000, 8000, 18000, 38000, 8000), "period": 7400.0, "heatc": 1500.0, "alap": 1200.0, "spare": 1, "binds": 12, "heat5": 500.0, "tries": (10, 1), "heat0": 1200.0, "heat4": 1000.0, "since": 0.0, "heat1": 150.0, "turns": 10, "heat2": 500.0, "heat3": 400.0, "any": 0.05, "far": 12, "hope": 30.0,
+    "polish": (3000, 12000, 12000, 4000, 9000, 19200, 8000, 20000), "seeds": ((3,), (4,), (1, 3)), "heat6": 300.0, "period": 7400.0, "heatc": 1500.0, "alap": 1200.0, "spare": 1, "binds": 8, "heat5": 500.0, "tries": (4, 1), "heat0": 1200.0, "heat4": 1000.0, "since": 0.0, "heat1": 150.0, "turns": 6, "heat2": 500.0, "heat3": 400.0, "any": 0.05, "far": 12, "hope": 30.0,
     "zbank": ("pb3", "pb3", "pb3"), "tbank": ("pc", "pc", "pc"), "sbank": ("pb3", "pb3", "pb3"),
-    "eqs": 0, "vparts": {}, "onS": ("kU4", "WU", "v16", "nW", "kcol", "uU", "cI4"), "quad": True, "khs": (), "ksc": (3,), "kload": ((0, 1024), (1024, 2560), (2560, 4096)), "xload": ((0, 2048), (2048, 4096)), "jbatches": ((3,), (2,), (1,), (0, 4)), "wV": 5, "apart": (), "kparts": ((10, 15, 0), (4, 10, 0), (0, 4, 1)), "half": (), "w0": 0, "kvv": (), "ke": 3, "xh": (), "gsp": 0, "wS": 6, "z4s": (0,),
-    "kbank": ("pb0", "pz", "pb2"), "inorder": False, "d1v": (), "flight": 2, "first": 7000.0, "piece": 2300.0, "ktv": (1, 2, 3), "abank": ("pa0", "pa1"), "batches": ((3,), (2,), (1, 4), (0,)), "spairs": {2: 11}, "gzx": True, "teams": ((0, 1), (2,), (3,)), "zv4": (0, 1, 2, 3), "cbank": "pc", "cbank2": "pc", "push": 2500.0, "early": True, "xparts": ((0, 4), (4, 8), (8, 12), (12, 15)),
+    "xcols": {0: (1, 1, 1, 1), 2: (1, 1, 1, 1)}, "eqs": 0, "vparts": {}, "onS": ("kU4", "WU", "GF", "nG", "uU", "cI4", "op", "nx"), "quad": True, "khs": (), "ksc": (3,), "kload": ((0, 1024), (1024, 2560), (2560, 4096)), "xload": ((0, 2048), (2048, 4096)), "jbatches": ((3,), (2,), (1,), (0, 4)), "wV": 5, "apart": (), "kparts": ((10, 15, 0), (4, 10, 0), (0, 4, 1)), "half": (), "w0": 0, "kvv": (), "ke": 3, "xh": (), "gsp": {0: ((2, 8),), 2: ((2, 8),)}, "sgv": (3,), "emerge": True, "apart2": None, "osplit": ((0, 352), (352, 512)), "iws": 256, "xblocks": 8, "ztr": (), "gap": (), "rv": (), "z3g": True, "d1T": True, "w54": True, "sg": (1, 2), "kfirst": True, "kwid": 2, "wS": 6, "z4s": (0,),
+    "kbank": ("pb0", "pz", "pb2"), "inorder": False, "d1v": (), "flight": 2, "first": 7000.0, "piece": 2300.0, "ktv": (1, 2, 3), "abank": ("pa0", "pa1"), "batches": ((3,), (2,), (1, 4), (0,)), "spairs": {2: 11}, "gzx": True, "teams": ((0, 1), (2,), (3,)), "zv4": (0, 1, 2, 3), "cbank": "pc", "cbank2": "pc", "push": 2500.0, "early": False, "xparts": ((0, 4), (4, 8), (8, 12), (12, 15)),
     "zv": (0, 2), "kv": ((1, 1), (2, 1), (3, 1)), "w8v": (3,), "wpos": 3, "run": 512.0, "zfirst": (1, 1), "dif": (0, 1, 2),
-    "bias": {}, "rounds": 60, "rounds2": 5, "lead": 13000.0, "heat": 150.0, "swap": 0.5, "rounds0": 0, "fb": 2, "parts": 0.3, "scols": 2, "seed": 52, "span": 4000.0, "shake": 1500.0,
+    "bias": {}, "rounds": 40, "rounds2": 5, "lead": 13000.0, "heat": 150.0, "swap": 0.5, "rounds0": 0, "fb": 2, "parts": 0.3, "scols": 2, "seed": 52, "span": 4000.0, "shake": 1500.0,
     "cyc": 1.05, "lat": 220.0, "gam": 1.85, "sig": 4.3, "pe": 0.52, "rem": 0.9,
-    "others": ({"weight": 1.1, "cyc": 0.85, "lat": 200.0, "gam": 1.5, "sig": 3.5, "pe": 0.45, "rem": 1.2},
-               {"weight": 0.6, "cyc": 1.22, "lat": 270.0, "gam": 1.7, "sig": 5.4, "pe": 0.62, "rem": 0.8},
-               {"weight": 1.1, "cyc": 1.24, "lat": 190.0, "gam": 2.05, "sig": 4.0, "pe": 0.58, "rem": 1.5}),
+    "others": ({"weight": 1.0, "cyc": 0.85, "lat": 180.0, "gam": 1.5, "sig": 3.5, "pe": 0.47, "rem": 1.2},
+               {"weight": 0.8, "cyc": 0.83, "lat": 250.0, "gam": 1.6, "sig": 3.8, "pe": 0.42, "rem": 0.6, "land": 1.1, "gx": 120.0},
+               {"weight": 1.0, "cyc": 1.23, "lat": 230.0, "gam": 1.9, "sig": 4.6, "pe": 0.6, "rem": 1.1}),
 }
+CFG.update({"seeds": ((6,), (1, 2, 3), (1, 2, 3)), "kfirst": True, "kwid": 2, "early": True, "iws": 256, "g1": 3500.0, "first": 5500.0})
+CFG["others"] += ({"weight": 0.9, "cyc": 1.15, "lat": 220.0, "gam": 1.15, "sig": 2.5, "pe": 0.6, "rem": 1.0},)
 PLAN = {}
 
 SCRATCH = {}
 PIECE = {}
 for _d, _l in (
-        ("bfloat16", (("xw", WIN), ("zx", 4096), ("xq", 1024), ("d0", 512), ("E", 2048), ("csu", 128), ("xg0", 512), ("xg1", 512), ("xg2", 512),
-                      ("zs", 240), ("zl", 720), ("zc", 720), ("on", 80), ("eq1", 5760), ("eqm", 7680), ("W8", 640), ("cs", 1280),
+        ("bfloat16", (("xw", WIN), ("ry", 512), ("xq", 1024), ("d0", 512), ("E", 1024), ("bsb", 96), ("cn2", 96), ("xg0", 512), ("xg1", 512), ("xm", 512),
+                      ("zs", 240), ("zl", 720), ("zc", 720), ("on", 96), ("W8", 640), ("cs", 320),
                       ("Bs", 960), ("xW", 240), ("xn", 240), ("idb", 128), ("idn", 128), ("idB", 128), ("idM", 128), ("idX", 128), ("idS", 512),
-                      ("U", 144), ("U1", 144), ("Us", 144), ("kc", 128), ("rm", 256), ("rz", 256), ("cst", 128), ("cneg", 128), ("cls", 64), ("gt4", 256), ("Un", 144), ("z3", 256), ("Wk", 32),
-                      ("thw", 240), ("idx", 1024), ("ones", 128))),
-        ("float16", (("shp", 4096), ("zh", 2304), ("ih2", 128), ("Dif", 16), ("ih", 128), ("ihn", 128), ("ih32", 128), ("ihd", 128),
-                     ("Uh", 144), ("zT", 768), ("En", 2048), ("zW", 240), ("toth", 1), ("val", 1680), ("v16", 80), ("v1h", 48), ("urep", 240), ("kt", 240), ("m2k", 480), ("zt", 1024), ("xr", 240), ("idk", 1024))),
-        ("float32", (("kw", K0 + WIN), ("iw", V), ("R", 1024), ("C", 1024), ("nb", 64), ("kcol", 64), ("nk", 64), ("k1c", 48), ("nW", 16), ("valf", 240),
+                      ("U", 144), ("U1", 144), ("Us", 144), ("rm", 128), ("rz", 256), ("cneg", 128), ("cls", 64), ("gt4", 256), ("Un", 144), ("z3", 256), ("Wk", 32),
+                      ("thw", 64), ("idx", 1024), ("ones", 128))),
+        ("float16", (("zh", 2304), ("ih2", 128), ("Dif", 48), ("ih", 128), ("ihn", 128), ("ih32", 128), ("ihd", 128),
+                     ("Uh", 144), ("zT", 768), ("En", 1024), ("zW", 240), ("toth", 1), ("val", 960), ("v16", 80), ("urep", 240), ("kt", 240), ("m2k", 480), ("zt", 1024), ("xr", 240), ("idk", 1024))),
+        ("float32", (("kw", K0 + WIN), ("iw", K0 + V), ("idf", 128), ("R", 1024), ("C", 1024), ("nb", 64), ("kcol", 64), ("nk", 64), ("GF", 16), ("nG", 16), ("th4", 16), ("valf", 64), ("kq", 64),
                      ("xs", 960), ("kp", 240), ("of", 80), ("Dm", 64), ("base", 64), ("bs", 64), ("ln", 16), ("bF", 16), ("ge", 16), ("xy", 16),
-                     ("d1", 64), ("w1", 64), ("tot", 16), ("zg", 1040), ("DJ", 16), ("v1K", 48), ("WF", 16), ("kF", 16), ("nw", 16), ("b4", 16), ("p4", 16), ("thr", 2), ("wt", 32), ("cm", 240), ("x3", 16), ("op", 16), ("op2", 16), ("g0", 16), ("wf", 16), ("ow1", 16), ("ow2", 16), ("ow4", 16), ("owE", 128), ("pF", 24), ("ox", 512), ("ok", 512), ("t8", 8))),
+                     ("d1", 64), ("w1", 64), ("tot", 16), ("zg", 1040), ("DJ", 16), ("v1K", 48), ("WF", 16), ("kF", 16), ("nw", 16), ("c4", 48), ("thr", 2), ("wt", 32), ("cm", 240), ("x3", 16), ("op", 16), ("op2", 16), ("g0", 16), ("wf", 16), ("ow1", 16), ("ow2", 16), ("ow4", 16), ("owE", 128), ("pF", 32), ("ox", 512), ("ok", 512), ("t8", 8))),
         ("int32", (("kin", V), ("vs", 45), ("vl", 135), ("vI", 48), ("wz", 64), ("u4", 64), ("m1", 32), ("m3", 96), ("fl", 48), ("own", 48),
-                   ("rcv", 432), ("rk", 48), ("xu", 16), ("x", 16), ("uI", 16), ("dI", 16), ("WI", 16), ("bI", 16), ("cI", 64), ("kI", 64), ("kz", 240), ("kn", 240),
-                   ("nI", 32), ("pI", 12))),
-        ("uint16", (("kvu", 256), ("vU", 240), ("kU", 64), ("WU", 16), ("bU", 16), ("uU", 16), ("nU", 16), ("XU", 16), ("GU", 16), ("offU", 80), ("w8l", 8)))):
+                   ("rcv", 432), ("rk", 48), ("xu", 16), ("x", 16), ("y", 16), ("uI", 16), ("dI", 16), ("WI", 16), ("bI", 16), ("cI", 64), ("kI", 64), ("kz", 240), ("kn", 240),
+                   ("nI", 64), ("ub", 48), ("pI", 16))),
+        ("uint16", (("kvu", 256), ("valu", 1200), ("vU", 240), ("kU", 64), ("WU", 16), ("bU", 16), ("uU", 16), ("nU", 16), ("XU", 16), ("GU", 16), ("offU", 80), ("w8l", 8)))):
     for _n, _w in _l:
         if _d == "float32" and _w <= 64:
             PIECE[_n] = ("small", 64 * len(PIECE), _w)
@@ -53,10 +56,13 @@ SCRATCH["Y"] = ("sbuf", [128, 16, 256], "bfloat16")
 BANKS = ["ps%d" % _n for _n in range(8)]
 for _n in BANKS:
     SCRATCH[_n] = ("psum", [128, 512], "float32")
-SCRATCH["zy"] = ("sbuf", [128, 256, 16], "bfloat16")
+SCRATCH["eqm"] = ("sbuf", [128, 600, 16], "bfloat16")
+SCRATCH["zx"] = ("sbuf", [128, 4096], "bfloat16")
+SCRATCH["shp"] = ("sbuf", [128, 4096], "float16")
 SCRATCH["cw"] = ("sbuf", [128, 3, 32], "float32")
 SCRATCH["Ys"] = ("sbuf", [128, 256, 16], "bfloat16")
 SCRATCH["kE"] = ("sbuf", [128, 16, 32], "float16")
+SCRATCH["kG"] = ("sbuf", [128, 16, 48], "float16")
 SEMAPHORES = ["qV", "qS", "qT", "qG", "zin", "vin", "ld0", "ld1", "ld2", "ld3", "ld4", "ld5", "az", "av", "a0", "a1", "a2",
               "lz", "lv", "l0", "l1", "l2", "oy", "ok0", "ok1", "e0", "e1", "e2", "f0", "f1", "f2", "u0", "u1", "u2", "w0", "w1", "w2"]
 
@@ -68,7 +74,7 @@ def planner(g, T, late_bound):
     bias = [0.0, (-1, ""), 0]
 
     def cost(p, m):
-        return p[0] + m["cyc"] * (p[1] + m["gam"] * p[2] + m["sig"] * p[3]) + m["pe"] * p[4] + m["rem"] * sum(p[5:])
+        return p[0] + m["cyc"] * (p[1] + m["gam"] * p[2] + m["sig"] * p[3]) + m["pe"] * p[4] + m["rem"] * sum(p[5:6]) + m.get("land", m["rem"]) * sum(p[6:7]) + m.get("gx", 0.0) * sum(p[7:])
 
     def is_psum(b):
         return b[0] == "@"
@@ -615,48 +621,55 @@ def planner(g, T, late_bound):
                     g[i] = max([g[k] + o[k] + (lat if x == CFG["lat"] else x) for k, x in succ[i] if k in inside and k not in need] + [0.0])
                 rest.append(g)
             score = lambda e: sum(w[0] * x for w, x in zip(models, e[1]))
-            tried = []
-            for _ in range(CFG["tries"][0]):
-                one = improve(sorted(need), {i: -prio[i] for i in range(n)}, CFG["rounds"])[1]
-                tried.append(better(sorted(need, key=lambda i: (one[i], i)), CFG["polish"][3], CFG["heat0"], lambda j, i: rest[j][i]))
-            PLAN["tried"] = [round(score(e)) for e in tried]
-            first, PLAN["first"] = better(min(tried, key=score)[0], CFG["polish"][3], CFG["heat2"], lambda j, i: rest[j][i])
-            one = place(first + sorted(inside - need, key=lambda i: (-near[i], i)), {i: [e for e in pred[i] if e[0] in inside] for i in race[1]})[0]
-            mid = sorted(race[1], key=lambda i: (one[i], i))
 
-            def like(t):
+            def like(mid, t):
                 rank = {ops[i]["id"][1:]: k for k, i in enumerate(mid)}
                 key = {}
                 for i in race[t]:
                     key[i] = max([rank.get(ops[i]["id"][1:], 0)] + [key[d] + 1e-3 for d, x in pred[i] if d in key])
                 return sorted(race[t], key=lambda i: (key[i], i))
-            after = follow(mid, like(2))
-            tried = [polish(mid, CFG["polish"][4], CFG["heat4"], lambda j, i: after(j, i) + push[i], CFG["since"]) for _ in range(CFG["tries"][1])]
-            PLAN["second"] = [round(score(e)) for e in tried]
-            mid = min(tried, key=score)[0]
-            mid, PLAN["free"] = better(mid, CFG["polish"][0], CFG["heat1"], after)
-            mid, lists = banks(mid, CFG["alap"], CFG["spare"])
-            best, PLAN["log"] = None, []
-            for r in range(CFG["binds"]):
-                e = better(mid, CFG["polish"][5] // CFG["binds"], CFG["heat5"] * (1.0 - r / CFG["binds"]), after, 2)
-                PLAN["log"].append(round(score(e)))
-                if best is None or score(e) < score(best[0]):
-                    best = (e, lists)
-                mid, lists = banks(e[0], None, 0)
-            (mid, PLAN["one"]), lists = best
+
+            def rebind(seq, lists, rounds, heat, after):
+                best = None
+                for r in range(CFG["binds"]):
+                    e = better(seq, rounds // CFG["binds"], heat * (1.0 - r / CFG["binds"]), after(r), 2)
+                    if best is None or score(e) < score(best[0]):
+                        best = (e, lists)
+                    seq, lists = banks(e[0], None, 0)
+                return best
+            found = []
+            for seed[0] in CFG["seeds"][0]:
+                bind({})
+                tried = []
+                for _ in range(CFG["tries"][0]):
+                    one = improve(sorted(need), {i: -prio[i] for i in range(n)}, CFG["rounds"])[1]
+                    tried.append(better(sorted(need, key=lambda i: (one[i], i)), CFG["polish"][3], CFG["heat0"], lambda j, i: rest[j][i]))
+                first, PLAN["first"] = better(min(tried, key=score)[0], CFG["polish"][3], CFG["heat2"], lambda j, i: rest[j][i])
+                one = place(first + sorted(inside - need, key=lambda i: (-near[i], i)), {i: [e for e in pred[i] if e[0] in inside] for i in race[1]})[0]
+                mid = sorted(race[1], key=lambda i: (one[i], i))
+                after = follow(mid, like(mid, 2))
+                mid = polish(mid, CFG["polish"][4], CFG["heat4"], lambda j, i: after(j, i) + push[i], CFG["since"])[0]
+                mid, PLAN["free"] = better(mid, CFG["polish"][0], CFG["heat1"], after)
+                mid, lists = banks(mid, CFG["alap"], CFG["spare"])
+                found.append(rebind(mid, lists, CFG["polish"][5], CFG["heat5"], lambda r: after) + (after,))
+            PLAN["found"] = [[round(x) for x in e[0][1]] for e in found]
+            (mid, PLAN["one"]), lists, after = min(found, key=lambda e: score(e[0]))
+            if CFG["polish"][7]:
+                bind(lists)
+                (mid, PLAN["one"]), lists = min(((mid, PLAN["one"]), lists), rebind(mid, lists, CFG["polish"][7], CFG["heat6"], lambda r: after), key=lambda e: score(e[0]))
+            if CFG.get("stop1"):
+                raise ValueError("probe")
             begin = [i for i in range(n) if ops[i]["id"][0] < 0 and i < race[0][0]]
             close = [i for i in range(n) if ops[i]["id"][0] < 0 and i > race[2][0]]
             bind(lists)
             one = times(mid, -1)[0]
-            bind({})
-            tail, last = banks(like(2) + close, None, 1)
-            best = None
-            for r in range(CFG["binds"] // 2):
-                e = better(tail, CFG["polish"][2] // (CFG["binds"] // 2), CFG["heat5"] * (1.0 - 2 * r / CFG["binds"]), lambda j, i: push[i] * (r < 2), 2)
-                if best is None or score(e) < score(best[0]):
-                    best = (e, last)
-                tail, last = banks(e[0], None, 0)
-            (tail, PLAN["tail"]), last = best
+            found = []
+            for seed[0] in CFG["seeds"][1]:
+                bind({})
+                tail, last = banks(like(mid, 2) + close, None, 1)
+                found.append(rebind(tail, last, CFG["polish"][2], CFG["heat5"], lambda r: lambda j, i: push[i] * (r < 2)))
+            PLAN["tails"] = [[round(x) for x in e[0][1]] for e in found]
+            (tail, PLAN["tail"]), last = min(found, key=lambda e: score(e[0]))
             ident = {ops[e[0]]["id"]: u for u, e in members.items()}
             whole = {b: [ident[(0,) + ops[members[u][0]]["id"][1:]] for u in e] + e + last[b] for b, e in lists.items()}
             for b, u in zip(BANKS, [u for u, e in members.items() if e[0] in begin]):
@@ -667,8 +680,12 @@ def planner(g, T, late_bound):
             head = begin + race[0]
             inside = set(head)
             st = place(topo(head, key), {i: [e for e in pred[i] if e[0] in inside] for i in head})[0]
-            head, PLAN["head"] = better(sorted(head, key=lambda i: (st[i], i)), CFG["polish"][1], CFG["heat3"], follow(head, mid))
-            head, PLAN["head"] = polish(head, CFG["polish"][6], CFG["heat3"], follow(head, mid), 0.0, 0.45)
+            found = []
+            for seed[0] in CFG["seeds"][2]:
+                e = better(sorted(head, key=lambda i: (st[i], i)), CFG["polish"][1], CFG["heat3"], follow(head, mid))
+                found.append(polish(e[0], CFG["polish"][6], CFG["heat3"], follow(head, mid), 0.0, 0.45))
+            PLAN["heads"] = [[round(x) for x in e[1]] for e in found]
+            head, PLAN["head"] = min(found, key=score)
             seq = head + mid + tail
             PLAN["all"] = [times(seq, j)[1] for j in range(len(models))]
             PLAN["seq"] = seq
@@ -764,12 +781,22 @@ def rank_program(g, core, T, topo):
         late.append([None, [(name, 0, 512)], 16 * (r1 - r0 - 1) + c, 4, True, False, [], (name, p0, p, 16 * r0, 16 * r1 - 16 + c)])
         return late[-1]
 
+    def Pc(name, lo, hi, p=128, p0=0):
+        late.append([None, [(name, 0, 512)], hi - lo, 4, True, False, [], (name, p0, p, lo, hi)])
+        return late[-1]
+
+    def EQ(b0, b1, c0=0, c1=16):
+        return (T.eqm[:, b0, c0:c1] if b1 == b0 + 1 else T.eqm[:, b0:b1, c0:c1], [("eqm", 16 * b0, 16 * b1)], (b1 - b0) * (c1 - c0), 2, False, False, [])
+
     def new():
         uses[0] += 1
         return "@%d" % uses[0]
 
     def Ke(a0, a1, w):
         return (T.kE[:, a0:a1, 16 * w:16 * w + 16], [("kE", 32 * a + 16 * w, 32 * a + 16 * w + 16) for a in range(a0, a1)], 16 * (a1 - a0), 2, False, False, [])
+
+    def Kg(a0, a1):
+        return (T.kG[:, a0:a1, 16:32], [("kG", 48 * a0, 48 * a1)], 16 * (a1 - a0), 2, False, False, [])
 
     def Tv(r0, r1, st=1, c=0):
         n = len(range(r0, r1, st))
@@ -832,17 +859,17 @@ def rank_program(g, core, T, topo):
         else:
             ts(out, in_, scale, A.mult, add, A.add)
 
-    def group(terms, cuts=(), start=True, stop=True):
+    def group(terms, cuts=(), start=True, stop=True, alone=False):
         run, dur = [], 0.0
         for i, (out, lhsT, rhs, *ends) in enumerate(terms):
-            run.append((out, lhsT[0], rhs[0], start and i == 0, stop and (i == len(terms) - 1 or any(ends))))
+            run.append((out, lhsT[0], rhs[0], alone or start and i == 0, alone or stop and (i == len(terms) - 1 or any(ends))))
             dur += max(min(64, lhsT[2]), rhs[2]) * (4 if rhs[3] == 4 else 1)
             if dur >= CFG["run"] or i + 1 in cuts or i + 1 - len(terms) in cuts or i + 1 == len(terms):
                 op("T", lambda e, run=run: [e.matmul(m[0][0], *m[1:]) for m in run][-1], out, [x for u in terms[i + 1 - len(run):i + 1] for x in u[1:3]], dur=(0, 0, 0, 0, dur))
                 run, dur = [], 0.0
 
     def gcp(out, in_, after=None, pieces=None):
-        rec("G", "c", lambda e: e.affine_select(out[0], in_[0], [[0, out[2]]], A.is_gt, 0.0, 1, 0), in_[1], pieces or out[1], (170, 2 * out[2], 0, 0, 0), LAT, after=after)
+        rec("G", "c", lambda e: e.affine_select(out[0], in_[0], [[0, out[2]]], A.is_gt, 0.0, 1, 0), in_[1], pieces or out[1], (170, 2 * out[2], 0, 0, 0, 0, 0, 1), LAT, after=after)
 
     def ms(out, val):
         op("V", lambda e: e.memset(out[0], val), out, [], rate=out[3] / 4)
@@ -858,15 +885,17 @@ def rank_program(g, core, T, topo):
         trs = [RemoteDMATransfer(dst_ids=ids, dma_engine_mask=sum(1 << e for e in eng[n * k:n * k + n]), remote_sem=T.sem[rsem], srcs=[u[0][0]], dsts=u[1], alu_op=0)
                for k, u in enumerate(pieces)]
         n *= len(pieces)
-        i = rec("G", "s", lambda e: e.remote_dma_fused(trs, local_sem=T.sem[lsem]), [r for u in pieces for r in u[0][1]], [], (0, 0, 0, 0, 0, 900.0), 1500.0, lsem, n, after=last.get("G"))
+        i = rec("G", "s", lambda e: e.remote_dma_fused(trs, local_sem=T.sem[lsem]), [r for u in pieces for r in u[0][1]], [], (CFG["g1"] * (rsem == "av"), 0, 0, 0, 0, 900.0), 1500.0, lsem, n, after=last.get("G"))
         last["G"] = i
-        rec("N", "n", None, [], [r for u in pieces for r in u[2][1]], (0, 0, 0, 0, 0, 2500.0) if now[0] >= 0 else CFG["first"], LAT, rsem, 3 * n, after=i)
+        rec("N", "n", None, [], [r for u in pieces for r in u[2][1]], (0, 0, 0, 0, 0, 0, 2500.0) if now[0] >= 0 else CFG["first"], LAT, rsem, 3 * n, after=i)
         return n
 
     phase("load")
     dma("S", "vin", T.vs[:], T.v0[:], [], [("vs", 0, 45)], 2000.0)
     dma("S", "zin", T.zs[:], T.z0[:], [], [("zs", 0, 240)], 2000.0)
     loads = [("xw", T.x0, lo, hi) for lo, hi in CFG["xload"]] + [("kin", T.k0, lo, hi) for lo, hi in CFG["kload"]]
+    if CFG["kfirst"]:
+        loads = loads[len(CFG["xload"]):] + loads[:len(CFG["xload"])]
     size = [CFG["piece"] * (hi - lo) / (1024 if name == "kin" else 2048) for name, src, lo, hi in loads]
     for i, (name, src, lo, hi) in enumerate(loads):
         w = CFG["flight"]
@@ -875,8 +904,6 @@ def rank_program(g, core, T, topo):
 
     iota(B("pI", 0, 1), [[0, 1]], 0, 1)
     iota(B("iw", 0, 256), [[1, 256]], 0, 0)
-    iota(B("kc"), [[0, 8], [-4096, 16]], 15 * 4096, 0)
-    iota(B("rm"), [[0, 16], [1, 16]], 0, 0)
     SW = 16 * max([a1 - a0 for a0, a1, k in GROUPS if k == "S"] + [0])
     VW = 16 * max([a1 - a0 for a0, a1, k in GROUPS if k == "V"] + [0])
     ne = send(B("vs"), [T.vl[:, 45 * j:45 * j + 45] for j in range(3)], B("vl"), "av", "lv")
@@ -887,11 +914,15 @@ def rank_program(g, core, T, topo):
     iota(B("Dm"), [[0, 4], [16, 16]], 0, 0)
     ms(B("base"), BIG)
     for s in range(S):
-        iota(B("base", 16 * s, 16 * s + 15), [[4096, 3], [0, 5]], 16384 * (s + 1) + 4096, 0)
+        iota(B("base", 16 * s, 16 * s + 15), [[12288, 3], [0, 5]], 65536 * (s + 1) + 28672, 0)
     for i in range(3):
         act(B("iw", 256 << i, 512 << i), B("iw", 0, 256 << i), bias=float(256 << i))
     act(B("iw", 2048, 3072), B("iw", 0, 1024), bias=2048.0)
     iota(B("iw", 3072, V), [[1, 1024]], 3072, 0)
+    for o in range(V, K0 + V, 1056):
+        iota(B("iw", o, o + 1056 - CFG["iws"]), [[1, 1056 - CFG["iws"]]], o, 0)
+        if CFG["iws"]:
+            act(B("iw", o + 1056 - CFG["iws"], o + 1056), B("iw", 0, CFG["iws"]), bias=float(o + 1056 - CFG["iws"]))
 
     def col(i):
         return B("pF", i, i + 1)
@@ -907,12 +938,17 @@ def rank_program(g, core, T, topo):
     ts(pi(6), pi(0), 3, A.arith_shift_right, 1, A.bitwise_and)
     cp(B("pF", 0, 7), B("pI", 0, 7))
     ts(col(7), col(3), -1.0, A.mult, 1.0, A.add)
-    ts(col(8), col(0), 16.0, A.add)
-    ts(col(9), col(0), -16.0, A.add)
     ts(col(10), col(2), 15.0, A.add)
-    ts(col(11), col(0), 16.0, A.mult, 15.0, A.add)
+    ts(pi(11), pi(0), 31, A.bitwise_and)
+    ts(pi(12), pi(0), 5, A.arith_shift_right)
+    ts(pi(13), pi(0), 5, A.arith_shift_right, 1, A.bitwise_and)
+    ts(pi(14), pi(0), 6, A.arith_shift_right)
+    cp(B("pF", 24, 28), B("pI", 11, 15))
+    ts(col(8), col(24), 16.0, A.mult, 3.0, A.add)
+    ts(col(11), col(25), 4.0, A.mult, col(8), A.add)
     ts(B("idb"), I128, col(0), A.is_equal)
-    for name, f in (("idn", -1.0), ("idB", -16384.0), ("idM", 8192.0), ("ih", 1.0), ("ihn", -1.0), ("ih2", -2.0), ("ih32", 32.0), ("ihd", 16.0), ("idX", -16.0)):
+    act(B("idf"), B("idb"))
+    for name, f in (("idn", -8192.0), ("idB", -16384.0), ("idM", 8192.0), ("ih", 1.0), ("ihn", -1.0), ("ih2", -2.0), ("ih32", 32.0), ("ihd", 16.0), ("idX", -16.0)):
         act(B(name), B("idb"), scale=f)
     for s in range(S):
         act(B("idS", 128 * s, 128 * s + 128), B("idb"), scale=32.0 * (s + 1))
@@ -924,21 +960,35 @@ def rank_program(g, core, T, topo):
     act(B("U"), B("U1"), scale=65536.0)
     act(B("Uh"), B("U1"))
     ts(B("Us"), B("iw", 0, 144), col(11), A.is_equal, 8192.0, A.mult)
-    ts(B("rm"), B("rm"), 1.0, A.min)
+    ms(B("rm"), 4096.0)
+    ms(B("rm", 0, 128, 16), -2.0 ** 30)
+    ms(B("vU"), 0)
+    for name in ("R", "C"):
+        ms(B(name, 255, 1024, 256), 0.0)
     ts(B("En", 0, 16 * SW), B("E", 0, 16 * SW), col(0), A.is_equal, -1.0, A.mult)
     ms(B("rz"), 2048.0)
     ms(B("rz", 0, 256, 16), -1024.0)
-    for name in ("on", "vI", "x", "ow4"):
+    if CFG["gsp"]:
+        ms(B("ry"), 2048.0)
+        ms(B("ry", 0, 256, 4), -1024.0)
+        ms(B("ry", 256, 512, 8), -1024.0)
+    for name in ("on", "vI", "x", "y", "ow4", "c4"):
         ms(B(name), 0)
     ms(B("ones"), 1.0)
+    ms(B("c4", 1, 48, 3), 1.0)
+    if CFG["gap"]:
+        ms((T.kG[:, :, :], [("kG", 0, 768)], 768, 2, False, False, []), 0.0)
     for o in [496] + list(range(1008, 2304, 256)):
         act(B("zh", o, o + 16), B("ones", 0, 16), scale=1024.0)
     for o in range(240, 1024, 256) if not CFG["quad"] else ():
         act(B("kvh", o, o + 16), B("ones", 0, 16))
     for a0, a1, k in GROUPS:
-        if k == "V":
+        if k != "S":
             ms(B("shp", 256 * a0, 256 * a1), 0.0)
-    ms((T.Ys[:, 240:256, :], [("Ys", 3840, 4096)], 256, 2, False, False, []), 0.0)
+    if GROUPS[-1][2] == "S":
+        ms((T.Ys[:, 240:256, :], [("Ys", 3840, 4096)], 256, 2, False, False, []), 0.0)
+    else:
+        ms((T.Y[:, 15, :], [("Y", 3840, 4096)], 256, 2, False, False, []), 0.0)
     for h in range(2 * bool(CFG["half"])):
         o = 1024 + 512 * h
         ts(B("En", o, o + 512), B("E", o, o + 512), col(0), A.is_equal, -1.0, A.mult)
@@ -946,21 +996,32 @@ def rank_program(g, core, T, topo):
     ms(B("cls", 48, 64), 12.0 * BIG)
     ms(B("gt4", 240, 256), 0.0)
     act(B("Un"), B("U1"), scale=-BIG)
-    ms(B("csu"), 2048.0)
-    ms(B("cst"), 0.0)
-    ms(B("cst", 15, 128, 16), 2048.0)
     if CFG["quad"]:
         ts(B("ge"), B("iw", 0, 16), col(1), A.is_equal)
         ts(B("xy"), B("iw", 0, 16), 1.0, A.add, col(1), A.is_equal)
-        tt(B("Dif"), B("ge"), B("xy"), A.subtract)
+        tt(B("Dif", 0, 16), B("ge"), B("xy"), A.subtract)
+        for w in range(2 * bool(CFG["gap"])):
+            act(B("Dif", 16 + 16 * w, 32 + 16 * w), B("Dif", 0, 16), scale=col(3 if w else 7))
         act(col(21), col(7), scale=-2048.0)
         act(col(22), col(3), scale=-2048.0)
     else:
         act(B("Pn"), B("Pm"), scale=-1.0)
     ms(B("cneg", 0, 48), -16384.0)
-    ms(B("cneg", 48, 96), 26624.0)
-    ms(B("cneg", 96, 112), 26624.0 + K0)
-    ms(B("cneg", 112, 128), 26624.0 + X0)
+    if CFG["emerge"]:
+        ms(B("cn2", 0, 48), -16384.0)
+        for s in range(1, S):
+            ms(B("cn2", 32 + 16 * s, 48 + 16 * s), -16.0 * (s in CFG["sgv"]))
+    ms(B("cneg", 48, 64), 26624.0)
+    ms(B("cneg", 64, 96), 18432.0)
+    for e in CFG["sg"]:
+        ms(B("on", 16 * e + 15, 16 * e + 16), -1.0)
+    if CFG["d1T"]:
+        act(B("bsb", 0, 48), B("base", 0, 48))
+        ms(B("bsb", 48, 96), 16.0 * BIG)
+    else:
+        act(B("bs", 0, 48), B("base", 0, 48), bias=16.0 * BIG)
+    ms(B("cneg", 96, 112), 24576.0)
+    ms(B("cneg", 112, 128), 24576.0 - X0)
     for i in range(4):
         ts(pi(7 + i), pi(1), i, A.arith_shift_right, 1, A.bitwise_and)
     for i in range(4):
@@ -969,9 +1030,13 @@ def rank_program(g, core, T, topo):
     tt(col(17), col(14), col(15), A.mult)
     tt(col(18), col(16), col(17), A.mult)
     ms(B("valf"), 0.5)
-    ms(B("kp"), 0.0)
-    ts(B("kp", 0, 1), B("valf", 0, 1), -5.0 * 2.0 ** 55, A.mult, 2.0 ** 60, A.mult)
-    scan(B("thw"), B("valf"), B("kp"), A.mult, A.add)
+    ms(B("valf", 0, 64, 4), 2.0 ** -13)
+    ms(B("kq"), 0.0)
+    ts(col(28), col(26), 2.0 ** -4 - 1.0, A.mult, 1.0, A.add)
+    ts(col(29), col(27), 2.0 ** -8 - 1.0, A.mult, 1.0, A.add)
+    ts(col(30), col(28), col(29), A.mult, -2.5 * 2.0 ** 55, A.mult)
+    ts(B("kq", 0, 1), col(30), 2.0 ** 60, A.mult)
+    scan(B("thw", 0, 60), B("valf", 0, 60), B("kq", 0, 60), A.mult, A.add)
     ms(B("ge"), 2.0 ** -16)
     ms(B("xy"), 0.0)
     ts(B("xy", 0, 1), col(18), 2.0 ** 55, A.mult, 2.0 ** 60, A.mult)
@@ -988,28 +1053,29 @@ def rank_program(g, core, T, topo):
     ts(B("t8"), B("iw", 0, 8), 2.0, A.mult, col(20), A.add)
     ts(B("w8l"), B("t8"), col(19), A.mult, 15.0, A.add)
 
-    for o in range(240, 1280, 256):
-        act(B("cs", o, o + 16), B("ones", 0, 16))
 
     KW = B("kw", K0, K0 + V)
     XW = B("kw", X0, X0 + V)
+
+    def xwin():
+        return B("xw", 0, V) if CFG["kfirst"] and now[0] == 0 else XW
 
     def vU(t, s, a0=0, a1=15):
         return B("vU", 80 * t + 16 * s + a0, 80 * t + 16 * s + a1)
 
     def spairs(o, vals, keys, since):
         for a in range(15):
-            n = 240 - 16 * a
+            n = 15 - a
             if a >= since:
-                act(B("eqm", o, o + n), B(vals[0], vals[1] + 16 * a, vals[1] + 240), ABS, bias=B(keys[0], keys[1] + a, keys[1] + a + 1))
-                act(B("eqm", o, o + n), B("eqm", o, o + n), RELU, bias=B("wt", a, a + 1), scale=B("wt", 16 + a, 17 + a))
+                act(EQ(o, o + n), B(vals[0], vals[1] + 16 * a, vals[1] + 240), ABS, bias=B(keys[0], keys[1] + a, keys[1] + a + 1))
+                act(EQ(o, o + n), EQ(o, o + n), RELU, bias=B("wt", a, a + 1), scale=B("wt", 16 + a, 17 + a))
             o += n
 
-    def pairs(dst, o, vals, keys, upto=15):
+    def pairs(o, vals, keys, upto=15):
         for a in range(15):
-            n = 240 - 16 * a
+            n = 15 - a
             if a < upto:
-                ts(B(dst, o, o + n), B("val", vals + 16 * a, vals + 240), B(keys[0], keys[1] + a, keys[1] + a + 1), A.is_equal, B("wt", a, a + 1), A.mult)
+                ts(EQ(o, o + n), B(vals[0], vals[1] + 16 * a, vals[1] + 240), B(keys[0], keys[1] + keys[2] * a, keys[1] + keys[2] * a + 1), A.is_equal, B("wt", a, a + 1), A.mult)
             o += n
 
     for t in range(RACES):
@@ -1020,20 +1086,16 @@ def rank_program(g, core, T, topo):
             act(B("zc", 240 * t + 80 * j, 240 * t + 80 * j + 80), B("zl", 240 * j + 80 * t, 240 * j + 80 * t + 80))
         cp(vU(t, 0), B("vI", 16 * t, 16 * t + 15))
     phase("start1")
-    ts(B("k1c"), B("vI"), -2048.0, A.add)
-    ts(B("v1h"), B("vI"), -2048.0, A.add)
     act(B("v1K"), B("vI"), bias=float(K0))
-    for t in range(RACES):
-        act(B("val", 960 + 240 * t, 1200 + 240 * t), IX(B("iw", 0, V), vU(t, 0)), bias=-2048.0)
-        if t < CFG["eqs"]:
-            pairs("eq1", 1920 * t, 960 + 240 * t, ("k1c", 16 * t))
     phase("start0")
     for o in range(0, V, 256):
-        (act if o // 256 % 4 else cp)(B("kw", K0 + o, K0 + o + 256), B("kin", o, o + 256))
-    for lo, hi in CFG["xload"]:
+        (act if o // 256 % CFG["kwid"] else cp)(B("kw", K0 + o, K0 + o + 256), B("kin", o, o + 256))
+    for lo, hi in CFG["xload"] if not CFG["kfirst"] else ():
         mid = lo + (hi - lo) // 4
         cp(B("kw", X0 + lo, X0 + mid), B("xw", lo, mid))
         act(B("kw", X0 + mid, X0 + hi), B("xw", mid, hi))
+    for o in range(0, V, 256) if CFG["kfirst"] else ():
+        gcp(B("kw", X0 + o, X0 + o + 256), B("xw", o, o + 256))
 
     TEAMS = CFG["teams"]
 
@@ -1046,33 +1108,27 @@ def rank_program(g, core, T, topo):
 
     def sh(gr, s):
         a0, a1, k = GROUPS[gr]
-        if k == "V" and s < S:
+        if k != "S" and s < S:
             return B("shp", 256 * a0, 256 * a1, 16)
         return zh(s, a0, a1)
-
-    def Zy(a0, a1, c0=0, c1=16):
-        ap = T.zy[:, 16 * a0:16 * a1, c0] if c1 == c0 + 1 else T.zy[:, 16 * a0:16 * a1, c0:c1]
-        return (ap, [("zy", 256 * a0, 256 * a1)], 16 * (a1 - a0) * (c1 - c0), 2, False, False, [])
-
-    def double(a0, a1, after=None):
-        for c in (1, 2, 4, 8):
-            gcp(Zy(a0, a1, c, 2 * c), Zy(a0, a1, 0, c), after)
 
     def zform(gr, s):
         a0, a1, k = GROUPS[gr]
         n = 16 * (a1 - a0)
-        if k == "V":
-            am = a1 - CFG["gsp"]
+        if k != "S":
+            am = a1
+            for w, c in CFG["gsp"].get((gr, s), CFG["gsp"].get(gr, ())) if s else ():
+                am, e = am - w, 256 * am
+                scan(B("zx", 256 * am, e, 16 // c), B("ry", 256 * (c == 8), 256 * (c == 8) + 16 * c * w), B("shp", 256 * am, e, 16 // c), A.min, A.add)
+                while c < 16:
+                    gcp(B("zx", 256 * am + 8 // c, e, 16 // c), B("zx", 256 * am, e, 16 // c))
+                    c *= 2
             for a in range(a0, am):
                 o = 256 * a
                 scan(B("zx", 256 * a, 256 * a + 256), B("rz", 0, 256), B("shp", o, o + 256), A.min, A.add)
-            if am < a1:
-                o = 0
-                lin("zy", Zy(am, a1, 0, 1), B("shp", o + 256 * am, o + 256 * a1, 16), 1.0, -1024.0)
-                double(am, a1)
         else:
             pb, zT = P(new(), 0, 8, p=n), B("zT", 128 * gr, 128 * gr + 128, p=n)
-            if s == 0:
+            if s == 0 or gr in CFG["ztr"]:
                 group([(pb, sh(gr, s), B("ih"))])
                 act(zT, pb)
             else:
@@ -1083,16 +1139,12 @@ def rank_program(g, core, T, topo):
     def zinit(t):
         act(zh(0), B("zc", 240 * t, 240 * t + 240), bias=1024.0)
         for gr, (a0, a1, k) in enumerate(GROUPS):
-            if k == "V" and not (t and CFG["gzx"]):
+            if k != "S" and not (t and CFG["gzx"]):
                 act(sh(gr, 0), B("zc", 240 * t + 16 * a0, 240 * t + 16 * a1), bias=1024.0)
-            if k == "V" and t and CFG["gzx"]:
-                am = a1 - CFG["gsp"]
-                for c in range(16 * (am > a0)):
-                    gcp(B("zx", 256 * a0 + c, 256 * am, 16), B("zc", 240 * t + 16 * a0, 240 * t + 16 * am), last["G"],
-                        [("zx", 256 * a + c, 256 * a + c + 1) for a in range(a0, am)])
-                if am < a1:
-                    gcp(Zy(am, a1, 0, 1), B("zc", 240 * t + 16 * am, 240 * t + 16 * a1), last["G"])
-                    double(am, a1, last["G"])
+            if k != "S" and t and CFG["gzx"]:
+                gcp(B("zx", 256 * a0, 256 * a1, 16), B("zc", 240 * t + 16 * a0, 240 * t + 16 * a1), last["G"])
+                for c in (16, 8, 4, 2):
+                    gcp(B("zx", 256 * a0 + c // 2, 256 * a1, c), B("zx", 256 * a0, 256 * a1, c))
             else:
                 zform(gr, 0)
 
@@ -1109,6 +1161,9 @@ def rank_program(g, core, T, topo):
             cp(B("kvu", 16 * a0, 16 * a1), IX(KW if t else B("kin"), vU(t, s - 1, a0, a1)))
         else:
             act(B("kvu", 16 * a0, 16 * a1), IX(KW if t else B("kin"), vU(t, s - 1, a0, a1)))
+        if (s, gr) in CFG["gap"]:
+            lin("kG%d%d" % (s, gr), Kg(a0, a1), B("kvu", 16 * a0, 16 * a1), 1.0, -2048.0)
+            return
         if CFG["quad"]:
             for w in range(2):
                 if (gr, w) in CFG["khs"]:
@@ -1125,14 +1180,10 @@ def rank_program(g, core, T, topo):
 
     def score(tm, pb):
         a0, a1 = span(tm)
-        w = 2 * ((a1 - a0 + 1) // 2)
-        group([(P(pb, 0, w), B("idb"), B("kc", 0, 16 * w))], stop=False)
         for gr in TEAMS[tm]:
-            al, ah = GROUPS[gr][:2]
-            end = a0 + w if ah == a1 else ah
+            al, end = GROUPS[gr][:2]
             cs = list(range(0, 16, 2)) + list(range(1, 16, 2))
-            group([(P(pb, al - a0, end - a0), B("U", 15 - c, 143 - c), Yv(al, end, c) if GROUPS[gr][2] == "V" else Ys(16 * al + c, 16 * end, 16)) for c in cs],
-                  start=False, stop=gr == TEAMS[tm][-1])
+            group([(P(pb, al - a0, end - a0), B("U", 15 - c, 143 - c), Yv(al, end, c) if GROUPS[gr][2] != "S" else Ys(16 * al + c, 16 * end, 16)) for c in cs])
 
     chunk = [0]
 
@@ -1147,43 +1198,61 @@ def rank_program(g, core, T, topo):
             act(Ys(16 * a0 + h, 16 * a1, 2), pa, RELU, bias=1024.0)
         for a in range(a0, a1, CFG["scols"]) if not halved(gr, now[1]) else ():
             e = min(a + CFG["scols"], a1)
-            xg, pa, o = B("xg%d" % (chunk[0] % 3), 0, 256 * (e - a)), P(new(), 0, 16 * (e - a)), 256 * (a - a0)
+            xg, pa, o = B(("xg0", "xg1", "xm")[chunk[0] % (3 if GROUPS[-1][2] == "S" else 2)], 0, 256 * (e - a)), P(new(), 0, 16 * (e - a)), 256 * (a - a0)
             chunk[0] += 1
-            act(xg, IX(XW, B("kvu", 16 * a, 16 * e)))
+            act(xg, IX(xwin(), B("kvu", 16 * a, 16 * e)))
             group([(pa, B("zT", 128 * gr, 128 * gr + 128, p=n), B("En", o, o + 256 * (e - a), p=n)), (pa, B("idb"), xg)][::CFG["zfirst"][a > a0]], (1,))
-            act(Ys(16 * a, 16 * e), pa, RELU, bias=1024.0)
+            if (now[1], a) in CFG["rv"]:
+                ts(Ys(16 * a, 16 * e), pa, 1024.0, A.add, 0.0, A.max)
+            else:
+                act(Ys(16 * a, 16 * e), pa, RELU, bias=1024.0)
+
+    def xmix(gr):
+        a = GROUPS[gr][0]
+        for n in CFG["xcols"][gr]:
+            o = 256 * (a - min(e[0] for e in GROUPS if e[2] == "M"))
+            act(B("xm", o, o + 256 * n), IX(xwin(), B("kvu", 16 * a, 16 * (a + n))))
+            tt(B("xm", o, o + 256 * n, 16), B("xm", o, o + 256 * n, 16), B("zx", 256 * a, 256 * (a + n), 16), A.max)
+            for e in range(a, a + n):
+                scan(Yv(e, e + 1), B("zx", 256 * e, 256 * e + 256), B("xm", o + 256 * (e - a), o + 256 * (e - a + 1)), A.min, A.max)
+            a += n
 
     def xvec(gr):
-        a0, a1, k = GROUPS[gr]
-        for a in range(a0, a1):
-            n = 8 if a - a0 in CFG["xh"] else 16
-            for l in range(16 * a, 16 * a + 16, n):
-                y = (T.Y[:, a, 16 * (l - 16 * a):16 * (l + n - 16 * a)], [("Y", 16 * l, 16 * (l + n))], 16 * n, 2, False, False, [])
-                z = (T.zy[:, l:l + n, :], [("zy", 16 * l, 16 * (l + n))], 16 * n, 2, False, False, [])
-                tt(y, IX(XW, B("kvu", l, l + n)), B("zx", 16 * l, 16 * (l + n)) if a < a1 - CFG["gsp"] else z, A.max)
+        a = GROUPS[gr][0]
+        for n in CFG["xcols"].get((gr, now[1]), CFG["xcols"][gr]):
+            for l in range(16 * a, 16 * a + 16, 8) if n == 0 else ():
+                y = (T.Y[:, a, 16 * (l - 16 * a):16 * (l + 8 - 16 * a)], [("Y", 16 * l, 16 * (l + 8))], 128, 2, False, False, [])
+                tt(y, IX(xwin(), B("kvu", l, l + 8)), B("zx", 16 * l, 16 * (l + 8)), A.max)
+            if n:
+                tt(Yv(a, a + n), IX(xwin(), B("kvu", 16 * a, 16 * (a + n))), B("zx", 256 * a, 256 * (a + n)), A.max)
+            a += n or 1
 
     def pick(t, gr, s):
         a0, a1 = span(gr)
         nb = (a1 - a0 + 1) // 2
-        n, o, pb = 32 * nb, 256 * (s - 1) + 16 * a0, new()
-        key, R, D, C = P(pb, 0, 2 * nb), B("R", o, o + n), B("d0", 16 * a0, 16 * a0 + n), B("C", o, o + n)
+        n, o, pb = 16 * (a1 - a0), 256 * (s - 1) + 16 * a0, new()
+        key, R, D, C = P(pb, 0, a1 - a0), B("R", o, o + n), B("d0", 16 * a0, 16 * a0 + n), B("C", o, o + n)
         pk = pb if gr in CFG["dif"] and gr not in CFG["apart"] else new()
-        d1 = P(pk, 16, 16 + 2 * nb)
+        d1 = P(pk, 16, 16 + a1 - a0)
         dif = gr in CFG["dif"]
-        terms = [(d1, B("idb"), B("cst" if dif else "csu", 0, n))]
+        terms = []
         for a in range(a1 - a0):
-            for q in range(0, 128, 32) if CFG["quad"] else ():
+            for q in range(0, 128, 32) if (s, gr) in CFG["gap"] else ():
+                for w in range(2):
+                    terms.append((P(pk, 16 + a, 17 + a, p=32, p0=q), (T.kG[q:q + 32, a0 + a, 16 - 16 * w:48 - 16 * w], [("kG", 48 * (a0 + a), 48 * (a0 + a) + 48)], 32, 2, False, False, []),
+                                  (T.Dif[q:q + 32, 16 + 16 * w:32 + 16 * w], [("Dif", 0, 48)], 16, 2, False, False, []), a == a1 - a0 - 1 and w == 1))
+            for q in range(0, 128, 32) if CFG["quad"] and (s, gr) not in CFG["gap"] else ():
                 terms.append((P(pk, 16 + a, 17 + a, p=32, p0=q), (T.kE[q:q + 32, a0 + a, :], [("kE", 32 * (a0 + a), 32 * (a0 + a) + 32)], 32, 2, False, False, []),
-                              (T.Dif[q:q + 32, :], [("Dif", 0, 16)], 16, 2, False, False, []), a == a1 - a0 - 1))
+                              (T.Dif[q:q + 32, 0:16], [("Dif", 0, 16)], 16, 2, False, False, []), a == a1 - a0 - 1))
             for w in range(2 * (not CFG["quad"])):
                 q, b = 128 * (2 * (a % 2) + w), a0 + a - a % 2 + w
                 terms.append((P(pk, 16 + a, 17 + a), B("Pm", q, q + 128), Tv(b, b + 1)))
                 if dif:
                     terms.append((P(pk, 16 + a, 17 + a, c=15), B("Pn", q, q + 128), Tv(b, b + 1, 1, 1)))
         if dif:
-            group(terms)
+            group(terms, alone=True)
         score(gr, pb)
-        scan(R, B("rm", 0, n), key, A.mult, A.max)
+        scan(R, B("rm", 0, n), key, A.add, A.max)
         if dif:
             tt(D, R, key, A.is_gt)
             scan(C, D, d1, A.mult, A.add)
@@ -1191,7 +1260,7 @@ def rank_program(g, core, T, topo):
             tt(D, R, key, A.subtract)
             group(terms + [(d1, B("idn"), D)], (-1,))
             scan(C, D, d1, A.min, A.max)
-        cp(vU(t, s, a0, a1), B("C", o + 15, o + 16 * (a1 - a0), 16))
+        ts(vU(t, s, a0, a1), B("C", o + 15, o + 16 * (a1 - a0), 16), 2048.0, A.add)
 
     nev = [0]
 
@@ -1199,7 +1268,7 @@ def rank_program(g, core, T, topo):
         t0, pz, o = span(tm)[0], new(), 256 * (s - 1)
         if s == S:
             a0, a1 = span(tm)
-            lst, zt = IX(XW, vU(t, s, a0, a1)), B("zt", o + 16 * a0, o + 16 * a1)
+            lst, zt = IX(xwin(), vU(t, s, a0, a1)), B("zt", o + 16 * a0, o + 16 * a1)
             tt(B("gt4", 16 * a0, 16 * a1), lst, B("z3", 16 * a0, 16 * a1), A.is_gt)
             if tm in CFG["z4s"]:
                 xq, pa = B("xq", o + 16 * a0, o + 16 * a1), P(pz, 8, 8 + a1 - a0)
@@ -1214,23 +1283,29 @@ def rank_program(g, core, T, topo):
         ons = [gr for gr in TEAMS[tm] if gr not in onv]
         for gr in onv:
             a0, a1, k = GROUPS[gr]
-            lst, zt = IX(XW, vU(t, s, a0, a1)), B("zt", o + 16 * a0, o + 16 * a1)
+            lst, zt = IX(xwin(), vU(t, s, a0, a1)), B("zt", o + 16 * a0, o + 16 * a1)
             tt(zt, lst, zh(s - 1, a0, a1), A.add)
             ts(sh(gr, s), zt, 0.5, A.mult, 511.75, A.add)
         if ons:
             b0, b1 = GROUPS[ons[0]][0], GROUPS[ons[-1]][1]
             xq = B("xq", o + 16 * b0, o + 16 * b1)
-            act(xq, IX(XW, vU(t, s, b0, b1)))
+            act(xq, IX(xwin(), vU(t, s, b0, b1)))
             group([(P(pz, 8 + b0 - t0, 8 + b1 - t0), B("idb"), xq)] + [(P(pz, 8 + GROUPS[gr][0] - t0, 8 + GROUPS[gr][1] - t0), B("ih"), zh(s - 1, *GROUPS[gr][:2])) for gr in ons])
             for gr in ons:
                 act(sh(gr, s), P(pz, 8 + GROUPS[gr][0] - t0, 8 + GROUPS[gr][1] - t0), bias=511.75, scale=0.5)
         for gr in TEAMS[tm]:
             a0, a1, k = GROUPS[gr]
             zform(gr, s)
-            if k == "V":
+            if k != "S":
                 gcp(zh(s, a0, a1), sh(gr, s))
-        if s == S - 1:
+        if s == S - 1 and not CFG["z3g"]:
             act(B("z3", 16 * span(tm)[0], 16 * span(tm)[1]), zh(s, *span(tm)), bias=-1024.0)
+        for gr in TEAMS[tm] if s == S - 1 and CFG["z3g"] else ():
+            a0, a1, k = GROUPS[gr]
+            if k != "S":
+                gcp(B("z3", 16 * a0, 16 * a1), B("zx", 256 * a0, 256 * a1, 16))
+            else:
+                act(B("z3", 16 * a0, 16 * a1), zh(s, a0, a1), bias=-1024.0)
         pz = new()
         for gr in onv:
             a0, a1, k = GROUPS[gr]
@@ -1240,14 +1315,13 @@ def rank_program(g, core, T, topo):
             pa = P(pz, 24 + b0 - t0, 24 + b1 - t0)
             group([(pa, B("idb"), xq), (pa, B("ihn"), zh(s - 1, b0, b1))])
         a0, a1 = span(tm)
-        act(B("zh", 1536 + o + 16 * a0, 1536 + o + 16 * a1), P(pz, 24, 24 + a1 - a0), SIGN, bias=1023.5)
+        if s in CFG["sgv"]:
+            ts(B("zh", 1536 + o + 16 * a0, 1536 + o + 16 * a1), P(pz, 24, 24 + a1 - a0), -1023.5, A.is_gt, 2.0, A.mult)
+        else:
+            act(B("zh", 1536 + o + 16 * a0, 1536 + o + 16 * a1), P(pz, 24, 24 + a1 - a0), SIGN, bias=1023.5)
 
     def race(t):
         chunk[0] = nev[0] = 0
-        now[0], now[1] = t, 1
-        phase("eqn")
-        if CFG["eqs"] == 0:
-            pairs("eq1", 1920 * t, 960 + 240 * t, ("k1c", 16 * t))
         for s in range(1, S + 1):
             now[0], now[1] = t, s
             for tm in range(len(TEAMS)):
@@ -1255,7 +1329,7 @@ def rank_program(g, core, T, topo):
                 knew(t, tm, s)
                 for gr in TEAMS[tm]:
                     phase("x%d" % gr)
-                    (xvec if GROUPS[gr][2] == "V" else xact)(gr)
+                    {"V": xvec, "S": xact, "M": xmix}[GROUPS[gr][2]](gr)
                 phase("p%d" % tm)
                 pick(t, tm, s)
                 phase("z%d" % tm)
@@ -1285,55 +1359,69 @@ def rank_program(g, core, T, topo):
     def early(t):
         phase("early")
         pc = new()
-        group([(P(pc, 3, 6), B("Uh", 15 - c, 143 - c), B("zh", 1536 + c, 2304, 16)) for c in range(16)])
+        if CFG["emerge"]:
+            group([(P(pc, 0, 6), B("idb"), B("cn2"))] + [(P(pc, 0, 6), B("Uh", 15 - c, 143 - c), B("zh", 768 + c, 2304, 16)) for c in range(16)], (1,))
+        else:
+            group([(P(pc, 3, 6), B("Uh", 15 - c, 143 - c), B("zh", 1536 + c, 2304, 16)) for c in range(16)])
         ts(B("cls", 0, 48), P(pc, 3, 6), B("thr", 0, 1), A.is_ge, -16.0 * BIG, A.mult)
-        ts(B("nb", 0, 48), P(pc, 3, 6), B("thr", 0, 1), A.is_lt, BIG, A.mult)
-        tt(B("op2"), B("cls", 0, 16), B("cls", 16, 32), A.min)
-        tt(B("fl", 16 * t, 16 * t + 16), B("op2"), B("cls", 32, 48), A.min)
-        rs = 144 + 48 * t
-        send(B("fl", 16 * t, 16 * t + 15), [T.rcv[:, rs + 30 - 15 * j:rs + 45 - 15 * j] for j in range(3)], B("rcv", rs, rs + 48), "e%d" % t, "f%d" % t)
-        least("x3", rs)
+        if CFG["early"]:
+            tt(B("op2"), B("cls", 0, 16), B("cls", 16, 32), A.min)
+            tt(B("fl", 16 * t, 16 * t + 16), B("op2"), B("cls", 32, 48), A.min)
+            rs = 144 + 48 * t
+            send(B("fl", 16 * t, 16 * t + 15), [T.rcv[:, rs + 30 - 15 * j:rs + 45 - 15 * j] for j in range(3)], B("rcv", rs, rs + 48), "e%d" % t, "f%d" % t)
+            least("x3", rs)
         phase("early2")
-        pc = new()
-        group([(P(pc, 0, 3), B("idb"), B("cneg", 0, 48))] + [(P(pc, 0, 3), B("Uh", 15 - c, 143 - c), B("zh", 768 + c, 1536, 16)) for c in range(16)], (1,))
-        tt(B("wz", 0, 48), B("C", 15, 768, 16), P(pc, 0, 3), A.mult)
+        if not CFG["emerge"]:
+            pc = new()
+            group([(P(pc, 0, 3), B("idb"), B("cneg", 0, 48))] + [(P(pc, 0, 3), B("Uh", 15 - c, 143 - c), B("zh", 768 + c, 1536, 16)) for c in range(16)], (1,))
+        tt(B("wz", 0, 48), vU(t, 1, 0, 48), P(pc, 0, 3), A.mult)
         ts(B("u4", 0, 48), B("wz", 0, 48), 4095, A.bitwise_and)
-        tt(B("d1", 0, 48), B("nb", 0, 48), B("base", 0, 48), A.add)
+        if CFG["d1T"]:
+            d1 = new()
+            group([(P(d1, 0, 3), B("idb"), B("bsb", 0, 48)), (P(d1, 0, 3), B("idb"), B("bsb", 48, 96)), (P(d1, 0, 3), B("idb"), B("cls", 0, 48))], (2,))
+            d1 = P(d1, 0, 3)
+        else:
+            d1 = B("d1", 0, 48)
+            tt(d1, B("cls", 0, 48), B("bs", 0, 48), A.add)
         def cw(s0, s1, c0, c1):
             return (T.cw[:, s0, c0:c1] if s1 == s0 + 1 else T.cw[:, s0:s1, c0:c1], [("cw", 32 * s + c0, 32 * s + c1) for s in range(s0, s1)], (s1 - s0) * (c1 - c0), 4, False, False, [])
-        tt(cw(0, 3, 0, 16), B("u4", 0, 48), B("d1", 0, 48), A.add)
-        tt(cw(0, 3, 16, 32), B("C", 15, 768, 16), B("d1", 0, 48), A.add)
+        tt(cw(0, 3, 0, 16), B("u4", 0, 48), d1, A.add)
+        tt(cw(0, 3, 16, 32), vU(t, 1, 0, 48), d1, A.add)
         tt(B("m1"), cw(0, 1, 0, 32), cw(1, 2, 0, 32), A.min)
-        m3 = B("m3", 32 * t, 32 * t + 16)
+        tt(cw(2, 3, 0, 16), cw(2, 3, 0, 16), B("base", 48, 64), A.min)
+        m3 = B("m3", 32 * t + 16, 32 * t + 32)
         tt(B("m3", 32 * t, 32 * t + 32), B("m1"), cw(2, 3, 0, 32), A.min)
-        ts(B("op"), B("fl", 16 * t, 16 * t + 16), 0.0, A.is_ge)
-        tt(B("g0"), m3, B("base", 48, 64), A.min)
+        if CFG["early"]:
+            lin("op", B("op"), B("fl", 16 * t, 16 * t + 16), 1.0 / (16 * BIG), 1.0)
+        else:
+            ts(B("op"), m3, BIG, A.is_ge)
+            act(B("op2"), B("op"), bias=BIG, scale=BIG / 2 - 1.0 - BIG)
         phase("masks")
         rows(0, CFG["ke"])
         phase("pairs")
-        act(B("v16", 16, 64), B("C", 15, 768, 16), bias=-2048.0)
+        act(B("v16", 16, 64), B("C", 15, 768, 16))
         for s in (4, 3, 2):
             phase("pairs%d" % s)
-            lin("kc%d" % s, B("kcol", 16 * s - 16, 16 * s), B("C", 256 * s - 512 + 15, 256 * s - 256, 16), 1.0, -2048.0)
             for a0, a1 in CFG["vparts"].get(s, ((0, 15),)):
                 act(B("val", 240 * s - 240 + 16 * a0, 240 * s - 240 + 16 * a1), IX(B("iw", 0, V), vU(t, s - 1, a0, a1)), bias=-2048.0)
             n = CFG["spairs"].get(s, 15)
             if n < 15:
-                act(B("nk", 16 * s - 16, 16 * s), B("C", 256 * s - 512 + 15, 256 * s - 256, 16), bias=2048.0, scale=-1.0)
-            spairs(1920 * (s - 1), ("val", 240 * s - 240), ("nk", 16 * s - 16), n)
-            pairs("eqm", 1920 * (s - 1), 240 * s - 240, ("kcol", 16 * s - 16), n)
+                act(B("nk", 16 * s - 16, 16 * s), B("C", 256 * s - 512 + 15, 256 * s - 256, 16), scale=-1.0)
+            spairs(120 * (s - 1), ("val", 240 * s - 240), ("nk", 16 * s - 16), n)
+            pairs(120 * (s - 1), ("val", 240 * s - 240), ("C", 256 * s - 512 + 15, 16), n)
 
     def finish(t):
         phase("own")
         own = B("own", 16 * t, 16 * t + 16)
-        tt(B("wf"), B("C", 768 + 15, 1024, 16), B("op"), A.mult)
+        tt(B("wf"), vU(t, S, 0, 16), B("op"), A.mult)
         rk, short = B("rk", 16 * t, 16 * t + 16), P(new(), 0, 1)
         group([(short, B("idb"), B("cls", 16 * s, 16 * s + 16)) for s in (3, 0, 1, 2)] + [(short, B("Un", 15 - c, 143 - c), B("gt4", c, 256, 16)) for c in range(16)], (4,))
-        tt(rk, short, B("g0"), A.max)
+        tt(rk, short, B("m3", 32 * t, 32 * t + 16), A.max)
         rs = 48 * t
         send(B("rk", 16 * t, 16 * t + 15), [T.rcv[:, rs + 30 - 15 * j:rs + 45 - 15 * j] for j in range(3)], B("rcv", rs, rs + 48), "a%d" % t, "l%d" % t)
         phase("ownu")
-        ts(B("nb", 48, 64), short, 0.0, A.is_gt, 16 * BIG, A.mult)
+        if not CFG["w54"]:
+            act(B("nb", 48, 64), short, scale=32.0)
         pa = P(new(), 0, 1)
         group([(pa, B("idb"), B("cneg", 0, 16))] + [(pa, B("Uh", 15 - c, 143 - c), B("zh", 256 + c, 512, 16)) for c in range(16)], (1,))
         tt(B("wz", 48, 64), B("wf"), pa, A.mult)
@@ -1342,33 +1430,43 @@ def rank_program(g, core, T, topo):
         ru = 288 + 48 * t
         send(B("own", 16 * t, 16 * t + 15), [T.rcv[:, ru + 30 - 15 * j:ru + 45 - 15 * j] for j in range(3)], B("rcv", ru, ru + 48), "u%d" % t, "w%d" % t)
         phase("logs")
-        act(B("w1", 0, 16), B("C", 768 + 15, 1024, 16), bias=16384.0 * S)
+        act(B("w1", 0, 16), B("C", 768 + 15, 1024, 16), bias=65536.0 * S + 2048.0)
         tt(B("dI"), B("m3", 32 * t + 16, 32 * t + 32), B("w1", 0, 16), A.min)
         ts(B("WI"), B("dI"), 4095, A.bitwise_and)
-        ts(B("bI"), B("dI"), 6, A.arith_shift_right, 1792, A.bitwise_and)
-        lin("WU", B("WU"), B("WI"))
-        lin("v16", B("v16", 0, 16), B("WI"), 1.0, -2048.0)
-        lin("nW", B("nW"), B("WI"), -1.0, 2048.0)
-        if CFG["wV"]:
-            lin("kcol", B("kcol", 0, 16), B("WI"), 1.0, -2048.0)
+        ts(B("bI"), B("dI"), 8, A.arith_shift_right, 1792, A.bitwise_and)
         joint = t < RACES - 1
+        if not joint:
+            lin("WU", B("WU"), B("WI"))
         tt(B("bF" if joint else "bU"), B("bI"), B("ln"), A.add)
-        if joint:
-            act(B("WF"), B("WI"), bias=float(X0))
+        act(B("WF"), B("WI"), bias=float(X0))
+        apart = not joint and CFG["apart2"]
+        if apart:
+            phase("eqn")
+            act(B("valu", 0, 240), IX(B("iw", K0), vU(t, 0)))
+            n0, n4 = CFG["apart2"]
+            if n0 < 15:
+                act(B("nG", 0, 15), B("v1K", 16 * t, 16 * t + 15), scale=-1.0)
+            spairs(0, ("valu", 0), ("nG", 0), n0)
+            pairs(0, ("valu", 0), ("v1K", 16 * t, 1), n0)
+            phase("wpairs")
+            act(B("valu", 960, 1200), IX(B("iw", X0), B("WU", 0, 15)))
+            if n4 < 15:
+                act(B("GF", 0, 15), B("WF", 0, 15), scale=-1.0)
+            spairs(480, ("valu", 960), ("GF", 0), n4)
+            pairs(480, ("valu", 960), ("WF", 0, 1), n4)
         phase("masks4")
         rows(CFG["ke"], S)
-        phase("wpairs")
-        act(B("val", 0, 240), IX(B("iw", 0, V), B("WU", 0, 15)), bias=-2048.0)
-        spairs(0, ("val", 0), ("nW", 0), CFG["wV"])
-        pairs("eqm", 0, 0, ("kcol", 0), CFG["wV"])
         phase("cm")
         pa = P(new(), 0, 15)
-        if CFG["quad"]:
+        if (S, 0) in CFG["gap"]:
+            group([(pa, B("ih"), Kg(0, 15)), (pa, B("idB"), B("Bs", 720, 960))], (1,))
+        elif CFG["quad"]:
             group([(pa, B("ih"), Ke(0, 15, 0)), (pa, B("ih"), Ke(0, 15, 1)), (pa, B("idB"), B("Bs", 720, 960))], (2,))
         else:
             group([(pa, B("ih32"), B("kvh", 768, 1008)), (pa, B("idB"), B("Bs", 720, 960))], (1,))
         act(B("cm"), pa, RELU, bias=2048.0)
-        act(B("b4"), B("C", 768 + 15, 1024, 16), bias=32.0 * S - 131072.0, scale=32.0)
+        act(B("ub", 2, 48, 3), B("C", 768 + 15, 1024, 16), bias=32.0 * S - 65536.0, scale=32.0)
+        act(B("c4", 2, 48, 3), B("C", 768 + 15, 1024, 16), bias=2048.0)
         phase("xnew")
         if not joint:
             act(B("xW"), IX(XW, B("WU", 0, 15)))
@@ -1384,10 +1482,15 @@ def rank_program(g, core, T, topo):
         phase("own4")
         x, ow, ow2 = B("x", 0, 15), B("ow1", 0, 15), B("ow2", 0, 15)
         ts(ow, B("rk", 16 * t, 16 * t + 15), BIG, A.min)
-        tt(ow2, B("rk", 16 * t, 16 * t + 15), B("nb", 48, 63), A.add)
+        if not CFG["w54"]:
+            tt(ow2, B("rk", 16 * t, 16 * t + 15), B("nb", 48, 63), A.max)
+        act(B("th4", 0, 15), ow, bias=33.0 * BIG, scale=-32.0)
         if CFG["early"]:
             tt(B("ow4", 0, 15), ow, B("x3", 0, 15), A.add)
-            act(B("owE"), IX(B("ow4"), B("w8l")))
+        else:
+            ts(B("xu", 0, 15), B("rk", 16 * t, 16 * t + 15), LAST, A.bitwise_and)
+            tt(B("ow4", 0, 15), B("xu", 0, 15), B("op2", 0, 15), A.max)
+        act(B("owE"), IX(B("ow4"), B("w8l")))
         phase("win")
         least("x", rs)
 
@@ -1397,28 +1500,52 @@ def rank_program(g, core, T, topo):
         if CFG["early"]:
             tt(on(3), x, B("ow4", 0, 15), A.is_lt)
         else:
-            ts(B("ge", 0, 15), x, 16384.0 * S, A.is_ge)
-            tt(on(3), on(0), B("ge", 0, 15), A.mult)
+            ts(B("y", 0, 15), x, LAST, A.bitwise_and)
+            tt(on(3), B("y", 0, 15), B("ow4", 0, 15), A.is_gt)
         phase("winu")
-        least("xu", ru)
-        ts(B("uI", 0, 15), B("xu", 0, 15), 4095, A.bitwise_and)
+        lin("nx", B("ub", 1, 45, 3), x, -1.0)
+        tt(B("ub", 0, 45, 3), B("rcv", ru + 5, ru + 20), B("rcv", ru + 25, ru + 40), A.min)
+        ts(B("uI", 0, 15), B("ub", 0, 45, 3), 4095, A.bitwise_and)
         lin("uU", B("uU", 0, 15), B("uI", 0, 15))
         phase("win2")
         tt(B("xy", 0, 15), x, on(0), A.mult)
         for s in (3, 2):
-            ts(on(s - 1), B("xy", 0, 15), 16384.0 * s, A.is_ge)
-        tt(on(4), ow2, x, A.is_lt)
-        if joint:
-            phase("joint")
+            if s - 1 in CFG["sg"]:
+                act(on(s - 1), B("xy", 0, 15), SIGN, bias=0.5 - 65536.0 * s)
+            else:
+                ts(on(s - 1), B("xy", 0, 15), 65536.0 * s, A.is_ge)
+        tt(on(5), x, B("th4", 0, 15), A.is_lt)
+        if CFG["w54"]:
+            tt(on(4), on(5), on(0), A.subtract)
+        else:
+            tt(on(4), ow2, x, A.is_lt)
+        phase("joint")
+        if apart:
+            pass
+        elif "nw" in CFG["onS"]:
+            act(B("nw", 0, 15), on(4), bias=1.0, scale=-1.0)
+        elif CFG["w54"]:
+            tt(B("nw", 0, 15), on(0), on(5), A.is_ge)
+        else:
             tt(B("nw", 0, 15), ow2, x, A.is_ge)
+        if not apart:
+            tt(B("XU", 0, 15), B("WF", 0, 15), on(4), A.mult)
+            tt(B("of", 0, 15), B("v1K", 16 * t, 16 * t + 15), B("nw", 0, 15), A.mult)
+            tt(B("GU", 0, 15), B("of", 0, 15), B("XU", 0, 15), A.add)
+        if joint:
             tt(B("kU", 0, 15), B("kF", 0, 15), B("nw", 0, 15), A.mult)
             act(B("Bs", 0, 240), IX(B("Wk"), B("kU", 0, 15)))
             tt(B("bU", 0, 15), B("bF", 0, 15), on(4), A.mult)
             act(B("zW"), IX(B("zg"), B("bU", 0, 15)))
-            tt(B("XU", 0, 15), B("WF", 0, 15), on(4), A.mult)
             act(B("xW"), IX(B("kw", 0, K0), B("XU", 0, 15)))
-            tt(B("bF", 0, 15), B("v1K", 16 * t, 16 * t + 15), B("nw", 0, 15), A.mult)
-            tt(B("GU", 0, 15), B("bF", 0, 15), B("XU", 0, 15), A.add)
+        phase("wpairs")
+        if not apart:
+            act(B("valu", 0, 240), IX(B("iw"), B("GU", 0, 15)))
+            lin("GF", B("GF", 0, 15), B("GU", 0, 15))
+            if CFG["wV"] < 15:
+                lin("nG", B("nG", 0, 15), B("GU", 0, 15), -1.0)
+            spairs(0, ("valu", 0), ("nG", 0), CFG["wV"])
+            pairs(0, ("valu", 0), ("GF", 0, 1), CFG["wV"])
         phase("xs")
         act(B("urep"), IX(B("iw", 0, V), B("uU", 0, 15)), bias=-2048.0)
         for s in (3, 2, 1):
@@ -1429,55 +1556,55 @@ def rank_program(g, core, T, topo):
         def event(e):
             phase("ev%d" % e)
             nev[0] += 1
-            p1, o = new(), 128 * e
-            src, r = ("eq1", 1920 * t) if e == 0 else ("eqm", 1920 * (e % 4))
-            lst = IX(B("on", 16 * e, 16 * e + 16), B("w8l"))
+            p1, o, r = new(), 128 * e, 120 * e
+            f = e if e or apart else 5
+            lst = IX(B("on", 16 * f, 16 * f + 16), B("w8l"))
             if e == S - 1 and CFG["early"]:
                 tt(B("W8", o, o + 128), IX(B("x"), B("w8l")), B("owE"), A.is_lt)
+            elif e == S - 1:
+                tt(B("W8", o, o + 128), IX(B("y"), B("w8l")), B("owE"), A.is_gt)
             elif e in CFG["w8v"]:
                 cp(B("W8", o, o + 128), lst)
+            elif e in CFG["sg"]:
+                act(B("W8", o, o + 128), lst, bias=0.5, scale=0.5)
             else:
                 act(B("W8", o, o + 128), lst)
-            terms = [(P(p1, 0, 15, p=8), B("idb", 0, 8), B("thw"))]
+            terms = [(Pc(p1, 0, 60), B("idb"), B("thw", 0, 60))]
             for a in range(15):
-                n = 240 - 16 * a
-                terms.append((P(p1, a, 15, p=8), B("W8", o + 8 * a, o + 8 * a + 8), B(src, r, r + n)))
-                r += n
+                for q in range(4):
+                    terms.append((Pc(p1, 4 * a, 60, p=8, p0=32 * q), B("W8", o + 8 * a, o + 8 * a + 8), EQ(r, r + 15 - a, 4 * q, 4 * q + 4), a == 14))
+                r += 15 - a
             group(terms, (1,))
-            act(B("cs", 256 * slot[e], 256 * slot[e] + 240, p=8), P(p1, 0, 15, p=8), SIGN)
+            act(B("cs", 64 * e, 64 * e + 60), Pc(p1, 0, 60), SIGN)
 
-        batches = CFG["jbatches" if joint else "batches"]
-        slot = {e: i for i, e in enumerate(e for batch in batches for e in batch)}
-        for batch in batches:
-            for e in batch:
-                event(e)
-            phase("of%d" % batch[0])
-            n, q = len(batch), slot[batch[0]]
-            c0 = 15 if n == 1 else 16
-            pb = new()
-            out = P(pb, 0, n, c=c0)
-            both = joint and batch == (0, 4)
-            terms = [(out, B("idb"), B("cneg", 96, 128) if both else B("cneg", 48, 32 + 16 * n + c0))]
-            for i, e in enumerate(batch):
-                vh = B("v1h", 16 * t, 16 * t + 15) if e == 0 else B("v16", 16 * (e % 4), 16 * (e % 4) + 15)
-                terms += [(P(pb, i, i + 1, c=15), B("ih"), vh), (P(pb, i, i + 1, c=15), B("idB"), on(e))]
-            group(terms + [(out, B("Us", 15 - c, 143 - c, p=8), B("cs", 256 * q + c, 256 * (q + n) - 256 + 16 * c0, 16, p=8)) for c in range(16)], (len(terms),))
-            e = 16 * (q + n) - 16 + c0
-            if both:
-                tt(B("of", 0, 15), P(pb, 0, 1, c=15), B("DJ", 0, 15), A.min)
-                tt(B("offU", 16 * q, 16 * q + 15), P(pb, 1, 2, c=15), B("of", 0, 15), A.min)
-            else:
-                tt(B("offU", 16 * q, e), out, B("Dm", 0, e - 16 * q), A.min)
+        def back(e, flag, const, vh, own):
+            out, o = P(new(), 0, 1, c=15), 64 * (e if apart else e % 4)
+            const = 64 if flag in CFG["sg"] else const
+            group([(out, B("idb"), B("cneg", const, const + 15)), (out, B("ih" if vh[3] == 2 else "idf"), vh), (out, B("idn" if flag in CFG["sg"] else "idB"), on(flag))]
+                  + [(out, B("Us", 3 - c, 131 - c), B("cs", o + c, o + 60, 4)) for c in range(4)], (3,))
+            tt(B("offU", 16 * e, 16 * e + 15), out, B(own, 0, 15), A.min)
+        slot = {e: e for e in range(5)}
+        for e in (3, 2, 1):
+            event(e)
+            phase("of%d" % e)
+            back(e, e, 48, B("v16", 16 * e, 16 * e + 15), "Dm")
+        event(0)
+        phase("of0")
+        back(0, 5 if joint else 0, 96, B("v1K", 16 * t, 16 * t + 15) if apart else B("GF", 0, 15), "DJ")
+        if apart:
+            event(4)
+        if not joint:
+            phase("of4")
+            back(4, 4, 112, B("WF" if apart else "GF", 0, 15), "Dm")
 
         def write(win, src, e):
             for a0, a1 in CFG["xparts"] if e == 4 else ((0, 15),):
                 cp(IX(win, B("offU", 16 * slot[e] + a0, 16 * slot[e] + a1)), B(src, 16 * a0, 16 * a1))
 
         phase("st4")
-        tt(B("p4", 0, 15), B("C", 768 + 15, 1008, 16), B("uI", 0, 15), A.mult)
-        tt(B("nI", 0, 15), B("p4", 0, 15), B("b4", 0, 15), A.add)
-        ts(B("nI", 16, 31), B("nI", 0, 15), 5, A.arith_shift_right, 4095, A.bitwise_and)
-        lin("nU", B("nU", 0, 15), B("nI", 16, 31))
+        scan(B("nI", 0, 45), B("c4", 0, 45), B("ub", 0, 45), A.mult, A.add)
+        ts(B("nI", 48, 63), B("nI", 2, 45, 3), 5, A.arith_shift_right, 4095, A.bitwise_and)
+        lin("nU", B("nU", 0, 15), B("nI", 48, 63))
         tt(B("kp"), IX(B("iw"), B("nU", 0, 15)), B("Bs", 720, 960), A.mult)
         tt(IX(B("kw", K0), B("offU", 16 * slot[S - 1], 16 * slot[S - 1] + 15)), B("kp"), B("cm"), A.add)
         for s in range(S - 1, 0, -1):
@@ -1498,7 +1625,7 @@ def rank_program(g, core, T, topo):
                 group([(pz, B("ih32"), kt)], start=False)
                 tt(B("kz", lo, hi), B("kp", lo, hi), pz, A.add)
                 ts(B("kn", lo, hi), B("kz", lo, hi), 5, A.arith_shift_right, 4095, A.bitwise_and)
-            write(B("kw") if joint and s == 1 else B("kw", K0), "kn", s - 1)
+            write(B("kw") if s == 1 else B("kw", K0), "kn", s - 1)
         if not joint:
             phase("xout")
             write(B("xw"), "xn", 4)
@@ -1524,25 +1651,26 @@ def rank_program(g, core, T, topo):
     phase("out")
     for a in range(8):
         act(B("idx", 128 * a, 128 * a + 128), B("idb"), scale=float(a + 1))
-        act(B("idk", 128 * a, 128 * a + 128), B("idb"), scale=float(a + 1))
+        act(B("idk", 128 * a, 128 * a + 128), B("idb"), scale=float(a + 1) if a else 35.0)
+    ms(B("shp", 0, 512), 2048.0)
     pa = P(new(), 0, 32)
-    group([(pa, B("idx", 128 * a, 128 * a + 128), B("xw", 512 * a, 512 * a + 512)) for a in range(8)])
-    act(B("ox"), pa)
+    group([(pa, B("idx", 128 * a, 128 * a + 128), B("xw", 512 * a, 512 * a + 512)) for a in range(8 - CFG["xblocks"], 8)])
+    if CFG["xblocks"] < 8:
+        tt(B("ox"), B("xw", 0, 512), pa, A.add)
+    else:
+        act(B("ox"), pa)
     dma("Y", "oy", T.yx[:], T.ox[:], [("ox", 0, 512)], [], 2000.0)
-    for h in range(2):
-        for a in range(8):
-            o = 512 * a + 256 * h
-            if a % 2:
-                act(B("shp", o, o + 256), B("kw", K0 + o, K0 + o + 256), bias=-2048.0)
+    for h, (lo, hi) in enumerate(CFG["osplit"]):
+        for a in range(1, 8):
+            o, e = 512 * a + lo, 512 * a + hi
+            if (a + h) % 2 == 0:
+                ts(B("shp", o, e), B("kw", K0 + o, K0 + e), -2048.0, A.add)
             else:
-                ts(B("shp", o, o + 256), B("kw", K0 + o, K0 + o + 256), -2048.0, A.add)
-        pb = P(new(), 0, 16)
-        group([(pb, B("idk", 128 * a, 128 * a + 128), B("shp", 512 * a + 256 * h, 512 * a + 256 * h + 256)) for a in range(8)], (2, 4, 6))
-        if h:
-            ts(B("ok", 256, 512), pb, 36.0 * 2048.0, A.add)
-        else:
-            act(B("ok", 0, 256), pb, bias=36.0 * 2048.0)
-        dma("YS"[h], "ok%d" % h, T.yk[:, 256 * h:256 * h + 256], T.ok[:, 256 * h:256 * h + 256], [("ok", 256 * h, 256 * h + 256)], [], 2000.0)
+                act(B("shp", o, e), B("kw", K0 + o, K0 + e), bias=-2048.0)
+        pb = Pc(new(), 0, hi - lo)
+        group([(pb, B("idk", 0, 128), B("shp", lo, hi))] + [(pb, B("idk", 128 * a, 128 * a + 128), B("shp", 512 * a + lo, 512 * a + hi)) for a in range(1, 8)], (1, 2, 4, 6))
+        tt(B("ok", lo, hi), B("kw", K0 + lo, K0 + hi), pb, A.add)
+        dma("YS"[h], "ok%d" % h, T.yk[:, lo:hi], T.ok[:, lo:hi], [("ok", lo, hi)], [], 2000.0)
     cnt = emit()
     for sem in ("oy", "ok0", "ok1"):
         g.sync.wait_ge(T.sem[sem], 16)

from concourse.bass import DstId, RemoteDMATransfer
from concourse.mybir import AluOpType, AxisListType, ActivationFunctionType

A = AluOpType
ID = ActivationFunctionType.Identity
RELU = ActivationFunctionType.Relu
ABS = ActivationFunctionType.Abs
SIGN = ActivationFunctionType.Sign
N, M, J, RACES, S, V = 4, 80, 3, 3, 4, 4096
L = J * M
WIN = V + 256
X0, K0 = 128, 128 + V
BIG = 2.0 ** 19
LAST = 2 ** 18 + 3 * 4096
CFG = {
    "groups": ((0, 4, "V"), (4, 8, "S"), (8, 12, "V"), (12, 15, "S")),
    "polish": (3000, 12000, 12000, 4000, 9000, 19200, 8000, 20000), "seeds": ((3,), (4,), (1, 3)), "heat6": 300.0, "period": 7400.0, "heatc": 1500.0, "alap": 1200.0, "spare": 1, "binds": 8, "heat5": 500.0, "tries": (4, 1), "heat0": 1200.0, "heat4": 1000.0, "since": 0.0, "heat1": 150.0, "turns": 6, "heat2": 500.0, "heat3": 400.0, "any": 0.05, "far": 12, "hope": 30.0,
    "zbank": ("pb3", "pb3", "pb3"), "tbank": ("pc", "pc", "pc"), "sbank": ("pb3", "pb3", "pb3"),
    "xcols": {0: (1, 1, 1, 1), 2: (1, 1, 1, 1)}, "eqs": 0, "vparts": {}, "onS": ("kU4", "WU", "GF", "nG", "uU", "cI4", "op", "nx"), "quad": True, "khs": (), "ksc": (3,), "kload": ((0, 1024), (1024, 2560), (2560, 4096)), "xload": ((0, 2048), (2048, 4096)), "jbatches": ((3,), (2,), (1,), (0, 4)), "wV": 5, "apart": (), "kparts": ((10, 15, 0), (4, 10, 0), (0, 4, 1)), "half": (), "w0": 0, "kvv": (), "ke": 3, "xh": (), "gsp": {0: ((2, 8),), 2: ((2, 8),)}, "sgv": (3,), "emerge": True, "apart2": None, "osplit": ((0, 352), (352, 512)), "iws": 256, "xblocks": 8, "ztr": (), "gap": (), "rv": (), "z3g": True, "d1T": True, "w54": True, "sg": (1, 2), "kfirst": True, "kwid": 2, "wS": 6, "z4s": (0,),
    "kbank": ("pb0", "pz", "pb2"), "inorder": False, "d1v": (), "flight": 2, "first": 7000.0, "piece": 2300.0, "ktv": (1, 2, 3), "abank": ("pa0", "pa1"), "batches": ((3,), (2,), (1, 4), (0,)), "spairs": {2: 11}, "gzx": True, "teams": ((0, 1), (2,), (3,)), "zv4": (0, 1, 2, 3), "cbank": "pc", "cbank2": "pc", "push": 2500.0, "early": False, "xparts": ((0, 4), (4, 8), (8, 12), (12, 15)),
    "zv": (0, 2), "kv": ((1, 1), (2, 1), (3, 1)), "w8v": (3,), "wpos": 3, "run": 512.0, "zfirst": (1, 1), "dif": (0, 1, 2),
    "bias": {}, "rounds": 40, "rounds2": 5, "lead": 13000.0, "heat": 150.0, "swap": 0.5, "rounds0": 0, "fb": 2, "parts": 0.3, "scols": 2, "seed": 52, "span": 4000.0, "shake": 1500.0,
    "cyc": 1.05, "lat": 220.0, "gam": 1.85, "sig": 4.3, "pe": 0.52, "rem": 0.9,
    "others": ({"weight": 1.0, "cyc": 0.85, "lat": 180.0, "gam": 1.5, "sig": 3.5, "pe": 0.47, "rem": 1.2},
               {"weight": 0.8, "cyc": 0.83, "lat": 250.0, "gam": 1.6, "sig": 3.8, "pe": 0.42, "rem": 0.6, "land": 1.1, "gx": 120.0},
               {"weight": 1.0, "cyc": 1.23, "lat": 230.0, "gam": 1.9, "sig": 4.6, "pe": 0.6, "rem": 1.1}),
}
CFG.update({"seeds": ((6,), (1, 2, 3), (1, 2, 3)), "kfirst": True, "kwid": 2, "early": True, "iws": 256, "g1": 3500.0, "first": 5500.0})
CFG["others"] += ({"weight": 0.9, "cyc": 1.15, "lat": 220.0, "gam": 1.15, "sig": 2.5, "pe": 0.6, "rem": 1.0},)
PLAN = {}

SCRATCH = {}
PIECE = {}
for _d, _l in (
        ("bfloat16", (("xw", WIN), ("ry", 512), ("xq", 1024), ("d0", 512), ("E", 1024), ("bsb", 96), ("cn2", 96), ("xg0", 512), ("xg1", 512), ("xm", 512),
                      ("zs", 240), ("zl", 720), ("zc", 720), ("on", 96), ("W8", 640), ("cs", 320),
                      ("Bs", 960), ("xW", 240), ("xn", 240), ("idb", 128), ("idn", 128), ("idB", 128), ("idM", 128), ("idX", 128), ("idS", 512),
                      ("U", 144), ("U1", 144), ("Us", 144), ("rm", 128), ("rz", 256), ("cneg", 128), ("cls", 64), ("gt4", 256), ("Un", 144), ("z3", 256), ("Wk", 32),
                      ("thw", 64), ("idx", 1024), ("ones", 128))),
        ("float16", (("zh", 2304), ("ih2", 128), ("Dif", 48), ("ih", 128), ("ihn", 128), ("ih32", 128), ("ihd", 128),
                     ("Uh", 144), ("zT", 768), ("En", 1024), ("zW", 240), ("toth", 1), ("val", 960), ("v16", 80), ("urep", 240), ("kt", 240), ("m2k", 480), ("zt", 1024), ("xr", 240), ("idk", 1024))),
        ("float32", (("kw", K0 + WIN), ("iw", K0 + V), ("idf", 128), ("R", 1024), ("C", 1024), ("nb", 64), ("kcol", 64), ("nk", 64), ("GF", 16), ("nG", 16), ("th4", 16), ("valf", 64), ("kq", 64),
                     ("xs", 960), ("kp", 240), ("of", 80), ("Dm", 64), ("base", 64), ("bs", 64), ("ln", 16), ("bF", 16), ("ge", 16), ("xy", 16),
                     ("d1", 64), ("w1", 64), ("tot", 16), ("zg", 1040), ("DJ", 16), ("v1K", 48), ("WF", 16), ("kF", 16), ("nw", 16), ("c4", 48), ("thr", 2), ("wt", 32), ("cm", 240), ("x3", 16), ("op", 16), ("op2", 16), ("g0", 16), ("wf", 16), ("ow1", 16), ("ow2", 16), ("ow4", 16), ("owE", 128), ("pF", 32), ("ox", 512), ("ok", 512), ("t8", 8))),
        ("int32", (("kin", V), ("vs", 45), ("vl", 135), ("vI", 48), ("wz", 64), ("u4", 64), ("m1", 32), ("m3", 96), ("fl", 48), ("own", 48),
                   ("rcv", 432), ("rk", 48), ("xu", 16), ("x", 16), ("y", 16), ("uI", 16), ("dI", 16), ("WI", 16), ("bI", 16), ("cI", 64), ("kI", 64), ("kz", 240), ("kn", 240),
                   ("nI", 64), ("ub", 48), ("pI", 16))),
        ("uint16", (("kvu", 256), ("valu", 1200), ("vU", 240), ("kU", 64), ("WU", 16), ("bU", 16), ("uU", 16), ("nU", 16), ("XU", 16), ("GU", 16), ("offU", 80), ("w8l", 8)))):
    for _n, _w in _l:
        if _d == "float32" and _w <= 64:
            PIECE[_n] = ("small", 64 * len(PIECE), _w)
        else:
            SCRATCH[_n] = ("sbuf", [128, _w], _d)
SCRATCH["small"] = ("sbuf", [128, 64 * len(PIECE)], "float32")
SCRATCH["Y"] = ("sbuf", [128, 16, 256], "bfloat16")
BANKS = ["ps%d" % _n for _n in range(8)]
for _n in BANKS:
    SCRATCH[_n] = ("psum", [128, 512], "float32")
SCRATCH["eqm"] = ("sbuf", [128, 600, 16], "bfloat16")
SCRATCH["zx"] = ("sbuf", [128, 4096], "bfloat16")
SCRATCH["shp"] = ("sbuf", [128, 4096], "float16")
SCRATCH["cw"] = ("sbuf", [128, 3, 32], "float32")
SCRATCH["Ys"] = ("sbuf", [128, 256, 16], "bfloat16")
SCRATCH["kE"] = ("sbuf", [128, 16, 32], "float16")
SCRATCH["kG"] = ("sbuf", [128, 16, 48], "float16")
SEMAPHORES = ["qV", "qS", "qT", "qG", "zin", "vin", "ld0", "ld1", "ld2", "ld3", "ld4", "ld5", "az", "av", "a0", "a1", "a2",
              "lz", "lv", "l0", "l1", "l2", "oy", "ok0", "ok1", "e0", "e1", "e2", "f0", "f1", "f2", "u0", "u1", "u2", "w0", "w1", "w2"]


def planner(g, T, late_bound):
    queues = {"V": g.vector, "S": g.scalar, "T": g.tensor, "G": g, "Y": g.sync}
    ops = []
    plan = {}
    bias = [0.0, (-1, ""), 0]

    def cost(p, m):
        return p[0] + m["cyc"] * (p[1] + m["gam"] * p[2] + m["sig"] * p[3]) + m["pe"] * p[4] + m["rem"] * sum(p[5:6]) + m.get("land", m["rem"]) * sum(p[6:7]) + m.get("gx", 0.0) * sum(p[7:])

    def is_psum(b):
        return b[0] == "@"

    def hazards(recs, q, R, W):
        out = []
        for b, lo, hi in R:
            ps = is_psum(b)
            for r in recs.get(b, []):
                if r[0] < hi and lo < r[1] and r[2] or ps and r[3] != q:
                    out.append(r)
        for b, lo, hi in W:
            ps = is_psum(b)
            for r in recs.get(b, []):
                if ps or (r[0] < hi and lo < r[1]):
                    out.append(r)
        return out

    def note(recs, q, R, W, tag):
        for b, lo, hi in W:
            recs[b] = [r for r in recs.get(b, []) if not (lo <= r[0] and r[1] <= hi)] + [(lo, hi, True, q, tag)]
        for b, lo, hi in R:
            recs[b] = recs.get(b, []) + [(lo, hi, False, q, tag)]

    def rec(q, kind, fn, R, W, dur, lat, sem=None, val=0, after=None):
        i = len(ops)
        parts = dur if isinstance(dur, tuple) else (dur, 0, 0, 0, 0)
        dur = cost(parts, CFG)
        rq = q if kind == "c" else kind + str(i)
        deps = {}
        for reads, found in ((True, hazards(plan, rq, R, [])), (False, hazards(plan, rq, [], W))):
            for r in found:
                x = 0 if r[3] == rq and (q == "T" or not reads and CFG["inorder"]) else ops[r[4]]["lat"]
                deps[r[4]] = max(deps.get(r[4], 0), x)
        if after is not None:
            deps[after] = 0
        note(plan, rq, R, W, i)
        bias[2] += 1
        ops.append({"id": (bias[1][0], bias[1][1], bias[2]), "q": q, "kind": kind, "fn": fn, "dur": dur, "parts": parts, "sem": sem, "val": val, "lat": lat, "deps": deps, "uses": {b for b, lo, hi in list(R) + list(W) if is_psum(b)}, "txt": (W[0][0] if W else kind)})
        return i

    def emit():
        n = len(ops)
        succ = [[] for _ in range(n)]
        left = [len(o["deps"]) for o in ops]
        for i, o in enumerate(ops):
            for d, x in o["deps"].items():
                succ[d].append((i, x))
        prio = [0.0] * n
        for i in range(n - 1, -1, -1):
            prio[i] = ops[i]["dur"] + max([x + prio[k] for k, x in succ[i]] + [0.0])
        push = [CFG["push"] if o["txt"] == "xw" and o["id"][0] >= 0 else 0.0 for o in ops]
        near = [0.0] * n
        for i in range(n - 1, -1, -1):
            near[i] = ops[i]["dur"] + max([x + near[k] for k, x in succ[i] if ops[k]["id"][0] == ops[i]["id"][0]] + [push[i]])
        pred = [list(o["deps"].items()) for o in ops]
        dur = [o["dur"] for o in ops]
        others = [(m["weight"], m["lat"], [cost(o["parts"], m) for o in ops]) for m in CFG["others"]]
        queue = [o["q"] for o in ops]
        twin = {o["id"]: i for i, o in enumerate(ops)}

        def place(rank, before):
            start = {}
            busy = {q: ([], []) for q in queues}
            end = [-1e9] * n
            for i in rank:
                t, w = 0.0, dur[i]
                for d, x in before[i]:
                    if end[d] + x > t:
                        t = end[d] + x
                if queue[i] != "N":
                    lo, hi = busy[queue[i]]
                    a = b = len(hi)
                    while a and hi[a - 1] > t:
                        a -= 1
                    while a < b and lo[a] < t + w:
                        if hi[a] > t:
                            t = hi[a]
                        a += 1
                    lo.insert(a, t)
                    hi.insert(a, t + w)
                start[i] = t
                end[i] = t + w
            return start, max(end)
        seed = [CFG["seed"]]

        def draw():
            seed[0] = (seed[0] * 1103515245 + 12345) % 2 ** 31
            return (seed[0] >> 8) % 4096 / 4096.0

        def improve(part, key, rounds):
            inside = set(part)
            fore = {i: [e for e in pred[i] if e[0] in inside] for i in part}
            back = {i: [e for e in succ[i] if e[0] in inside] for i in part}
            best = top = None
            for r in range(rounds):
                if r % CFG["fb"] == 0:
                    for i in part:
                        for d, x in fore[i]:
                            if key[i] <= key[d]:
                                key[i] = key[d] + 1e-3
                start, end = place(sorted(part, key=lambda i: (key[i], i)), fore)
                if best is None or end < 1.01 * best[0]:
                    rank, score = sorted(part, key=lambda i: (start[i], i)), end
                    for w, lat, other in others:
                        fin, free = {}, {q: 0.0 for q in "VSTGYN"}
                        for i in rank:
                            t = free[queue[i]] if queue[i] != "N" else 0.0
                            for d, x in fore[i]:
                                if fin[d] + (lat if x == CFG["lat"] else x) > t:
                                    t = fin[d] + (lat if x == CFG["lat"] else x)
                            fin[i] = free[queue[i]] = t + other[i]
                        score += w * max(fin.values())
                    if best is None or score < best[2] + CFG["heat"] * (1.0 - r / rounds) * draw():
                        best = (end, start, score)
                        top = best if top is None or score < top[2] else top
                        ahead, tight, i = {}, [], rank[-1]
                        free = {}
                        for j in rank:
                            ahead[j], free[queue[j]] = free.get(queue[j]), j
                            if start[j] + dur[j] > start[i] + dur[i]:
                                i = j
                        while i is not None:
                            j = [d for d, x in fore[i] if start[d] + dur[d] + x > start[i] - 1e-3]
                            if not j and ahead[i] is not None and start[ahead[i]] + dur[ahead[i]] > start[i] - 1e-3:
                                tight.append((ahead[i], i))
                                j = [ahead[i]]
                            i = j[0] if j else None
                if r % CFG["fb"] == CFG["fb"] - 1:
                    mid, key = draw() * best[0], dict(best[1])
                    if tight and draw() < CFG["swap"]:
                        for _ in range(1 + int(draw() * 2)):
                            j, i = tight[int(draw() * len(tight))]
                            key[j] = key[i] + 1.0 + draw() * draw() * CFG["shake"]
                    elif draw() < CFG["parts"]:
                        j, by = part[int(draw() * len(part))], (draw() - 0.5) * 2 * CFG["shake"]
                        for i in part:
                            if ops[i]["id"][:2] == ops[j]["id"][:2]:
                                key[i] += by
                    else:
                        for i in part:
                            if abs(key[i] - mid) < CFG["span"]:
                                key[i] += draw() * CFG["shake"]
                else:
                    late, end = place(sorted(part, key=lambda i: (-start[i] - dur[i], -i)), back)
                    key = {i: -late[i] - dur[i] for i in part}
            return top
        models = [(CFG["w0"], CFG["lat"], dur)] * (CFG["w0"] > 0) + others

        def polish(seq, rounds, heat, after=None, since=0.0, until=1.0):
            loc = {i: k for k, i in enumerate(seq)}
            m, nm = len(seq), len(models)
            above, ps = [0] * m, []
            for k, i in enumerate(seq):
                d0 = [(loc[d], x) for d, x in pred[i] if d in loc]
                ps.append([(d, x) for d, x in d0 if x not in (0, CFG["lat"]) or not any(above[e] >> d & 1 for e, y in d0)])
                for d, x in d0:
                    above[k] |= above[d] | 1 << d
            ss = [[] for _ in seq]
            for k in range(m):
                for d, x in ps[k]:
                    ss[d].append((k, x))
            du = [[o[i] for i in seq] for w, lat, o in models]
            pm = [[[(d, du[j][d] + (models[j][1] if x == CFG["lat"] else x)) for d, x in ps[k]] for k in range(m)] for j in range(nm)]
            sm = [[[(d, models[j][1] if x == CFG["lat"] else x) for d, x in ss[k]] for k in range(m)] for j in range(nm)]
            pd, sd = [[d for d, x in e] for e in ps], [[d for d, x in e] for e in ss]
            qu = [queue[i] for i in seq]
            ex = [[after(j, i) if after else 0.0 for i in seq] for j in range(nm)]
            wt = [w for w, lat, o in models]
            order, pos = list(range(m)), list(range(m))
            mp, mn, free = [-1] * m, [-1] * m, {}
            for k in order:
                if qu[k] != "N":
                    if qu[k] in free:
                        mp[k], mn[free[qu[k]]] = free[qu[k]], k
                    free[qu[k]] = k
            hd, tl = [[0.0] * m for _ in models], [[0.0] * m for _ in models]

            def heads(run, j, h):
                d, p = du[j], pm[j]
                for k in run:
                    e = mp[k]
                    t = h[e] + d[e] if e >= 0 else 0.0
                    for e, x in p[k]:
                        if h[e] + x > t:
                            t = h[e] + x
                    h[k] = t

            def tails(run, j, h):
                d, p, q = du[j], sm[j], ex[j]
                for k in run:
                    e = mn[k]
                    t = q[k]
                    if e >= 0 and h[e] > t:
                        t = h[e]
                    for e, x in p[k]:
                        if h[e] + x > t:
                            t = h[e] + x
                    h[k] = t + d[k]

            def link(run):
                for x, y in zip(run, run[1:]):
                    if x >= 0:
                        mn[x] = y
                    if y >= 0:
                        mp[y] = x

            def tight(j):
                h, g, top = hd[j], tl[j], cur[j] - 1e-3
                return [k for k in range(m) if h[k] + g[k] > top and since * top <= h[k] <= until * top and mp[k] >= 0 and h[mp[k]] + du[j][mp[k]] > h[k] - 1e-3 and h[mp[k]] + g[mp[k]] > top]
            for j in range(nm):
                heads(order, j, hd[j])
                tails(order[::-1], j, tl[j])
            cur = [max(a + b for a, b in zip(hd[j], tl[j])) for j in range(nm)]
            crit = [tight(j) for j in range(nm)]
            best = (sum(w * c for w, c in zip(wt, cur)), list(order), list(cur))
            for r in range(rounds):
                j = int(draw() * nm)
                c = crit[j] = crit[j] or tight(j)
                if not c or draw() < CFG["any"]:
                    v = order[int((since + draw() * (until - since)) * m)]
                    if mp[v] < 0:
                        continue
                else:
                    v = c[int(draw() * len(c))]
                u, far = mp[v], int(draw() ** 3 * CFG["far"])
                if draw() < 0.5:
                    while far and mp[u] >= 0:
                        u, far = mp[u], far - 1
                    win, mark, q = order[pos[u]:pos[v] + 1], {v}, qu[v]
                    for k in win[-2::-1]:
                        if (mn[k] in mark and qu[k] != q) or not mark.isdisjoint(sd[k]):
                            mark.add(k)
                    if u in mark:
                        continue
                    new = [k for k in win if k in mark] + [k for k in win if k not in mark]
                else:
                    while far and mn[v] >= 0:
                        v, far = mn[v], far - 1
                    win, mark, q = order[pos[u]:pos[v] + 1], {u}, qu[v]
                    for k in win[1:]:
                        if (mp[k] in mark and qu[k] != q) or not mark.isdisjoint(pd[k]):
                            mark.add(k)
                    if v in mark:
                        continue
                    new = [k for k in win if k not in mark] + [k for k in win if k in mark]
                a, b = mp[u], mn[v]
                link([a] + [k for k in new if qu[k] == q] + [b])
                keep, gain, room = [], 0.0, heat * (1.0 - r / rounds) * draw() ** 2
                for j in range(nm):
                    h, g = hd[j], tl[j]
                    keep.append(([h[k] for k in new], [g[k] for k in new]))
                    heads(new, j, h)
                    tails(new[::-1], j, g)
                    e = max(h[k] + g[k] for k in new) - cur[j]
                    gain += wt[j] * (e if e > 0 else max(e, -CFG["hope"]) * 0.5)
                if gain > room:
                    for j in range(nm):
                        for k, x, y in zip(new, *keep[j]):
                            hd[j][k], tl[j][k] = x, y
                    link([a] + [k for k in win if qu[k] == q] + [b])
                    continue
                p0 = pos[win[0]]
                order[p0:p0 + len(new)] = new
                for k, i in enumerate(new):
                    pos[i] = p0 + k
                hi = max([pos[e] for k in new for e in sd[k]] + [pos[mn[k]] for k in new if mn[k] >= 0] + [0])
                lo = min([pos[e] for k in new for e in pd[k]] + [pos[mp[k]] for k in new if mp[k] >= 0] + [m])
                for j in range(nm):
                    h, d, p, far, i = hd[j], du[j], pm[j], hi, p0 + len(new)
                    while i <= far:
                        k = order[i]
                        i += 1
                        e = mp[k]
                        t = h[e] + d[e] if e >= 0 else 0.0
                        for e, x in p[k]:
                            if h[e] + x > t:
                                t = h[e] + x
                        if t != h[k]:
                            h[k] = t
                            e = mn[k]
                            if e >= 0 and pos[e] > far:
                                far = pos[e]
                            for e in sd[k]:
                                if pos[e] > far:
                                    far = pos[e]
                    h, p, q, far, i = tl[j], sm[j], ex[j], lo, p0 - 1
                    while i >= far:
                        k = order[i]
                        i -= 1
                        e = mn[k]
                        t = q[k]
                        if e >= 0 and h[e] > t:
                            t = h[e]
                        for e, x in p[k]:
                            if h[e] + x > t:
                                t = h[e] + x
                        t += d[k]
                        if t != h[k]:
                            h[k] = t
                            e = mp[k]
                            if e >= 0 and pos[e] < far:
                                far = pos[e]
                            for e in pd[k]:
                                if pos[e] < far:
                                    far = pos[e]
                    cur[j] = max(h)
                crit = [None] * nm
                e = sum(w * c for w, c in zip(wt, cur))
                if e < best[0]:
                    best = (e, list(order), list(cur))
            return [seq[k] for k in best[1]], best[2]

        def times(seq, j):
            w, lat, o = models[j] if j >= 0 else (1.0, CFG["lat"], dur)
            start, free = {}, {}
            for i in seq:
                t = free.get(queue[i], 0.0) if queue[i] != "N" else 0.0
                for d, x in pred[i]:
                    if d in start:
                        t = max(t, start[d] + o[d] + (lat if x == CFG["lat"] else x))
                start[i] = t
                free[queue[i]] = t + o[i]
            return start, max(start[i] + o[i] for i in seq)

        def cyclic(seq, rounds, heat, after=None):
            loc = {i: k for k, i in enumerate(seq)}
            m, nm = len(seq), len(models)
            start = times(seq, -1)[0]
            step = [ops[i]["id"][1][0] for i in seq]
            names = [(ops[i]["id"][1][1], ops[i]["id"][2], ops[i]["id"][1][1][0] == "z" and s == S) for i, s in zip(seq, step)]
            kinds = {x: k for k, x in enumerate(sorted(set(names)))}
            kind, per = [kinds[x] for x in names], CFG["period"]
            ph = [0.0] * len(kinds)
            for s in (4, 1, 3, 2):
                for k, i in enumerate(seq):
                    if step[k] == s:
                        ph[kind[k]] = start[i] - per * s + 1e-3 * k
            ps = [[(loc[d], x) for d, x in pred[i] if d in loc] for i in seq]
            du = [[o[i] for i in seq] for w, lat, o in models]
            pm = [[[(d, du[j][d] + (models[j][1] if x == CFG["lat"] else x)) for d, x in ps[k]] for k in range(m)] for j in range(nm)]
            ex = [[du[j][k] + (after(j, i) if after else 0.0) for k, i in enumerate(seq)] for j in range(nm)]
            arcs = sorted({(kind[d], kind[k], per * (step[k] - step[d])) for k in range(m) for d, x in ps[k]})
            up, down = [[] for _ in kinds], [[] for _ in kinds]
            for a, b, c in arcs:
                up[b].append((a, c))
                down[a].append((b, c))
            qu = [queue[i] for i in seq]

            def mend(ph, todo, sign):
                for _ in range(400):
                    if not todo:
                        return True
                    b = todo.pop()
                    for a, c in (up if sign < 0 else down)[b]:
                        if sign < 0 and ph[a] >= ph[b] + c or sign > 0 and ph[a] + c <= ph[b]:
                            ph[a] = ph[b] - sign * c + sign * 0.01
                            todo.append(a)
                return False

            def rate(ph):
                order = sorted(range(m), key=lambda k: ph[kind[k]] + per * step[k])
                mp, free, hs = [-1] * m, {}, []
                for k in order:
                    if qu[k] != "N":
                        mp[k] = free.get(qu[k], -1)
                        free[qu[k]] = k
                for j in range(nm):
                    h, d, p = [0.0] * m, du[j], pm[j]
                    for k in order:
                        e = mp[k]
                        t = h[e] + d[e] if e >= 0 else 0.0
                        for e, x in p[k]:
                            if h[e] + x > t:
                                t = h[e] + x
                        h[k] = t
                    hs.append(h)
                ends = [max(map(sum, zip(hs[j], ex[j]))) for j in range(nm)]
                return sum(w[0] * e for w, e in zip(models, ends)), order, mp, hs, ends

            def tight(state, j):
                h, mp, out = state[3][j], state[2], []
                k = max(range(m), key=lambda k: h[k] + ex[j][k])
                while k >= 0:
                    e = [d for d, x in pm[j][k] if h[d] + x > h[k] - 1e-3]
                    if not e and mp[k] >= 0:
                        out.append(k)
                        e = [mp[k]]
                    k = e[0] if e else -1
                return out
            while not mend(ph, list(range(len(kinds))), 1):
                pass
            cur = best = rate(ph)
            crit = [None] * nm
            for r in range(rounds):
                j = int(draw() * nm)
                c = crit[j] = crit[j] or tight(cur, j)
                v = c[int(draw() * len(c))] if c and draw() > CFG["any"] else int(draw() * m)
                u, far, mp = cur[2][v], int(draw() ** 3 * CFG["far"]), cur[2]
                if u < 0 or kind[u] == kind[v]:
                    continue
                new = list(ph)
                if draw() < 0.5:
                    while far and mp[u] >= 0:
                        u, far = mp[u], far - 1
                    new[kind[v]] = ph[kind[u]] + per * (step[u] - step[v]) - 0.5 - draw()
                    ok = mend(new, [kind[v]], -1) and new[kind[u]] == ph[kind[u]]
                else:
                    new[kind[u]] = ph[kind[v]] + per * (step[v] - step[u]) + 0.5 + draw() + far * draw() * 150.0
                    ok = mend(new, [kind[u]], 1) and new[kind[v]] == ph[kind[v]]
                if ok:
                    e = rate(new)
                    if e[0] < cur[0] + heat * (1.0 - r / rounds) * draw() ** 2:
                        ph, cur, crit = new, e, [None] * nm
                        if e[0] < best[0]:
                            best = e
                        if r % 16 == 0:
                            t = [0.0] * len(kinds)
                            for k in cur[1]:
                                t[kind[k]] = ph[kind[k]]
            return [seq[k] for k in best[1]], best[4]

        def better(seq, rounds, heat, after=None, turns=CFG["turns"]):
            inside = set(seq)
            fore = {i: [e for e in pred[i] if e[0] in inside] for i in seq}
            back = {i: [e for e in succ[i] if e[0] in inside] for i in seq}
            best = None
            for r in range(turns):
                seq, e = polish(seq, rounds // turns, heat * (1.0 - r / turns), after)
                e0 = sum(w[0] * x for w, x in zip(models, e))
                if best is None or e0 < best[0]:
                    best = (e0, seq, e)
                start = times(seq, -1)[0]
                late = place(sorted(seq, key=lambda i: (-start[i] - dur[i], -i)), back)[0]
                start = place(sorted(seq, key=lambda i: (-late[i] - dur[i], i)), fore)[0]
                seq = sorted(seq, key=lambda i: (start[i], i))
            return best[1:]

        members, extra = {}, []
        for i in range(n):
            for u in ops[i]["uses"]:
                members.setdefault(u, []).append(i)

        def bind(lists):
            for d, i, x in extra:
                pred[i].remove((d, x))
                succ[d].remove((i, x))
            extra[:] = [(d, members[w][0], 0 if queue[d] == "T" else CFG["lat"]) for e in lists.values() for u, w in zip(e, e[1:]) for d in members[u]]
            for d, i, x in extra:
                pred[i].append((d, x))
                succ[d].append((i, x))

        def topo(part, key):
            inside = set(part)
            left = {i: sum(d in inside for d, x in pred[i]) for i in part}
            ready, out = [i for i in part if not left[i]], []
            while ready:
                i = min(ready, key=lambda i: (key[i], i))
                ready.remove(i)
                out.append(i)
                for k, x in succ[i]:
                    if k in inside:
                        left[k] -= 1
                        if not left[k]:
                            ready.append(k)
            return out

        def banks(seq, alap, spare):
            start = times(seq, -1)[0]
            bind({})
            mem = {u: e for u, e in members.items() if e[0] in start}
            bit, above, key = {u: 1 << k for k, u in enumerate(mem)}, {}, dict(start)
            for i in seq:
                above[i] = 0
                for d, x in pred[i]:
                    if d in start:
                        above[i] |= above[d] | sum(bit[u] for u in ops[d]["uses"])
            opens = {e[0]: u for u, e in mem.items()}
            for k0, i in reversed(list(enumerate(seq))):
                if alap is None:
                    key[i] = k0
                elif queue[i] == "T":
                    key[i] = max(start[i], min(key[k] - dur[i] - (alap if x else alap / 4) for k, x in succ[i] if k in start))
            need = {u: 0 for u in mem}
            for u, e in mem.items():
                for i in e:
                    need[u] |= above[i]
                need[u] &= ~bit[u]
            lists, where, todo, done, got = {b: [] for b in BANKS}, {}, {u: len(e) for u, e in mem.items()}, {b: -1.0 for b in BANKS}, 0
            left = {i: sum(d in start for d, x in pred[i]) for i in seq}
            ready, out = [i for i in seq if not left[i]], []
            while ready:
                idle = [b for b in BANKS if not lists[b] or not todo[lists[b][-1]]]
                i = min([i for i in ready if i not in opens or len(idle) > (spare if need[opens[i]] & ~got else 0)], key=lambda i: (key[i], i))
                if i in opens:
                    where[opens[i]] = min(idle, key=lambda b: (done[b], b))
                    lists[where[opens[i]]].append(opens[i])
                    got |= bit[opens[i]]
                for u in ops[i]["uses"]:
                    todo[u] -= 1
                    done[where[u]] = max(done[where[u]], start[i] + dur[i])
                ready.remove(i)
                out.append(i)
                for k, x in succ[i]:
                    if k in start:
                        left[k] -= 1
                        if not left[k]:
                            ready.append(k)
            bind(lists)
            return out, lists

        def follow(part, nxt):
            rest, first = [], []
            for w, lat, o in models:
                g, free = {}, {}
                for i in reversed(nxt):
                    t = max([g[k] + (lat if x == CFG["lat"] else x) for k, x in succ[i] if k in g] + [free.get(queue[i], 0.0)])
                    g[i] = t + o[i]
                    if queue[i] != "N":
                        free[queue[i]] = g[i]
                top = max(g.values())
                rest.append({i: max([g[k] + (lat if x == CFG["lat"] else x) - top for k, x in succ[i] if k in g] + [free.get(queue[i], 0.0) - top]) for i in part})
            return lambda j, i: rest[j][i]
        if n not in PLAN and CFG["polish"]:
            race = [[i for i in range(n) if ops[i]["id"][0] == t] for t in range(RACES)]
            if CFG.get("probe"):
                part = [i for i in race[1] if CFG["probe"](ops[i])]
                span, one, _ = improve(part, {i: -prio[i] for i in range(n)}, CFG["rounds"])
                mid, e = better(sorted(part, key=lambda i: (one[i], i)), CFG["polish"][1], CFG["heat2"])
                if CFG["polish"][2] > 1:
                    mid, e = cyclic(mid, CFG["polish"][2], CFG["heatc"])
                    PLAN["cyc"] = e
                mid, e = better(mid, CFG["polish"][0], CFG["heat1"])
                PLAN.update(ops=ops, seq=mid, e=e, st=times(mid, 0)[0])
                raise ValueError("probe")
            need = {i for i in race[1] if ops[i]["kind"] == "s"}
            for i in reversed(race[1]):
                if i in need:
                    need.update(d for d, x in pred[i] if ops[d]["id"][0] == 1)
            inside, rest = set(race[1]), []
            for w, lat, o in models:
                g = {}
                for i in reversed(race[1]):
                    g[i] = max([g[k] + o[k] + (lat if x == CFG["lat"] else x) for k, x in succ[i] if k in inside and k not in need] + [0.0])
                rest.append(g)
            score = lambda e: sum(w[0] * x for w, x in zip(models, e[1]))

            def like(mid, t):
                rank = {ops[i]["id"][1:]: k for k, i in enumerate(mid)}
                key = {}
                for i in race[t]:
                    key[i] = max([rank.get(ops[i]["id"][1:], 0)] + [key[d] + 1e-3 for d, x in pred[i] if d in key])
                return sorted(race[t], key=lambda i: (key[i], i))

            def rebind(seq, lists, rounds, heat, after):
                best = None
                for r in range(CFG["binds"]):
                    e = better(seq, rounds // CFG["binds"], heat * (1.0 - r / CFG["binds"]), after(r), 2)
                    if best is None or score(e) < score(best[0]):
                        best = (e, lists)
                    seq, lists = banks(e[0], None, 0)
                return best
            found = []
            for seed[0] in CFG["seeds"][0]:
                bind({})
                tried = []
                for _ in range(CFG["tries"][0]):
                    one = improve(sorted(need), {i: -prio[i] for i in range(n)}, CFG["rounds"])[1]
                    tried.append(better(sorted(need, key=lambda i: (one[i], i)), CFG["polish"][3], CFG["heat0"], lambda j, i: rest[j][i]))
                first, PLAN["first"] = better(min(tried, key=score)[0], CFG["polish"][3], CFG["heat2"], lambda j, i: rest[j][i])
                one = place(first + sorted(inside - need, key=lambda i: (-near[i], i)), {i: [e for e in pred[i] if e[0] in inside] for i in race[1]})[0]
                mid = sorted(race[1], key=lambda i: (one[i], i))
                after = follow(mid, like(mid, 2))
                mid = polish(mid, CFG["polish"][4], CFG["heat4"], lambda j, i: after(j, i) + push[i], CFG["since"])[0]
                mid, PLAN["free"] = better(mid, CFG["polish"][0], CFG["heat1"], after)
                mid, lists = banks(mid, CFG["alap"], CFG["spare"])
                found.append(rebind(mid, lists, CFG["polish"][5], CFG["heat5"], lambda r: after) + (after,))
            PLAN["found"] = [[round(x) for x in e[0][1]] for e in found]
            (mid, PLAN["one"]), lists, after = min(found, key=lambda e: score(e[0]))
            if CFG["polish"][7]:
                bind(lists)
                (mid, PLAN["one"]), lists = min(((mid, PLAN["one"]), lists), rebind(mid, lists, CFG["polish"][7], CFG["heat6"], lambda r: after), key=lambda e: score(e[0]))
            if CFG.get("stop1"):
                raise ValueError("probe")
            begin = [i for i in range(n) if ops[i]["id"][0] < 0 and i < race[0][0]]
            close = [i for i in range(n) if ops[i]["id"][0] < 0 and i > race[2][0]]
            bind(lists)
            one = times(mid, -1)[0]
            found = []
            for seed[0] in CFG["seeds"][1]:
                bind({})
                tail, last = banks(like(mid, 2) + close, None, 1)
                found.append(rebind(tail, last, CFG["polish"][2], CFG["heat5"], lambda r: lambda j, i: push[i] * (r < 2)))
            PLAN["tails"] = [[round(x) for x in e[0][1]] for e in found]
            (tail, PLAN["tail"]), last = min(found, key=lambda e: score(e[0]))
            ident = {ops[e[0]]["id"]: u for u, e in members.items()}
            whole = {b: [ident[(0,) + ops[members[u][0]]["id"][1:]] for u in e] + e + last[b] for b, e in lists.items()}
            for b, u in zip(BANKS, [u for u, e in members.items() if e[0] in begin]):
                whole[b].insert(0, u)
            bind(whole)
            PLAN["bank"], PLAN["extra"] = {u: b for b, e in whole.items() for u in e}, list(extra)
            key = {i: (prio[0] - prio[i] if ops[i]["id"][0] < 0 else CFG["lead"] + one[twin[(1,) + ops[i]["id"][1:]]]) for i in begin + race[0]}
            head = begin + race[0]
            inside = set(head)
            st = place(topo(head, key), {i: [e for e in pred[i] if e[0] in inside] for i in head})[0]
            found = []
            for seed[0] in CFG["seeds"][2]:
                e = better(sorted(head, key=lambda i: (st[i], i)), CFG["polish"][1], CFG["heat3"], follow(head, mid))
                found.append(polish(e[0], CFG["polish"][6], CFG["heat3"], follow(head, mid), 0.0, 0.45))
            PLAN["heads"] = [[round(x) for x in e[1]] for e in found]
            head, PLAN["head"] = min(found, key=score)
            seq = head + mid + tail
            PLAN["all"] = [times(seq, j)[1] for j in range(len(models))]
            PLAN["seq"] = seq
            PLAN[n] = (PLAN["all"][0], times(seq, 0)[0], sum(w[0] * e for w, e in zip(models, PLAN["all"])))
        if n not in PLAN:
            part = [i for i in range(n) if ops[i]["id"][0] == 1]
            key = {i: -prio[i] for i in range(n)}
            if CFG["rounds0"]:
                need = {max(i for i in part if ops[i]["kind"] == "s")}
                for i in reversed(part):
                    if i in need:
                        need.update(d for d, x in pred[i] if ops[d]["id"][0] == 1)
                span, one, _ = min((improve(sorted(need), dict(key), CFG["rounds0"]) for _ in range(CFG["tries"])), key=lambda b: b[2])
                PLAN["pre"] = span
                key = {i: one[i] if i in need else span + prio[max(need)] - prio[i] + 1e5 for i in part}
            span, one, _ = improve(part, key, CFG["rounds"])
            key = {i: (prio[0] - prio[i] if ops[i]["id"][0] < 0 else CFG["lead"] + span * ops[i]["id"][0] + one[twin[(1,) + ops[i]["id"][1:]]]) for i in range(n)}
            PLAN["one"] = span
            PLAN[n] = improve(list(range(n)), key, CFG["rounds2"])
        PLAN["ops"] = ops
        for d, i, x in PLAN["extra"]:
            ops[i]["deps"][d] = max(x, ops[i]["deps"].get(d, 0))
        for e in late_bound:
            u, p0, p, lo, hi = e[7]
            e[0] = T[PLAN["bank"][u]][p0:p0 + p, lo:hi]
        order = [(0, 0, i) for i in PLAN["seq"]] if "seq" in PLAN else sorted((PLAN[n][1][i], i, i) for i in range(n))
        cnt = {q: 0 for q in queues}
        clk = {q: {} for q in queues}
        snap = {}
        tag = {}
        for _, _, i in order:
            o = ops[i]
            q = o["q"]
            if o["kind"] == "n":
                tag[i] = (o["sem"], o["val"])
                snap[tag[i]] = {}
                continue
            need = {}
            for d in o["deps"]:
                if not o["deps"][d]:
                    continue
                sm, v = tag[d]
                if need.get(sm, 0) < v:
                    need[sm] = v
            c = clk[q]
            items = [(sm, v) for sm, v in need.items() if c.get(sm, 0) < v]
            for it in items:
                if not any(x != it and snap.get(x, {}).get(it[0], 0) >= it[1] for x in items):
                    queues[q].wait_ge(T.sem[it[0]], it[1])
            for it in items:
                for k2, v2 in list(snap.get(it, {}).items()) + [it]:
                    if c.get(k2, 0) < v2:
                        c[k2] = v2
            ins = o["fn"](queues[q])
            if o["kind"] == "c":
                cnt[q] += 1
                ins.then_inc(T.sem["q" + q], 1)
                tag[i] = ("q" + q, cnt[q])
            else:
                if o["kind"] == "d":
                    ins.then_inc(T.sem[o["sem"]], 16)
                tag[i] = (o["sem"], o["val"])
            snap[tag[i]] = dict(c)
        return cnt
    return rec, emit, bias


def rank_program(g, core, T, topo):
    rank = T.rank_of(core)
    if rank is None:
        return
    late, uses = [], [0]
    rec, emit, bias = planner(g, T, late)
    peers = [T.cores[(rank + j) % N] for j in (1, 2, 3)]
    GROUPS, CYC, LAT = CFG["groups"], CFG["cyc"], CFG["lat"]

    last = {}
    now = [-1, 0]

    def phase(name):
        bias[0] = CFG["bias"].get(name, 0.0)
        bias[1], bias[2] = (now[0], (now[1], name)), 0

    def B(name, lo=0, hi=None, st=1, p=128):
        if name in PIECE:
            name, o, w = PIECE[name]
            lo, hi = o + lo, o + (w if hi is None else hi)
        hi = SCRATCH[name][1][1] if hi is None else hi
        n = len(range(lo, hi, st))
        return (T[name][0:p, lo:hi:st], [(name, lo, lo + (n - 1) * st + 1)], n, 2 if "16" in SCRATCH[name][2] else 4, False, False, [])

    def P(name, r0, r1, c=16, p=128, p0=0):
        late.append([None, [(name, 0, 512)], 16 * (r1 - r0 - 1) + c, 4, True, False, [], (name, p0, p, 16 * r0, 16 * r1 - 16 + c)])
        return late[-1]

    def Pc(name, lo, hi, p=128, p0=0):
        late.append([None, [(name, 0, 512)], hi - lo, 4, True, False, [], (name, p0, p, lo, hi)])
        return late[-1]

    def EQ(b0, b1, c0=0, c1=16):
        return (T.eqm[:, b0, c0:c1] if b1 == b0 + 1 else T.eqm[:, b0:b1, c0:c1], [("eqm", 16 * b0, 16 * b1)], (b1 - b0) * (c1 - c0), 2, False, False, [])

    def new():
        uses[0] += 1
        return "@%d" % uses[0]

    def Ke(a0, a1, w):
        return (T.kE[:, a0:a1, 16 * w:16 * w + 16], [("kE", 32 * a + 16 * w, 32 * a + 16 * w + 16) for a in range(a0, a1)], 16 * (a1 - a0), 2, False, False, [])

    def Kg(a0, a1):
        return (T.kG[:, a0:a1, 16:32], [("kG", 48 * a0, 48 * a1)], 16 * (a1 - a0), 2, False, False, [])

    def Tv(r0, r1, st=1, c=0):
        n = len(range(r0, r1, st))
        return (T.Tt[:, r0, c:16] if n == 1 else T.Tt[:, r0:r1:st, c:16], [("Tt", 16 * r0, 16 * r1)], n * (16 - c), 2, False, False, [])

    def Yv(a0, a1, c=None):
        if c is None:
            return (T.Y[:, a0, :] if a1 == a0 + 1 else T.Y[:, a0:a1, :], [("Y", 256 * a0, 256 * a1)], 256 * (a1 - a0), 2, False, False, [])
        return (T.Y[:, a0:a1, 16 * c:16 * c + 16], [("Y", 256 * a0, 256 * a1)], 16 * (a1 - a0), 2, False, False, [])

    def IX(win, lst):
        return (win[0].indirect(lst[0]), win[1], 16 * lst[2], win[3], False, True, lst[1])

    def arg(x):
        return x[0] if isinstance(x, (tuple, list)) else x

    def op(q, fn, out, ins, rate=None, dur=None):
        full = [x for x in ins if isinstance(x, (tuple, list))]
        R = [r for x in full for r in x[1] + x[6]] + out[6]
        if dur is None:
            fix = 50 if q == "V" else 65
            if out[5]:
                dur = (fix, 0, 0, out[2], 0)
            elif any(x[5] for x in full):
                dur = (fix, 0, out[2], 0, 0)
            else:
                if rate is None:
                    rate = 0.5 if out[3] == 2 and all(x[3] == 2 for x in full if x[2] > 1) else 1
                dur = (0, max(64, out[2] * rate), 0, 0, 0)
        rec(q, "c", fn, R, out[1], dur, LAT)

    def iota(out, pattern, base, cm):
        if out[1][0][0] == "pI":
            fn = lambda e: e.iota(out[0], pattern, base, cm)
        else:
            fn = lambda e: e.iota(out[0], pattern, base, cm, allow_small_or_imprecise_dtypes=True)
        last["G"] = rec("G", "c", fn, [], out[1], (130, 2 * out[2], 0, 0, 0), LAT, after=last.get("G"))

    def ts(out, in0, s1, o0, s2=None, o1=None):
        if o1 is None:
            op("V", lambda e: e.tensor_scalar(out[0], in0[0], arg(s1), None, o0), out, [in0, s1])
        else:
            op("V", lambda e: e.tensor_scalar(out[0], in0[0], arg(s1), arg(s2), o0, o1), out, [in0, s1, s2])

    def tt(out, in0, in1, o):
        op("V", lambda e: e.tensor_tensor(out[0], in0[0], in1[0], o), out, [in0, in1], rate=1 if in0[4] or in1[4] else 2)

    def cp(out, in_):
        op("V", lambda e: e.tensor_copy(out[0], in_[0]), out, [in_])

    def scan(out, d0, d1, o0, o1):
        op("V", lambda e: e.tensor_tensor_scan(out[0], d0[0], d1[0], 0.0, o0, o1), out, [d0, d1])

    def act(out, in_, f=ID, bias=0.0, scale=1.0):
        op("S", lambda e: e.activation(out[0], in_[0], f, bias=arg(bias), scale=arg(scale)), out, [in_, bias, scale], rate=1)

    def lin(name, out, in_, scale=1.0, add=0.0):
        if name in CFG["onS"]:
            act(out, in_, bias=add, scale=scale)
        else:
            ts(out, in_, scale, A.mult, add, A.add)

    def group(terms, cuts=(), start=True, stop=True, alone=False):
        run, dur = [], 0.0
        for i, (out, lhsT, rhs, *ends) in enumerate(terms):
            run.append((out, lhsT[0], rhs[0], alone or start and i == 0, alone or stop and (i == len(terms) - 1 or any(ends))))
            dur += max(min(64, lhsT[2]), rhs[2]) * (4 if rhs[3] == 4 else 1)
            if dur >= CFG["run"] or i + 1 in cuts or i + 1 - len(terms) in cuts or i + 1 == len(terms):
                op("T", lambda e, run=run: [e.matmul(m[0][0], *m[1:]) for m in run][-1], out, [x for u in terms[i + 1 - len(run):i + 1] for x in u[1:3]], dur=(0, 0, 0, 0, dur))
                run, dur = [], 0.0

    def gcp(out, in_, after=None, pieces=None):
        rec("G", "c", lambda e: e.affine_select(out[0], in_[0], [[0, out[2]]], A.is_gt, 0.0, 1, 0), in_[1], pieces or out[1], (170, 2 * out[2], 0, 0, 0, 0, 0, 1), LAT, after=after)

    def ms(out, val):
        op("V", lambda e: e.memset(out[0], val), out, [], rate=out[3] / 4)

    def dma(q, sem, out, in_, R, W, lat):
        last[q] = rec(q, "d", lambda e: e.dma_start(out, in_), R, W, 60.0, lat, sem, 16, after=last.get(q))

    def send(src, dsts, W, rsem, lsem, more=()):
        ids = [DstId(rid=topo.addr(p)[0], pnc=topo.addr(p)[1]) for p in peers]
        eng = [e for e in topo.engines(core, peers[0]) if all(e in topo.engines(core, p) for p in peers)]
        pieces = [(src, dsts, W)] + list(more)
        n = len(eng) // len(pieces)
        trs = [RemoteDMATransfer(dst_ids=ids, dma_engine_mask=sum(1 << e for e in eng[n * k:n * k + n]), remote_sem=T.sem[rsem], srcs=[u[0][0]], dsts=u[1], alu_op=0)
               for k, u in enumerate(pieces)]
        n *= len(pieces)
        i = rec("G", "s", lambda e: e.remote_dma_fused(trs, local_sem=T.sem[lsem]), [r for u in pieces for r in u[0][1]], [], (CFG["g1"] * (rsem == "av"), 0, 0, 0, 0, 900.0), 1500.0, lsem, n, after=last.get("G"))
        last["G"] = i
        rec("N", "n", None, [], [r for u in pieces for r in u[2][1]], (0, 0, 0, 0, 0, 0, 2500.0) if now[0] >= 0 else CFG["first"], LAT, rsem, 3 * n, after=i)
        return n

    phase("load")
    dma("S", "vin", T.vs[:], T.v0[:], [], [("vs", 0, 45)], 2000.0)
    dma("S", "zin", T.zs[:], T.z0[:], [], [("zs", 0, 240)], 2000.0)
    loads = [("xw", T.x0, lo, hi) for lo, hi in CFG["xload"]] + [("kin", T.k0, lo, hi) for lo, hi in CFG["kload"]]
    if CFG["kfirst"]:
        loads = loads[len(CFG["xload"]):] + loads[:len(CFG["xload"])]
    size = [CFG["piece"] * (hi - lo) / (1024 if name == "kin" else 2048) for name, src, lo, hi in loads]
    for i, (name, src, lo, hi) in enumerate(loads):
        w = CFG["flight"]
        gate = [(loads[i - w][0], loads[i - w][2], loads[i - w][2] + 1)] if i >= w else []
        dma("Y", "ld%d" % i, T[name][:, lo:hi], src[:, lo:hi], gate, [(name, lo, hi)], 2200.0 + sum(size[:i + 1]) if i < w else sum(size[i + 1 - w:i + 1]))

    iota(B("pI", 0, 1), [[0, 1]], 0, 1)
    iota(B("iw", 0, 256), [[1, 256]], 0, 0)
    SW = 16 * max([a1 - a0 for a0, a1, k in GROUPS if k == "S"] + [0])
    VW = 16 * max([a1 - a0 for a0, a1, k in GROUPS if k == "V"] + [0])
    ne = send(B("vs"), [T.vl[:, 45 * j:45 * j + 45] for j in range(3)], B("vl"), "av", "lv")
    send(B("zs"), [T.zl[:, 240 * j:240 * j + 240] for j in range(3)], B("zl"), "az", "lz")
    iota(B("E", 0, 16 * SW), [[1, SW], [0, 16]], 0, 0)
    for h in range(2 * bool(CFG["half"])):
        iota(B("E", 1024 + 512 * h, 1536 + 512 * h), [[16, 4], [2, 8], [0, 16]], h, 0)
    iota(B("Dm"), [[0, 4], [16, 16]], 0, 0)
    ms(B("base"), BIG)
    for s in range(S):
        iota(B("base", 16 * s, 16 * s + 15), [[12288, 3], [0, 5]], 65536 * (s + 1) + 28672, 0)
    for i in range(3):
        act(B("iw", 256 << i, 512 << i), B("iw", 0, 256 << i), bias=float(256 << i))
    act(B("iw", 2048, 3072), B("iw", 0, 1024), bias=2048.0)
    iota(B("iw", 3072, V), [[1, 1024]], 3072, 0)
    for o in range(V, K0 + V, 1056):
        iota(B("iw", o, o + 1056 - CFG["iws"]), [[1, 1056 - CFG["iws"]]], o, 0)
        if CFG["iws"]:
            act(B("iw", o + 1056 - CFG["iws"], o + 1056), B("iw", 0, CFG["iws"]), bias=float(o + 1056 - CFG["iws"]))

    def col(i):
        return B("pF", i, i + 1)

    def pi(i):
        return B("pI", i, i + 1)
    I128 = B("iw", 0, 128)
    ts(pi(1), pi(0), 15, A.bitwise_and)
    ts(pi(2), pi(0), 112, A.bitwise_and)
    ts(pi(3), pi(0), 4, A.arith_shift_right, 1, A.bitwise_and)
    ts(pi(4), pi(0), 7, A.bitwise_and)
    ts(pi(5), pi(0), 4, A.arith_shift_right)
    ts(pi(6), pi(0), 3, A.arith_shift_right, 1, A.bitwise_and)
    cp(B("pF", 0, 7), B("pI", 0, 7))
    ts(col(7), col(3), -1.0, A.mult, 1.0, A.add)
    ts(col(10), col(2), 15.0, A.add)
    ts(pi(11), pi(0), 31, A.bitwise_and)
    ts(pi(12), pi(0), 5, A.arith_shift_right)
    ts(pi(13), pi(0), 5, A.arith_shift_right, 1, A.bitwise_and)
    ts(pi(14), pi(0), 6, A.arith_shift_right)
    cp(B("pF", 24, 28), B("pI", 11, 15))
    ts(col(8), col(24), 16.0, A.mult, 3.0, A.add)
    ts(col(11), col(25), 4.0, A.mult, col(8), A.add)
    ts(B("idb"), I128, col(0), A.is_equal)
    act(B("idf"), B("idb"))
    for name, f in (("idn", -8192.0), ("idB", -16384.0), ("idM", 8192.0), ("ih", 1.0), ("ihn", -1.0), ("ih2", -2.0), ("ih32", 32.0), ("ihd", 16.0), ("idX", -16.0)):
        act(B(name), B("idb"), scale=f)
    for s in range(S):
        act(B("idS", 128 * s, 128 * s + 128), B("idb"), scale=32.0 * (s + 1))
    for h in range(2 * (not CFG["quad"])):
        for w in range(2):
            o = 128 * (2 * h + w)
            ts(B("Pm", o, o + 128), I128, col({0: 0, 1: 8, -1: 9}[w - h]), A.is_equal, col(3 if h else 7), A.mult)
    ts(B("U1"), B("iw", 0, 144), col(10), A.is_equal)
    act(B("U"), B("U1"), scale=65536.0)
    act(B("Uh"), B("U1"))
    ts(B("Us"), B("iw", 0, 144), col(11), A.is_equal, 8192.0, A.mult)
    ms(B("rm"), 4096.0)
    ms(B("rm", 0, 128, 16), -2.0 ** 30)
    ms(B("vU"), 0)
    for name in ("R", "C"):
        ms(B(name, 255, 1024, 256), 0.0)
    ts(B("En", 0, 16 * SW), B("E", 0, 16 * SW), col(0), A.is_equal, -1.0, A.mult)
    ms(B("rz"), 2048.0)
    ms(B("rz", 0, 256, 16), -1024.0)
    if CFG["gsp"]:
        ms(B("ry"), 2048.0)
        ms(B("ry", 0, 256, 4), -1024.0)
        ms(B("ry", 256, 512, 8), -1024.0)
    for name in ("on", "vI", "x", "y", "ow4", "c4"):
        ms(B(name), 0)
    ms(B("ones"), 1.0)
    ms(B("c4", 1, 48, 3), 1.0)
    if CFG["gap"]:
        ms((T.kG[:, :, :], [("kG", 0, 768)], 768, 2, False, False, []), 0.0)
    for o in [496] + list(range(1008, 2304, 256)):
        act(B("zh", o, o + 16), B("ones", 0, 16), scale=1024.0)
    for o in range(240, 1024, 256) if not CFG["quad"] else ():
        act(B("kvh", o, o + 16), B("ones", 0, 16))
    for a0, a1, k in GROUPS:
        if k != "S":
            ms(B("shp", 256 * a0, 256 * a1), 0.0)
    if GROUPS[-1][2] == "S":
        ms((T.Ys[:, 240:256, :], [("Ys", 3840, 4096)], 256, 2, False, False, []), 0.0)
    else:
        ms((T.Y[:, 15, :], [("Y", 3840, 4096)], 256, 2, False, False, []), 0.0)
    for h in range(2 * bool(CFG["half"])):
        o = 1024 + 512 * h
        ts(B("En", o, o + 512), B("E", o, o + 512), col(0), A.is_equal, -1.0, A.mult)
    ms(B("thr", 0, 1), 8.0)
    ms(B("cls", 48, 64), 12.0 * BIG)
    ms(B("gt4", 240, 256), 0.0)
    act(B("Un"), B("U1"), scale=-BIG)
    if CFG["quad"]:
        ts(B("ge"), B("iw", 0, 16), col(1), A.is_equal)
        ts(B("xy"), B("iw", 0, 16), 1.0, A.add, col(1), A.is_equal)
        tt(B("Dif", 0, 16), B("ge"), B("xy"), A.subtract)
        for w in range(2 * bool(CFG["gap"])):
            act(B("Dif", 16 + 16 * w, 32 + 16 * w), B("Dif", 0, 16), scale=col(3 if w else 7))
        act(col(21), col(7), scale=-2048.0)
        act(col(22), col(3), scale=-2048.0)
    else:
        act(B("Pn"), B("Pm"), scale=-1.0)
    ms(B("cneg", 0, 48), -16384.0)
    if CFG["emerge"]:
        ms(B("cn2", 0, 48), -16384.0)
        for s in range(1, S):
            ms(B("cn2", 32 + 16 * s, 48 + 16 * s), -16.0 * (s in CFG["sgv"]))
    ms(B("cneg", 48, 64), 26624.0)
    ms(B("cneg", 64, 96), 18432.0)
    for e in CFG["sg"]:
        ms(B("on", 16 * e + 15, 16 * e + 16), -1.0)
    if CFG["d1T"]:
        act(B("bsb", 0, 48), B("base", 0, 48))
        ms(B("bsb", 48, 96), 16.0 * BIG)
    else:
        act(B("bs", 0, 48), B("base", 0, 48), bias=16.0 * BIG)
    ms(B("cneg", 96, 112), 24576.0)
    ms(B("cneg", 112, 128), 24576.0 - X0)
    for i in range(4):
        ts(pi(7 + i), pi(1), i, A.arith_shift_right, 1, A.bitwise_and)
    for i in range(4):
        ts(col(12 + i), pi(7 + i), 2.0 ** -(2 ** i) - 1.0, A.mult, 1.0, A.add)
    tt(col(16), col(12), col(13), A.mult)
    tt(col(17), col(14), col(15), A.mult)
    tt(col(18), col(16), col(17), A.mult)
    ms(B("valf"), 0.5)
    ms(B("valf", 0, 64, 4), 2.0 ** -13)
    ms(B("kq"), 0.0)
    ts(col(28), col(26), 2.0 ** -4 - 1.0, A.mult, 1.0, A.add)
    ts(col(29), col(27), 2.0 ** -8 - 1.0, A.mult, 1.0, A.add)
    ts(col(30), col(28), col(29), A.mult, -2.5 * 2.0 ** 55, A.mult)
    ts(B("kq", 0, 1), col(30), 2.0 ** 60, A.mult)
    scan(B("thw", 0, 60), B("valf", 0, 60), B("kq", 0, 60), A.mult, A.add)
    ms(B("ge"), 2.0 ** -16)
    ms(B("xy"), 0.0)
    ts(B("xy", 0, 1), col(18), 2.0 ** 55, A.mult, 2.0 ** 60, A.mult)
    scan(B("wt", 0, 15), B("ge", 0, 15), B("xy", 0, 15), A.mult, A.add)
    ts(B("wt", 16, 31), B("wt", 0, 15), -1.0, A.mult)
    ts(B("Wk"), B("iw", 0, 32), -1.0, A.add, col(1), A.is_equal)
    ts(B("ln"), B("Dm", 0, 16), col(1), A.add, -240.0, A.add)
    ts(B("DJ"), B("Dm", 0, 16), col(1), A.add, K0 + 4096.0, A.add)
    ms(B("zg", 0, 16), 1024.0)
    ms(B("kw", 0, X0), 0.0)
    ts(B("Dm"), B("Dm"), col(1), A.add, 4096.0, A.add)
    tt(col(19), col(4), col(5), A.is_equal)
    ts(col(20), col(6), -15.0, A.add)
    ts(B("t8"), B("iw", 0, 8), 2.0, A.mult, col(20), A.add)
    ts(B("w8l"), B("t8"), col(19), A.mult, 15.0, A.add)


    KW = B("kw", K0, K0 + V)
    XW = B("kw", X0, X0 + V)

    def xwin():
        return B("xw", 0, V) if CFG["kfirst"] and now[0] == 0 else XW

    def vU(t, s, a0=0, a1=15):
        return B("vU", 80 * t + 16 * s + a0, 80 * t + 16 * s + a1)

    def spairs(o, vals, keys, since):
        for a in range(15):
            n = 15 - a
            if a >= since:
                act(EQ(o, o + n), B(vals[0], vals[1] + 16 * a, vals[1] + 240), ABS, bias=B(keys[0], keys[1] + a, keys[1] + a + 1))
                act(EQ(o, o + n), EQ(o, o + n), RELU, bias=B("wt", a, a + 1), scale=B("wt", 16 + a, 17 + a))
            o += n

    def pairs(o, vals, keys, upto=15):
        for a in range(15):
            n = 15 - a
            if a < upto:
                ts(EQ(o, o + n), B(vals[0], vals[1] + 16 * a, vals[1] + 240), B(keys[0], keys[1] + keys[2] * a, keys[1] + keys[2] * a + 1), A.is_equal, B("wt", a, a + 1), A.mult)
            o += n

    for t in range(RACES):
        phase("start%d" % min(t, 1))
        for j in range(3):
            o = 45 * j + 15 * t + 5 * j
            (act if t else cp)(B("vI", 16 * t + 5 * j, 16 * t + 5 * j + 5), B("vl", o, o + 5))
            act(B("zc", 240 * t + 80 * j, 240 * t + 80 * j + 80), B("zl", 240 * j + 80 * t, 240 * j + 80 * t + 80))
        cp(vU(t, 0), B("vI", 16 * t, 16 * t + 15))
    phase("start1")
    act(B("v1K"), B("vI"), bias=float(K0))
    phase("start0")
    for o in range(0, V, 256):
        (act if o // 256 % CFG["kwid"] else cp)(B("kw", K0 + o, K0 + o + 256), B("kin", o, o + 256))
    for lo, hi in CFG["xload"] if not CFG["kfirst"] else ():
        mid = lo + (hi - lo) // 4
        cp(B("kw", X0 + lo, X0 + mid), B("xw", lo, mid))
        act(B("kw", X0 + mid, X0 + hi), B("xw", mid, hi))
    for o in range(0, V, 256) if CFG["kfirst"] else ():
        gcp(B("kw", X0 + o, X0 + o + 256), B("xw", o, o + 256))

    TEAMS = CFG["teams"]

    def span(tm):
        return min(GROUPS[gr][0] for gr in TEAMS[tm]), max(GROUPS[gr][1] for gr in TEAMS[tm])

    def zh(s, a0=0, a1=15):
        o = (0, 768, 1024, 1280, 256)[s]
        return B("zh", o + 16 * a0, o + 16 * a1)

    def sh(gr, s):
        a0, a1, k = GROUPS[gr]
        if k != "S" and s < S:
            return B("shp", 256 * a0, 256 * a1, 16)
        return zh(s, a0, a1)

    def zform(gr, s):
        a0, a1, k = GROUPS[gr]
        n = 16 * (a1 - a0)
        if k != "S":
            am = a1
            for w, c in CFG["gsp"].get((gr, s), CFG["gsp"].get(gr, ())) if s else ():
                am, e = am - w, 256 * am
                scan(B("zx", 256 * am, e, 16 // c), B("ry", 256 * (c == 8), 256 * (c == 8) + 16 * c * w), B("shp", 256 * am, e, 16 // c), A.min, A.add)
                while c < 16:
                    gcp(B("zx", 256 * am + 8 // c, e, 16 // c), B("zx", 256 * am, e, 16 // c))
                    c *= 2
            for a in range(a0, am):
                o = 256 * a
                scan(B("zx", 256 * a, 256 * a + 256), B("rz", 0, 256), B("shp", o, o + 256), A.min, A.add)
        else:
            pb, zT = P(new(), 0, 8, p=n), B("zT", 128 * gr, 128 * gr + 128, p=n)
            if s == 0 or gr in CFG["ztr"]:
                group([(pb, sh(gr, s), B("ih"))])
                act(zT, pb)
            else:
                o = 256 * (s - 1)
                group([(pb, B("ih", 0, n, p=n), zT), (pb, B("xq", o + 16 * a0, o + 16 * a1), B("idb"))], (1,))
                act(zT, pb, bias=511.75, scale=0.5)

    def zinit(t):
        act(zh(0), B("zc", 240 * t, 240 * t + 240), bias=1024.0)
        for gr, (a0, a1, k) in enumerate(GROUPS):
            if k != "S" and not (t and CFG["gzx"]):
                act(sh(gr, 0), B("zc", 240 * t + 16 * a0, 240 * t + 16 * a1), bias=1024.0)
            if k != "S" and t and CFG["gzx"]:
                gcp(B("zx", 256 * a0, 256 * a1, 16), B("zc", 240 * t + 16 * a0, 240 * t + 16 * a1), last["G"])
                for c in (16, 8, 4, 2):
                    gcp(B("zx", 256 * a0 + c // 2, 256 * a1, c), B("zx", 256 * a0, 256 * a1, c))
            else:
                zform(gr, 0)

    def halved(gr, s):
        return gr in CFG["half"] and (s, [tm for tm, team in enumerate(TEAMS) if gr in team][0]) not in CFG["kv"]

    def Ys(l0, l1, st=1):
        return (T.Ys[:, l0:l1:st, :], [("Ys", 16 * l, 16 * l + 16) for l in range(l0, l1, st)] if st > 1 else [("Ys", 16 * l0, 16 * l1)], 16 * len(range(l0, l1, st)), 2, False, False, [])

    def knew(t, gr, s):
        a0, a1 = span(gr)
        nb, o = (a1 - a0 + 1) // 2, 256 * (s - 1) + 16 * a0
        if (s, gr) in CFG["kv"]:
            cp(B("kvu", 16 * a0, 16 * a1), IX(KW if t else B("kin"), vU(t, s - 1, a0, a1)))
        else:
            act(B("kvu", 16 * a0, 16 * a1), IX(KW if t else B("kin"), vU(t, s - 1, a0, a1)))
        if (s, gr) in CFG["gap"]:
            lin("kG%d%d" % (s, gr), Kg(a0, a1), B("kvu", 16 * a0, 16 * a1), 1.0, -2048.0)
            return
        if CFG["quad"]:
            for w in range(2):
                if (gr, w) in CFG["khs"]:
                    act(Ke(a0, a1, w), B("kvu", 16 * a0, 16 * a1), bias=col(21 + w), scale=col(3 if w else 7))
                else:
                    ts(Ke(a0, a1, w), B("kvu", 16 * a0, 16 * a1), -2048.0, A.add, col(3 if w else 7), A.mult)
            return
        if gr in CFG["khs"]:
            act(B("kvh", o, o + 16 * (a1 - a0)), B("kvu", 16 * a0, 16 * a1), bias=-2048.0)
        else:
            ts(B("kvh", o, o + 16 * (a1 - a0)), B("kvu", 16 * a0, 16 * a1), -2048.0, A.add)
        tb, src = Tv(a0, a0 + 2 * nb), B("kvh", o, o + 32 * nb)
        op("V", lambda e: e.transpose(tb[0], src[0]), tb, [src])

    def score(tm, pb):
        a0, a1 = span(tm)
        for gr in TEAMS[tm]:
            al, end = GROUPS[gr][:2]
            cs = list(range(0, 16, 2)) + list(range(1, 16, 2))
            group([(P(pb, al - a0, end - a0), B("U", 15 - c, 143 - c), Yv(al, end, c) if GROUPS[gr][2] != "S" else Ys(16 * al + c, 16 * end, 16)) for c in cs])

    chunk = [0]

    def xact(gr):
        a0, a1, k = GROUPS[gr]
        n = 16 * (a1 - a0)
        for h in range(2 * halved(gr, now[1])):
            xg, pa = B("xg%d" % (chunk[0] % 3), 0, 8 * n), P(new(), 0, n // 2)
            chunk[0] += 1
            act(xg, IX(XW, B("kvu", 16 * a0 + h * n // 2, 16 * a0 + (h + 1) * n // 2)))
            group([(pa, B("zT", 128 * gr, 128 * gr + 128, p=n), B("En", 1024 + 512 * h, 1024 + 512 * h + 8 * n, p=n)), (pa, B("idb"), xg)][::CFG["zfirst"][h]], (1,))
            act(Ys(16 * a0 + h, 16 * a1, 2), pa, RELU, bias=1024.0)
        for a in range(a0, a1, CFG["scols"]) if not halved(gr, now[1]) else ():
            e = min(a + CFG["scols"], a1)
            xg, pa, o = B(("xg0", "xg1", "xm")[chunk[0] % (3 if GROUPS[-1][2] == "S" else 2)], 0, 256 * (e - a)), P(new(), 0, 16 * (e - a)), 256 * (a - a0)
            chunk[0] += 1
            act(xg, IX(xwin(), B("kvu", 16 * a, 16 * e)))
            group([(pa, B("zT", 128 * gr, 128 * gr + 128, p=n), B("En", o, o + 256 * (e - a), p=n)), (pa, B("idb"), xg)][::CFG["zfirst"][a > a0]], (1,))
            if (now[1], a) in CFG["rv"]:
                ts(Ys(16 * a, 16 * e), pa, 1024.0, A.add, 0.0, A.max)
            else:
                act(Ys(16 * a, 16 * e), pa, RELU, bias=1024.0)

    def xmix(gr):
        a = GROUPS[gr][0]
        for n in CFG["xcols"][gr]:
            o = 256 * (a - min(e[0] for e in GROUPS if e[2] == "M"))
            act(B("xm", o, o + 256 * n), IX(xwin(), B("kvu", 16 * a, 16 * (a + n))))
            tt(B("xm", o, o + 256 * n, 16), B("xm", o, o + 256 * n, 16), B("zx", 256 * a, 256 * (a + n), 16), A.max)
            for e in range(a, a + n):
                scan(Yv(e, e + 1), B("zx", 256 * e, 256 * e + 256), B("xm", o + 256 * (e - a), o + 256 * (e - a + 1)), A.min, A.max)
            a += n

    def xvec(gr):
        a = GROUPS[gr][0]
        for n in CFG["xcols"].get((gr, now[1]), CFG["xcols"][gr]):
            for l in range(16 * a, 16 * a + 16, 8) if n == 0 else ():
                y = (T.Y[:, a, 16 * (l - 16 * a):16 * (l + 8 - 16 * a)], [("Y", 16 * l, 16 * (l + 8))], 128, 2, False, False, [])
                tt(y, IX(xwin(), B("kvu", l, l + 8)), B("zx", 16 * l, 16 * (l + 8)), A.max)
            if n:
                tt(Yv(a, a + n), IX(xwin(), B("kvu", 16 * a, 16 * (a + n))), B("zx", 256 * a, 256 * (a + n)), A.max)
            a += n or 1

    def pick(t, gr, s):
        a0, a1 = span(gr)
        nb = (a1 - a0 + 1) // 2
        n, o, pb = 16 * (a1 - a0), 256 * (s - 1) + 16 * a0, new()
        key, R, D, C = P(pb, 0, a1 - a0), B("R", o, o + n), B("d0", 16 * a0, 16 * a0 + n), B("C", o, o + n)
        pk = pb if gr in CFG["dif"] and gr not in CFG["apart"] else new()
        d1 = P(pk, 16, 16 + a1 - a0)
        dif = gr in CFG["dif"]
        terms = []
        for a in range(a1 - a0):
            for q in range(0, 128, 32) if (s, gr) in CFG["gap"] else ():
                for w in range(2):
                    terms.append((P(pk, 16 + a, 17 + a, p=32, p0=q), (T.kG[q:q + 32, a0 + a, 16 - 16 * w:48 - 16 * w], [("kG", 48 * (a0 + a), 48 * (a0 + a) + 48)], 32, 2, False, False, []),
                                  (T.Dif[q:q + 32, 16 + 16 * w:32 + 16 * w], [("Dif", 0, 48)], 16, 2, False, False, []), a == a1 - a0 - 1 and w == 1))
            for q in range(0, 128, 32) if CFG["quad"] and (s, gr) not in CFG["gap"] else ():
                terms.append((P(pk, 16 + a, 17 + a, p=32, p0=q), (T.kE[q:q + 32, a0 + a, :], [("kE", 32 * (a0 + a), 32 * (a0 + a) + 32)], 32, 2, False, False, []),
                              (T.Dif[q:q + 32, 0:16], [("Dif", 0, 16)], 16, 2, False, False, []), a == a1 - a0 - 1))
            for w in range(2 * (not CFG["quad"])):
                q, b = 128 * (2 * (a % 2) + w), a0 + a - a % 2 + w
                terms.append((P(pk, 16 + a, 17 + a), B("Pm", q, q + 128), Tv(b, b + 1)))
                if dif:
                    terms.append((P(pk, 16 + a, 17 + a, c=15), B("Pn", q, q + 128), Tv(b, b + 1, 1, 1)))
        if dif:
            group(terms, alone=True)
        score(gr, pb)
        scan(R, B("rm", 0, n), key, A.add, A.max)
        if dif:
            tt(D, R, key, A.is_gt)
            scan(C, D, d1, A.mult, A.add)
        else:
            tt(D, R, key, A.subtract)
            group(terms + [(d1, B("idn"), D)], (-1,))
            scan(C, D, d1, A.min, A.max)
        ts(vU(t, s, a0, a1), B("C", o + 15, o + 16 * (a1 - a0), 16), 2048.0, A.add)

    nev = [0]

    def zstep(t, tm, s):
        t0, pz, o = span(tm)[0], new(), 256 * (s - 1)
        if s == S:
            a0, a1 = span(tm)
            lst, zt = IX(xwin(), vU(t, s, a0, a1)), B("zt", o + 16 * a0, o + 16 * a1)
            tt(B("gt4", 16 * a0, 16 * a1), lst, B("z3", 16 * a0, 16 * a1), A.is_gt)
            if tm in CFG["z4s"]:
                xq, pa = B("xq", o + 16 * a0, o + 16 * a1), P(pz, 8, 8 + a1 - a0)
                act(xq, lst)
                group([(pa, B("ih"), zh(s - 1, a0, a1)), (pa, B("idb"), xq)], (1,))
                act(zh(s, a0, a1), pa, bias=511.75, scale=0.5)
            else:
                tt(zt, lst, zh(s - 1, a0, a1), A.add)
                ts(zh(s, a0, a1), zt, 0.5, A.mult, 511.75, A.add)
            return
        onv = [gr for gr in TEAMS[tm] if gr in CFG["zv"]]
        ons = [gr for gr in TEAMS[tm] if gr not in onv]
        for gr in onv:
            a0, a1, k = GROUPS[gr]
            lst, zt = IX(xwin(), vU(t, s, a0, a1)), B("zt", o + 16 * a0, o + 16 * a1)
            tt(zt, lst, zh(s - 1, a0, a1), A.add)
            ts(sh(gr, s), zt, 0.5, A.mult, 511.75, A.add)
        if ons:
            b0, b1 = GROUPS[ons[0]][0], GROUPS[ons[-1]][1]
            xq = B("xq", o + 16 * b0, o + 16 * b1)
            act(xq, IX(xwin(), vU(t, s, b0, b1)))
            group([(P(pz, 8 + b0 - t0, 8 + b1 - t0), B("idb"), xq)] + [(P(pz, 8 + GROUPS[gr][0] - t0, 8 + GROUPS[gr][1] - t0), B("ih"), zh(s - 1, *GROUPS[gr][:2])) for gr in ons])
            for gr in ons:
                act(sh(gr, s), P(pz, 8 + GROUPS[gr][0] - t0, 8 + GROUPS[gr][1] - t0), bias=511.75, scale=0.5)
        for gr in TEAMS[tm]:
            a0, a1, k = GROUPS[gr]
            zform(gr, s)
            if k != "S":
                gcp(zh(s, a0, a1), sh(gr, s))
        if s == S - 1 and not CFG["z3g"]:
            act(B("z3", 16 * span(tm)[0], 16 * span(tm)[1]), zh(s, *span(tm)), bias=-1024.0)
        for gr in TEAMS[tm] if s == S - 1 and CFG["z3g"] else ():
            a0, a1, k = GROUPS[gr]
            if k != "S":
                gcp(B("z3", 16 * a0, 16 * a1), B("zx", 256 * a0, 256 * a1, 16))
            else:
                act(B("z3", 16 * a0, 16 * a1), zh(s, a0, a1), bias=-1024.0)
        pz = new()
        for gr in onv:
            a0, a1, k = GROUPS[gr]
            pa = P(pz, 24 + a0 - t0, 24 + a1 - t0)
            group([(pa, B("ih"), B("zt", o + 16 * a0, o + 16 * a1)), (pa, B("ih2"), zh(s - 1, a0, a1))])
        if ons:
            pa = P(pz, 24 + b0 - t0, 24 + b1 - t0)
            group([(pa, B("idb"), xq), (pa, B("ihn"), zh(s - 1, b0, b1))])
        a0, a1 = span(tm)
        if s in CFG["sgv"]:
            ts(B("zh", 1536 + o + 16 * a0, 1536 + o + 16 * a1), P(pz, 24, 24 + a1 - a0), -1023.5, A.is_gt, 2.0, A.mult)
        else:
            act(B("zh", 1536 + o + 16 * a0, 1536 + o + 16 * a1), P(pz, 24, 24 + a1 - a0), SIGN, bias=1023.5)

    def race(t):
        chunk[0] = nev[0] = 0
        for s in range(1, S + 1):
            now[0], now[1] = t, s
            for tm in range(len(TEAMS)):
                phase("k%d" % tm)
                knew(t, tm, s)
                for gr in TEAMS[tm]:
                    phase("x%d" % gr)
                    {"V": xvec, "S": xact, "M": xmix}[GROUPS[gr][2]](gr)
                phase("p%d" % tm)
                pick(t, tm, s)
                phase("z%d" % tm)
                zstep(t, tm, s)
            phase("zg")
            gcp(B("zg", 256 * s - 240, 256 * s + 16), zh(s, 0, 16))
            for o in range(1024 * s - 1024, 1024 * s, 512) if t == RACES - 1 else ():
                gcp(B("xw", o, o + 512), B("kw", X0 + o, X0 + o + 512))
            if s == S - 1:
                early(t)
        finish(t)

    def least(name, rs):
        tt(B(name, 0, 15), B("rcv", rs + 5, rs + 20), B("rcv", rs + 25, rs + 40), A.min)

    def rows(s0, s1):
        if s1 > s0:
            lin("cI%d" % s1, B("cI", 16 * s0, 16 * s1), B("R", 256 * s0 + 15, 256 * s1, 16))
            ts(B("kI", 16 * s0, 16 * s1), B("cI", 16 * s0, 16 * s1), 12, A.arith_shift_right, 15, A.bitwise_and)
            lin("kU%d" % s1, B("kU", 16 * s0, 16 * s1), B("kI", 16 * s0, 16 * s1), -1.0, 16.0)
        for s in range(s1, s0, -1):
            if s == 1 and now[0] < RACES - 1:
                act(B("kF"), B("kI", 0, 16), bias=16.0, scale=-1.0)
            else:
                act(B("Bs", 240 * s - 240, 240 * s), IX(B("Wk"), B("kU", 16 * s - 16, 16 * s - 1)))

    def early(t):
        phase("early")
        pc = new()
        if CFG["emerge"]:
            group([(P(pc, 0, 6), B("idb"), B("cn2"))] + [(P(pc, 0, 6), B("Uh", 15 - c, 143 - c), B("zh", 768 + c, 2304, 16)) for c in range(16)], (1,))
        else:
            group([(P(pc, 3, 6), B("Uh", 15 - c, 143 - c), B("zh", 1536 + c, 2304, 16)) for c in range(16)])
        ts(B("cls", 0, 48), P(pc, 3, 6), B("thr", 0, 1), A.is_ge, -16.0 * BIG, A.mult)
        if CFG["early"]:
            tt(B("op2"), B("cls", 0, 16), B("cls", 16, 32), A.min)
            tt(B("fl", 16 * t, 16 * t + 16), B("op2"), B("cls", 32, 48), A.min)
            rs = 144 + 48 * t
            send(B("fl", 16 * t, 16 * t + 15), [T.rcv[:, rs + 30 - 15 * j:rs + 45 - 15 * j] for j in range(3)], B("rcv", rs, rs + 48), "e%d" % t, "f%d" % t)
            least("x3", rs)
        phase("early2")
        if not CFG["emerge"]:
            pc = new()
            group([(P(pc, 0, 3), B("idb"), B("cneg", 0, 48))] + [(P(pc, 0, 3), B("Uh", 15 - c, 143 - c), B("zh", 768 + c, 1536, 16)) for c in range(16)], (1,))
        tt(B("wz", 0, 48), vU(t, 1, 0, 48), P(pc, 0, 3), A.mult)
        ts(B("u4", 0, 48), B("wz", 0, 48), 4095, A.bitwise_and)
        if CFG["d1T"]:
            d1 = new()
            group([(P(d1, 0, 3), B("idb"), B("bsb", 0, 48)), (P(d1, 0, 3), B("idb"), B("bsb", 48, 96)), (P(d1, 0, 3), B("idb"), B("cls", 0, 48))], (2,))
            d1 = P(d1, 0, 3)
        else:
            d1 = B("d1", 0, 48)
            tt(d1, B("cls", 0, 48), B("bs", 0, 48), A.add)
        def cw(s0, s1, c0, c1):
            return (T.cw[:, s0, c0:c1] if s1 == s0 + 1 else T.cw[:, s0:s1, c0:c1], [("cw", 32 * s + c0, 32 * s + c1) for s in range(s0, s1)], (s1 - s0) * (c1 - c0), 4, False, False, [])
        tt(cw(0, 3, 0, 16), B("u4", 0, 48), d1, A.add)
        tt(cw(0, 3, 16, 32), vU(t, 1, 0, 48), d1, A.add)
        tt(B("m1"), cw(0, 1, 0, 32), cw(1, 2, 0, 32), A.min)
        tt(cw(2, 3, 0, 16), cw(2, 3, 0, 16), B("base", 48, 64), A.min)
        m3 = B("m3", 32 * t + 16, 32 * t + 32)
        tt(B("m3", 32 * t, 32 * t + 32), B("m1"), cw(2, 3, 0, 32), A.min)
        if CFG["early"]:
            lin("op", B("op"), B("fl", 16 * t, 16 * t + 16), 1.0 / (16 * BIG), 1.0)
        else:
            ts(B("op"), m3, BIG, A.is_ge)
            act(B("op2"), B("op"), bias=BIG, scale=BIG / 2 - 1.0 - BIG)
        phase("masks")
        rows(0, CFG["ke"])
        phase("pairs")
        act(B("v16", 16, 64), B("C", 15, 768, 16))
        for s in (4, 3, 2):
            phase("pairs%d" % s)
            for a0, a1 in CFG["vparts"].get(s, ((0, 15),)):
                act(B("val", 240 * s - 240 + 16 * a0, 240 * s - 240 + 16 * a1), IX(B("iw", 0, V), vU(t, s - 1, a0, a1)), bias=-2048.0)
            n = CFG["spairs"].get(s, 15)
            if n < 15:
                act(B("nk", 16 * s - 16, 16 * s), B("C", 256 * s - 512 + 15, 256 * s - 256, 16), scale=-1.0)
            spairs(120 * (s - 1), ("val", 240 * s - 240), ("nk", 16 * s - 16), n)
            pairs(120 * (s - 1), ("val", 240 * s - 240), ("C", 256 * s - 512 + 15, 16), n)

    def finish(t):
        phase("own")
        own = B("own", 16 * t, 16 * t + 16)
        tt(B("wf"), vU(t, S, 0, 16), B("op"), A.mult)
        rk, short = B("rk", 16 * t, 16 * t + 16), P(new(), 0, 1)
        group([(short, B("idb"), B("cls", 16 * s, 16 * s + 16)) for s in (3, 0, 1, 2)] + [(short, B("Un", 15 - c, 143 - c), B("gt4", c, 256, 16)) for c in range(16)], (4,))
        tt(rk, short, B("m3", 32 * t, 32 * t + 16), A.max)
        rs = 48 * t
        send(B("rk", 16 * t, 16 * t + 15), [T.rcv[:, rs + 30 - 15 * j:rs + 45 - 15 * j] for j in range(3)], B("rcv", rs, rs + 48), "a%d" % t, "l%d" % t)
        phase("ownu")
        if not CFG["w54"]:
            act(B("nb", 48, 64), short, scale=32.0)
        pa = P(new(), 0, 1)
        group([(pa, B("idb"), B("cneg", 0, 16))] + [(pa, B("Uh", 15 - c, 143 - c), B("zh", 256 + c, 512, 16)) for c in range(16)], (1,))
        tt(B("wz", 48, 64), B("wf"), pa, A.mult)
        ts(B("u4", 48, 64), B("wz", 48, 64), 4095, A.bitwise_and)
        tt(own, B("u4", 48, 64), rk, A.add)
        ru = 288 + 48 * t
        send(B("own", 16 * t, 16 * t + 15), [T.rcv[:, ru + 30 - 15 * j:ru + 45 - 15 * j] for j in range(3)], B("rcv", ru, ru + 48), "u%d" % t, "w%d" % t)
        phase("logs")
        act(B("w1", 0, 16), B("C", 768 + 15, 1024, 16), bias=65536.0 * S + 2048.0)
        tt(B("dI"), B("m3", 32 * t + 16, 32 * t + 32), B("w1", 0, 16), A.min)
        ts(B("WI"), B("dI"), 4095, A.bitwise_and)
        ts(B("bI"), B("dI"), 8, A.arith_shift_right, 1792, A.bitwise_and)
        joint = t < RACES - 1
        if not joint:
            lin("WU", B("WU"), B("WI"))
        tt(B("bF" if joint else "bU"), B("bI"), B("ln"), A.add)
        act(B("WF"), B("WI"), bias=float(X0))
        apart = not joint and CFG["apart2"]
        if apart:
            phase("eqn")
            act(B("valu", 0, 240), IX(B("iw", K0), vU(t, 0)))
            n0, n4 = CFG["apart2"]
            if n0 < 15:
                act(B("nG", 0, 15), B("v1K", 16 * t, 16 * t + 15), scale=-1.0)
            spairs(0, ("valu", 0), ("nG", 0), n0)
            pairs(0, ("valu", 0), ("v1K", 16 * t, 1), n0)
            phase("wpairs")
            act(B("valu", 960, 1200), IX(B("iw", X0), B("WU", 0, 15)))
            if n4 < 15:
                act(B("GF", 0, 15), B("WF", 0, 15), scale=-1.0)
            spairs(480, ("valu", 960), ("GF", 0), n4)
            pairs(480, ("valu", 960), ("WF", 0, 1), n4)
        phase("masks4")
        rows(CFG["ke"], S)
        phase("cm")
        pa = P(new(), 0, 15)
        if (S, 0) in CFG["gap"]:
            group([(pa, B("ih"), Kg(0, 15)), (pa, B("idB"), B("Bs", 720, 960))], (1,))
        elif CFG["quad"]:
            group([(pa, B("ih"), Ke(0, 15, 0)), (pa, B("ih"), Ke(0, 15, 1)), (pa, B("idB"), B("Bs", 720, 960))], (2,))
        else:
            group([(pa, B("ih32"), B("kvh", 768, 1008)), (pa, B("idB"), B("Bs", 720, 960))], (1,))
        act(B("cm"), pa, RELU, bias=2048.0)
        act(B("ub", 2, 48, 3), B("C", 768 + 15, 1024, 16), bias=32.0 * S - 65536.0, scale=32.0)
        act(B("c4", 2, 48, 3), B("C", 768 + 15, 1024, 16), bias=2048.0)
        phase("xnew")
        if not joint:
            act(B("xW"), IX(XW, B("WU", 0, 15)))
            act(B("zW"), IX(B("zg"), B("bU", 0, 15)))
            pa = P(new(), 0, 15)
            group([(pa, B("idb"), B("xW")), (pa, B("ih"), B("zW"))])
            act(B("xr"), pa, bias=511.75, scale=0.5)
            act(B("xn"), B("xr"), bias=-1024.0)
        if t + 1 < RACES:
            phase("zinit")
            zinit(t + 1)

        phase("own4")
        x, ow, ow2 = B("x", 0, 15), B("ow1", 0, 15), B("ow2", 0, 15)
        ts(ow, B("rk", 16 * t, 16 * t + 15), BIG, A.min)
        if not CFG["w54"]:
            tt(ow2, B("rk", 16 * t, 16 * t + 15), B("nb", 48, 63), A.max)
        act(B("th4", 0, 15), ow, bias=33.0 * BIG, scale=-32.0)
        if CFG["early"]:
            tt(B("ow4", 0, 15), ow, B("x3", 0, 15), A.add)
        else:
            ts(B("xu", 0, 15), B("rk", 16 * t, 16 * t + 15), LAST, A.bitwise_and)
            tt(B("ow4", 0, 15), B("xu", 0, 15), B("op2", 0, 15), A.max)
        act(B("owE"), IX(B("ow4"), B("w8l")))
        phase("win")
        least("x", rs)

        def on(e):
            return B("on", 16 * e, 16 * e + 15)
        tt(on(0), x, ow, A.is_lt)
        if CFG["early"]:
            tt(on(3), x, B("ow4", 0, 15), A.is_lt)
        else:
            ts(B("y", 0, 15), x, LAST, A.bitwise_and)
            tt(on(3), B("y", 0, 15), B("ow4", 0, 15), A.is_gt)
        phase("winu")
        lin("nx", B("ub", 1, 45, 3), x, -1.0)
        tt(B("ub", 0, 45, 3), B("rcv", ru + 5, ru + 20), B("rcv", ru + 25, ru + 40), A.min)
        ts(B("uI", 0, 15), B("ub", 0, 45, 3), 4095, A.bitwise_and)
        lin("uU", B("uU", 0, 15), B("uI", 0, 15))
        phase("win2")
        tt(B("xy", 0, 15), x, on(0), A.mult)
        for s in (3, 2):
            if s - 1 in CFG["sg"]:
                act(on(s - 1), B("xy", 0, 15), SIGN, bias=0.5 - 65536.0 * s)
            else:
                ts(on(s - 1), B("xy", 0, 15), 65536.0 * s, A.is_ge)
        tt(on(5), x, B("th4", 0, 15), A.is_lt)
        if CFG["w54"]:
            tt(on(4), on(5), on(0), A.subtract)
        else:
            tt(on(4), ow2, x, A.is_lt)
        phase("joint")
        if apart:
            pass
        elif "nw" in CFG["onS"]:
            act(B("nw", 0, 15), on(4), bias=1.0, scale=-1.0)
        elif CFG["w54"]:
            tt(B("nw", 0, 15), on(0), on(5), A.is_ge)
        else:
            tt(B("nw", 0, 15), ow2, x, A.is_ge)
        if not apart:
            tt(B("XU", 0, 15), B("WF", 0, 15), on(4), A.mult)
            tt(B("of", 0, 15), B("v1K", 16 * t, 16 * t + 15), B("nw", 0, 15), A.mult)
            tt(B("GU", 0, 15), B("of", 0, 15), B("XU", 0, 15), A.add)
        if joint:
            tt(B("kU", 0, 15), B("kF", 0, 15), B("nw", 0, 15), A.mult)
            act(B("Bs", 0, 240), IX(B("Wk"), B("kU", 0, 15)))
            tt(B("bU", 0, 15), B("bF", 0, 15), on(4), A.mult)
            act(B("zW"), IX(B("zg"), B("bU", 0, 15)))
            act(B("xW"), IX(B("kw", 0, K0), B("XU", 0, 15)))
        phase("wpairs")
        if not apart:
            act(B("valu", 0, 240), IX(B("iw"), B("GU", 0, 15)))
            lin("GF", B("GF", 0, 15), B("GU", 0, 15))
            if CFG["wV"] < 15:
                lin("nG", B("nG", 0, 15), B("GU", 0, 15), -1.0)
            spairs(0, ("valu", 0), ("nG", 0), CFG["wV"])
            pairs(0, ("valu", 0), ("GF", 0, 1), CFG["wV"])
        phase("xs")
        act(B("urep"), IX(B("iw", 0, V), B("uU", 0, 15)), bias=-2048.0)
        for s in (3, 2, 1):
            pa = P(new(), 0, 15)
            group([(pa, B("idM"), B("Bs", 240 * s - 240, 240 * s)), (pa, B("ih"), B("urep"))], (1,))
            act(B("xs", 240 * s - 240, 240 * s), pa, RELU, bias=2048.0 - 8192.0)

        def event(e):
            phase("ev%d" % e)
            nev[0] += 1
            p1, o, r = new(), 128 * e, 120 * e
            f = e if e or apart else 5
            lst = IX(B("on", 16 * f, 16 * f + 16), B("w8l"))
            if e == S - 1 and CFG["early"]:
                tt(B("W8", o, o + 128), IX(B("x"), B("w8l")), B("owE"), A.is_lt)
            elif e == S - 1:
                tt(B("W8", o, o + 128), IX(B("y"), B("w8l")), B("owE"), A.is_gt)
            elif e in CFG["w8v"]:
                cp(B("W8", o, o + 128), lst)
            elif e in CFG["sg"]:
                act(B("W8", o, o + 128), lst, bias=0.5, scale=0.5)
            else:
                act(B("W8", o, o + 128), lst)
            terms = [(Pc(p1, 0, 60), B("idb"), B("thw", 0, 60))]
            for a in range(15):
                for q in range(4):
                    terms.append((Pc(p1, 4 * a, 60, p=8, p0=32 * q), B("W8", o + 8 * a, o + 8 * a + 8), EQ(r, r + 15 - a, 4 * q, 4 * q + 4), a == 14))
                r += 15 - a
            group(terms, (1,))
            act(B("cs", 64 * e, 64 * e + 60), Pc(p1, 0, 60), SIGN)

        def back(e, flag, const, vh, own):
            out, o = P(new(), 0, 1, c=15), 64 * (e if apart else e % 4)
            const = 64 if flag in CFG["sg"] else const
            group([(out, B("idb"), B("cneg", const, const + 15)), (out, B("ih" if vh[3] == 2 else "idf"), vh), (out, B("idn" if flag in CFG["sg"] else "idB"), on(flag))]
                  + [(out, B("Us", 3 - c, 131 - c), B("cs", o + c, o + 60, 4)) for c in range(4)], (3,))
            tt(B("offU", 16 * e, 16 * e + 15), out, B(own, 0, 15), A.min)
        slot = {e: e for e in range(5)}
        for e in (3, 2, 1):
            event(e)
            phase("of%d" % e)
            back(e, e, 48, B("v16", 16 * e, 16 * e + 15), "Dm")
        event(0)
        phase("of0")
        back(0, 5 if joint else 0, 96, B("v1K", 16 * t, 16 * t + 15) if apart else B("GF", 0, 15), "DJ")
        if apart:
            event(4)
        if not joint:
            phase("of4")
            back(4, 4, 112, B("WF" if apart else "GF", 0, 15), "Dm")

        def write(win, src, e):
            for a0, a1 in CFG["xparts"] if e == 4 else ((0, 15),):
                cp(IX(win, B("offU", 16 * slot[e] + a0, 16 * slot[e] + a1)), B(src, 16 * a0, 16 * a1))

        phase("st4")
        scan(B("nI", 0, 45), B("c4", 0, 45), B("ub", 0, 45), A.mult, A.add)
        ts(B("nI", 48, 63), B("nI", 2, 45, 3), 5, A.arith_shift_right, 4095, A.bitwise_and)
        lin("nU", B("nU", 0, 15), B("nI", 48, 63))
        tt(B("kp"), IX(B("iw"), B("nU", 0, 15)), B("Bs", 720, 960), A.mult)
        tt(IX(B("kw", K0), B("offU", 16 * slot[S - 1], 16 * slot[S - 1] + 15)), B("kp"), B("cm"), A.add)
        for s in range(S - 1, 0, -1):
            phase("st%d" % s)
            r = 240 * s - 240
            for a0, a1, onv in CFG["kparts"]:
                lo, hi, pz = 16 * a0, 16 * a1, P(new(), a0, a1)
                both = joint and s == 1
                lst = IX(B("kw", 0, K0 + V), B("GU", a0, a1)) if both else IX(KW, vU(t, s - 1, a0, a1))
                kt = B("kt", lo, hi)
                group([(pz, B("ih32"), B("m2k", 240 * both + lo, 240 * both + hi)), (pz, B("idS", 128 * s - 128, 128 * s), B("Bs", r + lo, r + hi))]
                      + [(pz, B("ihd"), B("zW", lo, hi)), (pz, B("idX"), B("xW", lo, hi))] * both, stop=False)
                if onv:
                    ts(kt, lst, -2048.0, A.add)
                else:
                    act(kt, lst, bias=-2048.0)
                tt(B("kp", lo, hi), lst, B("xs", r + lo, r + hi), A.mult)
                group([(pz, B("ih32"), kt)], start=False)
                tt(B("kz", lo, hi), B("kp", lo, hi), pz, A.add)
                ts(B("kn", lo, hi), B("kz", lo, hi), 5, A.arith_shift_right, 4095, A.bitwise_and)
            write(B("kw") if s == 1 else B("kw", K0), "kn", s - 1)
        if not joint:
            phase("xout")
            write(B("xw"), "xn", 4)
        if t + 1 < RACES:
            phase("thr")
            pa = P(new(), 0, 1, c=15)
            group([(pa, B("ones"), on(4))])
            op("S", lambda e: e.activation(B("tot", 1, 16)[0], pa[0], ID, accum_out=B("tot", 0, 1)[0]), B("tot"), [pa], dur=(20, 64, 0, 0, 0))
            act(B("toth"), B("tot", 0, 1), bias=1023.75, scale=0.5)
            act(B("tot", 1, 2), B("tot", 0, 1), bias=4104.0, scale=2.0)
            act(B("thr", 0, 1), B("toth"), bias=B("tot", 1, 2), scale=-4.0)
            act(B("thr", 1, 2), B("thr", 0, 1), bias=8.0 * BIG, scale=BIG / 2)
            act(B("cls", 48, 64), B("ones", 0, 16), scale=B("thr", 1, 2))

    phase("start1")
    ms(B("m2k", 0, 240), -2048.0)
    ms(B("m2k", 240, 480), -2560.0)
    phase("start0")
    zinit(0)
    for t in range(RACES):
        race(t)
    now[0] = -1
    phase("out")
    for a in range(8):
        act(B("idx", 128 * a, 128 * a + 128), B("idb"), scale=float(a + 1))
        act(B("idk", 128 * a, 128 * a + 128), B("idb"), scale=float(a + 1) if a else 35.0)
    ms(B("shp", 0, 512), 2048.0)
    pa = P(new(), 0, 32)
    group([(pa, B("idx", 128 * a, 128 * a + 128), B("xw", 512 * a, 512 * a + 512)) for a in range(8 - CFG["xblocks"], 8)])
    if CFG["xblocks"] < 8:
        tt(B("ox"), B("xw", 0, 512), pa, A.add)
    else:
        act(B("ox"), pa)
    dma("Y", "oy", T.yx[:], T.ox[:], [("ox", 0, 512)], [], 2000.0)
    for h, (lo, hi) in enumerate(CFG["osplit"]):
        for a in range(1, 8):
            o, e = 512 * a + lo, 512 * a + hi
            if (a + h) % 2 == 0:
                ts(B("shp", o, e), B("kw", K0 + o, K0 + e), -2048.0, A.add)
            else:
                act(B("shp", o, e), B("kw", K0 + o, K0 + e), bias=-2048.0)
        pb = Pc(new(), 0, hi - lo)
        group([(pb, B("idk", 0, 128), B("shp", lo, hi))] + [(pb, B("idk", 128 * a, 128 * a + 128), B("shp", 512 * a + lo, 512 * a + hi)) for a in range(1, 8)], (1, 2, 4, 6))
        tt(B("ok", lo, hi), B("kw", K0 + lo, K0 + hi), pb, A.add)
        dma("YS"[h], "ok%d" % h, T.yk[:, lo:hi], T.ok[:, lo:hi], [("ok", lo, hi)], [], 2000.0)
    cnt = emit()
    for sem in ("oy", "ok0", "ok1"):
        g.sync.wait_ge(T.sem[sem], 16)
    for q in "VSTG":
        g.wait_ge(T.sem["q" + q], cnt[q])
    for l in ("lz", "lv", "l0", "l1", "l2", "w0", "w1", "w2") + ("f0", "f1", "f2") * CFG["early"]:
        g.wait_ge(T.sem[l], ne)
